import numpy as np, ml_dtypes
CORES = [48,51,52,55]
N = 4
BF = ml_dtypes.bfloat16
V, S, Q, RO, W = 2048, 8, 256, 6, 3328
def pack(res, cap, B, T, K, wt, ka):
    w = B + 4096 * T - 65536 * K
    return {"res": np.ascontiguousarray(res).reshape(N, 128, W).astype(np.float32).astype(BF), "cap": np.ascontiguousarray(cap).reshape(N, 128, V).astype(np.float32).astype(BF),
            "br": np.ascontiguousarray(w).reshape(N, 128, V).astype(np.int32), "wt": np.ascontiguousarray(wt).reshape(N, 128, 1).astype(np.int32), "ka": np.ascontiguousarray(ka).reshape(N, 128, 1).astype(np.int32)}
def parts(rng):
    sh = (N, 8, 16, V)
    res = (rng.integers(4, 29, (N, 8, 1, W)) * rng.random((N, 8, 16, W))).astype(np.int64)
    heavy = (rng.random((N, 8, 1, W)) < 0.06) & (rng.random((N, 8, 16, W)) < 0.7)
    res = np.where(heavy, rng.integers(0, 256, res.shape), res)
    cap = rng.integers(0, 64, sh); dead = rng.choice(np.array([0.0, 0.25, 0.5]), (N, 8, 1, 1))
    B = rng.integers(0, W, sh); T = np.where(rng.random(sh) < dead, 0, rng.integers(0, 16, sh)); K = np.where(rng.random(sh) < 0.5, 0, rng.integers(0, 16, sh))
    return res, cap, B, T, K, rng.integers(0, 256, (N, 8, 16, 1)), rng.integers(0, V, (N, 8, 16, 1))
def setup_inputs(rng):
    return pack(*parts(rng))
def setup_inputs_corners(rng):
    res, cap, B, T, K, wt, ka = parts(rng)
    v = np.arange(V); t0 = v % S + 1; row = np.arange(16).reshape(16, 1)
    res[..., W - 16:] = np.where(row < np.arange(16), 200, 0)
    res[:, 5, :, 0:V:2] = 255; res[:, 6, :, 0:V:2] = 0; cap[:, 6, :, ::2] = 63
    cl = rng.integers(0, 9, (N, 8, 1, V)); one = rng.integers(0, 16, (N, 8, 1, V)); near = W - 16 + rng.integers(3, 7, (N, 8, 1, V)); same = rng.integers(0, W, (N, 8, 1, V))
    T = np.where(cl == 0, t0 - 1, T); K = np.where(cl == 0, 0, K)
    T = np.where(cl == 1, 15, T); K = np.where(cl == 1, 0, K)
    T = np.where(cl == 2, np.where(row % 2 == 0, t0, t0 - 1), T); K = np.where(cl == 2, 0, K)
    T = np.where(cl == 3, 15, T); K = np.where(cl == 3, np.where(row % 2 == 0, t0 - 1, t0), K)
    T = np.where(cl == 4, np.where(row == one, 15, 0), T); K = np.where(cl == 4, 0, K); B = np.where(cl == 4, near, B); cap = np.where(cl == 4, 63, cap)
    T = np.where(cl == 5, 15, T); K = np.where(cl == 5, 0, K); B = np.where(cl == 5, same, B)
    cap = np.where(cl == 5, np.minimum(np.take_along_axis(res, same, 3), 63), cap)
    chain = np.where(row == 0, v, np.where(row == 1, np.maximum(v - 1, 0), np.where(row == 2, W - 1, np.where(row == 3, 0, V))))
    T = np.where(cl == 6, np.where(row < 5, 15, 0), T); K = np.where(cl == 6, 0, K); B = np.where(cl == 6, chain, B)
    two = (cl == 7) & ((row == 3) | (row == 15))
    T = np.where(two, 15, T); K = np.where(two, 0, K); B = np.where(two, near, B); cap = np.where(cl == 7, 63, cap)
    q = rng.permutation(N); T[q[0], 7] = 0; T[q[1], 7] = 15; K[q[1], 7] = 0
    wt[:, 0] = 0; wt[:, 1] = 255; ka[:, 2] = 0; ka[:, 3] = V - 1; ka[:, 4] = rng.choice(np.array([0, V >> 1]), (N, 16, 1))
    return pack(res, cap, B, T, K, wt, ka)
def setup_inputs_ends(rng):
    sh = (N, 8, 16, V); lane = np.arange(16).reshape(16, 1)
    kd = rng.choice(6, (N, 8, 1, W), p=[0.38, 0.12, 0.25, 0.1, 0.08, 0.07])
    kd[:, :, 0, W - 1] = np.where(np.arange(8) % 2 == 1, 1, 2); kd[:, 7, 0, V - 1] = 5; kd[:, 7, 0, V - 2] = 4
    rot = (lane + rng.integers(0, 16, (N, 8, 1, W))) % 16; some = 255 * (rng.random((N, 8, 16, W)) < 0.2)
    res = np.where(kd == 1, 255, np.where(kd == 2, some, np.where(kd == 3, 63, np.where(kd == 4, np.where(rot < 4, 255, 63), np.where(kd == 5, np.where(rot < 5, 255, 63), 0)))))
    ck = rng.choice(3, (N, 8, 1, V), p=[0.5, 0.15, 0.35]); cap = np.where(ck == 0, 63, np.where(ck == 1, 0, 63 * rng.integers(0, 2, sh)))
    up = rng.random(sh) < rng.choice(np.array([0.0, 0.1, 0.2]), (N, 8, 1, V))
    B = np.where(up, W - 1, 0); T = np.where(up, 15, 0); K = np.where(up, 0, 15)
    fr = rng.random(sh) < rng.choice(np.array([0.0, 0.1, 0.2, 0.4]), (N, 8, 1, V)); live = rng.random(sh) < 0.8
    B = np.where(fr, np.where(rng.random(sh) < 0.7, rng.integers(0, W, sh), rng.choice(np.array([0, V - 1, V, W - 1]), sh)), B)
    T = np.where(fr, np.where(live, 15, 15 * rng.integers(0, 2, sh)), T); K = np.where(fr, np.where(live, 0, 15 * rng.integers(0, 2, sh)), K)
    for j, first, col, c in ((0, 15, V - 1, 63), (1, 15, V - 2, 63), (2, 14, W - 1, 0)):
        a = S * (Q - 1 - j)
        B[:, 7, :, a:a + S] = 0; T[:, 7, :, a:a + S] = 0; K[:, 7, :, a:a + S] = 15; cap[:, 7, :, a:a + S] = c
        B[:, 7, first:, a:a + S] = col; T[:, 7, first:, a:a + S] = 15; K[:, 7, first:, a:a + S] = 0
    wt = np.where(rng.random((N, 8, 16, 1)) < 0.8, 255 * rng.integers(0, 2, (N, 8, 16, 1)), rng.integers(0, 256, (N, 8, 16, 1))); wt[:, 7] = 255; wt[:, 0, 0] = 0
    ka = np.where(rng.random((N, 8, 16, 1)) < 0.8, (V - 1) * rng.integers(0, 2, (N, 8, 16, 1)), rng.integers(0, V, (N, 8, 16, 1)))
    ka[:, 7] = rng.integers(0, V, (N, 16, 1)); ka[:, 0, 0] = 0; ka[:, 0, 1] = V - 1; ka[:, 7, 15] = V - 1
    return pack(res, cap, B, T, K, wt, ka)
def setup_inputs_full(rng):
    res, cap, B, T, K, wt, ka = parts(rng); q = rng.permutation(N); i = np.arange(Q); lane = np.arange(16).reshape(16, 1)
    res[..., W - 16:] = np.where(lane < np.arange(16), 200, 0)
    a = q[0]; T[a, :, :, 0::S] = 0; T[a, :, :, 1::S] = 0; cap[a, :, :, 1::S] = 63
    odd = rng.permutation(8 * Q)[:2 * int(rng.integers(1, 100)) + 1]; k = rng.integers(0, 16, odd.size); g = odd // Q; v = S * (odd % Q)
    B[a, g, k, v] = W - 16 + rng.integers(6, 16, odd.size); T[a, g, k, v] = 15; K[a, g, k, v] = 0
    a = q[1]; hit = lane == rng.integers(0, 16, (8, 1, Q))
    B[a, :, :, 0::S] = np.where(hit, W - 16 + rng.integers(6, 16, (8, 1, Q)), B[a, :, :, 0::S]); T[a, :, :, 0::S] = np.where(hit, 15, T[a, :, :, 0::S]); K[a, :, :, 0::S] = np.where(hit, 0, K[a, :, :, 0::S])
    for a, s in ((q[0], 2), (q[1], 1)):
        five = rng.random((8, 1, Q)) < 0.6; hit = lane == rng.integers(0, 16, (8, 1, Q))
        B[a, :, :, s::S] = np.where(five & hit, W - 11, B[a, :, :, s::S]); K[a, :, :, s::S] = np.where(five & hit, 0, K[a, :, :, s::S])
        T[a, :, :, s::S] = np.where(five, np.where(hit, 15, 0), T[a, :, :, s::S])
    a = q[2]; T[a] = 15; K[a] = 0; B[a, 1::2] = rng.integers(V, W, (4, 16, V))
    for g in (0, 4):
        base = rng.integers(200, 249, 16); turn = (lane + rng.integers(0, 16, (1, Q - 16))) % 16
        res[a, g, :, W - Q:W - 16] = base[turn] + (lane < rng.integers(0, 8, (1, Q - 16)))
        B[a, g] = np.where(rng.random((1, V)) < 0.5, rng.integers(W - Q, W - 16, (16, V)), B[a, g])
    a = q[3]; r = (a + 1) % N; T[a, :, :, 0::S] = 0
    for g in range(8):
        x, y = rng.permutation(16)[:2]; wt[r, g] = 0; wt[r, g, x] = 16; wt[r, g, y] = 1
        if g != 3: ka[r, g] = int(ka[r, g, 0, 0])
        o = rng.permutation(4096); p = ((o * o >> 5) + int(ka[r, g, 0, 0]) * o) & (V - 1)
        first = rng.permutation(np.unique(p, return_index=True)[1]); n = (Q, 8, Q, 1, Q, 8, Q, 1)[g]
        s = (o[first[rng.permutation(Q) % n]] - 37 * i) & 4095; col = V + rng.permutation(Q); k = rng.integers(0, 16, Q)
        res[a, g, :, V:V + Q] = 0; res[a, g, x, col] = s >> 4; res[a, g, y, col] = s & 15
        B[a, g, k, S * i] = col; T[a, g, k, S * i] = 15; K[a, g, k, S * i] = 0
    return pack(res, cap, B, T, K, wt, ka)
def setup_inputs_spread(rng):
    res, cap, B, T, K, wt, ka = parts(rng)
    res = (np.exp2(8 * rng.random((N, 8, 1, W)) ** 3) * rng.random((N, 8, 16, W))).astype(np.int64)
    res = np.where(rng.random((N, 8, 1, W)) < 0.02, rng.integers(0, 256, res.shape), np.minimum(res, 255))
    cap = np.minimum((np.exp2(6 - 6 * rng.random((N, 8, 1, V)) ** 3) * rng.random(cap.shape)).astype(np.int64), 63)
    B = np.minimum((W * rng.random(B.shape) ** rng.choice(np.array([0.5, 1.0, 3.0]), (N, 8, 1, 1))).astype(np.int64), W - 1)
    wt = np.minimum(np.exp2(8 * rng.random(wt.shape)).astype(np.int64), 255)
    return pack(res, cap, B, T, K, wt, ka)
def setup_inputs_ties(rng):
    res, cap, B, T, K, wt, ka = parts(rng)
    lane = np.arange(16).reshape(16, 1); turn = (lane + rng.integers(0, 16, (N, 8, 1, W))) % 16
    res = np.where(turn < rng.integers(2, 4, (N, 8, 1, W)), 40, 0)
    cap = np.broadcast_to(rng.choice(np.array([0, 20, 20, 39, 40, 63]), (N, 8, 1, V)), cap.shape)
    live = rng.random(B.shape) < rng.choice(np.array([0.1, 0.2, 0.3]), (N, 8, 1, 1))
    T = np.where(live, 15, 0); K = np.where(live, 0, K)
    wt[:, ::2] = 1; ka[:, 1::2] = rng.choice(np.array([0, 1, V >> 1, V - 1]), (N, 4, 16, 1))
    return pack(res, cap, B, T, K, wt, ka)
def check_inputs(d):
    bad = []
    for k, lo, hi in (("res", 0, 255), ("cap", 0, 63), ("br", -983040, 64767), ("wt", 0, 255), ("ka", 0, V - 1)):
        v = np.asarray(d[k]).astype(np.float64)
        if not np.all((v >= lo) & (v <= hi) & (v == np.floor(v))): bad.append("range of " + k)
    if np.any((np.asarray(d["br"]).astype(np.int64) & 4095) >= W): bad.append("column numbers in br")
    return bad
def reference(res, cap, br, wt, ka):
    R = res.astype(np.float32).astype(np.int32).reshape(N, 8, 16, W); C = cap.astype(np.float32).astype(np.int32).reshape(N, 8, 16, V)
    b = np.array(br, dtype=np.int32).reshape(N, 8, 16, V); w = wt.astype(np.int64).reshape(N, 8, 16, 1); kf = ka.astype(np.int64).reshape(N, 8, 16, 1)
    A = [0] * N; row = np.arange(16).reshape(1, 16, 1); i = np.arange(Q)
    for t in range(1, RO + 1):
        v = S * i + (t - 1) % S; sent = []
        for r in range(N):
            x = b[r][:, :, v]; on = (((x >> 12) & 15) >= t) & (-(x >> 16) < t)
            c = C[r][:, :, v]; most = 4 + (A[r] & 1)
            pick = np.take_along_axis(R[r], (x & 4095).reshape(8, 1, 16 * Q), 2).reshape(8, 16, 16, Q) * on[:, None]
            m = np.max(pick, axis=2); fail = np.sum(m > c, axis=1) > most
            over = np.where(on, np.sum(np.maximum(pick - c[:, :, None], 0), axis=1), -1)
            gone = fail[:, None] & (row == np.argmax(over, axis=1)[:, None])
            m = np.max(pick * (~gone)[:, None], axis=2)
            m = np.where((np.sum(m > c, axis=1) > most)[:, None], 0, m)
            b[r][:, :, v] = np.where(gone, (x & 65535) - 65536 * (t + S), x)
            R[r][:, :, v] = m; A[r] = int(np.sum(fail)); sent.append(m)
        for r in range(N):
            m = sent[(r - 1 - (t - 1) % (N - 1)) % N]
            u = (np.sum(w[r] * m, axis=1) + 37 * i) & 4095
            p = ((u * u >> 5)[:, None] + kf[r] * u[:, None]) & (V - 1)
            slack = np.maximum(C[r] - R[r][:, :, :V], 0)
            sl = np.take_along_axis(slack, p.reshape(8, 1, 16 * Q), 2).reshape(8, 16, 16, Q)
            score = np.sum(np.minimum(m[:, :, None], sl), axis=1)
            par = np.take_along_axis(p, np.argmax(score, axis=1)[:, None], 1)[:, 0]
            for g in range(8):
                node, first = np.unique(par[g], return_index=True)
                b[r, g, first & 15, node] = V + Q * (t - 1) + first + 4096 * (t + 2)
            if t < RO: R[r][:, :, V + Q * (t - 1):V + Q * t] = m
    return {"yr": np.ascontiguousarray(R[..., :V]).reshape(N, 128, V).astype(np.float32).astype(BF), "yb": b.reshape(N, 128, V).astype(np.float32)}

@@ -1,0 +1,469 @@
+from concourse.mybir import AluOpType as A, ActivationFunctionType as F
+
+NT = 6
+Q = 256
+ZC = 3328
+TR = 4128
+MAGIC = 12582912.0
+SCRATCH = {
+    "RES": ("sbuf", [128, 3344], "bfloat16"),
+    "WD": ("sbuf", [128, 2304], "float32"),
+    "BRI": ("sbuf", [128, 2048], "int32"),
+    "PK": ("sbuf", [128, 4384], "bfloat16"),
+    "EQ": ("sbuf", [128, 16, 256], "bfloat16"),
+    "SND": ("sbuf", [128, NT * Q], "bfloat16"),
+    "LAND": ("sbuf", [128, NT * Q], "bfloat16"),
+    "D16": ("sbuf", [128, 144], "bfloat16"),
+    "D32": ("sbuf", [128, 144], "bfloat16"),
+    "SW0": ("sbuf", [128, 160], "bfloat16"),
+    "SW1": ("sbuf", [128, 160], "bfloat16"),
+    "IO256": ("sbuf", [128, 16], "bfloat16"),
+    "XB": ("sbuf", [128, 16], "bfloat16"),
+    "HB": ("sbuf", [128, 32], "bfloat16"),
+    "HL": ("sbuf", [128, 32], "int32"),
+    "XK": ("sbuf", [128, 8], "float32"),
+}
+for _n in ("FB", "CM", "CX0", "CX1", "MX", "SC", "SEG", "SP"):
+    SCRATCH[_n] = ("sbuf", [128, 4096], "bfloat16")
+for _n in ("CAP", "SL"):
+    SCRATCH[_n] = ("sbuf", [128, 2048], "bfloat16")
+for _n in ("CC", "P0", "ZER", "ONES", "IOBF", "OFFD", "CMP1", "CMP2", "M1", "M2", "SGN", "DELB", "DELI", "N12", "N16", "N16B", "BD1", "BD2", "NEB", "R0"):
+    SCRATCH[_n] = ("sbuf", [128, 256], "bfloat16")
+for _n in ("IOT", "IO16", "NDEL", "NEW", "MB", "RM", "OFS", "KT", "KSC", "KRV", "KB", "KEY", "VS", "CNS", "WOLD", "FA", "FM"):
+    SCRATCH[_n] = ("sbuf", [128, 256], "float32")
+for _n in ("BO", "NBO", "BO4", "BT4", "WTL", "ID", "NID", "N20", "IDT", "C37", "KC", "KC2", "KR16", "NEG", "FOUR", "LIMT"):
+    SCRATCH[_n] = ("sbuf", [128, 128], "bfloat16")
+for _n in ("IOB", "PAR"):
+    SCRATCH[_n] = ("sbuf", [128, 128], "float32")
+for _n in ("UI", "UU", "SQ", "PI2"):
+    SCRATCH[_n] = ("sbuf", [128, 256], "int32")
+for _n in ("EO", "P16", "VB", "OFFC"):
+    SCRATCH[_n] = ("sbuf", [128, 256], "uint16")
+for _n in ("WTI", "KAI", "PI", "KI", "HI"):
+    SCRATCH[_n] = ("sbuf", [128, 1], "int32")
+for _n in ("WTF", "KAF", "PF", "KF", "G16", "G15", "P16F", "H0", "H1", "SACC", "PA", "PB", "PC", "ODD"):
+    SCRATCH[_n] = ("sbuf", [128, 1], "float32")
+for _n in ("IL", "TP", "TW", "LX", "LW", "LB", "LC"):
+    SCRATCH[_n] = ("sbuf", [128, 16], "float32")
+for _n in ("XI", "XI2"):
+    SCRATCH[_n] = ("sbuf", [128, 16], "int32")
+for _n in ("KL", "PL", "PW"):
+    SCRATCH[_n] = ("sbuf", [128, 16], "uint16")
+for _n in range(8):
+    SCRATCH["B%d" % _n] = ("psum", [128, 512], "float32")
+SEMAPHORES = ["cv", "ct", "ca", "cp", "dbr", "dres", "dcap", "dwt", "dka", "dyr", "dyb", "loc"] + ["arr%d" % t for t in range(1, NT + 1)]
+
+
+def rank_program(g, core, T, topo):
+    rank = T.rank_of(core)
+    if rank is None:
+        return
+    cores = T.cores
+    n = len(cores)
+    queues = {"v": g.vector, "t": g.tensor, "a": g.scalar, "p": g, "s": g.sync}
+    own = {"v": "cv", "t": "ct", "a": "ca", "p": "cp"}
+    count = {k: 0 for k in ("v", "t", "a", "p")}
+    known = {k: {} for k in queues}
+    lastw, readers, banks = {}, {}, {}
+
+    def wait_for(eng, toks):
+        best = {}
+        for tok in toks:
+            if tok[0] not in best or best[tok[0]][1] < tok[1]:
+                best[tok[0]] = tok
+        kn = known[eng]
+        for s, val, snap in sorted(best.values(), key=lambda x: -len(x[2])):
+            if kn.get(s, 0) >= val:
+                continue
+            queues[eng].wait_ge(T.sem[s], val)
+            kn[s] = val
+            for s2, v2 in snap.items():
+                if kn.get(s2, 0) < v2:
+                    kn[s2] = v2
+
+    def banks_of(r, w):
+        return set(x.split(".")[0] for x in list(r) + list(w) if "." in x)
+
+    def deps(eng, r, w):
+        toks = []
+        for k in r:
+            if k in lastw:
+                toks.append(lastw[k])
+        for k in w:
+            if k in lastw:
+                toks.append(lastw[k])
+            toks += list(readers.get(k, {}).values())
+        for k in banks_of(r, w):
+            toks += [tok for e, tok in banks.get(k, {}).items() if e != eng]
+        if eng == "t":
+            toks = [x for x in toks if x[0] != "ct"]
+        return toks
+
+    def note(eng, tok, r, w):
+        for k in r:
+            readers.setdefault(k, {})[tok[0]] = tok
+        for k in w:
+            lastw[k] = tok
+            readers[k] = {}
+        for k in banks_of(r, w):
+            banks.setdefault(k, {})[eng] = tok
+
+    def op(eng, f, r, w):
+        wait_for(eng, deps(eng, r, w))
+        count[eng] += 1
+        tok = (own[eng], count[eng], dict(known[eng]))
+        f().then_inc(T.sem[own[eng]], 1)
+        note(eng, tok, r, w)
+
+    def dma(eng, out, in_, sem, r, w):
+        wait_for(eng, deps(eng, r, w))
+        queues[eng].dma_start(out, in_).then_inc(T.sem[sem], 16)
+        note(eng, (sem, 16, dict(known[eng])), r, w)
+
+    V, PE, AC = g.vector, g.tensor, g.scalar
+
+    def v(f, r, w):
+        op("v", f, r, w)
+
+    def mm(out, lhs, rhs, st, sp, r, w):
+        op("t", lambda: PE.matmul(out, lhs, rhs, st, sp), r, w)
+
+    def act(out, in_, r, w, func=F.Copy, bias=0.0, scale=1.0):
+        op("a", lambda: AC.activation(out, in_, func, bias=bias, scale=scale), r, w)
+
+    def fill(ap, c, k):
+        v(lambda: V.memset(ap, c), [], [k])
+
+    def pfill(ap, c, k, cols):
+        op("p", lambda: g.iota(ap, [[0, cols]], c, 0, allow_small_or_imprecise_dtypes=True), [], [k])
+
+    def ts(out, in0, s1, s2, o0, o1, r, w):
+        if o1 is None:
+            v(lambda: V.tensor_scalar(out, in0, s1, None, o0), r, w)
+        else:
+            v(lambda: V.tensor_scalar(out, in0, s1, s2, o0, o1), r, w)
+
+    def tt(out, a, b, o, r, w):
+        v(lambda: V.tensor_tensor(out, a, b, o), r, w)
+
+    def cp(out, a, r, w):
+        v(lambda: V.tensor_copy(out, a), r, w)
+
+    def scan(out, d0, d1, o0, o1, r, w):
+        v(lambda: V.tensor_tensor_scan(out, d0, d1, 0.0, o0, o1), r, w)
+
+    dma("s", T.BRI[:], T.br[:], "dbr", [], ["BRI"])
+    dma("a", T.RES[:, 0:ZC], T.res[:], "dres", [], ["RES"])
+    dma("s", T.CAP[:], T.cap[:], "dcap", [], ["CAP"])
+    dma("s", T.WTI[:], T.wt[:], "dwt", [], ["WTI"])
+    dma("s", T.KAI[:], T.ka[:], "dka", [], ["KAI"])
+    op("p", lambda: g.iota(T.PI[:], [[0, 1]], 0, 1), [], ["PI"])
+    op("p", lambda: g.iota(T.IOT[:], [[1, 256]], 0, 0, allow_small_or_imprecise_dtypes=True), [], ["IOT"])
+    op("p", lambda: g.iota(T.IO16[:], [[0, 16], [1, 16]], 0, 0, allow_small_or_imprecise_dtypes=True), [], ["IO16"])
+    op("p", lambda: g.iota(T.IOB[:], [[16, 8], [0, 16]], 0, 0, allow_small_or_imprecise_dtypes=True), [], ["IOB"])
+    pfill(T.SP[:], 0, "SP", 4096)
+    pfill(T.ONES[:], 1, "ONES", 256)
+    pfill(T.LIMT[:], 18, "LIMT", 128)
+    pfill(T.ZER[:], 0, "ZER", 256)
+    pfill(T.VS[:], 0, "VS", 256)
+    pfill(T.PAR[:], 1, "PAR", 128)
+    pfill(T.FOUR[:], 4, "FOUR", 128)
+    pfill(T.C37[:], 37, "C37", 128)
+    pfill(T.NEG[:], -131072, "NEG", 128)
+    fill(T.RES[:, ZC:ZC + 16], 0.0, "RESZ")
+    fill(T.SEG[:], 1.0, "SEG")
+    fill(T.SEG[:, 0:4096:16], 0.0, "SEG")
+    fill(T.MB[:], 1e9, "MB")
+    fill(T.MB[:, 0:256:16], -1e9, "MB")
+    fill(T.RM[:], 1.0, "RM")
+    fill(T.RM[:, 15:256:16], 0.0, "RM")
+    act(T.KC[:], T.IO16[:, 0:128], ["IO16"], ["KC"], bias=15.0, scale=-1.0)
+    act(T.KC2[:], T.IO16[:, 0:128], ["IO16"], ["KC2"], bias=30720.0, scale=-2048.0)
+    act(T.KR16[:], T.IO16[:, 0:128], ["IO16"], ["KR16"], scale=16.0)
+    act(T.IO256[:], T.IOT[:, 0:16], ["IOT"], ["IO256"], scale=256.0)
+    act(T.IOBF[:], T.IOT[:], ["IOT"], ["IOBF"])
+    ts(T.KI[:], T.PI[:], 15, None, A.bitwise_and, None, ["PI"], ["KI"])
+    ts(T.HI[:], T.PI[:], 16, None, A.bitwise_and, None, ["PI"], ["HI"])
+    cp(T.PF[:], T.PI[:], ["PI"], ["PF"])
+    cp(T.KF[:], T.KI[:], ["KI"], ["KF"])
+    tt(T.G16[:], T.PF[:], T.KF[:], A.subtract, ["PF", "KF"], ["G16"])
+    ts(T.G15[:], T.G16[:], 15.0, None, A.add, None, ["G16"], ["G15"])
+    ts(T.P16F[:], T.PF[:], 16.0, None, A.add, None, ["PF"], ["P16F"])
+    ts(T.H1[:], T.HI[:], 0.0625, None, A.mult, None, ["HI"], ["H1"])
+    ts(T.H0[:], T.HI[:], -0.0625, 1.0, A.mult, A.add, ["HI"], ["H0"])
+    ts(T.D16[:], T.IOT[:, 0:144], T.G15[:, 0:1], 16.0, A.is_equal, A.mult, ["IOT", "G15"], ["D16"])
+    ts(T.NBO[:], T.IOB[:], T.G16[:, 0:1], -512.0, A.is_equal, A.mult, ["IOB", "G16"], ["NBO"])
+
+    def one_hot(out, off, pos, value, r, w):
+        if value is None:
+            ts(out, off, pos, None, A.is_equal, None, r, w)
+        else:
+            ts(out, off, pos, value, A.is_equal, A.mult, r, w)
+
+    def more_constants():
+        one_hot(T.ID[:], T.IOT[:, 0:128], T.PF[:, 0:1], None, ["IOT", "PF"], ["ID"])
+        one_hot(T.SW0[:], T.IOT[:, 0:160], T.P16F[:, 0:1], T.H0[:, 0:1], ["IOT", "P16F", "H0"], ["SW0"])
+        one_hot(T.SW1[:], T.IOT[:, 0:160], T.P16F[:, 0:1], T.H1[:, 0:1], ["IOT", "P16F", "H1"], ["SW1"])
+        one_hot(T.DELB[:], T.IO16[:], T.KF[:, 0:1], None, ["IO16", "KF"], ["DELB"])
+        ts(T.BT4[:], T.IO16[:, 0:128], T.KF[:, 0:1], 8192.0, A.is_gt, A.mult, ["IO16", "KF"], ["BT4"])
+        act(T.BO[:], T.NBO[:], ["NBO"], ["BO"], scale=-0.001953125)
+        act(T.NID[:], T.ID[:], ["ID"], ["NID"], scale=-1.0)
+        act(T.N20[:], T.ID[:], ["ID"], ["N20"], scale=-1048576.0)
+        act(T.BO4[:], T.NBO[:], ["NBO"], ["BO4"], scale=-16.0)
+        act(T.D32[:], T.D16[:], ["D16"], ["D32"], scale=2048.0)
+        act(T.NDEL[:], T.DELB[:], ["DELB"], ["NDEL"], bias=1.0, scale=-1.0)
+        act(T.OFFD[:], T.DELB[:], ["DELB"], ["OFFD"], bias=-2097152.0, scale=2097152.0)
+        op("a", lambda: AC.activation(T.IL[:], T.IOT[:, 0:16], F.Identity, bias=T.KF[:, 0:1], scale=16.0), ["IOT", "KF"], ["IL"])
+        act(T.TP[:], T.IL[:], ["IL"], ["TP"], bias=float(TR))
+        act(T.TW[:], T.IL[:], ["IL"], ["TW"], bias=2048.0)
+        op("a", lambda: AC.activation(T.XK[:], T.IOT[:, 0:8], F.Identity, bias=T.KF[:, 0:1], scale=-2.0), ["IOT", "KF"], ["XK"])
+
+    def last_constants():
+        tt(T.BT4[:], T.BT4[:], T.BO[:], A.mult, ["BT4", "BO"], ["BT4"])
+        tt(T.DELI[:], T.IOT[:], T.DELB[:], A.mult, ["IOT", "DELB"], ["DELI"])
+        cp(T.OFFC[:], T.IOT[:], ["IOT"], ["OFFC"])
+        cp(T.WTF[:], T.WTI[:], ["WTI"], ["WTF"])
+        cp(T.KAF[:], T.KAI[:], ["KAI"], ["KAF"])
+        ts(T.WTL[:], T.BO[:], T.WTF[:, 0:1], None, A.mult, None, ["BO", "WTF"], ["WTL"])
+
+    def floors(src, size, out, ok, sign):
+        act(T.FA[:], src, ["WD"], ["FA"], bias=-0.5 + 0.5 / size, scale=1.0 / size)
+        act(T.FM[:], T.FA[:], ["FA"], ["FM"], bias=MAGIC)
+        act(out, T.FM[:], ["FM"], [ok], bias=-sign * size * MAGIC, scale=sign * size)
+
+    def first_offsets():
+        src = T.BRI[:, 0:2048:8]
+        ts(T.OFS[:], src, 0.0, 4096.0, A.is_lt, A.mult, ["BRI"], ["OFS"])
+        ts(T.UU[:], src, 65535, None, A.bitwise_and, None, ["BRI"], ["UU"])
+        ts(T.UI[:], src, 4095, None, A.bitwise_and, None, ["BRI"], ["UI"])
+        ts(T.KT[:], T.UU[:], 4096.0, 4096.0, A.is_lt, A.mult, ["UU"], ["KT"])
+        tt(T.OFS[:], T.OFS[:], T.KT[:], A.max, ["OFS", "KT"], ["OFS"])
+        tt(T.OFS[:], T.OFS[:], T.UI[:], A.max, ["OFS", "UI"], ["OFS"])
+        ts(T.EO[:], T.OFS[:], float(ZC), None, A.min, None, ["OFS"], ["EO"])
+
+    def offsets_a(t):
+        w = T.WD[:, t - 1:2048:8]
+        floors(w, 4096.0, T.N12[:], "N12", 1.0)
+        floors(w, 65536.0, T.N16[:], "N16", -1.0)
+        act(T.BD2[:], T.N16[:], ["N16"], ["BD2"], F.Relu, bias=-65536.0 * (t - 1))
+
+    def offsets_b(t):
+        mm(T.B6[:, 256:512], T.ID[:], T.N12[:], True, False, ["ID", "N12"], ["B6.t"])
+        mm(T.B6[:, 256:512], T.ID[:], T.N16[:], False, True, ["ID", "N16"], ["B6.t"])
+        act(T.BD1[:], T.B6[:, 256:512], ["B6.t"], ["BD1"], F.Relu, bias=4096.0 * t, scale=-1.0)
+        mm(T.B2[:, 256:512], T.NID[:], T.N12[:], True, False, ["NID", "N12"], ["B2.off"])
+        mm(T.B2[:, 256:512], T.ID[:], T.BD1[:], False, False, ["ID", "BD1"], ["B2.off"])
+        mm(T.B2[:, 256:512], T.ID[:], T.BD2[:], False, True, ["ID", "BD2"], ["B2.off"])
+
+    def offsets_c(t):
+        tt(T.OFS[:], T.WD[:, t - 1:2048:8], T.B2[:, 256:512], A.add, ["WD", "B2.off"], ["OFS"])
+        ts(T.EO[:], T.OFS[:], float(ZC), None, A.min, None, ["OFS"], ["EO"])
+
+    def bulk():
+        act(T.PK[:, 0:4096], T.RES[:, 0:3344].indirect(T.EO[:, 0:256]), ["RES", "RESZ", "EO"], ["PK"])
+
+    def cap_room(t):
+        act(T.B0[:, 0:256], T.CAP[:, t - 1:2048:8], ["CAP"], ["B0.cap"])
+
+    def cap_wide(t, half):
+        cx = "CX%d" % (t & 1)
+        if half or t == 2:
+            act(T.CC[:], T.CAP[:, t - 1:2048:8], ["CAP"], ["CC"])
+        act(T[cx][:, 2048 * half:2048 * half + 2048], T.CC[:].indirect(T.OFFC[:, 128 * half:128 * half + 128]), ["CC", "OFFC"], ["%s%d" % (cx, half)])
+
+    def to_list(col, key, parts, wkey, first):
+        for ip in (0, 1):
+            for h in (0, 1):
+                sw, o = (T.SW0, (16, 0)[h]) if ip == 0 else (T.SW1, (32, 16)[h])
+                for j, p in enumerate(parts):
+                    mm(T.B4[:, col + ip:col + 16:2], sw[:, o:o + 128], p[:, h:16:2], first and h == 0 and j == 0,
+                       (first or ip == 1) and h == 1 and j == len(parts) - 1, ["SW0", "SW1", key], [wkey])
+
+    def set_words():
+        tt(T.WOLD[:], T.WD[:, 0:2304].indirect(T.PW[:, 0:16]), T.NDEL[:], A.mult, ["WD", "PW", "NDEL"], ["WOLD"])
+        tt(T.WD[:, 0:2304].indirect(T.PW[:, 0:16]), T.WOLD[:], T.NEW[:], A.add, ["WOLD", "NEW", "PW"], ["WD"])
+
+    def suspended(t):
+        tt(T.WD[:, t - 1:2048:8], T.WD[:, t - 1:2048:8], T.B3[:, 256:512], A.subtract, ["WD", "B3.z"], ["WD"])
+
+    def parity():
+        op("a", lambda: AC.activation(T.SGN[:], T.B2[:, 0:256], F.Sign, accum_out=T.SACC[:]), ["B2.c1"], ["SGN", "SACC"])
+        mm(T.B5[:, 0:1], T.PAR[:], T.SACC[:], True, True, ["PAR", "SACC"], ["B5.par"])
+        act(T.PA[:], T.B5[:, 0:1], ["B5.par"], ["PA"], scale=-0.03125)
+        act(T.PB[:], T.PA[:], ["PA"], ["PB"], bias=-0.25, scale=0.5)
+        act(T.PC[:], T.PB[:], ["PB"], ["PC"], bias=MAGIC)
+        act(T.PB[:], T.PC[:], ["PC"], ["PB"], bias=2.0 * MAGIC, scale=-2.0)
+        op("a", lambda: AC.activation(T.ODD[:], T.PB[:], F.Identity, bias=T.PA[:, 0:1]), ["PA", "PB"], ["ODD"])
+
+    def new_words():
+        mm(T.B7[:, 256:512], T.ID[:], T.DELI[:], True, False, ["ID", "DELI"], ["B7.n"])
+        mm(T.B7[:, 256:512], T.IDT[:], T.DELB[:], False, True, ["IDT", "DELB"], ["B7.n"])
+        act(T.NEW[:], T.B7[:, 256:512], ["B7.n"], ["NEW"])
+
+    more_constants()
+    first_offsets()
+    act(T.PK[:, 0:3072], T.RES[:, 0:3344].indirect(T.EO[:, 0:192]), ["RES", "RESZ", "EO"], ["PK"])
+    cap_room(1)
+    cp(T.SP[:, 0:4096:16], T.CAP[:, 0:2048:8], ["CAP"], ["SP"])
+    scan(T.CX1[:], T.SEG[:], T.SP[:], A.mult, A.max, ["SEG", "SP"], ["CX10", "CX11"])
+    cp(T.PK[:, 3072:4096], T.RES[:, 0:3344].indirect(T.EO[:, 192:256]), ["RES", "RESZ", "EO"], ["PKx"])
+    last_constants()
+    for j in range(4):
+        b, k = (T.B5, "B5.x") if j % 2 else (T.B7, "B7.x")
+        s = slice(512 * j, 512 * j + 512)
+        mm(b[:], T.ID[:], T.CAP[:, s], True, False, ["ID", "CAP"], [k])
+        mm(b[:], T.NID[:], T.RES[:, s], False, True, ["NID", "RES"], [k])
+        act(T.SL[:, s], b[:], [k], ["SL"], F.Relu)
+
+    for t in range(1, NT + 1):
+        c = t - 1
+        cx = "CX%d" % (t & 1)
+        L0 = c * Q
+        land, lk = T.LAND[:, L0:L0 + Q], "LAND%d" % t
+        snd, sk = T.SND[:, L0:L0 + Q], "SND%d" % t
+        cp(T.P0[:], T.PK[:, 0:4096:16], ["PK", "PKx"], ["P0"])
+        v(lambda: V.memset(T.PK[:, 0:4096:16], 255.0), [], ["PK"])
+        mm(T.B1[:, 0:256], T.KC[0:1, :], T.ONES[0:1, :], True, False, ["KC", "ONES"], ["B1.ks"])
+        mm(T.B1[:, 0:256], T.D16[:, 15:143], T.CAP[:, c:2048:8], False, False, ["D16", "CAP"], ["B1.ks"])
+        mm(T.B3[:, 256:512], T.ID[:], T.P0[:], True, False, ["ID", "P0"], ["B3.z"])
+        mm(T.B3[:, 256:512], T.NID[:], T.CAP[:, c:2048:8], False, True, ["NID", "CAP"], ["B3.z"])
+        act(T.R0[:], T.B3[:, 256:512], ["B3.z"], ["R0"], F.Relu)
+        for j in range(2):
+            s = slice(2048 * j, 2048 * j + 2048)
+            scan(T.CM[:, s], T[cx][:, s], T.PK[:, s], A.min, A.max, ["%s%d" % (cx, j), "PK"], ["CM%d" % j])
+            for k in range(1, 16):
+                mm(T.B1[:, 128 * j:128 * j + 128], T.D16[:, 15 - k:143 - k], T.CM[:, 2048 * j + k:2048 * j + 2048:16], False, False,
+                   ["D16", "CM%d" % j], ["B1.ks"])
+        mm(T.B1[:, 0:256], T.D16[:, 15:143], T.R0[:], False, True, ["D16", "R0"], ["B1.ks"])
+        cp(T.PK[:, 0:4096:16], T.P0[:], ["P0"], ["PK"])
+        if 1 < t < NT:
+            cap_wide(t + 1, 1)
+        if t > 1:
+            set_words()
+        else:
+            cp(T.WD[:, 0:2048], T.BRI[:], ["BRI"], ["WD"])
+            fill(T.WD[:, 2048:2304], 0.0, "WD")
+        if t < NT:
+            offsets_a(t + 1)
+        floors(T.WD[:, c:2048:8], 65536.0, T.N16B[:], "N16B", -1.0)
+        act(T.IDT[:], T.ID[:], ["ID"], ["IDT"], scale=2048.0 + 256.0 * c + 4096.0 * (t + 2))
+        scan(T.FB[:], T.SEG[:], T.PK[:, 0:4096], A.mult, A.max, ["SEG", "PK"], ["FB"])
+        tt(T.CMP1[:], T.FB[:, 15:4096:16], T.B0[:, 0:256], A.is_gt, ["FB", "B0.cap"], ["CMP1"])
+        mm(T.B2[:, 0:256], T.LIMT[:], T.ONES[:], True, False, ["LIMT", "ONES"], ["B2.c1"])
+        mm(T.B2[:, 0:256], T.NBO[:], T.CMP1[:], False, True, ["NBO", "CMP1"], ["B2.c1"])
+        mm(T.B4[:, 0:16], T.KR16[0:1, :], T.ONES[0:1, 0:16], True, False, ["KR16", "ONES"], ["B4.kl"])
+        mm(T.B4[:, 0:16], T.ONES[0:1, 0:128], T.IO256[0:1, :], False, False, ["IO256", "ONES"], ["B4.kl"])
+        v(lambda: V.transpose(T.KT[:], T.B1[:, 0:256]), ["B1.ks"], ["KT"])
+        scan(T.KSC[:], T.MB[:], T.KT[:], A.min, A.max, ["MB", "KT"], ["KSC"])
+        cp(T.XI[:], T.KSC[:, 15:256:16], ["KSC"], ["XI"])
+        ts(T.XI2[:], T.XI[:], 15, None, A.bitwise_and, None, ["XI"], ["XI2"])
+        ts(T.XB[:], T.XI2[:], -1.0, 15.0, A.mult, A.add, ["XI2"], ["XB"])
+        to_list(0, "XB", [T.XB], "B4.kl", False)
+        tt(T.M1[:], T.FB[:, 15:4096:16], T.B2[:, 0:256], A.min, ["FB", "B2.c1"], ["M1"])
+        act(T.B0[:, 256:512], T.M1[:], ["M1"], ["B0.m1"], F.Relu)
+        if t < NT:
+            offsets_b(t + 1)
+        new_words()
+        act(T.R0[:], T.B2[:, 0:256], ["B2.c1"], ["R0"], F.Relu, scale=4096.0)
+        cp(T.KL[:], T.B4[:, 0:16], ["B4.kl"], ["KL"])
+        v(lambda: V.tensor_copy(T.PK[:, 0:4096].indirect(T.KL[:, 0:16]), T.ZER[:]), ["KL", "ZER"], ["PK"])
+        scan(T.FB[:], T.SEG[:], T.PK[:, 0:4096], A.mult, A.max, ["SEG", "PK"], ["FB"])
+        tt(T.CMP2[:], T.FB[:, 15:4096:16], T.B0[:, 0:256], A.is_gt, ["FB", "B0.cap"], ["CMP2"])
+        mm(T.B3[:, 0:256], T.LIMT[:], T.ONES[:], True, False, ["LIMT", "ONES"], ["B3.c2"])
+        mm(T.B3[:, 0:256], T.NBO[:], T.CMP2[:], False, True, ["NBO", "CMP2"], ["B3.c2"])
+        if t < NT:
+            parity()
+        tt(T.M2[:], T.FB[:, 15:4096:16], T.B3[:, 0:256], A.min, ["FB", "B3.c2"], ["M2"])
+        tt(snd, T.M2[:], T.B0[:, 256:512], A.max, ["M2", "B0.m1"], [sk])
+        dst = cores[(rank + 1 + c % (n - 1)) % n]
+        rid, pid, _s = topo.addr(dst)
+        wait_for("p", deps("p", [sk], []))
+        g.remote_dma(land, snd, T.sem["arr%d" % t], T.sem.loc, pid, rid, topo.mask(core, dst))
+        lastw[lk] = ("arr%d" % t, len(topo.engines(core, dst)), {})
+        mm(T.B5[:, 256:512], T.ID[:], T.CAP[:, c:2048:8], True, False, ["ID", "CAP"], ["B5.sl"])
+        mm(T.B5[:, 256:512], T.NID[:], snd, False, True, ["NID", sk], ["B5.sl"])
+        act(T.SL[:, c:2048:8], T.B5[:, 256:512], ["B5.sl"], ["SL"], F.Relu)
+        act(T.RES[:, c:2048:8], snd, [sk], ["RES"])
+        if t == NT:
+            dma("s", T.yr[:], T.RES[:, 0:2048], "dyr", ["RES"], ["yr"])
+        if t < NT:
+            cap_room(t + 1)
+            op("a", lambda: AC.activation(T.LIMT[:], T.FOUR[:], F.Copy, bias=18.0, scale=T.ODD[:, 0:1]), ["FOUR", "ODD"], ["LIMT"])
+        scan(T.KRV[:, ::-1], T.RM[:, ::-1], T.KSC[:, ::-1], A.mult, A.max, ["RM", "KSC"], ["KRV"])
+        v(lambda: V.transpose(T.KB[:], T.KRV[:]), ["KRV"], ["KB"])
+        tt(T.NEB[:], T.B1[:, 0:256], T.KB[:], A.not_equal, ["B1.ks", "KB"], ["NEB"])
+        if t < NT:
+            offsets_c(t + 1)
+        mm(T.B5[:, 0:256], T.C37[0:1, :], T.IOBF[0:1, :], True, False, ["C37", "IOBF"], ["B5.u"])
+        mm(T.B5[:, 0:256], T.WTL[:], land, False, True, ["WTL", lk], ["B5.u"])
+        for j in range(4):
+            act(T.MX[:, 1024 * j:1024 * j + 1024], land.indirect(T.OFFC[:, 64 * j:64 * j + 64]), [lk, "OFFC"], ["MX%d" % j])
+        mm(T.B3[:, 256:512], T.NID[:], T.N16B[:], True, False, ["NID", "N16B"], ["B3.z"])
+        mm(T.B3[:, 256:512], T.N20[:], T.NEB[:], False, False, ["N20", "NEB"], ["B3.z"])
+        mm(T.B3[:, 256:512], T.NID[:], T.R0[:], False, True, ["NID", "R0"], ["B3.z"])
+        cp(T.UI[:], T.B5[:, 0:256], ["B5.u"], ["UI"])
+        ts(T.UU[:], T.UI[:], 4095, None, A.bitwise_and, None, ["UI"], ["UU"])
+        ts(T.B5[:, 256:512], T.UU[:], T.KAF[:, 0:1], None, A.mult, None, ["UU", "KAF"], ["B5.fu"])
+        tt(T.SQ[:], T.UU[:], T.UU[:], A.mult, ["UU"], ["SQ"])
+        ts(T.SQ[:], T.SQ[:], 5, None, A.arith_shift_right, None, ["SQ"], ["SQ"])
+        tt(T.PI2[:], T.SQ[:], T.B5[:, 256:512], A.add, ["SQ", "B5.fu"], ["PI2"])
+        ts(T.PI2[:], T.PI2[:], 2047, None, A.bitwise_and, None, ["PI2"], ["PI2"])
+        cp(T.P16[:], T.PI2[:], ["PI2"], ["P16"])
+        act(T.B3[:, 256:512], T.B3[:, 256:512], ["B3.z"], ["B3.z"], F.Relu, bias=65536.0 * (t + 8))
+        if t < NT:
+            act(T.RES[:, 2048 + L0:2048 + L0 + Q], land, [lk], ["RES"])
+            bulk()
+            cap_wide(t + 1, 0)
+        if t == 1:
+            cap_wide(2, 1)
+        mm(T.B6[:, 0:256], T.NEG[:], T.ONES[:], True, False, ["NEG", "ONES"], ["B6.x"])
+        mm(T.B6[:, 0:256], T.KC2[0:1, :], T.ONES[0:1, :], False, False, ["KC2", "ONES"], ["B6.x"])
+        for j in range(4):
+            s = slice(1024 * j, 1024 * j + 1024)
+            tt(T.SC[:, s], T.SL[:, 0:2048].indirect(T.P16[:, 64 * j:64 * j + 64]), T.MX[:, s], A.min, ["SL", "P16", "MX%d" % j], ["SC%d" % j])
+            for k in range(16):
+                mm(T.B6[:, 64 * j:64 * j + 64], T.D32[:, 15 - k:143 - k], T.SC[:, 1024 * j + k:1024 * j + 1024:16], False, j == 3 and k == 15,
+                   ["D32", "SC%d" % j], ["B6.x"])
+        mm(T.B7[:, 0:256], T.ID[:], T.OFFD[:], True, False, ["ID", "OFFD"], ["B7.x"])
+        suspended(t)
+        tt(T.KEY[:], T.B6[:, 0:256], T.PI2[:], A.add, ["B6.x", "PI2"], ["KEY"])
+        v(lambda: V.transpose(T.KT[:], T.KEY[:]), ["KEY"], ["KT"])
+        scan(T.KSC[:], T.MB[:], T.KT[:], A.min, A.max, ["MB", "KT"], ["KSC"])
+        cp(T.XI[:], T.KSC[:, 15:256:16], ["KSC"], ["XI"])
+        ts(T.HL[:, 0:16], T.XI[:], 2040, None, A.bitwise_and, None, ["XI"], ["HLa"])
+        ts(T.HL[:, 16:32], T.XI[:], 7, None, A.bitwise_and, None, ["XI"], ["HLb"])
+        cp(T.HB[:], T.HL[:], ["HLa", "HLb"], ["HB"])
+        to_list(32, "HB", [T.HB, T.HB[:, 16:32]], "B4.lv", True)
+        to_list(48, "HB", [T.HB[:, 16:32]], "B4.lv", True)
+        tt(T.VS[:, 15:256:16], T.HL[:, 0:16], T.HL[:, 16:32], A.add, ["HLa", "HLb"], ["VS"])
+        scan(T.KRV[:, ::-1], T.RM[:, ::-1], T.VS[:, ::-1], A.mult, A.max, ["RM", "VS"], ["KRV"])
+        v(lambda: V.transpose(T.KB[:], T.KRV[:]), ["KRV"], ["KB"])
+        cp(T.VB[:], T.KB[:], ["KB"], ["VB"])
+        for i in range(16):
+                ts(T.EQ[:, i, 0:256 - 16 * i], T.VB[:, 16 * i:256], T.B4[:, 32 + i:33 + i], None, A.is_equal, None, ["VB", "B4.lv"], ["EQ%d" % i])
+                mm(T.B7[:, 16 * i:16 * i + 16], T.BT4[:], T.EQ[:, i, 0:16], False, i == 15, ["BT4", "EQ%d" % i], ["B7.x"])
+                if i < 15:
+                    mm(T.B7[:, 16 * i + 16:256], T.BO4[:], T.EQ[:, i, 16:256 - 16 * i], False, False, ["BO4", "EQ%d" % i], ["B7.x"])
+        lv = T.B4[:, 32:48]
+        if t < NT:
+            ts(T.LW[:], T.B4[:, 48:64], float(t), 8192.0, A.not_equal, A.mult, ["B4.lv"], ["LW"])
+            ts(T.LX[:], lv, 2.0, T.XK[:, t:t + 1], A.mult, A.add, ["B4.lv", "XK"], ["LX"])
+            tt(T.LW[:], T.LW[:], T.TP[:], A.min, ["LW", "TP"], ["LW"])
+            tt(T.LX[:], T.LW[:], T.LX[:], A.max, ["LW", "LX"], ["LX"])
+        scan(T.CNS[:], T.MB[:], T.B7[:, 0:256], A.min, A.max, ["MB", "B7.x"], ["CNS"])
+        if t < NT:
+            tt(T.LB[:], T.CNS[:, 15:256:16], T.TP[:], A.min, ["CNS", "TP"], ["LB"])
+            tt(T.LC[:], T.LB[:], T.LX[:], A.max, ["LB", "LX"], ["LC"])
+            cp(T.PL[:], T.LC[:], ["LC"], ["PL"])
+            v(lambda: V.tensor_copy(T.PK[:, 0:4384].indirect(T.PL[:, 0:16]), land), ["PL", lk], ["PK"])
+        tt(T.LB[:], T.CNS[:, 15:256:16], T.TW[:], A.min, ["CNS", "TW"], ["LB"])
+        tt(T.LC[:], T.LB[:], lv, A.max, ["LB", "B4.lv"], ["LC"])
+        cp(T.PW[:], T.LC[:], ["LC"], ["PW"])
+
+    set_words()
+    dma("s", T.yb[:], T.WD[:, 0:2048], "dyb", ["WD"], ["yb"])
+    g.wait_ge(T.sem.loc, sum(len(topo.engines(core, cores[(rank + 1 + c % (n - 1)) % n])) for c in range(NT)))
+    for s, k in own.items():
+        g.wait_ge(T.sem[k], count[s])
+    for s in ("dyr", "dyb", "dbr", "dres", "dcap", "dwt", "dka"):
+        g.wait_ge(T.sem[s], 16)

@@ -2,56 +2,60 @@ from concourse.mybir import AluOpType as A, ActivationFunctionType as F
 
 NT = 6
 Q = 256
+H = 128
 ZC = 3328
-TR = 4128
-MAGIC = 12582912.0
+P0 = 4096
+TR = 4352
 SCRATCH = {
     "RES": ("sbuf", [128, 3344], "bfloat16"),
     "WD": ("sbuf", [128, 2304], "float32"),
     "BRI": ("sbuf", [128, 2048], "int32"),
-    "PK": ("sbuf", [128, 4384], "bfloat16"),
+    "PK": ("sbuf", [128, 4608], "bfloat16"),
     "EQ": ("sbuf", [128, 16, 256], "bfloat16"),
     "SND": ("sbuf", [128, NT * Q], "bfloat16"),
     "LAND": ("sbuf", [128, NT * Q], "bfloat16"),
-    "D16": ("sbuf", [128, 144], "bfloat16"),
-    "D32": ("sbuf", [128, 144], "bfloat16"),
-    "SW0": ("sbuf", [128, 160], "bfloat16"),
-    "SW1": ("sbuf", [128, 160], "bfloat16"),
+    "IO2K": ("sbuf", [128, 2048], "float32"),
+    "PF": ("sbuf", [128, 256], "float16"),
+    "XW": ("sbuf", [128, 256], "float16"),
+    "IDH": ("sbuf", [128, 128], "float16"),
+    "BOH": ("sbuf", [128, 8], "float16"),
     "IO256": ("sbuf", [128, 16], "bfloat16"),
-    "XB": ("sbuf", [128, 16], "bfloat16"),
-    "HB": ("sbuf", [128, 32], "bfloat16"),
-    "HL": ("sbuf", [128, 32], "int32"),
     "XK": ("sbuf", [128, 8], "float32"),
+    "SACC": ("sbuf", [128, 2], "float32"),
 }
-for _n in ("FB", "CM", "CX0", "CX1", "MX", "SC", "SEG", "SP"):
+for _n in ("FB", "CM", "CX0", "CX1", "MX", "SC"):
     SCRATCH[_n] = ("sbuf", [128, 4096], "bfloat16")
-for _n in ("CAP", "SL"):
+for _n in ("CAP", "SL", "SEG", "TOH"):
     SCRATCH[_n] = ("sbuf", [128, 2048], "bfloat16")
-for _n in ("CC", "P0", "ZER", "ONES", "IOBF", "OFFD", "CMP1", "CMP2", "M1", "M2", "SGN", "DELB", "DELI", "N12", "N16", "N16B", "BD1", "BD2", "NEB", "R0"):
+for _n in ("ONES", "IOBF", "OFFD", "CMP1", "CMP2", "MA", "SGN", "DELB", "N12", "KN", "KP", "BD1", "BD2", "R0", "XS", "XA", "OH", "FQ"):
     SCRATCH[_n] = ("sbuf", [128, 256], "bfloat16")
-for _n in ("IOT", "IO16", "NDEL", "NEW", "MB", "RM", "OFS", "KT", "KSC", "KRV", "KB", "KEY", "VS", "CNS", "WOLD", "FA", "FM"):
+for _n in ("IOT", "IO16", "NDEL", "NEW", "MB", "OFS", "KT", "KS", "CNS", "WOLD", "IOTM", "SQ"):
     SCRATCH[_n] = ("sbuf", [128, 256], "float32")
-for _n in ("BO", "NBO", "BO4", "BT4", "WTL", "ID", "NID", "N20", "IDT", "C37", "KC", "KC2", "KR16", "NEG", "FOUR", "LIMT"):
+for _n in ("BO", "NBO", "BO4", "BT4", "WTL", "ID", "NID", "N12M", "N16M", "P16M", "P20M", "N19M", "C37", "CU", "KC", "KC2", "KR16", "NEG", "FOUR", "LIMT"):
     SCRATCH[_n] = ("sbuf", [128, 128], "bfloat16")
-for _n in ("IOB", "PAR"):
+for _n in ("B16", "B32K", "NB8"):
+    SCRATCH[_n] = ("sbuf", [128, 8], "bfloat16")
+for _n in ("IOB", "PAR", "IDF"):
     SCRATCH[_n] = ("sbuf", [128, 128], "float32")
-for _n in ("UI", "UU", "SQ", "PI2"):
+for _n in ("UI", "UU", "PI2"):
     SCRATCH[_n] = ("sbuf", [128, 256], "int32")
 for _n in ("EO", "P16", "VB", "OFFC"):
     SCRATCH[_n] = ("sbuf", [128, 256], "uint16")
-for _n in ("WTI", "KAI", "PI", "KI", "HI"):
+for _n in ("WTI", "KAI", "PI", "KI"):
     SCRATCH[_n] = ("sbuf", [128, 1], "int32")
-for _n in ("WTF", "KAF", "PF", "KF", "G16", "G15", "P16F", "H0", "H1", "SACC", "PA", "PB", "PC", "ODD"):
+for _n in ("WTF", "KAF", "PFL", "KF", "G16", "MULP", "ADDP", "SUBP", "PB", "PC", "ODD"):
     SCRATCH[_n] = ("sbuf", [128, 1], "float32")
 for _n in ("IL", "TP", "TW", "LX", "LW", "LB", "LC"):
     SCRATCH[_n] = ("sbuf", [128, 16], "float32")
-for _n in ("XI", "XI2"):
+for _n in ("XI", "XI2", "LI"):
     SCRATCH[_n] = ("sbuf", [128, 16], "int32")
-for _n in ("KL", "PL", "PW"):
+for _n in ("KL", "PL", "PW", "LV"):
     SCRATCH[_n] = ("sbuf", [128, 16], "uint16")
 for _n in range(8):
     SCRATCH["B%d" % _n] = ("psum", [128, 512], "float32")
-SEMAPHORES = ["cv", "ct", "ca", "cp", "dbr", "dres", "dcap", "dwt", "dka", "dyr", "dyb", "loc"] + ["arr%d" % t for t in range(1, NT + 1)]
+SEMAPHORES = (["cv", "ct", "ca", "cp", "dbr", "dres", "dcap", "dwt", "dka", "dyr", "dyb", "loc"]
+              + ["arr%d%d" % (t, h) for t in range(1, NT + 1) for h in (0, 1)])
+MAGIC = 12582912.0
 
 
 def rank_program(g, core, T, topo):
@@ -134,8 +138,8 @@ def rank_program(g, core, T, topo):
     def fill(ap, c, k):
         v(lambda: V.memset(ap, c), [], [k])
 
-    def pfill(ap, c, k, cols):
-        op("p", lambda: g.iota(ap, [[0, cols]], c, 0, allow_small_or_imprecise_dtypes=True), [], [k])
+    def iota(ap, pattern, base, cm, k):
+        op("p", lambda: g.iota(ap, pattern, base, cm, allow_small_or_imprecise_dtypes=True), [], [k])
 
     def ts(out, in0, s1, s2, o0, o1, r, w):
         if o1 is None:
@@ -152,317 +156,482 @@ def rank_program(g, core, T, topo):
     def scan(out, d0, d1, o0, o1, r, w):
         v(lambda: V.tensor_tensor_scan(out, d0, d1, 0.0, o0, o1), r, w)
 
+    def half(h, size=H):
+        return slice(size * h, size * h + size)
+
+    def nodes(t, h):
+        return slice(t - 1 + 1024 * h, 1024 * h + 1024, 8)
+
+    BA = [T.B1, T.B2]
+    BG = [T.B3, T.B4]
+    BU = [T.B5, T.B6]
+
     dma("s", T.BRI[:], T.br[:], "dbr", [], ["BRI"])
-    dma("a", T.RES[:, 0:ZC], T.res[:], "dres", [], ["RES"])
+    dma("s", T.RES[:, 0:ZC], T.res[:], "dres", [], ["RES", "RESG"])
     dma("s", T.CAP[:], T.cap[:], "dcap", [], ["CAP"])
-    dma("s", T.WTI[:], T.wt[:], "dwt", [], ["WTI"])
-    dma("s", T.KAI[:], T.ka[:], "dka", [], ["KAI"])
+    dma("a", T.WTI[:], T.wt[:], "dwt", [], ["WTI"])
+    dma("a", T.KAI[:], T.ka[:], "dka", [], ["KAI"])
     op("p", lambda: g.iota(T.PI[:], [[0, 1]], 0, 1), [], ["PI"])
-    op("p", lambda: g.iota(T.IOT[:], [[1, 256]], 0, 0, allow_small_or_imprecise_dtypes=True), [], ["IOT"])
-    op("p", lambda: g.iota(T.IO16[:], [[0, 16], [1, 16]], 0, 0, allow_small_or_imprecise_dtypes=True), [], ["IO16"])
-    op("p", lambda: g.iota(T.IOB[:], [[16, 8], [0, 16]], 0, 0, allow_small_or_imprecise_dtypes=True), [], ["IOB"])
-    pfill(T.SP[:], 0, "SP", 4096)
-    pfill(T.ONES[:], 1, "ONES", 256)
-    pfill(T.LIMT[:], 18, "LIMT", 128)
-    pfill(T.ZER[:], 0, "ZER", 256)
-    pfill(T.VS[:], 0, "VS", 256)
-    pfill(T.PAR[:], 1, "PAR", 128)
-    pfill(T.FOUR[:], 4, "FOUR", 128)
-    pfill(T.C37[:], 37, "C37", 128)
-    pfill(T.NEG[:], -131072, "NEG", 128)
+    iota(T.IOT[:], [[1, 256]], 0, 0, "IOT")
+    iota(T.IO16[:], [[0, 16], [1, 16]], 0, 0, "IO16")
+    iota(T.IOB[:], [[16, 8], [0, 16]], 0, 0, "IOB")
+    iota(T.ONES[:], [[0, 256]], 1, 0, "ONES")
+    for name, c in (("LIMT", 18), ("PAR", 1), ("FOUR", 8), ("C37", 37), ("CU", 532480), ("NEG", -131072)):
+        iota(T[name][:], [[0, 128]], c, 0, name)
+    iota(T.IO2K[:], [[1, 2048]], 0, 0, "IO2K")
     fill(T.RES[:, ZC:ZC + 16], 0.0, "RESZ")
     fill(T.SEG[:], 1.0, "SEG")
-    fill(T.SEG[:, 0:4096:16], 0.0, "SEG")
+    fill(T.SEG[:, 0:2048:16], 0.0, "SEG")
     fill(T.MB[:], 1e9, "MB")
     fill(T.MB[:, 0:256:16], -1e9, "MB")
-    fill(T.RM[:], 1.0, "RM")
-    fill(T.RM[:, 15:256:16], 0.0, "RM")
+    fill(T.PK[:, TR:TR + Q], 0.0, "PKT")
+    fill(T.WD[:, 2048:2304], 0.0, "WDT")
     act(T.KC[:], T.IO16[:, 0:128], ["IO16"], ["KC"], bias=15.0, scale=-1.0)
     act(T.KC2[:], T.IO16[:, 0:128], ["IO16"], ["KC2"], bias=30720.0, scale=-2048.0)
-    act(T.KR16[:], T.IO16[:, 0:128], ["IO16"], ["KR16"], scale=16.0)
+    act(T.KR16[:], T.IO16[:, 0:128], ["IO16"], ["KR16"], bias=15.0, scale=16.0)
     act(T.IO256[:], T.IOT[:, 0:16], ["IOT"], ["IO256"], scale=256.0)
     act(T.IOBF[:], T.IOT[:], ["IOT"], ["IOBF"])
     ts(T.KI[:], T.PI[:], 15, None, A.bitwise_and, None, ["PI"], ["KI"])
-    ts(T.HI[:], T.PI[:], 16, None, A.bitwise_and, None, ["PI"], ["HI"])
-    cp(T.PF[:], T.PI[:], ["PI"], ["PF"])
+    cp(T.PFL[:], T.PI[:], ["PI"], ["PFL"])
     cp(T.KF[:], T.KI[:], ["KI"], ["KF"])
-    tt(T.G16[:], T.PF[:], T.KF[:], A.subtract, ["PF", "KF"], ["G16"])
-    ts(T.G15[:], T.G16[:], 15.0, None, A.add, None, ["G16"], ["G15"])
-    ts(T.P16F[:], T.PF[:], 16.0, None, A.add, None, ["PF"], ["P16F"])
-    ts(T.H1[:], T.HI[:], 0.0625, None, A.mult, None, ["HI"], ["H1"])
-    ts(T.H0[:], T.HI[:], -0.0625, 1.0, A.mult, A.add, ["HI"], ["H0"])
-    ts(T.D16[:], T.IOT[:, 0:144], T.G15[:, 0:1], 16.0, A.is_equal, A.mult, ["IOT", "G15"], ["D16"])
-    ts(T.NBO[:], T.IOB[:], T.G16[:, 0:1], -512.0, A.is_equal, A.mult, ["IOB", "G16"], ["NBO"])
-
-    def one_hot(out, off, pos, value, r, w):
-        if value is None:
-            ts(out, off, pos, None, A.is_equal, None, r, w)
-        else:
-            ts(out, off, pos, value, A.is_equal, A.mult, r, w)
-
-    def more_constants():
-        one_hot(T.ID[:], T.IOT[:, 0:128], T.PF[:, 0:1], None, ["IOT", "PF"], ["ID"])
-        one_hot(T.SW0[:], T.IOT[:, 0:160], T.P16F[:, 0:1], T.H0[:, 0:1], ["IOT", "P16F", "H0"], ["SW0"])
-        one_hot(T.SW1[:], T.IOT[:, 0:160], T.P16F[:, 0:1], T.H1[:, 0:1], ["IOT", "P16F", "H1"], ["SW1"])
-        one_hot(T.DELB[:], T.IO16[:], T.KF[:, 0:1], None, ["IO16", "KF"], ["DELB"])
-        ts(T.BT4[:], T.IO16[:, 0:128], T.KF[:, 0:1], 8192.0, A.is_gt, A.mult, ["IO16", "KF"], ["BT4"])
-        act(T.BO[:], T.NBO[:], ["NBO"], ["BO"], scale=-0.001953125)
-        act(T.NID[:], T.ID[:], ["ID"], ["NID"], scale=-1.0)
-        act(T.N20[:], T.ID[:], ["ID"], ["N20"], scale=-1048576.0)
-        act(T.BO4[:], T.NBO[:], ["NBO"], ["BO4"], scale=-16.0)
-        act(T.D32[:], T.D16[:], ["D16"], ["D32"], scale=2048.0)
-        act(T.NDEL[:], T.DELB[:], ["DELB"], ["NDEL"], bias=1.0, scale=-1.0)
-        act(T.OFFD[:], T.DELB[:], ["DELB"], ["OFFD"], bias=-2097152.0, scale=2097152.0)
-        op("a", lambda: AC.activation(T.IL[:], T.IOT[:, 0:16], F.Identity, bias=T.KF[:, 0:1], scale=16.0), ["IOT", "KF"], ["IL"])
-        act(T.TP[:], T.IL[:], ["IL"], ["TP"], bias=float(TR))
-        act(T.TW[:], T.IL[:], ["IL"], ["TW"], bias=2048.0)
-        op("a", lambda: AC.activation(T.XK[:], T.IOT[:, 0:8], F.Identity, bias=T.KF[:, 0:1], scale=-2.0), ["IOT", "KF"], ["XK"])
-
-    def last_constants():
-        tt(T.BT4[:], T.BT4[:], T.BO[:], A.mult, ["BT4", "BO"], ["BT4"])
-        tt(T.DELI[:], T.IOT[:], T.DELB[:], A.mult, ["IOT", "DELB"], ["DELI"])
-        cp(T.OFFC[:], T.IOT[:], ["IOT"], ["OFFC"])
-        cp(T.WTF[:], T.WTI[:], ["WTI"], ["WTF"])
-        cp(T.KAF[:], T.KAI[:], ["KAI"], ["KAF"])
-        ts(T.WTL[:], T.BO[:], T.WTF[:, 0:1], None, A.mult, None, ["BO", "WTF"], ["WTL"])
-
-    def floors(src, size, out, ok, sign):
-        act(T.FA[:], src, ["WD"], ["FA"], bias=-0.5 + 0.5 / size, scale=1.0 / size)
-        act(T.FM[:], T.FA[:], ["FA"], ["FM"], bias=MAGIC)
-        act(out, T.FM[:], ["FM"], [ok], bias=-sign * size * MAGIC, scale=sign * size)
+    tt(T.G16[:], T.PFL[:], T.KF[:], A.subtract, ["PFL", "KF"], ["G16"])
+    ts(T.ID[:], T.IOT[:, 0:128], T.PFL[:, 0:1], None, A.is_equal, None, ["IOT", "PFL"], ["ID"])
+    ts(T.DELB[:], T.IO16[:], T.KF[:, 0:1], None, A.is_equal, None, ["IO16", "KF"], ["DELB"])
+    ts(T.BT4[:], T.IO16[:, 0:128], T.KF[:, 0:1], 8192.0, A.is_gt, A.mult, ["IO16", "KF"], ["BT4"])
+    ts(T.BO[:], T.IOB[:], T.G16[:, 0:1], None, A.is_equal, None, ["IOB", "G16"], ["BO"])
+    ts(T.MULP[:], T.KF[:], 0.0, -1.875, A.is_equal, A.mult, ["KF"], ["MULP"])
+    ts(T.ADDP[:], T.KF[:], 0.0, float(P0), A.is_equal, A.mult, ["KF"], ["ADDP"])
+    ts(T.MULP[:], T.MULP[:], 2.0, None, A.add, None, ["MULP"], ["MULP"])
+    tt(T.ADDP[:], T.ADDP[:], T.KF[:], A.add, ["ADDP", "KF"], ["ADDP"])
+    ts(T.SUBP[:], T.MULP[:], -1.0, None, A.mult, None, ["MULP"], ["SUBP"])
+    ts(T.XK[:], T.IOT[:, 0:8], T.SUBP[:, 0:1], T.ADDP[:, 0:1], A.mult, A.add, ["IOT", "SUBP", "ADDP"], ["XK"])
+    cp(T.IDH[:], T.ID[:], ["ID"], ["IDH"])
+    cp(T.BOH[:], T.BO[:, 0:128:16], ["BO"], ["BOH"])
+    cp(T.OFFC[:], T.IOT[:], ["IOT"], ["OFFC"])
+    tt(T.BT4[:], T.BT4[:], T.BO[:], A.mult, ["BT4", "BO"], ["BT4"])
+    cp(T.WTF[:], T.WTI[:], ["WTI"], ["WTF"])
+    cp(T.KAF[:], T.KAI[:], ["KAI"], ["KAF"])
+    ts(T.WTL[:], T.BO[:], T.WTF[:, 0:1], None, A.mult, None, ["BO", "WTF"], ["WTL"])
+    for name, c in (("NID", -1.0), ("N12M", -4096.0), ("N16M", -16.0), ("P16M", 65536.0), ("P20M", 1048576.0), ("N19M", -524288.0), ("IDF", 1.0)):
+        act(T[name][:], T.ID[:], ["ID"], [name], scale=c)
+    for name, c in (("NBO", -512.0), ("BO4", 8192.0)):
+        act(T[name][:], T.BO[:], ["BO"], [name], scale=c)
+    for name, c in (("B16", 16.0), ("B32K", 32768.0), ("NB8", -1.0)):
+        act(T[name][:], T.BO[:, 0:128:16], ["BO"], [name], scale=c)
+    act(T.NDEL[:], T.DELB[:], ["DELB"], ["NDEL"], bias=1.0, scale=-1.0)
+    act(T.OFFD[:], T.DELB[:], ["DELB"], ["OFFD"], bias=-2097152.0, scale=2097152.0)
+    op("a", lambda: AC.activation(T.IL[:], T.IOT[:, 0:16], F.Identity, bias=T.KF[:, 0:1], scale=16.0), ["IOT", "KF"], ["IL"])
+    act(T.TP[:], T.IL[:], ["IL"], ["TP"], bias=float(TR))
+    act(T.TW[:], T.IL[:], ["IL"], ["TW"], bias=2048.0)
+    act(T.TOH[:, 0:256], T.DELB[:], ["DELB"], ["TOH"])
+    for s in (256, 512, 1024):
+        act(T.TOH[:, s:2 * s], T.TOH[:, 0:s], ["TOH"], ["TOH"])
+    tt(T.IOTM[:], T.IOT[:], T.OFFD[:], A.add, ["IOT", "OFFD"], ["IOTM"])
 
     def first_offsets():
         src = T.BRI[:, 0:2048:8]
         ts(T.OFS[:], src, 0.0, 4096.0, A.is_lt, A.mult, ["BRI"], ["OFS"])
-        ts(T.UU[:], src, 65535, None, A.bitwise_and, None, ["BRI"], ["UU"])
+        ts(T.UU[:], src, 65535, None, A.bitwise_and, None, ["BRI"], ["UU0", "UU1"])
         ts(T.UI[:], src, 4095, None, A.bitwise_and, None, ["BRI"], ["UI"])
-        ts(T.KT[:], T.UU[:], 4096.0, 4096.0, A.is_lt, A.mult, ["UU"], ["KT"])
-        tt(T.OFS[:], T.OFS[:], T.KT[:], A.max, ["OFS", "KT"], ["OFS"])
+        ts(T.KT[:], T.UU[:], 4096.0, 4096.0, A.is_lt, A.mult, ["UU0", "UU1"], ["KT"])
         tt(T.OFS[:], T.OFS[:], T.UI[:], A.max, ["OFS", "UI"], ["OFS"])
+        tt(T.OFS[:], T.OFS[:], T.KT[:], A.max, ["OFS", "KT"], ["OFS"])
         ts(T.EO[:], T.OFS[:], float(ZC), None, A.min, None, ["OFS"], ["EO"])
+
+    def k_part(out, key, t):
+        act(out, T.WD[:, t - 1:2048:8], ["WD"], [key], bias=199.50390625, scale=1.0 / 65536)
 
     def offsets_a(t):
-        w = T.WD[:, t - 1:2048:8]
-        floors(w, 4096.0, T.N12[:], "N12", 1.0)
-        floors(w, 65536.0, T.N16[:], "N16", -1.0)
-        act(T.BD2[:], T.N16[:], ["N16"], ["BD2"], F.Relu, bias=-65536.0 * (t - 1))
+        act(T.N12[:], T.WD[:, t - 1:2048:8], ["WD"], ["N12"], bias=219.5625, scale=1.0 / 4096)
+        k_part(T.KN[:], "KN", t)
+        mm(T.B7[:, 256:512], T.ID[:], T.N12[:], True, False, ["ID", "N12"], ["B7.hi"])
+        mm(T.B7[:, 256:512], T.N16M[:], T.KN[:], False, True, ["N16M", "KN"], ["B7.hi"])
+        act(T.BD2[:], T.KN[:], ["KN"], ["BD2"], F.Relu, bias=4096.0 * (201 - t), scale=-4096.0)
+        act(T.BD1[:], T.B7[:, 256:512], ["B7.hi"], ["BD1"], F.Relu, bias=4096.0 * (t - 2980), scale=-4096.0)
 
     def offsets_b(t):
-        mm(T.B6[:, 256:512], T.ID[:], T.N12[:], True, False, ["ID", "N12"], ["B6.t"])
-        mm(T.B6[:, 256:512], T.ID[:], T.N16[:], False, True, ["ID", "N16"], ["B6.t"])
-        act(T.BD1[:], T.B6[:, 256:512], ["B6.t"], ["BD1"], F.Relu, bias=4096.0 * t, scale=-1.0)
-        mm(T.B2[:, 256:512], T.NID[:], T.N12[:], True, False, ["NID", "N12"], ["B2.off"])
-        mm(T.B2[:, 256:512], T.ID[:], T.BD1[:], False, False, ["ID", "BD1"], ["B2.off"])
-        mm(T.B2[:, 256:512], T.ID[:], T.BD2[:], False, True, ["ID", "BD2"], ["B2.off"])
+        mm(T.B7[:, 0:256], T.IDF[:], T.WD[:, t - 1:2048:8], True, False, ["IDF", "WD"], ["B7.x"])
+        mm(T.B7[:, 0:256], T.N12M[:], T.N12[:], False, False, ["N12M", "N12"], ["B7.x"])
+        mm(T.B7[:, 0:256], T.ID[:], T.BD1[:], False, False, ["ID", "BD1"], ["B7.x"])
+        mm(T.B7[:, 0:256], T.ID[:], T.BD2[:], False, True, ["ID", "BD2"], ["B7.x"])
 
-    def offsets_c(t):
-        tt(T.OFS[:], T.WD[:, t - 1:2048:8], T.B2[:, 256:512], A.add, ["WD", "B2.off"], ["OFS"])
-        ts(T.EO[:], T.OFS[:], float(ZC), None, A.min, None, ["OFS"], ["EO"])
+    def offsets_c():
+        ts(T.EO[:], T.B7[:, 0:256], 901120.0, float(ZC), A.add, A.min, ["B7.x"], ["EO"])
 
-    def bulk():
-        act(T.PK[:, 0:4096], T.RES[:, 0:3344].indirect(T.EO[:, 0:256]), ["RES", "RESZ", "EO"], ["PK"])
+    def rows(lo, hi, h, eng="a"):
+        out, src = T.PK[:, 16 * lo:16 * hi], T.RES[:, 0:3344].indirect(T.EO[:, lo:hi])
+        if eng == "a":
+            act(out, src, ["RES", "RESG", "RESZ", "EO"], ["PK%d" % h])
+        else:
+            cp(out, src, ["RES", "RESG", "RESZ", "EO"], ["PKx"])
+
+    def row0(h):
+        return T.PK[:, 2048 * h:2048 * h + 2048:16]
+
+    def aside(h):
+        return T.PK[:, P0 + H * h:P0 + H * h + H]
+
+    def row0_aside(h):
+        act(aside(h), row0(h), ["PK%d" % h, "PKx"], ["P0%d" % h])
+        act(row0(h), T.ONES[:, 0:H], ["ONES"], ["PK%d" % h], scale=255.0)
+
+    def cap_wide(t, ks):
+        cx = "CX%d" % (t & 1)
+        for k in ks:
+            op("p", lambda: g.affine_select(T[cx][:, k:4096:16], T.CAP[:, t - 1:2048:8], [[0, Q]], A.is_ge, 0.0, 0, 0), ["CAP"], [cx + "k%d" % k])
 
     def cap_room(t):
         act(T.B0[:, 0:256], T.CAP[:, t - 1:2048:8], ["CAP"], ["B0.cap"])
 
-    def cap_wide(t, half):
-        cx = "CX%d" % (t & 1)
-        if half or t == 2:
-            act(T.CC[:], T.CAP[:, t - 1:2048:8], ["CAP"], ["CC"])
-        act(T[cx][:, 2048 * half:2048 * half + 2048], T.CC[:].indirect(T.OFFC[:, 128 * half:128 * half + 128]), ["CC", "OFFC"], ["%s%d" % (cx, half)])
+    def word_list():
+        tt(T.LB[:], T.CNS[:, 15:256:16], T.TW[:], A.min, ["CNS", "TW"], ["LB"])
+        tt(T.LC[:], T.LB[:], T.B0[:, 256:272], A.max, ["LB", "B0.lv"], ["LC"])
+        cp(T.PW[:], T.LC[:], ["LC"], ["PW"])
 
-    def to_list(col, key, parts, wkey, first):
-        for ip in (0, 1):
-            for h in (0, 1):
-                sw, o = (T.SW0, (16, 0)[h]) if ip == 0 else (T.SW1, (32, 16)[h])
-                for j, p in enumerate(parts):
-                    mm(T.B4[:, col + ip:col + 16:2], sw[:, o:o + 128], p[:, h:16:2], first and h == 0 and j == 0,
-                       (first or ip == 1) and h == 1 and j == len(parts) - 1, ["SW0", "SW1", key], [wkey])
+    def old_words():
+        tt(T.WOLD[:], T.WD[:, 0:2304].indirect(T.PW[:, 0:16]), T.NDEL[:], A.mult, ["WD", "WDT", "PW", "NDEL"], ["WOLD"])
 
     def set_words():
-        tt(T.WOLD[:], T.WD[:, 0:2304].indirect(T.PW[:, 0:16]), T.NDEL[:], A.mult, ["WD", "PW", "NDEL"], ["WOLD"])
-        tt(T.WD[:, 0:2304].indirect(T.PW[:, 0:16]), T.WOLD[:], T.NEW[:], A.add, ["WOLD", "NEW", "PW"], ["WD"])
+        tt(T.WD[:, 0:2304].indirect(T.PW[:, 0:16]), T.WOLD[:], T.NEW[:], A.add, ["WOLD", "NEW", "PW"], ["WD", "WDT"])
 
-    def suspended(t):
-        tt(T.WD[:, t - 1:2048:8], T.WD[:, t - 1:2048:8], T.B3[:, 256:512], A.subtract, ["WD", "B3.z"], ["WD"])
+    def marks():
+        act(T.OH[:], T.TOH[:].indirect(T.KL[:]), ["TOH", "KL0", "KL1"], ["OH"])
+        for h in (0, 1):
+            op("a", lambda: AC.activation(T.SGN[:, half(h)], BG[h][:, 0:H], F.Sign, accum_out=T.SACC[:, h:h + 1]),
+               ["B%d.g0" % (3 + h)], ["SGN%d" % h, "SACC%d" % h])
+
+    def suspended_a(t):
+        z = T.B7[:, 256:512]
+        k_part(T.KP[:], "KP", t)
+        mm(z, T.P20M[:], T.OH[:], True, False, ["P20M", "OH"], ["B7.hi"])
+        mm(z, T.N19M[:], T.SGN[:], False, False, ["N19M", "SGN0", "SGN1"], ["B7.hi"])
+        mm(z, T.P16M[:], T.KP[:], False, True, ["P16M", "KP"], ["B7.hi"])
+        act(z, z, ["B7.hi"], ["B7.hi"], F.Relu, bias=65536.0 * (t + 8 - 200) - 1572864.0)
+
+    def suspended_b(t):
+        tt(T.WD[:, t - 1:2048:8], T.WD[:, t - 1:2048:8], T.B7[:, 256:512], A.subtract, ["WD", "B7.hi"], ["WD"])
+
+    def new_words(t):
+        act(T.NEW[:], T.IOTM[:], ["IOTM"], ["NEW"], F.Relu, bias=2048.0 + 256.0 * (t - 1) + 4096.0 * (t + 2))
 
     def parity():
-        op("a", lambda: AC.activation(T.SGN[:], T.B2[:, 0:256], F.Sign, accum_out=T.SACC[:]), ["B2.c1"], ["SGN", "SACC"])
-        mm(T.B5[:, 0:1], T.PAR[:], T.SACC[:], True, True, ["PAR", "SACC"], ["B5.par"])
-        act(T.PA[:], T.B5[:, 0:1], ["B5.par"], ["PA"], scale=-0.03125)
-        act(T.PB[:], T.PA[:], ["PA"], ["PB"], bias=-0.25, scale=0.5)
+        mm(T.B7[:, 0:1], T.PAR[:], T.SACC[:, 0:1], True, False, ["PAR", "SACC0"], ["B7.x"])
+        mm(T.B7[:, 0:1], T.PAR[:], T.SACC[:, 1:2], False, True, ["PAR", "SACC1"], ["B7.x"])
+        act(T.PB[:], T.B7[:, 0:1], ["B7.x"], ["PB"], bias=-0.25, scale=-0.015625)
         act(T.PC[:], T.PB[:], ["PB"], ["PC"], bias=MAGIC)
-        act(T.PB[:], T.PC[:], ["PC"], ["PB"], bias=2.0 * MAGIC, scale=-2.0)
-        op("a", lambda: AC.activation(T.ODD[:], T.PB[:], F.Identity, bias=T.PA[:, 0:1]), ["PA", "PB"], ["ODD"])
+        act(T.PC[:], T.PC[:], ["PC"], ["PC"], bias=MAGIC + 0.0, scale=-1.0)
+        op("a", lambda: AC.activation(T.ODD[:], T.PB[:], F.Identity, bias=T.PC[:, 0:1]), ["PB", "PC"], ["ODD"])
+        op("a", lambda: AC.activation(T.LIMT[:], T.FOUR[:], F.Copy, bias=20.0, scale=T.ODD[:, 0:1]), ["FOUR", "ODD"], ["LIMT"])
 
-    def new_words():
-        mm(T.B7[:, 256:512], T.ID[:], T.DELI[:], True, False, ["ID", "DELI"], ["B7.n"])
-        mm(T.B7[:, 256:512], T.IDT[:], T.DELB[:], False, True, ["IDT", "DELB"], ["B7.n"])
-        act(T.NEW[:], T.B7[:, 256:512], ["B7.n"], ["NEW"])
-
-    more_constants()
     first_offsets()
-    act(T.PK[:, 0:3072], T.RES[:, 0:3344].indirect(T.EO[:, 0:192]), ["RES", "RESZ", "EO"], ["PK"])
+    rows(0, 128, 0)
+    rows(160, 256, 1, "v")
+    row0_aside(0)
+    rows(128, 160, 1)
+    cap_wide(1, (0, 1, 2))
+    for k in range(3, 16):
+        cp(T.CX1[:, k:4096:16], T.CAP[:, 0:2048:8], ["CAP"], ["CX1k%d" % k])
+    cap_wide(2, range(8))
+    row0_aside(1)
     cap_room(1)
-    cp(T.SP[:, 0:4096:16], T.CAP[:, 0:2048:8], ["CAP"], ["SP"])
-    scan(T.CX1[:], T.SEG[:], T.SP[:], A.mult, A.max, ["SEG", "SP"], ["CX10", "CX11"])
-    cp(T.PK[:, 3072:4096], T.RES[:, 0:3344].indirect(T.EO[:, 192:256]), ["RES", "RESZ", "EO"], ["PKx"])
-    last_constants()
-    for j in range(4):
-        b, k = (T.B5, "B5.x") if j % 2 else (T.B7, "B7.x")
-        s = slice(512 * j, 512 * j + 512)
-        mm(b[:], T.ID[:], T.CAP[:, s], True, False, ["ID", "CAP"], [k])
-        mm(b[:], T.NID[:], T.RES[:, s], False, True, ["NID", "RES"], [k])
-        act(T.SL[:, s], b[:], [k], ["SL"], F.Relu)
 
     for t in range(1, NT + 1):
         c = t - 1
         cx = "CX%d" % (t & 1)
+        cxk = [cx + "k%d" % k for k in range(16)]
         L0 = c * Q
-        land, lk = T.LAND[:, L0:L0 + Q], "LAND%d" % t
-        snd, sk = T.SND[:, L0:L0 + Q], "SND%d" % t
-        cp(T.P0[:], T.PK[:, 0:4096:16], ["PK", "PKx"], ["P0"])
-        v(lambda: V.memset(T.PK[:, 0:4096:16], 255.0), [], ["PK"])
-        mm(T.B1[:, 0:256], T.KC[0:1, :], T.ONES[0:1, :], True, False, ["KC", "ONES"], ["B1.ks"])
-        mm(T.B1[:, 0:256], T.D16[:, 15:143], T.CAP[:, c:2048:8], False, False, ["D16", "CAP"], ["B1.ks"])
-        mm(T.B3[:, 256:512], T.ID[:], T.P0[:], True, False, ["ID", "P0"], ["B3.z"])
-        mm(T.B3[:, 256:512], T.NID[:], T.CAP[:, c:2048:8], False, True, ["NID", "CAP"], ["B3.z"])
-        act(T.R0[:], T.B3[:, 256:512], ["B3.z"], ["R0"], F.Relu)
-        for j in range(2):
-            s = slice(2048 * j, 2048 * j + 2048)
-            scan(T.CM[:, s], T[cx][:, s], T.PK[:, s], A.min, A.max, ["%s%d" % (cx, j), "PK"], ["CM%d" % j])
+        dst = cores[(rank + 1 + c % (n - 1)) % n]
+        rid, pid, _s = topo.addr(dst)
+
+        def land(h):
+            return T.LAND[:, L0 + H * h:L0 + H * h + H]
+
+        def snd(h):
+            return T.SND[:, L0 + H * h:L0 + H * h + H]
+
+        def lk(h):
+            return "LAND%d%d" % (t, h)
+
+        def sk(h):
+            return "SND%d%d" % (t, h)
+
+        def sums_begin(h):
+            b, key = BA[h], "B%d.k" % (1 + h)
+            mm(b[:, 0:H], T.ONES[0:1, 0:H], T.KC[0:1, :], True, False, ["KC", "ONES"], [key])
+            mm(b[:, 0:H:16], T.CAP[:, nodes(t, h)], T.B16[:], False, False, ["B16", "CAP"], [key])
+            d, dk = BU[h][:, 384:512], "B%d.d" % (5 + h)
+            mm(d, T.NID[:], T.CAP[:, nodes(t, h)], True, False, ["NID", "CAP"], [dk])
+            mm(d, T.ID[:], aside(h), False, True, ["ID", "P0%d" % h], [dk])
+            act(T.R0[:, half(h)], d, [dk], ["R0%d" % h], F.Relu)
+
+        def clipped(h):
+            s = half(h, 2048)
+            scan(T.CM[:, s], T[cx][:, s], T.PK[:, s], A.min, A.max, cxk + ["PK%d" % h], ["CM%d" % h])
+            b, key = BA[h], "B%d.k" % (1 + h)
             for k in range(1, 16):
-                mm(T.B1[:, 128 * j:128 * j + 128], T.D16[:, 15 - k:143 - k], T.CM[:, 2048 * j + k:2048 * j + 2048:16], False, False,
-                   ["D16", "CM%d" % j], ["B1.ks"])
-        mm(T.B1[:, 0:256], T.D16[:, 15:143], T.R0[:], False, True, ["D16", "R0"], ["B1.ks"])
-        cp(T.PK[:, 0:4096:16], T.P0[:], ["P0"], ["PK"])
-        if 1 < t < NT:
-            cap_wide(t + 1, 1)
+                mm(b[:, k:H:16], T.CM[:, 2048 * h + k:2048 * h + 2048:16], T.B16[:], False, False, ["B16", "CM%d" % h], [key])
+            mm(b[:, 0:H:16], T.R0[:, half(h)], T.B16[:], False, True, ["B16", "R0%d" % h], [key])
+            act(row0(h), aside(h), ["P0%d" % h], ["PK%d" % h])
+
+        def worst_a(h):
+            scan(T.KS[:, half(h)], T.MB[:, 0:H], BA[h][:, 0:H], A.min, A.max, ["MB", "B%d.k" % (1 + h)], ["KS%d" % h])
+
+        def worst_b(h):
+            cp(T.XI[:, half(h, 8)], T.KS[:, H * h + 15:H * h + H:16], ["KS%d" % h], ["XI%d" % h])
+
+        def worst_c(h):
+            ts(T.XI2[:, half(h, 8)], T.XI[:, half(h, 8)], 15, None, A.bitwise_and, None, ["XI%d" % h], ["XJ%d" % h])
+
+        def worst_d(h):
+            tt(T.XA[:, half(h)], T.XI2[:, half(h, 8)].indirect(T.OFFC[:, 0:8]), T.DELB[:, 0:H], A.mult, ["XJ%d" % h, "OFFC", "DELB"], ["XA%d" % h])
+            o, key = BG[h][:, 256:264], "B%d.kl" % (3 + h)
+            mm(o, T.KR16[0:1, :], T.ONES[0:1, 0:8], True, False, ["KR16", "ONES"], [key])
+            mm(o, T.ONES[0:1, 0:H], T.IO256[0:1, 0:8], False, False, ["IO256", "ONES"], [key])
+            mm(o, T.XA[:, half(h)], T.NB8[:], False, True, ["XA%d" % h, "NB8"], [key])
+
+        def worst_e(h):
+            cp(T.KL[:, half(h, 8)], BG[h][:, 256:264], ["B%d.kl" % (3 + h)], ["KL%d" % h])
+
+        def win(h):
+            return T.PK[:, half(h, 2048)].indirect(T.KL[:, half(h, 8)])
+
+        def swap_a(h):
+            cp(T.XS[:, half(h)], win(h), ["PK%d" % h, "KL%d" % h], ["XS%d" % h])
+
+        def swap_b(h):
+            cp(win(h), aside(h), ["P0%d" % h, "KL%d" % h], ["PK%d" % h])
+
+        def swap_c(h):
+            cp(row0(h), T.XS[:, half(h)], ["XS%d" % h], ["PK%d" % h])
+
+        def largest(h):
+            lo = 2048 * h
+            s = slice(lo + 2047, lo - 1 if lo else None, -1)
+            scan(T.FB[:, s], T.SEG[:], T.PK[:, s], A.mult, A.max, ["SEG", "PK%d" % h], ["FB%d" % h])
+
+        def m_of(h, j):
+            return T.FB[:, 2048 * h + j:2048 * h + 2048:16]
+
+        def test(h, j):
+            cm, key = (T.CMP1, T.CMP2)[j][:, half(h)], "CMP%d%d" % (j, h)
+            tt(cm, m_of(h, j), T.B0[:, half(h)], A.is_gt, ["FB%d" % h, "B0.cap"], [key])
+            o, ok = BG[h][:, half(j)], "B%d.g%d" % (3 + h, j)
+            mm(o, T.LIMT[:], T.ONES[:, 0:H], True, False, ["LIMT", "ONES"], [ok])
+            mm(o, T.NBO[:], cm, False, True, ["NBO", key], [ok])
+
+        def clip(h):
+            gk = "B%d.g0" % (3 + h)
+            act(BU[h][:, 0:H], BG[h][:, 0:H], [gk], ["B%d.u0" % (5 + h)], F.Relu)
+
+        def keep_a(h):
+            tt(T.MA[:, half(h)], m_of(h, 1), BG[h][:, H:2 * H], A.min, ["FB%d" % h, "B%d.g1" % (3 + h)], ["MA%d" % h])
+
+        def keep_b(h):
+            tt(BU[h][:, 0:H], m_of(h, 0), BU[h][:, 0:H], A.min, ["FB%d" % h, "B%d.u0" % (5 + h)], ["B%d.u0" % (5 + h)])
+
+        def send(h):
+            tt(snd(h), T.MA[:, half(h)], BU[h][:, 0:H], A.max, ["MA%d" % h, "B%d.u0" % (5 + h)], [sk(h)])
+            wait_for("p", deps("p", [sk(h)], []))
+            g.remote_dma(land(h), snd(h), T.sem["arr%d%d" % (t, h)], T.sem.loc, pid, rid, topo.mask(core, dst))
+            lastw[lk(h)] = ("arr%d%d" % (t, h), len(topo.engines(core, dst)), {})
+
+        def step2(h):
+            d, dk = BU[h][:, 384:512], "B%d.d" % (5 + h)
+            mm(d, T.ID[:], T.CAP[:, nodes(t, h)], True, False, ["ID", "CAP"], [dk])
+            mm(d, T.NID[:], snd(h), False, True, ["NID", sk(h)], [dk])
+            act(T.SL[:, nodes(t, h)], d, [dk], ["SL"], F.Relu)
+
+        def step2_res(h):
+            act(T.RES[:, nodes(t, h)], snd(h), [sk(h)], ["RES"])
+
+        def weighed(o, key, h, stop):
+            mm(o, T.C37[0:1, :], T.IOBF[0:1, half(h)], True, False, ["C37", "IOBF"], [key])
+            mm(o, T.WTL[:], land(h), False, stop, ["WTL", lk(h)], [key])
+
+        def u_a(h):
+            o, key = BA[h][:, 256:384], "B%d.u0" % (1 + h)
+            weighed(o, key, h, True)
+            act(T.FQ[:, half(h)], o, [key], ["FQ%d" % h], bias=129.5001220703125, scale=1.0 / 4096)
+
+        def u_b(h):
+            b, bk = BU[h], "B%d." % (5 + h)
+            o = b[:, H:2 * H]
+            weighed(o, bk + "u", h, False)
+            mm(o, T.CU[0:1, :], T.ONES[0:1, 0:H], False, False, ["CU", "ONES"], [bk + "u"])
+            mm(o, T.N12M[:], T.FQ[:, half(h)], False, True, ["N12M", "FQ%d" % h], [bk + "u"])
+            act(T.SQ[:, half(h)], o, [bk + "u"], ["SQ%d" % h], F.Square)
+            op("a", lambda: AC.activation(b[:, 256:384], o, F.Copy, scale=T.KAF[:, 0:1]), [bk + "u", "KAF"], [bk + "fu"])
+
+        def p_of(h):
+            s = half(h)
+            return [
+                lambda: ts(T.UU[:, s], T.SQ[:, s], 0.03125, -0.375, A.mult, A.add, ["SQ%d" % h], ["UU%d" % h]),
+                lambda: tt(T.PI2[:, s], T.UU[:, s], BU[h][:, 256:384], A.add, ["UU%d" % h, "B%d.fu" % (5 + h)], ["PI%d" % h]),
+                lambda: ts(T.PI2[:, s], T.PI2[:, s], 2047, None, A.bitwise_and, None, ["PI%d" % h], ["PI%d" % h]),
+                lambda: cp(T.P16[:, s], T.PI2[:, s], ["PI%d" % h], ["P16%d" % h]),
+                lambda: cp(T.PF[:, s], T.PI2[:, s], ["PI%d" % h], ["PF%d" % h]),
+            ]
+
+        def wide(h, j):
+            act(T.MX[:, 2048 * h + 1024 * j:2048 * h + 1024 * j + 1024], land(h).indirect(T.OFFC[:, half(j, 64)]), [lk(h), "OFFC"], ["MX%d%d" % (h, j)])
+
+        def keys_begin(h):
+            o, key = BA[h][:, H:2 * H], "B%d.k" % (1 + h)
+            mm(o, T.ONES[:, 0:H], T.NEG[:], True, False, ["NEG", "ONES"], [key])
+            mm(o, T.ONES[0:1, 0:H], T.KC2[0:1, :], False, False, ["KC2", "ONES"], [key])
+            mm(o, T.PF[:, half(h)], T.IDH[:], False, False, ["PF%d" % h, "IDH"], [key])
+
+        def scores(h, j):
+            s = slice(2048 * h + 1024 * j, 2048 * h + 1024 * j + 1024)
+            tt(T.SC[:, s], T.SL[:, 0:2048].indirect(T.P16[:, H * h + 64 * j:H * h + 64 * j + 64]), T.MX[:, s], A.min,
+               ["SL", "P16%d" % h, "MX%d%d" % (h, j)], ["SC%d%d" % (h, j)])
+
+        def keys_end(h):
+            for m in range(16):
+                mm(BA[h][:, H + m:2 * H:16], T.SC[:, 2048 * h + m:2048 * h + 2048:16], T.B32K[:], False, m == 15,
+                   ["B32K", "SC%d0" % h, "SC%d1" % h], ["B%d.k" % (1 + h)])
+
+        def best(h):
+            scan(T.KS[:, half(h)], T.MB[:, 0:H], BA[h][:, H:2 * H], A.min, A.max, ["MB", "B%d.k" % (1 + h)], ["KS%d" % h])
+
         if t > 1:
+            marks()
+            suspended_a(t - 1)
+        sums_begin(0)
+        sums_begin(1)
+        if t > 1:
+            parity()
+        clipped(0)
+        clipped(1)
+        if t > 1:
+            cap_room(t)
+            new_words(t - 1)
+        else:
+            for j in range(8):
+                b, k = (T.B0, "B0.lv") if j % 2 else (T.B7, "B7.hi")
+                s = half(j, 256)
+                mm(b[:, 256:512], T.ID[:], T.CAP[:, s], True, False, ["ID", "CAP"], [k])
+                mm(b[:, 256:512], T.NID[:], T.RES[:, s], False, True, ["NID", "RES"], [k])
+                act(T.SL[:, s], b[:, 256:512], [k], ["SL"], F.Relu)
+        for f in (worst_a, worst_b, worst_c, worst_d):
+            f(0)
+        worst_a(1)
+        worst_b(1)
+        worst_e(0)
+        worst_c(1)
+        swap_a(0)
+        worst_d(1)
+        swap_b(0)
+        if t > 1:
+            word_list()
+        swap_c(0)
+        worst_e(1)
+        largest(0)
+        test(0, 0)
+        clip(0)
+        test(0, 1)
+        swap_a(1)
+        swap_b(1)
+        keep_a(0)
+        keep_b(0)
+        swap_c(1)
+        send(0)
+        step2(0)
+        step2_res(0)
+        if t > 1:
+            suspended_b(t - 1)
+            old_words()
             set_words()
         else:
             cp(T.WD[:, 0:2048], T.BRI[:], ["BRI"], ["WD"])
-            fill(T.WD[:, 2048:2304], 0.0, "WD")
         if t < NT:
             offsets_a(t + 1)
-        floors(T.WD[:, c:2048:8], 65536.0, T.N16B[:], "N16B", -1.0)
-        act(T.IDT[:], T.ID[:], ["ID"], ["IDT"], scale=2048.0 + 256.0 * c + 4096.0 * (t + 2))
-        scan(T.FB[:], T.SEG[:], T.PK[:, 0:4096], A.mult, A.max, ["SEG", "PK"], ["FB"])
-        tt(T.CMP1[:], T.FB[:, 15:4096:16], T.B0[:, 0:256], A.is_gt, ["FB", "B0.cap"], ["CMP1"])
-        mm(T.B2[:, 0:256], T.LIMT[:], T.ONES[:], True, False, ["LIMT", "ONES"], ["B2.c1"])
-        mm(T.B2[:, 0:256], T.NBO[:], T.CMP1[:], False, True, ["NBO", "CMP1"], ["B2.c1"])
-        mm(T.B4[:, 0:16], T.KR16[0:1, :], T.ONES[0:1, 0:16], True, False, ["KR16", "ONES"], ["B4.kl"])
-        mm(T.B4[:, 0:16], T.ONES[0:1, 0:128], T.IO256[0:1, :], False, False, ["IO256", "ONES"], ["B4.kl"])
-        v(lambda: V.transpose(T.KT[:], T.B1[:, 0:256]), ["B1.ks"], ["KT"])
-        scan(T.KSC[:], T.MB[:], T.KT[:], A.min, A.max, ["MB", "KT"], ["KSC"])
-        cp(T.XI[:], T.KSC[:, 15:256:16], ["KSC"], ["XI"])
-        ts(T.XI2[:], T.XI[:], 15, None, A.bitwise_and, None, ["XI"], ["XI2"])
-        ts(T.XB[:], T.XI2[:], -1.0, 15.0, A.mult, A.add, ["XI2"], ["XB"])
-        to_list(0, "XB", [T.XB], "B4.kl", False)
-        tt(T.M1[:], T.FB[:, 15:4096:16], T.B2[:, 0:256], A.min, ["FB", "B2.c1"], ["M1"])
-        act(T.B0[:, 256:512], T.M1[:], ["M1"], ["B0.m1"], F.Relu)
+        largest(1)
+        test(1, 0)
+        u_a(0)
+        clip(1)
+        test(1, 1)
+        u_b(0)
         if t < NT:
             offsets_b(t + 1)
-        new_words()
-        act(T.R0[:], T.B2[:, 0:256], ["B2.c1"], ["R0"], F.Relu, scale=4096.0)
-        cp(T.KL[:], T.B4[:, 0:16], ["B4.kl"], ["KL"])
-        v(lambda: V.tensor_copy(T.PK[:, 0:4096].indirect(T.KL[:, 0:16]), T.ZER[:]), ["KL", "ZER"], ["PK"])
-        scan(T.FB[:], T.SEG[:], T.PK[:, 0:4096], A.mult, A.max, ["SEG", "PK"], ["FB"])
-        tt(T.CMP2[:], T.FB[:, 15:4096:16], T.B0[:, 0:256], A.is_gt, ["FB", "B0.cap"], ["CMP2"])
-        mm(T.B3[:, 0:256], T.LIMT[:], T.ONES[:], True, False, ["LIMT", "ONES"], ["B3.c2"])
-        mm(T.B3[:, 0:256], T.NBO[:], T.CMP2[:], False, True, ["NBO", "CMP2"], ["B3.c2"])
+        keep_a(1)
+        keep_b(1)
+        send(1)
+        wide(0, 0)
+        step2(1)
+        if t == 1:
+            cap_wide(2, range(8, 16))
+        if t + 2 <= NT:
+            cap_wide(t + 2, range(1, 16))
+        for f in p_of(0):
+            f()
         if t < NT:
-            parity()
-        tt(T.M2[:], T.FB[:, 15:4096:16], T.B3[:, 0:256], A.min, ["FB", "B3.c2"], ["M2"])
-        tt(snd, T.M2[:], T.B0[:, 256:512], A.max, ["M2", "B0.m1"], [sk])
-        dst = cores[(rank + 1 + c % (n - 1)) % n]
-        rid, pid, _s = topo.addr(dst)
-        wait_for("p", deps("p", [sk], []))
-        g.remote_dma(land, snd, T.sem["arr%d" % t], T.sem.loc, pid, rid, topo.mask(core, dst))
-        lastw[lk] = ("arr%d" % t, len(topo.engines(core, dst)), {})
-        mm(T.B5[:, 256:512], T.ID[:], T.CAP[:, c:2048:8], True, False, ["ID", "CAP"], ["B5.sl"])
-        mm(T.B5[:, 256:512], T.NID[:], snd, False, True, ["NID", sk], ["B5.sl"])
-        act(T.SL[:, c:2048:8], T.B5[:, 256:512], ["B5.sl"], ["SL"], F.Relu)
-        act(T.RES[:, c:2048:8], snd, [sk], ["RES"])
+            offsets_c()
+        keys_begin(0)
+        wide(0, 1)
+        scores(0, 0)
+        u_a(1)
+        step2_res(1)
+        u_b(1)
         if t == NT:
             dma("s", T.yr[:], T.RES[:, 0:2048], "dyr", ["RES"], ["yr"])
+        scores(0, 1)
+        keys_end(0)
+        wide(1, 0)
+        wide(1, 1)
+        for f in p_of(1):
+            f()
+        keys_begin(1)
+        scores(1, 0)
+        scores(1, 1)
+        keys_end(1)
         if t < NT:
-            cap_room(t + 1)
-            op("a", lambda: AC.activation(T.LIMT[:], T.FOUR[:], F.Copy, bias=18.0, scale=T.ODD[:, 0:1]), ["FOUR", "ODD"], ["LIMT"])
-        scan(T.KRV[:, ::-1], T.RM[:, ::-1], T.KSC[:, ::-1], A.mult, A.max, ["RM", "KSC"], ["KRV"])
-        v(lambda: V.transpose(T.KB[:], T.KRV[:]), ["KRV"], ["KB"])
-        tt(T.NEB[:], T.B1[:, 0:256], T.KB[:], A.not_equal, ["B1.ks", "KB"], ["NEB"])
-        if t < NT:
-            offsets_c(t + 1)
-        mm(T.B5[:, 0:256], T.C37[0:1, :], T.IOBF[0:1, :], True, False, ["C37", "IOBF"], ["B5.u"])
-        mm(T.B5[:, 0:256], T.WTL[:], land, False, True, ["WTL", lk], ["B5.u"])
-        for j in range(4):
-            act(T.MX[:, 1024 * j:1024 * j + 1024], land.indirect(T.OFFC[:, 64 * j:64 * j + 64]), [lk, "OFFC"], ["MX%d" % j])
-        mm(T.B3[:, 256:512], T.NID[:], T.N16B[:], True, False, ["NID", "N16B"], ["B3.z"])
-        mm(T.B3[:, 256:512], T.N20[:], T.NEB[:], False, False, ["N20", "NEB"], ["B3.z"])
-        mm(T.B3[:, 256:512], T.NID[:], T.R0[:], False, True, ["NID", "R0"], ["B3.z"])
-        cp(T.UI[:], T.B5[:, 0:256], ["B5.u"], ["UI"])
-        ts(T.UU[:], T.UI[:], 4095, None, A.bitwise_and, None, ["UI"], ["UU"])
-        ts(T.B5[:, 256:512], T.UU[:], T.KAF[:, 0:1], None, A.mult, None, ["UU", "KAF"], ["B5.fu"])
-        tt(T.SQ[:], T.UU[:], T.UU[:], A.mult, ["UU"], ["SQ"])
-        ts(T.SQ[:], T.SQ[:], 5, None, A.arith_shift_right, None, ["SQ"], ["SQ"])
-        tt(T.PI2[:], T.SQ[:], T.B5[:, 256:512], A.add, ["SQ", "B5.fu"], ["PI2"])
-        ts(T.PI2[:], T.PI2[:], 2047, None, A.bitwise_and, None, ["PI2"], ["PI2"])
-        cp(T.P16[:], T.PI2[:], ["PI2"], ["P16"])
-        act(T.B3[:, 256:512], T.B3[:, 256:512], ["B3.z"], ["B3.z"], F.Relu, bias=65536.0 * (t + 8))
-        if t < NT:
-            act(T.RES[:, 2048 + L0:2048 + L0 + Q], land, [lk], ["RES"])
-            bulk()
-            cap_wide(t + 1, 0)
-        if t == 1:
-            cap_wide(2, 1)
-        mm(T.B6[:, 0:256], T.NEG[:], T.ONES[:], True, False, ["NEG", "ONES"], ["B6.x"])
-        mm(T.B6[:, 0:256], T.KC2[0:1, :], T.ONES[0:1, :], False, False, ["KC2", "ONES"], ["B6.x"])
-        for j in range(4):
-            s = slice(1024 * j, 1024 * j + 1024)
-            tt(T.SC[:, s], T.SL[:, 0:2048].indirect(T.P16[:, 64 * j:64 * j + 64]), T.MX[:, s], A.min, ["SL", "P16", "MX%d" % j], ["SC%d" % j])
-            for k in range(16):
-                mm(T.B6[:, 64 * j:64 * j + 64], T.D32[:, 15 - k:143 - k], T.SC[:, 1024 * j + k:1024 * j + 1024:16], False, j == 3 and k == 15,
-                   ["D32", "SC%d" % j], ["B6.x"])
+            act(T.RES[:, 2048 + L0:2048 + L0 + Q], T.LAND[:, L0:L0 + Q], [lk(0), lk(1)], ["RESG"])
+            rows(0, 128, 0)
+            row0_aside(0)
+            rows(128, 256, 1)
+            row0_aside(1)
+        else:
+            marks()
+            suspended_a(t)
+            new_words(t)
+        best(0)
+        best(1)
+        cp(T.XI[:], T.KS[:, 15:256:16], ["KS0", "KS1"], ["XI0", "XI1"])
+        ts(T.XI2[:], T.XI[:], 2047, None, A.bitwise_and, None, ["XI0", "XI1"], ["XJ0", "XJ1"])
+        tt(T.XW[:], T.XI2[:].indirect(T.OFFC[:, 0:16]), T.DELB[:], A.mult, ["XJ0", "XJ1", "OFFC", "DELB"], ["XW"])
+        lv = T.B0[:, 256:272]
+        for h in (0, 1):
+            mm(T.B0[:, 256 + 8 * h:264 + 8 * h], T.XW[:, half(h)], T.BOH[:], True, True, ["XW", "BOH"], ["B0.lv"])
         mm(T.B7[:, 0:256], T.ID[:], T.OFFD[:], True, False, ["ID", "OFFD"], ["B7.x"])
-        suspended(t)
-        tt(T.KEY[:], T.B6[:, 0:256], T.PI2[:], A.add, ["B6.x", "PI2"], ["KEY"])
-        v(lambda: V.transpose(T.KT[:], T.KEY[:]), ["KEY"], ["KT"])
-        scan(T.KSC[:], T.MB[:], T.KT[:], A.min, A.max, ["MB", "KT"], ["KSC"])
-        cp(T.XI[:], T.KSC[:, 15:256:16], ["KSC"], ["XI"])
-        ts(T.HL[:, 0:16], T.XI[:], 2040, None, A.bitwise_and, None, ["XI"], ["HLa"])
-        ts(T.HL[:, 16:32], T.XI[:], 7, None, A.bitwise_and, None, ["XI"], ["HLb"])
-        cp(T.HB[:], T.HL[:], ["HLa", "HLb"], ["HB"])
-        to_list(32, "HB", [T.HB, T.HB[:, 16:32]], "B4.lv", True)
-        to_list(48, "HB", [T.HB[:, 16:32]], "B4.lv", True)
-        tt(T.VS[:, 15:256:16], T.HL[:, 0:16], T.HL[:, 16:32], A.add, ["HLa", "HLb"], ["VS"])
-        scan(T.KRV[:, ::-1], T.RM[:, ::-1], T.VS[:, ::-1], A.mult, A.max, ["RM", "VS"], ["KRV"])
-        v(lambda: V.transpose(T.KB[:], T.KRV[:]), ["KRV"], ["KB"])
-        cp(T.VB[:], T.KB[:], ["KB"], ["VB"])
+        cp(T.LV[:], lv, ["B0.lv"], ["LV"])
+        cp(T.VB[:], T.IO2K[:].indirect(T.LV[:]), ["IO2K", "LV"], ["VB"])
         for i in range(16):
-                ts(T.EQ[:, i, 0:256 - 16 * i], T.VB[:, 16 * i:256], T.B4[:, 32 + i:33 + i], None, A.is_equal, None, ["VB", "B4.lv"], ["EQ%d" % i])
-                mm(T.B7[:, 16 * i:16 * i + 16], T.BT4[:], T.EQ[:, i, 0:16], False, i == 15, ["BT4", "EQ%d" % i], ["B7.x"])
-                if i < 15:
-                    mm(T.B7[:, 16 * i + 16:256], T.BO4[:], T.EQ[:, i, 16:256 - 16 * i], False, False, ["BO4", "EQ%d" % i], ["B7.x"])
-        lv = T.B4[:, 32:48]
+            ts(T.EQ[:, i, 0:256 - 16 * i], T.VB[:, 16 * i:256], T.B0[:, 256 + i:257 + i], None, A.is_equal, None, ["VB", "B0.lv"], ["EQ%d" % i])
+            if i < 15:
+                mm(T.B7[:, 16 * i + 16:256], T.BO4[:], T.EQ[:, i, 16:256 - 16 * i], False, False, ["BO4", "EQ%d" % i], ["B7.x"])
+        mm(T.B7[:, 0:256], T.BT4[:], T.EQ[:, :, 0:16], False, True, ["BT4"] + ["EQ%d" % i for i in range(16)], ["B7.x"])
         if t < NT:
-            ts(T.LW[:], T.B4[:, 48:64], float(t), 8192.0, A.not_equal, A.mult, ["B4.lv"], ["LW"])
-            ts(T.LX[:], lv, 2.0, T.XK[:, t:t + 1], A.mult, A.add, ["B4.lv", "XK"], ["LX"])
+            cp(T.LI[:], lv, ["B0.lv"], ["LI"])
+            ts(T.LX[:], lv, T.MULP[:, 0:1], T.XK[:, t:t + 1], A.mult, A.add, ["B0.lv", "MULP", "XK"], ["LX"])
+            ts(T.LI[:], T.LI[:], 7, None, A.bitwise_and, None, ["LI"], ["LI"])
+            ts(T.LW[:], T.LI[:], float(t), 8192.0, A.not_equal, A.mult, ["LI"], ["LW"])
             tt(T.LW[:], T.LW[:], T.TP[:], A.min, ["LW", "TP"], ["LW"])
             tt(T.LX[:], T.LW[:], T.LX[:], A.max, ["LW", "LX"], ["LX"])
+        else:
+            suspended_b(t)
         scan(T.CNS[:], T.MB[:], T.B7[:, 0:256], A.min, A.max, ["MB", "B7.x"], ["CNS"])
         if t < NT:
             tt(T.LB[:], T.CNS[:, 15:256:16], T.TP[:], A.min, ["CNS", "TP"], ["LB"])
             tt(T.LC[:], T.LB[:], T.LX[:], A.max, ["LB", "LX"], ["LC"])
             cp(T.PL[:], T.LC[:], ["LC"], ["PL"])
-            v(lambda: V.tensor_copy(T.PK[:, 0:4384].indirect(T.PL[:, 0:16]), land), ["PL", lk], ["PK"])
-        tt(T.LB[:], T.CNS[:, 15:256:16], T.TW[:], A.min, ["CNS", "TW"], ["LB"])
-        tt(T.LC[:], T.LB[:], lv, A.max, ["LB", "B4.lv"], ["LC"])
-        cp(T.PW[:], T.LC[:], ["LC"], ["PW"])
+            cp(T.PK[:].indirect(T.PL[:]), T.LAND[:, L0:L0 + Q], ["PL", lk(0), lk(1)], ["PK0", "PK1", "P00", "P01", "PKT"])
 
+    word_list()
+    old_words()
     set_words()
     dma("s", T.yb[:], T.WD[:, 0:2048], "dyb", ["WD"], ["yb"])
-    g.wait_ge(T.sem.loc, sum(len(topo.engines(core, cores[(rank + 1 + c % (n - 1)) % n])) for c in range(NT)))
+    g.wait_ge(T.sem.loc, 2 * sum(len(topo.engines(core, cores[(rank + 1 + c % (n - 1)) % n])) for c in range(NT)))
     for s, k in own.items():
         g.wait_ge(T.sem[k], count[s])
     for s in ("dyr", "dyb", "dbr", "dres", "dcap", "dwt", "dka"):

@@ -1,11 +1,15 @@
 from concourse.mybir import AluOpType as A, ActivationFunctionType as F
 
 NT = 6
+GS = 152
 Q = 256
 H = 128
 ZC = 3328
 P0 = 4096
 TR = 4352
+UP = 12288
+CH = ((0, 32), (32, 64), (64, 128), (128, 192), (192, 256))
+MAGIC = 12582912.0
 SCRATCH = {
     "RES": ("sbuf", [128, 3344], "bfloat16"),
     "WD": ("sbuf", [128, 2304], "float32"),
@@ -15,47 +19,54 @@ SCRATCH = {
     "SND": ("sbuf", [128, NT * Q], "bfloat16"),
     "LAND": ("sbuf", [128, NT * Q], "bfloat16"),
     "IO2K": ("sbuf", [128, 2048], "float32"),
+    "LXT": ("sbuf", [128, 2064], "float32"),
+    "TAB": ("sbuf", [128, 4096], "float32"),
+    "ROWS": ("sbuf", [128, 4096], "float16"),
+    "FT": ("sbuf", [128, 1024], "bfloat16"),
+    "RI": ("sbuf", [128, 128], "int32"),
+    "U32": ("sbuf", [128, 32], "int32"),
+    "K4": ("sbuf", [128, 4], "float16"),
     "PF": ("sbuf", [128, 256], "float16"),
     "XW": ("sbuf", [128, 256], "float16"),
-    "IDH": ("sbuf", [128, 128], "float16"),
     "BOH": ("sbuf", [128, 8], "float16"),
-    "IO256": ("sbuf", [128, 16], "bfloat16"),
-    "XK": ("sbuf", [128, 8], "float32"),
-    "SACC": ("sbuf", [128, 2], "float32"),
+    "W16": ("sbuf", [128, 144], "bfloat16"),
 }
-for _n in ("FB", "CM", "CX0", "CX1", "MX", "SC"):
+for _n in ("FB", "CM", "CX0", "CX1", "MX", "SC", "TOH"):
     SCRATCH[_n] = ("sbuf", [128, 4096], "bfloat16")
-for _n in ("CAP", "SL", "SEG", "TOH"):
+for _n in ("CAP", "SL", "SEG"):
     SCRATCH[_n] = ("sbuf", [128, 2048], "bfloat16")
-for _n in ("ONES", "IOBF", "OFFD", "CMP1", "CMP2", "MA", "SGN", "DELB", "N12", "KN", "KP", "BD1", "BD2", "R0", "XS", "XA", "OH", "FQ"):
+for _n in ("ONES", "OFFD", "CMP1", "CMP2", "SGN", "DELB", "N12", "KN", "KP", "BD1", "BD2", "R0", "XS", "XA", "OH", "KC", "KC2", "NEG"):
     SCRATCH[_n] = ("sbuf", [128, 256], "bfloat16")
-for _n in ("IOT", "IO16", "NDEL", "NEW", "MB", "OFS", "KT", "KS", "CNS", "WOLD", "IOTM", "SQ"):
+for _n in ("IOT", "IO16", "NDEL", "NEW", "MB", "KS", "CNS", "WOLD", "IOTM", "LXW"):
     SCRATCH[_n] = ("sbuf", [128, 256], "float32")
-for _n in ("BO", "NBO", "BO4", "BT4", "WTL", "ID", "NID", "N12M", "N16M", "P16M", "P20M", "N19M", "C37", "CU", "KC", "KC2", "KR16", "NEG", "FOUR", "LIMT"):
+for _n in ("BO", "NBO", "BO4", "BT4", "ID", "NID", "N11M", "N12M", "N16M", "P16M", "P20M", "N19M", "C37", "CUP", "KR", "KR16", "EIGHT", "LIMT"):
     SCRATCH[_n] = ("sbuf", [128, 128], "bfloat16")
+for _n in ("IDH", "RH", "KR4"):
+    SCRATCH[_n] = ("sbuf", [128, 128], "float16")
 for _n in ("B16", "B32K", "NB8"):
     SCRATCH[_n] = ("sbuf", [128, 8], "bfloat16")
+for _n in ("IO256", "I16B"):
+    SCRATCH[_n] = ("sbuf", [128, 16], "bfloat16")
 for _n in ("IOB", "PAR", "IDF"):
     SCRATCH[_n] = ("sbuf", [128, 128], "float32")
-for _n in ("UI", "UU", "PI2"):
+for _n in ("UI", "UU"):
     SCRATCH[_n] = ("sbuf", [128, 256], "int32")
 for _n in ("EO", "P16", "VB", "OFFC"):
     SCRATCH[_n] = ("sbuf", [128, 256], "uint16")
 for _n in ("WTI", "KAI", "PI", "KI"):
     SCRATCH[_n] = ("sbuf", [128, 1], "int32")
-for _n in ("WTF", "KAF", "PFL", "KF", "G16", "MULP", "ADDP", "SUBP", "PB", "PC", "ODD"):
+for _n in ("WTF", "PFL", "KF", "G16", "G15", "MULP", "ADDP", "PB", "PC", "ODD", "SACC"):
     SCRATCH[_n] = ("sbuf", [128, 1], "float32")
-for _n in ("IL", "TP", "TW", "LX", "LW", "LB", "LC"):
+for _n in ("TP", "TW", "LB", "LC", "LD"):
     SCRATCH[_n] = ("sbuf", [128, 16], "float32")
-for _n in ("XI", "XI2", "LI"):
+for _n in ("XI", "XI2"):
     SCRATCH[_n] = ("sbuf", [128, 16], "int32")
-for _n in ("KL", "PL", "PW", "LV"):
+for _n in ("KL", "PL", "PW", "LV", "LV2", "UL"):
     SCRATCH[_n] = ("sbuf", [128, 16], "uint16")
 for _n in range(8):
     SCRATCH["B%d" % _n] = ("psum", [128, 512], "float32")
-SEMAPHORES = (["cv", "ct", "ca", "cp", "dbr", "dres", "dcap", "dwt", "dka", "dyr", "dyb", "loc"]
-              + ["arr%d%d" % (t, h) for t in range(1, NT + 1) for h in (0, 1)])
-MAGIC = 12582912.0
+DMAS = ["dbr", "dres", "dcap", "dwt", "dka", "dyr", "dyb"] + ["dr%d" % k for k in range(4)] + ["dt%d" % k for k in range(5)]
+SEMAPHORES = ["cv", "ct", "ca", "cp", "loc"] + DMAS + ["arr%d" % t for t in range(1, NT + 1)]
 
 
 def rank_program(g, core, T, topo):
@@ -141,6 +152,9 @@ def rank_program(g, core, T, topo):
     def iota(ap, pattern, base, cm, k):
         op("p", lambda: g.iota(ap, pattern, base, cm, allow_small_or_imprecise_dtypes=True), [], [k])
 
+    def gcopy(out, in_, cols, r, w):
+        op("p", lambda: g.affine_select(out, in_, [[0, cols]], A.is_ge, 0.0, 0, 0), r, w)
+
     def ts(out, in0, s1, s2, o0, o1, r, w):
         if o1 is None:
             v(lambda: V.tensor_scalar(out, in0, s1, None, o0), r, w)
@@ -159,84 +173,119 @@ def rank_program(g, core, T, topo):
     def half(h, size=H):
         return slice(size * h, size * h + size)
 
-    def nodes(t, h):
-        return slice(t - 1 + 1024 * h, 1024 * h + 1024, 8)
-
-    BA = [T.B1, T.B2]
-    BG = [T.B3, T.B4]
-    BU = [T.B5, T.B6]
-
     dma("s", T.BRI[:], T.br[:], "dbr", [], ["BRI"])
-    dma("s", T.RES[:, 0:ZC], T.res[:], "dres", [], ["RES", "RESG"])
-    dma("s", T.CAP[:], T.cap[:], "dcap", [], ["CAP"])
-    dma("a", T.WTI[:], T.wt[:], "dwt", [], ["WTI"])
     dma("a", T.KAI[:], T.ka[:], "dka", [], ["KAI"])
+    dma("a", T.WTI[:], T.wt[:], "dwt", [], ["WTI"])
+    op("p", lambda: g.iota(T.U32[:], [[1, 32]], 0, 32), [], ["U32"])
     op("p", lambda: g.iota(T.PI[:], [[0, 1]], 0, 1), [], ["PI"])
     iota(T.IOT[:], [[1, 256]], 0, 0, "IOT")
     iota(T.IO16[:], [[0, 16], [1, 16]], 0, 0, "IO16")
     iota(T.IOB[:], [[16, 8], [0, 16]], 0, 0, "IOB")
     iota(T.ONES[:], [[0, 256]], 1, 0, "ONES")
-    for name, c in (("LIMT", 18), ("PAR", 1), ("FOUR", 8), ("C37", 37), ("CU", 532480), ("NEG", -131072)):
+    for name, c in (("LIMT", 18), ("PAR", 1), ("EIGHT", 8), ("C37", 37), ("CUP", UP)):
         iota(T[name][:], [[0, 128]], c, 0, name)
-    iota(T.IO2K[:], [[1, 2048]], 0, 0, "IO2K")
+    iota(T.NEG[:], [[0, 256]], -131072, 0, "NEG")
+    iota(T.IO2K[:], [[1, 2048]], UP, 0, "IO2K")
+    fill(T.RI[:, 96:128], 2048, "RI3")
+    ts(T.RI[:, 0:32], T.U32[:], 2016, None, A.bitwise_and, None, ["U32"], ["RI0"])
+    ts(T.RI[:, 32:64], T.U32[:], 31, None, A.bitwise_and, None, ["U32"], ["RI1"])
+    tt(T.RI[:, 64:96], T.U32[:], T.U32[:], A.mult, ["U32"], ["RI2"])
     fill(T.RES[:, ZC:ZC + 16], 0.0, "RESZ")
-    fill(T.SEG[:], 1.0, "SEG")
-    fill(T.SEG[:, 0:2048:16], 0.0, "SEG")
-    fill(T.MB[:], 1e9, "MB")
-    fill(T.MB[:, 0:256:16], -1e9, "MB")
-    fill(T.PK[:, TR:TR + Q], 0.0, "PKT")
-    fill(T.WD[:, 2048:2304], 0.0, "WDT")
-    act(T.KC[:], T.IO16[:, 0:128], ["IO16"], ["KC"], bias=15.0, scale=-1.0)
-    act(T.KC2[:], T.IO16[:, 0:128], ["IO16"], ["KC2"], bias=30720.0, scale=-2048.0)
-    act(T.KR16[:], T.IO16[:, 0:128], ["IO16"], ["KR16"], bias=15.0, scale=16.0)
-    act(T.IO256[:], T.IOT[:, 0:16], ["IOT"], ["IO256"], scale=256.0)
-    act(T.IOBF[:], T.IOT[:], ["IOT"], ["IOBF"])
+    ts(T.RI[:, 64:96], T.RI[:, 64:96], 5, 2047, A.arith_shift_right, A.bitwise_and, ["RI2"], ["RI2"])
+    fill(T.K4[:, 2:3], 1.0, "K42")
+    cp(T.RH[:], T.RI[:], ["RI0", "RI1", "RI2", "RI3"], ["RH"])
+    for k in range(4):
+        dma("s", T.ROWS[k:k + 1, :], T.RH[:, 32 * k:32 * k + 32], "dr%d" % k, ["RH"], ["ROW%d" % k])
+    dma("s", T.RES[:, 0:ZC], T.res[:], "dres", [], ["RES", "RESG"])
+    dma("s", T.CAP[:], T.cap[:], "dcap", [], ["CAP"])
+    fill(T.K4[:, 3:4], 130.0, "K43")
     ts(T.KI[:], T.PI[:], 15, None, A.bitwise_and, None, ["PI"], ["KI"])
     cp(T.PFL[:], T.PI[:], ["PI"], ["PFL"])
     cp(T.KF[:], T.KI[:], ["KI"], ["KF"])
-    tt(T.G16[:], T.PFL[:], T.KF[:], A.subtract, ["PFL", "KF"], ["G16"])
     ts(T.ID[:], T.IOT[:, 0:128], T.PFL[:, 0:1], None, A.is_equal, None, ["IOT", "PFL"], ["ID"])
-    ts(T.DELB[:], T.IO16[:], T.KF[:, 0:1], None, A.is_equal, None, ["IO16", "KF"], ["DELB"])
-    ts(T.BT4[:], T.IO16[:, 0:128], T.KF[:, 0:1], 8192.0, A.is_gt, A.mult, ["IO16", "KF"], ["BT4"])
-    ts(T.BO[:], T.IOB[:], T.G16[:, 0:1], None, A.is_equal, None, ["IOB", "G16"], ["BO"])
-    ts(T.MULP[:], T.KF[:], 0.0, -1.875, A.is_equal, A.mult, ["KF"], ["MULP"])
-    ts(T.ADDP[:], T.KF[:], 0.0, float(P0), A.is_equal, A.mult, ["KF"], ["ADDP"])
-    ts(T.MULP[:], T.MULP[:], 2.0, None, A.add, None, ["MULP"], ["MULP"])
-    tt(T.ADDP[:], T.ADDP[:], T.KF[:], A.add, ["ADDP", "KF"], ["ADDP"])
-    ts(T.SUBP[:], T.MULP[:], -1.0, None, A.mult, None, ["MULP"], ["SUBP"])
-    ts(T.XK[:], T.IOT[:, 0:8], T.SUBP[:, 0:1], T.ADDP[:, 0:1], A.mult, A.add, ["IOT", "SUBP", "ADDP"], ["XK"])
+    tt(T.G16[:], T.PFL[:], T.KF[:], A.subtract, ["PFL", "KF"], ["G16"])
     cp(T.IDH[:], T.ID[:], ["ID"], ["IDH"])
-    cp(T.BOH[:], T.BO[:, 0:128:16], ["BO"], ["BOH"])
-    cp(T.OFFC[:], T.IOT[:], ["IOT"], ["OFFC"])
-    tt(T.BT4[:], T.BT4[:], T.BO[:], A.mult, ["BT4", "BO"], ["BT4"])
-    cp(T.WTF[:], T.WTI[:], ["WTI"], ["WTF"])
-    cp(T.KAF[:], T.KAI[:], ["KAI"], ["KAF"])
-    ts(T.WTL[:], T.BO[:], T.WTF[:, 0:1], None, A.mult, None, ["BO", "WTF"], ["WTL"])
-    for name, c in (("NID", -1.0), ("N12M", -4096.0), ("N16M", -16.0), ("P16M", 65536.0), ("P20M", 1048576.0), ("N19M", -524288.0), ("IDF", 1.0)):
+    ts(T.DELB[:], T.IO16[:], T.KF[:, 0:1], None, A.is_equal, None, ["IO16", "KF"], ["DELB"])
+    ts(T.BO[:], T.IOB[:], T.G16[:, 0:1], None, A.is_equal, None, ["IOB", "G16"], ["BO"])
+    ts(T.XI[:, 0:1], T.KAI[:], 63, None, A.bitwise_and, None, ["KAI"], ["XI"])
+    cp(T.K4[:, 1:2], T.KAI[:], ["KAI"], ["K41"])
+    cp(T.K4[:, 0:1], T.XI[:, 0:1], ["XI"], ["K40"])
+    mm(T.B1[0:4, 0:128], T.K4[:], T.IDH[:], True, True, ["K40", "K41", "K42", "K43", "IDH"], ["B1.k"])
+    fill(T.SEG[:], 1.0, "SEG")
+    cp(T.KR4[0:4, :], T.B1[0:4, 0:128], ["B1.k"], ["KR4"])
+    fill(T.SEG[:, 0:2048:16], 0.0, "SEG")
+    fill(T.MB[:], 1e9, "MB")
+    fill(T.PK[:, TR:TR + Q], 0.0, "PKT")
+    fill(T.MB[:, 0:256:16], -1e9, "MB")
+    fill(T.WD[:, 2048:2304], 0.0, "WDT")
+    for name, c in (("N11M", -2048.0), ("NID", -1.0)):
         act(T[name][:], T.ID[:], ["ID"], [name], scale=c)
-    for name, c in (("NBO", -512.0), ("BO4", 8192.0)):
-        act(T[name][:], T.BO[:], ["BO"], [name], scale=c)
-    for name, c in (("B16", 16.0), ("B32K", 32768.0), ("NB8", -1.0)):
-        act(T[name][:], T.BO[:, 0:128:16], ["BO"], [name], scale=c)
-    act(T.NDEL[:], T.DELB[:], ["DELB"], ["NDEL"], bias=1.0, scale=-1.0)
-    act(T.OFFD[:], T.DELB[:], ["DELB"], ["OFFD"], bias=-2097152.0, scale=2097152.0)
-    op("a", lambda: AC.activation(T.IL[:], T.IOT[:, 0:16], F.Identity, bias=T.KF[:, 0:1], scale=16.0), ["IOT", "KF"], ["IL"])
-    act(T.TP[:], T.IL[:], ["IL"], ["TP"], bias=float(TR))
-    act(T.TW[:], T.IL[:], ["IL"], ["TW"], bias=2048.0)
-    act(T.TOH[:, 0:256], T.DELB[:], ["DELB"], ["TOH"])
-    for s in (256, 512, 1024):
-        act(T.TOH[:, s:2 * s], T.TOH[:, 0:s], ["TOH"], ["TOH"])
-    tt(T.IOTM[:], T.IOT[:], T.OFFD[:], A.add, ["IOT", "OFFD"], ["IOTM"])
+    act(T.B16[:], T.BO[:, 0:128:16], ["BO"], ["B16"], scale=16.0)
+    act(T.KC[0:1, :], T.IO16[0:1, :], ["IO16"], ["KC"], bias=15.0, scale=-1.0)
+
+    def table(j):
+        def raw(i):
+            mm(T.B2[:], T.KR4[0:3, :], T.ROWS[0:3, half(i, 512)], True, True, ["KR4", "ROW0", "ROW1", "ROW2"], ["B2.k"])
+            act(T.FT[:, half(i & 1, 512)], T.B2[:], ["B2.k"], ["FT%d" % (i & 1)], bias=129.500244140625, scale=1.0 / 2048)
+        if j == 0:
+            raw(0)
+        if j < 7:
+            raw(j + 1)
+        mm(T.B7[:], T.KR4[0:4, :], T.ROWS[0:4, half(j, 512)], True, False, ["KR4", "ROW0", "ROW1", "ROW2", "ROW3"], ["B7.x", "B7.hi"])
+        mm(T.B7[:], T.N11M[:], T.FT[:, half(j & 1, 512)], False, True, ["N11M", "FT%d" % (j & 1)], ["B7.x", "B7.hi"])
+        act(T.TAB[:, half(j, 512)], T.B7[:], ["B7.x", "B7.hi"], ["TAB"])
+
+    def more_constants():
+        act(T.KR16[0:1, :], T.IO16[0:1, 0:128], ["IO16"], ["KR16"], bias=15.0, scale=16.0)
+        act(T.IO256[0:1, :], T.IOT[0:1, 0:16], ["IOT"], ["IO256"], scale=256.0)
+        act(T.NB8[:], T.BO[:, 0:128:16], ["BO"], ["NB8"], scale=-1.0)
+        act(T.NBO[:], T.BO[:], ["BO"], ["NBO"], scale=-512.0)
+
+    def vector_constants():
+        cp(T.WTF[:], T.WTI[:], ["WTI"], ["WTF"])
+        ts(T.G15[:], T.G16[:], 15.0, None, A.add, None, ["G16"], ["G15"])
+        ts(T.BT4[:], T.IO16[:, 0:128], T.KF[:, 0:1], 16384.0, A.is_gt, A.mult, ["IO16", "KF"], ["BT4"])
+        ts(T.W16[:], T.IOT[:, 0:144], T.G15[:, 0:1], T.WTF[:, 0:1], A.is_equal, A.mult, ["IOT", "G15", "WTF"], ["W16"])
+        ts(T.MULP[:], T.KF[:], 0.0, -15.0, A.is_equal, A.mult, ["KF"], ["MULP"])
+        ts(T.ADDP[:], T.KF[:], 0.0, float(P0), A.is_equal, A.mult, ["KF"], ["ADDP"])
+        ts(T.MULP[:], T.MULP[:], 16.0, None, A.add, None, ["MULP"], ["MULP"])
+        tt(T.ADDP[:], T.ADDP[:], T.KF[:], A.add, ["ADDP", "KF"], ["ADDP"])
+        tt(T.BT4[:], T.BT4[:], T.BO[:], A.mult, ["BT4", "BO"], ["BT4"])
+        cp(T.BOH[:], T.BO[:, 0:128:16], ["BO"], ["BOH"])
+        ts(T.LXT[:, 8:2056:8], T.IOT[:], T.MULP[:, 0:1], T.ADDP[:, 0:1], A.mult, A.add, ["IOT", "MULP", "ADDP"], ["LXT"])
+
+    def late_constants():
+        for name, c in (("N12M", -4096.0), ("N16M", -16.0), ("IDF", 1.0)):
+            act(T[name][:], T.ID[:], ["ID"], [name], scale=c)
+        act(T.KR[0:1, :], T.IO16[0:1, 0:128], ["IO16"], ["KR"])
+        act(T.I16B[0:1, :], T.IOT[0:1, 0:16], ["IOT"], ["I16B"], scale=16.0)
+        act(T.KC2[0:1, :], T.IO16[0:1, :], ["IO16"], ["KC2"], bias=30720.0, scale=-2048.0)
+        act(T.B32K[:], T.BO[:, 0:128:16], ["BO"], ["B32K"], scale=32768.0)
+
+    def last_constants():
+        for name, c in (("P16M", 65536.0), ("P20M", 1048576.0), ("N19M", -524288.0)):
+            act(T[name][:], T.ID[:], ["ID"], [name], scale=c)
+        act(T.BO4[:], T.BO[:], ["BO"], ["BO4"], scale=16384.0)
+        act(T.NDEL[:], T.DELB[:], ["DELB"], ["NDEL"], bias=1.0, scale=-1.0)
+        act(T.OFFD[:], T.DELB[:], ["DELB"], ["OFFD"], bias=-8388608.0, scale=8388608.0)
+        op("a", lambda: AC.activation(T.LB[:], T.IOT[:, 0:16], F.Identity, bias=T.KF[:, 0:1], scale=16.0), ["IOT", "KF"], ["LB"])
+        act(T.TP[:], T.LB[:], ["LB"], ["TP"], bias=float(TR))
+        act(T.TW[:], T.LB[:], ["LB"], ["TW"], bias=2048.0 + UP)
+
+    def one_hot_table():
+        dma("s", T.TOH[:, 0:256], T.DELB[:], "dt0", ["DELB", "CAP"], ["TOH"])
+        for j, s in enumerate((256, 512, 1024, 2048)):
+            dma("s", T.TOH[:, s:2 * s], T.TOH[:, 0:s], "dt%d" % (j + 1), ["TOH"], ["TOH"])
 
     def first_offsets():
         src = T.BRI[:, 0:2048:8]
-        ts(T.OFS[:], src, 0.0, 4096.0, A.is_lt, A.mult, ["BRI"], ["OFS"])
-        ts(T.UU[:], src, 65535, None, A.bitwise_and, None, ["BRI"], ["UU0", "UU1"])
+        ts(T.UU[:], src, 65535, None, A.bitwise_and, None, ["BRI"], ["UU"])
+        ts(T.B3[:, 0:256], src, 0.0, 4096.0, A.is_lt, A.mult, ["BRI"], ["B3.g"])
         ts(T.UI[:], src, 4095, None, A.bitwise_and, None, ["BRI"], ["UI"])
-        ts(T.KT[:], T.UU[:], 4096.0, 4096.0, A.is_lt, A.mult, ["UU0", "UU1"], ["KT"])
-        tt(T.OFS[:], T.OFS[:], T.UI[:], A.max, ["OFS", "UI"], ["OFS"])
-        tt(T.OFS[:], T.OFS[:], T.KT[:], A.max, ["OFS", "KT"], ["OFS"])
-        ts(T.EO[:], T.OFS[:], float(ZC), None, A.min, None, ["OFS"], ["EO"])
+        ts(T.B4[:, 0:256], T.UU[:], 4096.0, 4096.0, A.is_lt, A.mult, ["UU"], ["B4.g"])
+        tt(T.KS[:], T.UI[:], T.B3[:, 0:256], A.max, ["B3.g", "UI"], ["KS"])
+        tt(T.CNS[:], T.KS[:], T.B4[:, 0:256], A.max, ["B4.g", "KS"], ["CNS"])
+        ts(T.EO[:], T.CNS[:], float(ZC), None, A.min, None, ["CNS"], ["EO"])
 
     def k_part(out, key, t):
         act(out, T.WD[:, t - 1:2048:8], ["WD"], [key], bias=199.50390625, scale=1.0 / 65536)
@@ -246,94 +295,96 @@ def rank_program(g, core, T, topo):
         k_part(T.KN[:], "KN", t)
         mm(T.B7[:, 256:512], T.ID[:], T.N12[:], True, False, ["ID", "N12"], ["B7.hi"])
         mm(T.B7[:, 256:512], T.N16M[:], T.KN[:], False, True, ["N16M", "KN"], ["B7.hi"])
-        act(T.BD2[:], T.KN[:], ["KN"], ["BD2"], F.Relu, bias=4096.0 * (201 - t), scale=-4096.0)
-        act(T.BD1[:], T.B7[:, 256:512], ["B7.hi"], ["BD1"], F.Relu, bias=4096.0 * (t - 2980), scale=-4096.0)
 
     def offsets_b(t):
-        mm(T.B7[:, 0:256], T.IDF[:], T.WD[:, t - 1:2048:8], True, False, ["IDF", "WD"], ["B7.x"])
-        mm(T.B7[:, 0:256], T.N12M[:], T.N12[:], False, False, ["N12M", "N12"], ["B7.x"])
-        mm(T.B7[:, 0:256], T.ID[:], T.BD1[:], False, False, ["ID", "BD1"], ["B7.x"])
-        mm(T.B7[:, 0:256], T.ID[:], T.BD2[:], False, True, ["ID", "BD2"], ["B7.x"])
+        act(T.BD2[:], T.KN[:], ["KN"], ["BD2"], F.Relu, bias=4096.0 * (201 - t), scale=-4096.0)
+        act(T.BD1[:], T.B7[:, 256:512], ["B7.hi"], ["BD1"], F.Relu, bias=4096.0 * (t - 2980), scale=-4096.0)
+        o = T.B5[:, 256:512]
+        mm(o, T.IDF[:], T.WD[:, t - 1:2048:8], True, False, ["IDF", "WD"], ["B5.off"])
+        mm(o, T.N12M[:], T.N12[:], False, False, ["N12M", "N12"], ["B5.off"])
+        mm(o, T.ID[:], T.BD2[:], False, False, ["ID", "BD2"], ["B5.off"])
+        mm(o, T.ID[:], T.BD1[:], False, True, ["ID", "BD1"], ["B5.off"])
 
     def offsets_c():
-        ts(T.EO[:], T.B7[:, 0:256], 901120.0, float(ZC), A.add, A.min, ["B7.x"], ["EO"])
+        ts(T.EO[:], T.B5[:, 256:512], 901120.0, float(ZC), A.add, A.min, ["B5.off"], ["EO"])
 
-    def rows(lo, hi, h, eng="a"):
+    def rows(lo, hi, eng, key):
         out, src = T.PK[:, 16 * lo:16 * hi], T.RES[:, 0:3344].indirect(T.EO[:, lo:hi])
-        if eng == "a":
-            act(out, src, ["RES", "RESG", "RESZ", "EO"], ["PK%d" % h])
-        else:
-            cp(out, src, ["RES", "RESG", "RESZ", "EO"], ["PKx"])
+        (act if eng == "a" else cp)(out, src, ["RES", "RESG", "RESZ", "EO"], key)
 
-    def row0(h):
-        return T.PK[:, 2048 * h:2048 * h + 2048:16]
+    row0, aside = T.PK[:, 0:4096:16], T.PK[:, P0:P0 + Q]
+    pk = ["PK0", "PK1"]
 
-    def aside(h):
-        return T.PK[:, P0 + H * h:P0 + H * h + H]
-
-    def row0_aside(h):
-        act(aside(h), row0(h), ["PK%d" % h, "PKx"], ["P0%d" % h])
-        act(row0(h), T.ONES[:, 0:H], ["ONES"], ["PK%d" % h], scale=255.0)
+    def row0_aside():
+        act(aside, row0, pk + ["PKx"], ["P0"])
+        act(row0, T.ONES[:], ["ONES"], pk, scale=255.0)
 
     def cap_wide(t, ks):
         cx = "CX%d" % (t & 1)
         for k in ks:
-            op("p", lambda: g.affine_select(T[cx][:, k:4096:16], T.CAP[:, t - 1:2048:8], [[0, Q]], A.is_ge, 0.0, 0, 0), ["CAP"], [cx + "k%d" % k])
+            gcopy(T[cx][:, k:4096:16], T.CAP[:, t - 1:2048:8], Q, ["CAP"], [cx + "k%d" % k])
 
     def cap_room(t):
         act(T.B0[:, 0:256], T.CAP[:, t - 1:2048:8], ["CAP"], ["B0.cap"])
 
     def word_list():
-        tt(T.LB[:], T.CNS[:, 15:256:16], T.TW[:], A.min, ["CNS", "TW"], ["LB"])
-        tt(T.LC[:], T.LB[:], T.B0[:, 256:272], A.max, ["LB", "B0.lv"], ["LC"])
-        cp(T.PW[:], T.LC[:], ["LC"], ["PW"])
+        return [
+            lambda: tt(T.LD[:], T.CNS[:, 15:256:16], T.TW[:], A.min, ["CNS", "TW"], ["LD"]),
+            lambda: tt(T.LC[:], T.LD[:], T.B0[:, 256:272], A.max, ["LD", "B0.lv"], ["LC"]),
+            lambda: ts(T.PW[:], T.LC[:], -float(UP), None, A.add, None, ["LC"], ["PW"]),
+        ]
 
     def old_words():
-        tt(T.WOLD[:], T.WD[:, 0:2304].indirect(T.PW[:, 0:16]), T.NDEL[:], A.mult, ["WD", "WDT", "PW", "NDEL"], ["WOLD"])
+        tt(T.WOLD[:], T.WD[:, 0:2304].indirect(T.PW[:]), T.NDEL[:], A.mult, ["WD", "WDT", "PW", "NDEL"], ["WOLD"])
 
     def set_words():
-        tt(T.WD[:, 0:2304].indirect(T.PW[:, 0:16]), T.WOLD[:], T.NEW[:], A.add, ["WOLD", "NEW", "PW"], ["WD", "WDT"])
+        tt(T.WD[:, 0:2304].indirect(T.PW[:]), T.WOLD[:], T.NEW[:], A.add, ["WOLD", "NEW", "PW"], ["WD", "WDT"])
 
     def marks():
-        act(T.OH[:], T.TOH[:].indirect(T.KL[:]), ["TOH", "KL0", "KL1"], ["OH"])
-        for h in (0, 1):
-            op("a", lambda: AC.activation(T.SGN[:, half(h)], BG[h][:, 0:H], F.Sign, accum_out=T.SACC[:, h:h + 1]),
-               ["B%d.g0" % (3 + h)], ["SGN%d" % h, "SACC%d" % h])
+        act(T.OH[:], T.TOH[:].indirect(T.KL[:]), ["TOH", "KL"], ["OH"])
+        op("a", lambda: AC.activation(T.SGN[:], T.B3[:, 0:256], F.Sign, accum_out=T.SACC[:]), ["B3.g"], ["SGN", "SACC"])
 
     def suspended_a(t):
-        z = T.B7[:, 256:512]
+        z = T.B5[:, 256:512]
         k_part(T.KP[:], "KP", t)
-        mm(z, T.P20M[:], T.OH[:], True, False, ["P20M", "OH"], ["B7.hi"])
-        mm(z, T.N19M[:], T.SGN[:], False, False, ["N19M", "SGN0", "SGN1"], ["B7.hi"])
-        mm(z, T.P16M[:], T.KP[:], False, True, ["P16M", "KP"], ["B7.hi"])
-        act(z, z, ["B7.hi"], ["B7.hi"], F.Relu, bias=65536.0 * (t + 8 - 200) - 1572864.0)
+        mm(z, T.P20M[:], T.OH[:], True, False, ["P20M", "OH"], ["B5.off"])
+        mm(z, T.N19M[:], T.SGN[:], False, False, ["N19M", "SGN"], ["B5.off"])
+        mm(z, T.P16M[:], T.KP[:], False, True, ["P16M", "KP"], ["B5.off"])
+        act(z, z, ["B5.off"], ["B5.off"], F.Relu, bias=65536.0 * (t + 8 - 200) - 1572864.0)
 
     def suspended_b(t):
-        tt(T.WD[:, t - 1:2048:8], T.WD[:, t - 1:2048:8], T.B7[:, 256:512], A.subtract, ["WD", "B7.hi"], ["WD"])
+        tt(T.WD[:, t - 1:2048:8], T.WD[:, t - 1:2048:8], T.B5[:, 256:512], A.subtract, ["WD", "B5.off"], ["WD"])
 
     def new_words(t):
         act(T.NEW[:], T.IOTM[:], ["IOTM"], ["NEW"], F.Relu, bias=2048.0 + 256.0 * (t - 1) + 4096.0 * (t + 2))
 
     def parity():
-        mm(T.B7[:, 0:1], T.PAR[:], T.SACC[:, 0:1], True, False, ["PAR", "SACC0"], ["B7.x"])
-        mm(T.B7[:, 0:1], T.PAR[:], T.SACC[:, 1:2], False, True, ["PAR", "SACC1"], ["B7.x"])
-        act(T.PB[:], T.B7[:, 0:1], ["B7.x"], ["PB"], bias=-0.25, scale=-0.015625)
+        o = T.B4[:, 256:257]
+        mm(o, T.PAR[:], T.SACC[:], True, True, ["PAR", "SACC"], ["B4.par"])
+        act(T.PB[:], o, ["B4.par"], ["PB"], bias=-0.25, scale=-0.015625)
         act(T.PC[:], T.PB[:], ["PB"], ["PC"], bias=MAGIC)
-        act(T.PC[:], T.PC[:], ["PC"], ["PC"], bias=MAGIC + 0.0, scale=-1.0)
+        act(T.PC[:], T.PC[:], ["PC"], ["PC"], bias=MAGIC, scale=-1.0)
         op("a", lambda: AC.activation(T.ODD[:], T.PB[:], F.Identity, bias=T.PC[:, 0:1]), ["PB", "PC"], ["ODD"])
-        op("a", lambda: AC.activation(T.LIMT[:], T.FOUR[:], F.Copy, bias=20.0, scale=T.ODD[:, 0:1]), ["FOUR", "ODD"], ["LIMT"])
+        op("a", lambda: AC.activation(T.LIMT[:], T.EIGHT[:], F.Copy, bias=20.0, scale=T.ODD[:, 0:1]), ["EIGHT", "ODD"], ["LIMT"])
 
+    more_constants()
+    late_constants()
+    last_constants()
+    cp(T.OFFC[:], T.IOT[:], ["IOT"], ["OFFC"])
     first_offsets()
-    rows(0, 128, 0)
-    rows(160, 256, 1, "v")
-    row0_aside(0)
-    rows(128, 160, 1)
+    rows(0, GS, "a", pk)
+    rows(GS, Q, "v", ["PKx"])
     cap_wide(1, (0, 1, 2))
+    left = [(T.B2, ["B2.k"]), (T.B3, ["B3.g"]), (T.B4, ["B4.g", "B4.par"]), (T.B7, ["B7.x", "B7.hi"])]
+    for j, (b, k) in enumerate(left):
+        mm(b[:], T.ID[:], T.CAP[:, half(j, 512)], True, False, ["ID", "CAP"], k)
+        mm(b[:], T.NID[:], T.RES[:, half(j, 512)], False, True, ["NID", "RES"], k)
     for k in range(3, 16):
         cp(T.CX1[:, k:4096:16], T.CAP[:, 0:2048:8], ["CAP"], ["CX1k%d" % k])
     cap_wide(2, range(8))
-    row0_aside(1)
-    cap_room(1)
+    iota(T.LXT[:], [[0, 2064]], 8192, 0, "LXT")
+    one_hot_table()
+    row0_aside()
 
     for t in range(1, NT + 1):
         c = t - 1
@@ -342,297 +393,184 @@ def rank_program(g, core, T, topo):
         L0 = c * Q
         dst = cores[(rank + 1 + c % (n - 1)) % n]
         rid, pid, _s = topo.addr(dst)
-
-        def land(h):
-            return T.LAND[:, L0 + H * h:L0 + H * h + H]
-
-        def snd(h):
-            return T.SND[:, L0 + H * h:L0 + H * h + H]
-
-        def lk(h):
-            return "LAND%d%d" % (t, h)
-
-        def sk(h):
-            return "SND%d%d" % (t, h)
-
-        def sums_begin(h):
-            b, key = BA[h], "B%d.k" % (1 + h)
-            mm(b[:, 0:H], T.ONES[0:1, 0:H], T.KC[0:1, :], True, False, ["KC", "ONES"], [key])
-            mm(b[:, 0:H:16], T.CAP[:, nodes(t, h)], T.B16[:], False, False, ["B16", "CAP"], [key])
-            d, dk = BU[h][:, 384:512], "B%d.d" % (5 + h)
-            mm(d, T.NID[:], T.CAP[:, nodes(t, h)], True, False, ["NID", "CAP"], [dk])
-            mm(d, T.ID[:], aside(h), False, True, ["ID", "P0%d" % h], [dk])
-            act(T.R0[:, half(h)], d, [dk], ["R0%d" % h], F.Relu)
-
-        def clipped(h):
+        land, lk = T.LAND[:, L0:L0 + Q], "LAND%d" % t
+        snd, sk = T.SND[:, L0:L0 + Q], "SND%d" % t
+        cap = T.CAP[:, c:2048:8]
+        ka, d = T.B1, T.B6[:, 256:512]
+        mm(ka[:, 0:256], T.ONES[0:1, 0:H], T.KC[0:1, :], True, False, ["KC", "ONES"], ["B1.k"])
+        for h in (0, 1):
+            mm(ka[:, H * h:H * h + H:16], T.CAP[:, c + 1024 * h:1024 * h + 1024:8], T.B16[:], False, False, ["B16", "CAP"], ["B1.k"])
+        mm(d, T.NID[:], cap, True, False, ["NID", "CAP"], ["B6.d"])
+        mm(d, T.ID[:], aside, False, True, ["ID", "P0"], ["B6.d"])
+        act(T.R0[:], d, ["B6.d"], ["R0"], F.Relu)
+        for h in (0, 1):
             s = half(h, 2048)
             scan(T.CM[:, s], T[cx][:, s], T.PK[:, s], A.min, A.max, cxk + ["PK%d" % h], ["CM%d" % h])
-            b, key = BA[h], "B%d.k" % (1 + h)
             for k in range(1, 16):
-                mm(b[:, k:H:16], T.CM[:, 2048 * h + k:2048 * h + 2048:16], T.B16[:], False, False, ["B16", "CM%d" % h], [key])
-            mm(b[:, 0:H:16], T.R0[:, half(h)], T.B16[:], False, True, ["B16", "R0%d" % h], [key])
-            act(row0(h), aside(h), ["P0%d" % h], ["PK%d" % h])
-
-        def worst_a(h):
-            scan(T.KS[:, half(h)], T.MB[:, 0:H], BA[h][:, 0:H], A.min, A.max, ["MB", "B%d.k" % (1 + h)], ["KS%d" % h])
-
-        def worst_b(h):
-            cp(T.XI[:, half(h, 8)], T.KS[:, H * h + 15:H * h + H:16], ["KS%d" % h], ["XI%d" % h])
-
-        def worst_c(h):
-            ts(T.XI2[:, half(h, 8)], T.XI[:, half(h, 8)], 15, None, A.bitwise_and, None, ["XI%d" % h], ["XJ%d" % h])
-
-        def worst_d(h):
-            tt(T.XA[:, half(h)], T.XI2[:, half(h, 8)].indirect(T.OFFC[:, 0:8]), T.DELB[:, 0:H], A.mult, ["XJ%d" % h, "OFFC", "DELB"], ["XA%d" % h])
-            o, key = BG[h][:, 256:264], "B%d.kl" % (3 + h)
-            mm(o, T.KR16[0:1, :], T.ONES[0:1, 0:8], True, False, ["KR16", "ONES"], [key])
-            mm(o, T.ONES[0:1, 0:H], T.IO256[0:1, 0:8], False, False, ["IO256", "ONES"], [key])
-            mm(o, T.XA[:, half(h)], T.NB8[:], False, True, ["XA%d" % h, "NB8"], [key])
-
-        def worst_e(h):
-            cp(T.KL[:, half(h, 8)], BG[h][:, 256:264], ["B%d.kl" % (3 + h)], ["KL%d" % h])
-
-        def win(h):
-            return T.PK[:, half(h, 2048)].indirect(T.KL[:, half(h, 8)])
-
-        def swap_a(h):
-            cp(T.XS[:, half(h)], win(h), ["PK%d" % h, "KL%d" % h], ["XS%d" % h])
-
-        def swap_b(h):
-            cp(win(h), aside(h), ["P0%d" % h, "KL%d" % h], ["PK%d" % h])
-
-        def swap_c(h):
-            cp(row0(h), T.XS[:, half(h)], ["XS%d" % h], ["PK%d" % h])
-
-        def largest(h):
+                mm(ka[:, H * h + k:H * h + H:16], T.CM[:, 2048 * h + k:2048 * h + 2048:16], T.B16[:], False, False, ["B16", "CM%d" % h], ["B1.k"])
+        for h in (0, 1):
+            mm(ka[:, H * h:H * h + H:16], T.R0[:, half(h)], T.B16[:], False, h == 1, ["B16", "R0"], ["B1.k"])
+        cap_room(t)
+        if t > 1:
+            act(row0, aside, ["P0"], pk)
+            parity()
+            new_words(t - 1)
+            wl = word_list()
+            wl[0]()
+            wl[1]()
+        else:
+            for j, (b, k) in enumerate(left):
+                if j == 2:
+                    act(row0, aside, ["P0"], pk)
+                act(T.SL[:, half(j, 512)], b[:], k, ["SL"], F.Relu)
+            tt(T.IOTM[:], T.IOT[:], T.OFFD[:], A.add, ["IOT", "OFFD"], ["IOTM"])
+        scan(T.KS[:], T.MB[:], ka[:, 0:256], A.min, A.max, ["MB", "B1.k"], ["KS"])
+        if t > 1:
+            wl[2]()
+        cp(T.XI[:], T.KS[:, 15:256:16], ["KS"], ["XI"])
+        ts(T.XI2[:], T.XI[:], 15, None, A.bitwise_and, None, ["XI"], ["XJ"])
+        tt(T.XA[:], T.XI2[:].indirect(T.OFFC[:, 0:16]), T.DELB[:], A.mult, ["XJ", "OFFC", "DELB"], ["XA"])
+        o = ka[:, 256:272]
+        mm(o, T.KR16[0:1, :], T.ONES[0:1, 0:16], True, False, ["KR16", "ONES"], ["B1.kl"])
+        mm(o, T.ONES[0:1, 0:H], T.IO256[0:1, :], False, False, ["IO256", "ONES"], ["B1.kl"])
+        for h in (0, 1):
+            mm(ka[:, 256 + 8 * h:264 + 8 * h], T.XA[:, half(h)], T.NB8[:], False, h == 1, ["XA", "NB8"], ["B1.kl"])
+        if t == 1:
+            for j in range(0, 3):
+                table(j)
+        cp(T.KL[:], o, ["B1.kl"], ["KL"])
+        win = T.PK[:, 0:4096].indirect(T.KL[:])
+        cp(T.XS[:], win, pk + ["KL"], ["XS"])
+        cp(win, aside, ["P0", "KL"], pk)
+        cp(row0, T.XS[:], ["XS"], pk)
+        verdict = [(T.B3[:, 0:256], "B3.g"), (T.B4[:, 0:256], "B4.g")]
+        for o, key in verdict:
+            mm(o, T.LIMT[:], T.ONES[:], True, False, ["LIMT", "ONES"], [key])
+        for h in (0, 1):
             lo = 2048 * h
             s = slice(lo + 2047, lo - 1 if lo else None, -1)
             scan(T.FB[:, s], T.SEG[:], T.PK[:, s], A.mult, A.max, ["SEG", "PK%d" % h], ["FB%d" % h])
-
-        def m_of(h, j):
-            return T.FB[:, 2048 * h + j:2048 * h + 2048:16]
-
-        def test(h, j):
-            cm, key = (T.CMP1, T.CMP2)[j][:, half(h)], "CMP%d%d" % (j, h)
-            tt(cm, m_of(h, j), T.B0[:, half(h)], A.is_gt, ["FB%d" % h, "B0.cap"], [key])
-            o, ok = BG[h][:, half(j)], "B%d.g%d" % (3 + h, j)
-            mm(o, T.LIMT[:], T.ONES[:, 0:H], True, False, ["LIMT", "ONES"], [ok])
-            mm(o, T.NBO[:], cm, False, True, ["NBO", key], [ok])
-
-        def clip(h):
-            gk = "B%d.g0" % (3 + h)
-            act(BU[h][:, 0:H], BG[h][:, 0:H], [gk], ["B%d.u0" % (5 + h)], F.Relu)
-
-        def keep_a(h):
-            tt(T.MA[:, half(h)], m_of(h, 1), BG[h][:, H:2 * H], A.min, ["FB%d" % h, "B%d.g1" % (3 + h)], ["MA%d" % h])
-
-        def keep_b(h):
-            tt(BU[h][:, 0:H], m_of(h, 0), BU[h][:, 0:H], A.min, ["FB%d" % h, "B%d.u0" % (5 + h)], ["B%d.u0" % (5 + h)])
-
-        def send(h):
-            tt(snd(h), T.MA[:, half(h)], BU[h][:, 0:H], A.max, ["MA%d" % h, "B%d.u0" % (5 + h)], [sk(h)])
-            wait_for("p", deps("p", [sk(h)], []))
-            g.remote_dma(land(h), snd(h), T.sem["arr%d%d" % (t, h)], T.sem.loc, pid, rid, topo.mask(core, dst))
-            lastw[lk(h)] = ("arr%d%d" % (t, h), len(topo.engines(core, dst)), {})
-
-        def step2(h):
-            d, dk = BU[h][:, 384:512], "B%d.d" % (5 + h)
-            mm(d, T.ID[:], T.CAP[:, nodes(t, h)], True, False, ["ID", "CAP"], [dk])
-            mm(d, T.NID[:], snd(h), False, True, ["NID", sk(h)], [dk])
-            act(T.SL[:, nodes(t, h)], d, [dk], ["SL"], F.Relu)
-
-        def step2_res(h):
-            act(T.RES[:, nodes(t, h)], snd(h), [sk(h)], ["RES"])
-
-        def weighed(o, key, h, stop):
-            mm(o, T.C37[0:1, :], T.IOBF[0:1, half(h)], True, False, ["C37", "IOBF"], [key])
-            mm(o, T.WTL[:], land(h), False, stop, ["WTL", lk(h)], [key])
-
-        def u_a(h):
-            o, key = BA[h][:, 256:384], "B%d.u0" % (1 + h)
-            weighed(o, key, h, True)
-            act(T.FQ[:, half(h)], o, [key], ["FQ%d" % h], bias=129.5001220703125, scale=1.0 / 4096)
-
-        def u_b(h):
-            b, bk = BU[h], "B%d." % (5 + h)
-            o = b[:, H:2 * H]
-            weighed(o, bk + "u", h, False)
-            mm(o, T.CU[0:1, :], T.ONES[0:1, 0:H], False, False, ["CU", "ONES"], [bk + "u"])
-            mm(o, T.N12M[:], T.FQ[:, half(h)], False, True, ["N12M", "FQ%d" % h], [bk + "u"])
-            act(T.SQ[:, half(h)], o, [bk + "u"], ["SQ%d" % h], F.Square)
-            op("a", lambda: AC.activation(b[:, 256:384], o, F.Copy, scale=T.KAF[:, 0:1]), [bk + "u", "KAF"], [bk + "fu"])
-
-        def p_of(h):
-            s = half(h)
-            return [
-                lambda: ts(T.UU[:, s], T.SQ[:, s], 0.03125, -0.375, A.mult, A.add, ["SQ%d" % h], ["UU%d" % h]),
-                lambda: tt(T.PI2[:, s], T.UU[:, s], BU[h][:, 256:384], A.add, ["UU%d" % h, "B%d.fu" % (5 + h)], ["PI%d" % h]),
-                lambda: ts(T.PI2[:, s], T.PI2[:, s], 2047, None, A.bitwise_and, None, ["PI%d" % h], ["PI%d" % h]),
-                lambda: cp(T.P16[:, s], T.PI2[:, s], ["PI%d" % h], ["P16%d" % h]),
-                lambda: cp(T.PF[:, s], T.PI2[:, s], ["PI%d" % h], ["PF%d" % h]),
-            ]
-
-        def wide(h, j):
-            act(T.MX[:, 2048 * h + 1024 * j:2048 * h + 1024 * j + 1024], land(h).indirect(T.OFFC[:, half(j, 64)]), [lk(h), "OFFC"], ["MX%d%d" % (h, j)])
-
-        def keys_begin(h):
-            o, key = BA[h][:, H:2 * H], "B%d.k" % (1 + h)
-            mm(o, T.ONES[:, 0:H], T.NEG[:], True, False, ["NEG", "ONES"], [key])
-            mm(o, T.ONES[0:1, 0:H], T.KC2[0:1, :], False, False, ["KC2", "ONES"], [key])
-            mm(o, T.PF[:, half(h)], T.IDH[:], False, False, ["PF%d" % h, "IDH"], [key])
-
-        def scores(h, j):
-            s = slice(2048 * h + 1024 * j, 2048 * h + 1024 * j + 1024)
-            tt(T.SC[:, s], T.SL[:, 0:2048].indirect(T.P16[:, H * h + 64 * j:H * h + 64 * j + 64]), T.MX[:, s], A.min,
-               ["SL", "P16%d" % h, "MX%d%d" % (h, j)], ["SC%d%d" % (h, j)])
-
-        def keys_end(h):
-            for m in range(16):
-                mm(BA[h][:, H + m:2 * H:16], T.SC[:, 2048 * h + m:2048 * h + 2048:16], T.B32K[:], False, m == 15,
-                   ["B32K", "SC%d0" % h, "SC%d1" % h], ["B%d.k" % (1 + h)])
-
-        def best(h):
-            scan(T.KS[:, half(h)], T.MB[:, 0:H], BA[h][:, H:2 * H], A.min, A.max, ["MB", "B%d.k" % (1 + h)], ["KS%d" % h])
-
-        if t > 1:
-            marks()
-            suspended_a(t - 1)
-        sums_begin(0)
-        sums_begin(1)
-        if t > 1:
-            parity()
-        clipped(0)
-        clipped(1)
-        if t > 1:
-            cap_room(t)
-            new_words(t - 1)
-        else:
-            for j in range(8):
-                b, k = (T.B0, "B0.lv") if j % 2 else (T.B7, "B7.hi")
-                s = half(j, 256)
-                mm(b[:, 256:512], T.ID[:], T.CAP[:, s], True, False, ["ID", "CAP"], [k])
-                mm(b[:, 256:512], T.NID[:], T.RES[:, s], False, True, ["NID", "RES"], [k])
-                act(T.SL[:, s], b[:, 256:512], [k], ["SL"], F.Relu)
-        for f in (worst_a, worst_b, worst_c, worst_d):
-            f(0)
-        worst_a(1)
-        worst_b(1)
-        worst_e(0)
-        worst_c(1)
-        swap_a(0)
-        worst_d(1)
-        swap_b(0)
-        if t > 1:
-            word_list()
-        swap_c(0)
-        worst_e(1)
-        largest(0)
-        test(0, 0)
-        clip(0)
-        test(0, 1)
-        swap_a(1)
-        swap_b(1)
-        keep_a(0)
-        keep_b(0)
-        swap_c(1)
-        send(0)
-        step2(0)
-        step2_res(0)
+        fb = ["FB0", "FB1"]
+        for j, cm in enumerate((T.CMP1, T.CMP2)):
+            tt(cm[:], T.FB[:, j:4096:16], T.B0[:, 0:256], A.is_gt, fb + ["B0.cap"], ["CMP%d" % j])
+            mm(verdict[j][0], T.NBO[:], cm[:], False, True, ["NBO", "CMP%d" % j], [verdict[j][1]])
+        mb = T.B5[:, 0:256]
+        act(mb, T.B3[:, 0:256], ["B3.g"], ["B5.m"], F.Relu)
+        tt(T.XS[:], T.FB[:, 1:4096:16], T.B4[:, 0:256], A.min, fb + ["B4.g"], ["XS"])
+        tt(mb, T.FB[:, 0:4096:16], mb, A.min, fb + ["B5.m"], ["B5.m"])
+        tt(snd, T.XS[:], mb, A.max, ["XS", "B5.m"], [sk])
+        wait_for("p", deps("p", [sk], []))
+        g.remote_dma(land, snd, T.sem["arr%d" % t], T.sem.loc, pid, rid, topo.mask(core, dst))
+        lastw[lk] = ("arr%d" % t, len(topo.engines(core, dst)), {})
+        if t == 1:
+            for j in range(3, 8):
+                table(j)
+        mm(d, T.ID[:], cap, True, False, ["ID", "CAP"], ["B6.d"])
+        mm(d, T.NID[:], snd, False, True, ["NID", sk], ["B6.d"])
+        act(T.SL[:, c:2048:8], d, ["B6.d"], ["SL"], F.Relu)
+        gcopy(T.RES[:, c:2048:8], snd, Q, [sk], ["RES"])
+        if t == NT:
+            dma("s", T.yr[:], T.RES[:, 0:2048], "dyr", ["RES"], ["yr"])
         if t > 1:
             suspended_b(t - 1)
             old_words()
             set_words()
         else:
+            vector_constants()
             cp(T.WD[:, 0:2048], T.BRI[:], ["BRI"], ["WD"])
+        ul = T.B2[:, 256:272]
+        mm(ul, T.KR[0:1, :], T.C37[0:1, 0:16], True, False, ["KR", "C37"], ["B2.u"])
+        mm(ul, T.C37[0:1, :], T.I16B[0:1, :], False, False, ["I16B", "C37"], ["B2.u"])
+        for r in range(16):
+            mm(ul, T.W16[:, 15 - r:143 - r], T.LAND[:, L0 + r:L0 + Q:16], False, r == 15, ["W16", lk], ["B2.u"])
         if t < NT:
-            offsets_a(t + 1)
-        largest(1)
-        test(1, 0)
-        u_a(0)
-        clip(1)
-        test(1, 1)
-        u_b(0)
-        if t < NT:
-            offsets_b(t + 1)
-        keep_a(1)
-        keep_b(1)
-        send(1)
-        wide(0, 0)
-        step2(1)
+            gcopy(T.RES[:, 2048 + L0:2048 + L0 + Q], land, Q, [lk], ["RESG"])
+        lo, hi = CH[-1]
+        for k in range(16):
+            gcopy(T.MX[:, 16 * lo + k:16 * hi:16], T.LAND[:, L0 + lo:L0 + hi], hi - lo, [lk], ["MXk%d" % k])
         if t == 1:
             cap_wide(2, range(8, 16))
         if t + 2 <= NT:
             cap_wide(t + 2, range(1, 16))
-        for f in p_of(0):
-            f()
+
+        def wide(j):
+            lo, hi = CH[j]
+            act(T.MX[:, 16 * lo:16 * hi], land.indirect(T.OFFC[:, lo:hi]), [lk, "OFFC"], ["MX%d" % j])
+        wide(0)
         if t < NT:
-            offsets_c()
-        keys_begin(0)
-        wide(0, 1)
-        scores(0, 0)
-        u_a(1)
-        step2_res(1)
-        u_b(1)
+            offsets_a(t + 1)
+        wide(1)
+        cp(T.XI[:], ul, ["B2.u"], ["XI"])
+        ts(T.XI2[:], T.XI[:], 4095, None, A.bitwise_and, None, ["XI"], ["XJ"])
+        cp(T.UL[:], T.XI2[:], ["XJ"], ["UL"])
+        cp(T.P16[:], T.TAB[:].indirect(T.UL[:]), ["TAB", "UL"], ["P16"])
+        wide(2)
+        if t < NT:
+            offsets_b(t + 1)
+        wide(3)
+        kb = T.B2
+        for j in (0, 1, 2, 4, 3):
+            lo, hi = CH[j]
+            s = slice(16 * lo, 16 * hi)
+            mx = ["MX%d" % j] if j < len(CH) - 1 else ["MXk%d" % k for k in range(16)]
+            tt(T.SC[:, s], T.SL[:, 0:2048].indirect(T.P16[:, lo:hi]), T.MX[:, s], A.min, ["SL", "P16"] + mx, ["SC%d" % j])
+            if j == 0:
+                cp(T.PF[:], T.P16[:], ["P16"], ["PF"])
+                mm(kb[:, 0:256], T.ONES[:, 0:H], T.NEG[:], True, False, ["NEG", "ONES"], ["B2.k"])
+                mm(kb[:, 0:256], T.ONES[0:1, 0:H], T.KC2[0:1, :], False, False, ["KC2", "ONES"], ["B2.k"])
+                for h in (0, 1):
+                    mm(kb[:, half(h)], T.PF[:, half(h)], T.IDH[:], False, False, ["PF", "IDH"], ["B2.k"])
+            if j == 2 and t < NT:
+                offsets_c()
+            if j in (2, 3):
+                h = lo // H
+                for m in range(16):
+                    mm(kb[:, H * h + m:H * h + H:16], T.SC[:, 2048 * h + m:2048 * h + 2048:16], T.B32K[:], False, h == 1 and m == 15,
+                       ["B32K"] + ["SC%d" % i for i in ((0, 1, 2), (3, 4))[h]], ["B2.k"])
+        if t < NT:
+            rows(0, Q, "a", pk)
+            row0_aside()
+        marks()
         if t == NT:
-            dma("s", T.yr[:], T.RES[:, 0:2048], "dyr", ["RES"], ["yr"])
-        scores(0, 1)
-        keys_end(0)
-        wide(1, 0)
-        wide(1, 1)
-        for f in p_of(1):
-            f()
-        keys_begin(1)
-        scores(1, 0)
-        scores(1, 1)
-        keys_end(1)
-        if t < NT:
-            act(T.RES[:, 2048 + L0:2048 + L0 + Q], T.LAND[:, L0:L0 + Q], [lk(0), lk(1)], ["RESG"])
-            rows(0, 128, 0)
-            row0_aside(0)
-            rows(128, 256, 1)
-            row0_aside(1)
-        else:
-            marks()
-            suspended_a(t)
             new_words(t)
-        best(0)
-        best(1)
-        cp(T.XI[:], T.KS[:, 15:256:16], ["KS0", "KS1"], ["XI0", "XI1"])
-        ts(T.XI2[:], T.XI[:], 2047, None, A.bitwise_and, None, ["XI0", "XI1"], ["XJ0", "XJ1"])
-        tt(T.XW[:], T.XI2[:].indirect(T.OFFC[:, 0:16]), T.DELB[:], A.mult, ["XJ0", "XJ1", "OFFC", "DELB"], ["XW"])
         lv = T.B0[:, 256:272]
+        mm(lv, T.CUP[0:1, :], T.ONES[0:1, 0:16], True, False, ["CUP", "ONES"], ["B0.lv"])
+        scan(T.KS[:], T.MB[:], kb[:, 0:256], A.min, A.max, ["MB", "B2.k"], ["KS"])
+        cp(T.XI[:], T.KS[:, 15:256:16], ["KS"], ["XI"])
+        ts(T.XI2[:], T.XI[:], 2047, None, A.bitwise_and, None, ["XI"], ["XJ"])
+        tt(T.XW[:], T.XI2[:].indirect(T.OFFC[:, 0:16]), T.DELB[:], A.mult, ["XJ", "OFFC", "DELB"], ["XW"])
         for h in (0, 1):
-            mm(T.B0[:, 256 + 8 * h:264 + 8 * h], T.XW[:, half(h)], T.BOH[:], True, True, ["XW", "BOH"], ["B0.lv"])
+            mm(T.B0[:, 256 + 8 * h:264 + 8 * h], T.XW[:, half(h)], T.BOH[:], False, h == 1, ["XW", "BOH"], ["B0.lv"])
         mm(T.B7[:, 0:256], T.ID[:], T.OFFD[:], True, False, ["ID", "OFFD"], ["B7.x"])
-        cp(T.LV[:], lv, ["B0.lv"], ["LV"])
+        ts(T.LV[:], lv, -float(UP), None, A.add, None, ["B0.lv"], ["LV"])
+        if t < NT:
+            ts(T.LV2[:], lv, 8.0 - t - UP, None, A.add, None, ["B0.lv"], ["LV2"])
         cp(T.VB[:], T.IO2K[:].indirect(T.LV[:]), ["IO2K", "LV"], ["VB"])
+        if t < NT:
+            cp(T.LXW[:], T.LXT[:].indirect(T.LV2[:]), ["LXT", "LV2"], ["LXW"])
+            mm(T.B7[:, 0:256], T.IDF[:], T.LXW[:], False, False, ["IDF", "LXW"], ["B7.x"])
         for i in range(16):
             ts(T.EQ[:, i, 0:256 - 16 * i], T.VB[:, 16 * i:256], T.B0[:, 256 + i:257 + i], None, A.is_equal, None, ["VB", "B0.lv"], ["EQ%d" % i])
             if i < 15:
                 mm(T.B7[:, 16 * i + 16:256], T.BO4[:], T.EQ[:, i, 16:256 - 16 * i], False, False, ["BO4", "EQ%d" % i], ["B7.x"])
         mm(T.B7[:, 0:256], T.BT4[:], T.EQ[:, :, 0:16], False, True, ["BT4"] + ["EQ%d" % i for i in range(16)], ["B7.x"])
-        if t < NT:
-            cp(T.LI[:], lv, ["B0.lv"], ["LI"])
-            ts(T.LX[:], lv, T.MULP[:, 0:1], T.XK[:, t:t + 1], A.mult, A.add, ["B0.lv", "MULP", "XK"], ["LX"])
-            ts(T.LI[:], T.LI[:], 7, None, A.bitwise_and, None, ["LI"], ["LI"])
-            ts(T.LW[:], T.LI[:], float(t), 8192.0, A.not_equal, A.mult, ["LI"], ["LW"])
-            tt(T.LW[:], T.LW[:], T.TP[:], A.min, ["LW", "TP"], ["LW"])
-            tt(T.LX[:], T.LW[:], T.LX[:], A.max, ["LW", "LX"], ["LX"])
-        else:
-            suspended_b(t)
+        suspended_a(t)
         scan(T.CNS[:], T.MB[:], T.B7[:, 0:256], A.min, A.max, ["MB", "B7.x"], ["CNS"])
         if t < NT:
             tt(T.LB[:], T.CNS[:, 15:256:16], T.TP[:], A.min, ["CNS", "TP"], ["LB"])
-            tt(T.LC[:], T.LB[:], T.LX[:], A.max, ["LB", "LX"], ["LC"])
-            cp(T.PL[:], T.LC[:], ["LC"], ["PL"])
-            cp(T.PK[:].indirect(T.PL[:]), T.LAND[:, L0:L0 + Q], ["PL", lk(0), lk(1)], ["PK0", "PK1", "P00", "P01", "PKT"])
+            cp(T.PL[:], T.LB[:], ["LB"], ["PL"])
+            cp(T.PK[:].indirect(T.PL[:]), land, ["PL", lk], pk + ["P0", "PKT"])
 
-    word_list()
+    wl = word_list()
+    wl[0]()
+    suspended_b(NT)
+    wl[1]()
+    wl[2]()
     old_words()
     set_words()
     dma("s", T.yb[:], T.WD[:, 0:2048], "dyb", ["WD"], ["yb"])
-    g.wait_ge(T.sem.loc, 2 * sum(len(topo.engines(core, cores[(rank + 1 + c % (n - 1)) % n])) for c in range(NT)))
+    g.wait_ge(T.sem.loc, sum(len(topo.engines(core, cores[(rank + 1 + c % (n - 1)) % n])) for c in range(NT)))
     for s, k in own.items():
         g.wait_ge(T.sem[k], count[s])
-    for s in ("dyr", "dyb", "dbr", "dres", "dcap", "dwt", "dka"):
+    for s in DMAS:
         g.wait_ge(T.sem[s], 16)

@@ -1,15 +1,21 @@
 from concourse.mybir import AluOpType as A, ActivationFunctionType as F
 
 NT = 6
-GS = 152
 Q = 256
 H = 128
 ZC = 3328
 P0 = 4096
 TR = 4352
-UP = 12288
-CH = ((0, 32), (32, 64), (64, 128), (128, 192), (192, 256))
+FAR = 131072
 MAGIC = 12582912.0
+GS = 4
+GC = 4
+CLIP = (6, 7)
+SHARE = (2, 3)
+WIDE = {0: "v", 4: "v", 6: "a", 7: "p"}
+CYCLE, GATHER, SCATTER = 0.83, 1.56, 4.0
+WAKE, DMA, LAT, FIRST = 75.0, 1700.0, 1500.0, 4200.0
+PASSES, TOL, URG, RATIO = 6, 60, 100, 1.0
 SCRATCH = {
     "RES": ("sbuf", [128, 3344], "bfloat16"),
     "WD": ("sbuf", [128, 2304], "float32"),
@@ -19,31 +25,31 @@ SCRATCH = {
     "SND": ("sbuf", [128, NT * Q], "bfloat16"),
     "LAND": ("sbuf", [128, NT * Q], "bfloat16"),
     "IO2K": ("sbuf", [128, 2048], "float32"),
-    "LXT": ("sbuf", [128, 2064], "float32"),
+    "LXT": ("sbuf", [128, 2048], "float32"),
     "TAB": ("sbuf", [128, 4096], "float32"),
     "ROWS": ("sbuf", [128, 4096], "float16"),
     "FT": ("sbuf", [128, 1024], "bfloat16"),
-    "RI": ("sbuf", [128, 128], "int32"),
-    "U32": ("sbuf", [128, 32], "int32"),
+    "SACC": ("sbuf", [128, 2], "float32"),
     "K4": ("sbuf", [128, 4], "float16"),
-    "PF": ("sbuf", [128, 256], "float16"),
     "XW": ("sbuf", [128, 256], "float16"),
     "BOH": ("sbuf", [128, 8], "float16"),
     "W16": ("sbuf", [128, 144], "bfloat16"),
+    "COL": ("sbuf", [128, 16], "float32"),
 }
-for _n in ("FB", "CM", "CX0", "CX1", "MX", "SC", "TOH"):
+for _n in ("FB", "CM", "CX0", "CX1", "MX", "SC"):
     SCRATCH[_n] = ("sbuf", [128, 4096], "bfloat16")
-for _n in ("CAP", "SL", "SEG"):
+for _n in ("CAP", "SL", "SEG", "TOH", "SP"):
     SCRATCH[_n] = ("sbuf", [128, 2048], "bfloat16")
-for _n in ("ONES", "OFFD", "CMP1", "CMP2", "SGN", "DELB", "N12", "KN", "KP", "BD1", "BD2", "R0", "XS", "XA", "OH", "KC", "KC2", "NEG"):
+for _n in ("ONES", "OFFD", "OFFA", "DELB", "N12", "KN", "KP", "BD1", "BD2", "R0", "XS", "XA", "OH", "SG", "LXW", "CMP0", "CMP1"):
     SCRATCH[_n] = ("sbuf", [128, 256], "bfloat16")
-for _n in ("IOT", "IO16", "NDEL", "NEW", "MB", "KS", "CNS", "WOLD", "IOTM", "LXW"):
+for _n in ("IOT", "IO16", "NDEL", "NEW", "MB", "KS", "CNS", "WOLD", "IOTM", "PF"):
     SCRATCH[_n] = ("sbuf", [128, 256], "float32")
-for _n in ("BO", "NBO", "BO4", "BT4", "ID", "NID", "N11M", "N12M", "N16M", "P16M", "P20M", "N19M", "C37", "CUP", "KR", "KR16", "EIGHT", "LIMT"):
+for _n in ("BO", "NBO", "BO4", "BT4", "BW32K", "ID", "NID", "N11M", "N12M", "N16M", "P16M", "P20M", "N19M", "MULD", "C37", "CFAR", "NEG",
+           "KC", "KC2", "KR", "KR16", "EIGHT", "LIMT"):
     SCRATCH[_n] = ("sbuf", [128, 128], "bfloat16")
 for _n in ("IDH", "RH", "KR4"):
     SCRATCH[_n] = ("sbuf", [128, 128], "float16")
-for _n in ("B16", "B32K", "NB8"):
+for _n in ("B16", "B32K", "NB32K", "NB8"):
     SCRATCH[_n] = ("sbuf", [128, 8], "bfloat16")
 for _n in ("IO256", "I16B"):
     SCRATCH[_n] = ("sbuf", [128, 16], "bfloat16")
@@ -55,18 +61,105 @@ for _n in ("EO", "P16", "VB", "OFFC"):
     SCRATCH[_n] = ("sbuf", [128, 256], "uint16")
 for _n in ("WTI", "KAI", "PI", "KI"):
     SCRATCH[_n] = ("sbuf", [128, 1], "int32")
-for _n in ("WTF", "PFL", "KF", "G16", "G15", "MULP", "ADDP", "PB", "PC", "ODD", "SACC"):
-    SCRATCH[_n] = ("sbuf", [128, 1], "float32")
 for _n in ("TP", "TW", "LB", "LC", "LD"):
     SCRATCH[_n] = ("sbuf", [128, 16], "float32")
 for _n in ("XI", "XI2"):
     SCRATCH[_n] = ("sbuf", [128, 16], "int32")
-for _n in ("KL", "PL", "PW", "LV", "LV2", "UL"):
+for _n in ("KL", "PL", "PW", "LV", "UL"):
     SCRATCH[_n] = ("sbuf", [128, 16], "uint16")
 for _n in range(8):
     SCRATCH["B%d" % _n] = ("psum", [128, 512], "float32")
-DMAS = ["dbr", "dres", "dcap", "dwt", "dka", "dyr", "dyb"] + ["dr%d" % k for k in range(4)] + ["dt%d" % k for k in range(5)]
-SEMAPHORES = ["cv", "ct", "ca", "cp", "loc"] + DMAS + ["arr%d" % t for t in range(1, NT + 1)]
+DMAS = ["dbr", "dres", "dcap", "dwt", "dka", "dyr", "dyb"] + ["dr%d" % k for k in range(4)] + ["dt%d" % k for k in range(4)]
+SEMAPHORES = ["cv", "ct", "ca", "cp", "loc"] + DMAS + ["arr%d%d" % (t, h) for t in range(1, NT + 1) for h in (0, 1)]
+COLS = ("WTF", "PFL", "KF", "G16", "G15", "MULP", "ADDP", "PB", "PC", "ODD")
+ORDERS = {}
+
+
+def banks_of(keys):
+    return set(x.split(".")[0] for x in keys if "." in x)
+
+
+def issue_order(calls):
+    n = len(calls)
+    before, after = [set() for _ in calls], [[] for _ in calls]
+    lastw, readers = {}, {}
+    for i, (q, _f, r, w, _ns, _lat) in enumerate(calls):
+        w = list(w) + (["T" + b for b in banks_of(list(r) + list(w))] if q == "t" else [])
+        for k in list(r) + w:
+            if k in lastw:
+                before[i].add(lastw[k])
+        for k in w:
+            before[i].update(readers.get(k, []))
+        before[i].discard(i)
+        for k in r:
+            readers.setdefault(k, []).append(i)
+        for k in w:
+            lastw[k] = i
+            readers[k] = []
+        for p in before[i]:
+            after[p].append(i)
+    banks = [banks_of(list(c[2]) + list(c[3])) for c in calls]
+    loads = [i for i in range(n) if calls[i][0] == "s"]
+    behind = dict(zip(loads, loads[1:]))
+
+    def run(way, first_of, next_of, back):
+        missing = [len(b) for b in first_of]
+        held = set() if back else set(behind.values())
+        ready = {q: [] for q in "vatps"}
+        at, end, free, bank, dmas = [0.0] * n, [0.0] * n, {q: 0.0 for q in ready}, {}, 0.0
+        for i in range(n):
+            if not missing[i]:
+                ready[calls[i][0]].append(i)
+        order = []
+
+        def start(i):
+            q = calls[i][0]
+            s = max(free[q], at[i])
+            for b in banks[i]:
+                if b in bank and bank[b][0] != q:
+                    s = max(s, bank[b][1] + WAKE)
+            return s
+
+        while len(order) < n:
+            pick = None
+            for q, cand in ready.items():
+                st = {i: start(i) for i in cand if i not in held}
+                if not st:
+                    continue
+                soon = min(st.values())
+                first = max([i for i in st if st[i] <= soon + TOL], key=lambda i: (way[i], -i))
+                for i in st:
+                    if way[i] > way[first] + URG and st[first] + calls[first][4] - st[i] > RATIO * (st[i] - st[first]):
+                        first = i
+                if pick is None or st[first] < pick[0]:
+                    pick = (st[first], first)
+            s, i = pick
+            q, _f, _r, _w, ns, lat = calls[i]
+            ready[q].remove(i)
+            held.discard(behind.get(i))
+            order.append(i)
+            free[q] = s + ns
+            end[i] = s + ns + (0.0 if back else lat)
+            if lat and q != "p" and not back:
+                end[i] = dmas = max(s + DMA, dmas) + lat
+            for b in banks[i]:
+                bank[b] = (q, s + ns)
+            for j in next_of[i]:
+                late = calls[j][5] + (DMA if calls[j][5] and calls[j][0] != "p" else 0.0) if back else 0.0
+                at[j] = max(at[j], end[i] + late + (0.0 if q == calls[j][0] == "t" else WAKE))
+                missing[j] -= 1
+                if not missing[j]:
+                    ready[calls[j][0]].append(j)
+        return order, end
+
+    way = [-50.0 * i for i in range(n)]
+    best = None
+    for _ in range(PASSES):
+        order, end = run(way, before, after, False)
+        if best is None or max(end) < best[0]:
+            best = (max(end), order, way)
+        way = run(end, after, before, True)[1]
+    return best[1]
 
 
 def rank_program(g, core, T, topo):
@@ -75,207 +168,171 @@ def rank_program(g, core, T, topo):
         return
     cores = T.cores
     n = len(cores)
-    queues = {"v": g.vector, "t": g.tensor, "a": g.scalar, "p": g, "s": g.sync}
-    own = {"v": "cv", "t": "ct", "a": "ca", "p": "cp"}
-    count = {k: 0 for k in ("v", "t", "a", "p")}
-    known = {k: {} for k in queues}
-    lastw, readers, banks = {}, {}, {}
-
-    def wait_for(eng, toks):
-        best = {}
-        for tok in toks:
-            if tok[0] not in best or best[tok[0]][1] < tok[1]:
-                best[tok[0]] = tok
-        kn = known[eng]
-        for s, val, snap in sorted(best.values(), key=lambda x: -len(x[2])):
-            if kn.get(s, 0) >= val:
-                continue
-            queues[eng].wait_ge(T.sem[s], val)
-            kn[s] = val
-            for s2, v2 in snap.items():
-                if kn.get(s2, 0) < v2:
-                    kn[s2] = v2
-
-    def banks_of(r, w):
-        return set(x.split(".")[0] for x in list(r) + list(w) if "." in x)
-
-    def deps(eng, r, w):
-        toks = []
-        for k in r:
-            if k in lastw:
-                toks.append(lastw[k])
-        for k in w:
-            if k in lastw:
-                toks.append(lastw[k])
-            toks += list(readers.get(k, {}).values())
-        for k in banks_of(r, w):
-            toks += [tok for e, tok in banks.get(k, {}).items() if e != eng]
-        if eng == "t":
-            toks = [x for x in toks if x[0] != "ct"]
-        return toks
-
-    def note(eng, tok, r, w):
-        for k in r:
-            readers.setdefault(k, {})[tok[0]] = tok
-        for k in w:
-            lastw[k] = tok
-            readers[k] = {}
-        for k in banks_of(r, w):
-            banks.setdefault(k, {})[eng] = tok
-
-    def op(eng, f, r, w):
-        wait_for(eng, deps(eng, r, w))
-        count[eng] += 1
-        tok = (own[eng], count[eng], dict(known[eng]))
-        f().then_inc(T.sem[own[eng]], 1)
-        note(eng, tok, r, w)
-
-    def dma(eng, out, in_, sem, r, w):
-        wait_for(eng, deps(eng, r, w))
-        queues[eng].dma_start(out, in_).then_inc(T.sem[sem], 16)
-        note(eng, (sem, 16, dict(known[eng])), r, w)
-
     V, PE, AC = g.vector, g.tensor, g.scalar
+    calls = []
 
-    def v(f, r, w):
-        op("v", f, r, w)
+    def cols(ap):
+        c = 1
+        for x in ap.shape[1:]:
+            c *= x
+        return c
+
+    def narrow(*aps):
+        return all("16" in str(a.dtype) for a in aps)
+
+    def vec(f, r, w, n_cols, rate):
+        calls.append(("v", f, r, w, 60.0 + max(64.0, n_cols * rate) * CYCLE, 0.0))
 
     def mm(out, lhs, rhs, st, sp, r, w):
-        op("t", lambda: PE.matmul(out, lhs, rhs, st, sp), r, w)
+        ns = max(min(64, cols(lhs)), cols(rhs)) * CYCLE * (1 if narrow(lhs) else 4)
+        calls.append(("t", lambda: PE.matmul(out, lhs, rhs, st, sp), r, w, ns, 0.0))
 
-    def act(out, in_, r, w, func=F.Copy, bias=0.0, scale=1.0):
-        op("a", lambda: AC.activation(out, in_, func, bias=bias, scale=scale), r, w)
+    def act(out, in_, r, w, func=F.Copy, bias=0.0, scale=1.0, accum=None, rate=1.0):
+        calls.append(("a", lambda: AC.activation(out, in_, func, bias=bias, scale=scale, accum_out=accum), r, w,
+                      75.0 + max(64, cols(out)) * rate * CYCLE, 0.0))
 
     def fill(ap, c, k):
-        v(lambda: V.memset(ap, c), [], [k])
+        vec(lambda: V.memset(ap, c), [], [k], cols(ap), 0.5 if narrow(ap) else 1.0)
 
     def iota(ap, pattern, base, cm, k):
-        op("p", lambda: g.iota(ap, pattern, base, cm, allow_small_or_imprecise_dtypes=True), [], [k])
+        small = "int" not in str(ap.dtype)
+        calls.append(("p", lambda: g.iota(ap, pattern, base, cm, allow_small_or_imprecise_dtypes=small), [], [k], 130.0 + 2 * cols(ap) * CYCLE, 0.0))
 
-    def gcopy(out, in_, cols, r, w):
-        op("p", lambda: g.affine_select(out, in_, [[0, cols]], A.is_ge, 0.0, 0, 0), r, w)
+    def gcopy(out, in_, r, w):
+        calls.append(("p", lambda: g.affine_select(out, in_, [[0, cols(out)]], A.is_ge, 0.0, 0, 0), r, w, 170.0 + 2 * cols(out) * CYCLE, 0.0))
 
     def ts(out, in0, s1, s2, o0, o1, r, w):
+        rate = 0.5 if narrow(out, in0) else 1.0
         if o1 is None:
-            v(lambda: V.tensor_scalar(out, in0, s1, None, o0), r, w)
+            vec(lambda: V.tensor_scalar(out, in0, s1, None, o0), r, w, cols(out), rate)
         else:
-            v(lambda: V.tensor_scalar(out, in0, s1, s2, o0, o1), r, w)
+            vec(lambda: V.tensor_scalar(out, in0, s1, s2, o0, o1), r, w, cols(out), rate)
 
-    def tt(out, a, b, o, r, w):
-        v(lambda: V.tensor_tensor(out, a, b, o), r, w)
+    def tt(out, a, b, o, r, w, rate=None):
+        vec(lambda: V.tensor_tensor(out, a, b, o), r, w, cols(b), rate or (1.0 if banks_of(r) else 2.0))
 
     def cp(out, a, r, w):
-        v(lambda: V.tensor_copy(out, a), r, w)
+        vec(lambda: V.tensor_copy(out, a), r, w, cols(out), 0.5 if narrow(out, a) else 1.0)
+
+    def gather(q, out, win, off, r, w):
+        if q == "a":
+            act(out, win.indirect(off), r, w, rate=GATHER)
+        else:
+            vec(lambda: V.tensor_copy(out, win.indirect(off)), r, w, cols(out), GATHER)
+
+    def scatter(win, off, src, r, w):
+        vec(lambda: V.tensor_copy(win.indirect(off), src), r, w, cols(src), SCATTER)
 
     def scan(out, d0, d1, o0, o1, r, w):
-        v(lambda: V.tensor_tensor_scan(out, d0, d1, 0.0, o0, o1), r, w)
+        vec(lambda: V.tensor_tensor_scan(out, d0, d1, 0.0, o0, o1), r, w, cols(out), 0.5 if narrow(out, d0, d1) else 1.0)
+
+    def dma(q, out, in_, sem, r, w, kib):
+        calls.append((q, (out, in_, sem), r, w, 100.0, 3.0 * kib + 1.0))
 
     def half(h, size=H):
         return slice(size * h, size * h + size)
 
-    dma("s", T.BRI[:], T.br[:], "dbr", [], ["BRI"])
-    dma("a", T.KAI[:], T.ka[:], "dka", [], ["KAI"])
-    dma("a", T.WTI[:], T.wt[:], "dwt", [], ["WTI"])
-    op("p", lambda: g.iota(T.U32[:], [[1, 32]], 0, 32), [], ["U32"])
-    op("p", lambda: g.iota(T.PI[:], [[0, 1]], 0, 1), [], ["PI"])
+    def col(name):
+        j = COLS.index(name)
+        return T.COL[:, j:j + 1]
+
+    dma("s", T.BRI[:], T.br[:], "dbr", [], ["BRI"], 1024)
+    dma("a", T.KAI[:], T.ka[:], "dka", [], ["KAI"], 1)
+    dma("a", T.WTI[:], T.wt[:], "dwt", [], ["WTI"], 1)
+    u32 = T.UI[:, 0:32]
+    iota(u32, [[1, 32]], 0, 32, "UI")
+    iota(T.PI[:], [[0, 1]], 0, 1, "PI")
     iota(T.IOT[:], [[1, 256]], 0, 0, "IOT")
     iota(T.IO16[:], [[0, 16], [1, 16]], 0, 0, "IO16")
     iota(T.IOB[:], [[16, 8], [0, 16]], 0, 0, "IOB")
     iota(T.ONES[:], [[0, 256]], 1, 0, "ONES")
-    for name, c in (("LIMT", 18), ("PAR", 1), ("EIGHT", 8), ("C37", 37), ("CUP", UP)):
+    for name, c in (("LIMT", 18), ("PAR", 1), ("EIGHT", 8), ("C37", 37), ("CFAR", FAR), ("NEG", -131072)):
         iota(T[name][:], [[0, 128]], c, 0, name)
-    iota(T.NEG[:], [[0, 256]], -131072, 0, "NEG")
-    iota(T.IO2K[:], [[1, 2048]], UP, 0, "IO2K")
-    fill(T.RI[:, 96:128], 2048, "RI3")
-    ts(T.RI[:, 0:32], T.U32[:], 2016, None, A.bitwise_and, None, ["U32"], ["RI0"])
-    ts(T.RI[:, 32:64], T.U32[:], 31, None, A.bitwise_and, None, ["U32"], ["RI1"])
-    tt(T.RI[:, 64:96], T.U32[:], T.U32[:], A.mult, ["U32"], ["RI2"])
-    fill(T.RES[:, ZC:ZC + 16], 0.0, "RESZ")
-    ts(T.RI[:, 64:96], T.RI[:, 64:96], 5, 2047, A.arith_shift_right, A.bitwise_and, ["RI2"], ["RI2"])
-    fill(T.K4[:, 2:3], 1.0, "K42")
-    cp(T.RH[:], T.RI[:], ["RI0", "RI1", "RI2", "RI3"], ["RH"])
+    for j in range(2):
+        iota(T.SP[:, half(j, 1024)], [[0, 1024]], 0, 0, "SP%d" % j)
+    for j in range(4):
+        iota(T.IO2K[:, half(j, 512)], [[1, 512]], 512 * j, 0, "IO2K")
+        iota(T.LXT[:, half(j, 512)], [[1, 64], [768, 8]], 64 * j, 0, "LXT")
+    fill(T.UU[:, 96:128], 2048, "RI3")
+    ts(T.UU[:, 0:32], u32, 2016, None, A.bitwise_and, None, ["UI"], ["RI0"])
+    ts(T.UU[:, 32:64], u32, 31, None, A.bitwise_and, None, ["UI"], ["RI1"])
+    tt(T.UU[:, 64:96], u32, u32, A.mult, ["UI"], ["RI2"])
+    ts(T.UU[:, 64:96], T.UU[:, 64:96], 5, 2047, A.arith_shift_right, A.bitwise_and, ["RI2"], ["RI2"])
+    cp(T.RH[:], T.UU[:, 0:128], ["RI0", "RI1", "RI2", "RI3", "UU"], ["RH"])
     for k in range(4):
-        dma("s", T.ROWS[k:k + 1, :], T.RH[:, 32 * k:32 * k + 32], "dr%d" % k, ["RH"], ["ROW%d" % k])
-    dma("s", T.RES[:, 0:ZC], T.res[:], "dres", [], ["RES", "RESG"])
-    dma("s", T.CAP[:], T.cap[:], "dcap", [], ["CAP"])
+        dma("s", T.ROWS[k:k + 1, :], T.RH[:, 32 * k:32 * k + 32], "dr%d" % k, ["RH"], ["ROW%d" % k], 8)
+    dma("s", T.RES[:, 0:ZC], T.res[:], "dres", [], ["RES", "RESG"], 832)
+    dma("s", T.CAP[:], T.cap[:], "dcap", [], ["CAP"], 512)
+    fill(T.RES[:, ZC:ZC + 16], 0.0, "RESZ")
+    fill(T.K4[:, 2:3], 1.0, "K42")
     fill(T.K4[:, 3:4], 130.0, "K43")
     ts(T.KI[:], T.PI[:], 15, None, A.bitwise_and, None, ["PI"], ["KI"])
-    cp(T.PFL[:], T.PI[:], ["PI"], ["PFL"])
-    cp(T.KF[:], T.KI[:], ["KI"], ["KF"])
-    ts(T.ID[:], T.IOT[:, 0:128], T.PFL[:, 0:1], None, A.is_equal, None, ["IOT", "PFL"], ["ID"])
-    tt(T.G16[:], T.PFL[:], T.KF[:], A.subtract, ["PFL", "KF"], ["G16"])
+    cp(col("PFL"), T.PI[:], ["PI"], ["PFL"])
+    cp(col("KF"), T.KI[:], ["KI"], ["KF"])
+    ts(T.ID[:], T.IOT[:, 0:128], col("PFL"), None, A.is_equal, None, ["IOT", "PFL"], ["ID"])
+    tt(col("G16"), col("PFL"), col("KF"), A.subtract, ["PFL", "KF"], ["G16"])
     cp(T.IDH[:], T.ID[:], ["ID"], ["IDH"])
-    ts(T.DELB[:], T.IO16[:], T.KF[:, 0:1], None, A.is_equal, None, ["IO16", "KF"], ["DELB"])
-    ts(T.BO[:], T.IOB[:], T.G16[:, 0:1], None, A.is_equal, None, ["IOB", "G16"], ["BO"])
-    ts(T.XI[:, 0:1], T.KAI[:], 63, None, A.bitwise_and, None, ["KAI"], ["XI"])
+    ts(T.DELB[:], T.IO16[:], col("KF"), None, A.is_equal, None, ["IO16", "KF"], ["DELB"])
+    ts(T.BO[:], T.IOB[:], col("G16"), None, A.is_equal, None, ["IOB", "G16"], ["BO"])
+    ts(T.XI[:, 0:1], T.KAI[:], 63, None, A.bitwise_and, None, ["KAI"], ["XI0"])
     cp(T.K4[:, 1:2], T.KAI[:], ["KAI"], ["K41"])
-    cp(T.K4[:, 0:1], T.XI[:, 0:1], ["XI"], ["K40"])
+    cp(T.K4[:, 0:1], T.XI[:, 0:1], ["XI0"], ["K40"])
     mm(T.B1[0:4, 0:128], T.K4[:], T.IDH[:], True, True, ["K40", "K41", "K42", "K43", "IDH"], ["B1.k"])
-    fill(T.SEG[:], 1.0, "SEG")
     cp(T.KR4[0:4, :], T.B1[0:4, 0:128], ["B1.k"], ["KR4"])
+    fill(T.SEG[:], 1.0, "SEG")
     fill(T.SEG[:, 0:2048:16], 0.0, "SEG")
     fill(T.MB[:], 1e9, "MB")
-    fill(T.PK[:, TR:TR + Q], 0.0, "PKT")
     fill(T.MB[:, 0:256:16], -1e9, "MB")
+    fill(T.PK[:, TR:TR + Q], 0.0, "PKT")
     fill(T.WD[:, 2048:2304], 0.0, "WDT")
-    for name, c in (("N11M", -2048.0), ("NID", -1.0)):
+    cp(T.OFFC[:], T.IOT[:], ["IOT"], ["OFFC"])
+    cp(col("WTF"), T.WTI[:], ["WTI"], ["WTF"])
+    ts(col("G15"), col("G16"), 15.0, None, A.add, None, ["G16"], ["G15"])
+    ts(T.W16[:], T.IOT[:, 0:144], col("G15"), col("WTF"), A.is_equal, A.mult, ["IOT", "G15", "WTF"], ["W16"])
+    ts(T.BT4[:], T.IO16[:, 0:128], col("KF"), 2.0 * FAR, A.is_gt, A.mult, ["IO16", "KF"], ["BT4"])
+    tt(T.BT4[:], T.BT4[:], T.BO[:], A.mult, ["BT4", "BO"], ["BT4"])
+    cp(T.BOH[:], T.BO[:, 0:128:16], ["BO"], ["BOH"])
+    for name, c in (("N11M", -2048.0), ("NID", -1.0), ("N12M", -4096.0), ("N16M", -16.0), ("IDF", 1.0), ("P16M", 65536.0), ("P20M", 1048576.0),
+                    ("N19M", -524288.0)):
         act(T[name][:], T.ID[:], ["ID"], [name], scale=c)
-    act(T.B16[:], T.BO[:, 0:128:16], ["BO"], ["B16"], scale=16.0)
-    act(T.KC[0:1, :], T.IO16[0:1, :], ["IO16"], ["KC"], bias=15.0, scale=-1.0)
+    for name, c in (("NBO", -512.0), ("BO4", 2.0 * FAR), ("BW32K", 32768.0)):
+        act(T[name][:], T.BO[:], ["BO"], [name], scale=c)
+    for name, c in (("B16", 16.0), ("NB8", -1.0), ("B32K", 32768.0), ("NB32K", -32768.0)):
+        act(T[name][:], T.BO[:, 0:128:16], ["BO"], [name], scale=c)
+    act(T.KC[0:1, :], T.IO16[0:1, 0:H], ["IO16"], ["KC"], bias=15.0, scale=-1.0)
+    act(T.KC2[0:1, :], T.IO16[0:1, 0:H], ["IO16"], ["KC2"], bias=30720.0, scale=-2048.0)
+    act(T.KR16[0:1, :], T.IO16[0:1, 0:H], ["IO16"], ["KR16"], bias=15.0, scale=16.0)
+    act(T.KR[0:1, :], T.IO16[0:1, 0:H], ["IO16"], ["KR"])
+    act(T.IO256[0:1, :], T.IOT[0:1, 0:16], ["IOT"], ["IO256"], scale=256.0)
+    act(T.I16B[0:1, :], T.IOT[0:1, 0:16], ["IOT"], ["I16B"], scale=16.0)
+    act(T.NDEL[:], T.DELB[:], ["DELB"], ["NDEL"], bias=1.0, scale=-1.0)
+    act(T.OFFD[:], T.DELB[:], ["DELB"], ["OFFD"], bias=-67108864.0, scale=67108864.0)
+    act(T.LB[:], T.IOT[:, 0:16], ["IOT", "KF"], ["LB"], F.Identity, bias=col("KF"), scale=16.0)
+    act(T.TP[:], T.LB[:], ["LB"], ["TP"], bias=float(TR))
+    act(T.TW[:], T.LB[:], ["LB"], ["TW"], bias=2048.0 + FAR)
+    tt(T.IOTM[:], T.IOT[:], T.OFFD[:], A.add, ["IOT", "OFFD"], ["IOTM"])
+    ts(col("MULP"), col("KF"), 0.0, -15.0, A.is_equal, A.mult, ["KF"], ["MULP"])
+    ts(col("ADDP"), col("KF"), 0.0, float(P0), A.is_equal, A.mult, ["KF"], ["ADDP"])
+    ts(col("MULP"), col("MULP"), 16.0, None, A.add, None, ["MULP"], ["MULP"])
+    tt(col("ADDP"), col("ADDP"), col("KF"), A.add, ["ADDP", "KF"], ["ADDP"])
+    ts(T.MULD[:], T.ID[:], col("MULP"), None, A.mult, None, ["ID", "MULP"], ["MULD"])
+    ts(T.OFFA[:], T.DELB[:], col("ADDP"), None, A.mult, None, ["DELB", "ADDP"], ["OFFA"])
+    tt(T.OFFA[:], T.OFFA[:], T.OFFD[:], A.add, ["OFFA", "OFFD"], ["OFFA"])
+    dma("s", T.TOH[:, 0:256], T.DELB[:], "dt0", ["DELB", "CAP"], ["TOH"], 64)
+    for j, s in enumerate((256, 512, 1024)):
+        dma("s", T.TOH[:, s:2 * s], T.TOH[:, 0:s], "dt%d" % (j + 1), ["TOH"], ["TOH"], s // 4)
 
-    def table(j):
-        def raw(i):
-            mm(T.B2[:], T.KR4[0:3, :], T.ROWS[0:3, half(i, 512)], True, True, ["KR4", "ROW0", "ROW1", "ROW2"], ["B2.k"])
-            act(T.FT[:, half(i & 1, 512)], T.B2[:], ["B2.k"], ["FT%d" % (i & 1)], bias=129.500244140625, scale=1.0 / 2048)
-        if j == 0:
-            raw(0)
-        if j < 7:
-            raw(j + 1)
-        mm(T.B7[:], T.KR4[0:4, :], T.ROWS[0:4, half(j, 512)], True, False, ["KR4", "ROW0", "ROW1", "ROW2", "ROW3"], ["B7.x", "B7.hi"])
-        mm(T.B7[:], T.N11M[:], T.FT[:, half(j & 1, 512)], False, True, ["N11M", "FT%d" % (j & 1)], ["B7.x", "B7.hi"])
-        act(T.TAB[:, half(j, 512)], T.B7[:], ["B7.x", "B7.hi"], ["TAB"])
+    whole_bank = {0: ["B0.cap", "B0.lv0", "B0.lv1", "B0.par", "B0.far0", "B0.far1"], 3: ["B3.g", "B3.z"], 4: ["B4.g"],
+                  6: ["B6.m", "B6.d"], 7: ["B7.x", "B7.hi"]}
+    tab = ["TAB%d" % j for j in range(8)]
 
-    def more_constants():
-        act(T.KR16[0:1, :], T.IO16[0:1, 0:128], ["IO16"], ["KR16"], bias=15.0, scale=16.0)
-        act(T.IO256[0:1, :], T.IOT[0:1, 0:16], ["IOT"], ["IO256"], scale=256.0)
-        act(T.NB8[:], T.BO[:, 0:128:16], ["BO"], ["NB8"], scale=-1.0)
-        act(T.NBO[:], T.BO[:], ["BO"], ["NBO"], scale=-512.0)
-
-    def vector_constants():
-        cp(T.WTF[:], T.WTI[:], ["WTI"], ["WTF"])
-        ts(T.G15[:], T.G16[:], 15.0, None, A.add, None, ["G16"], ["G15"])
-        ts(T.BT4[:], T.IO16[:, 0:128], T.KF[:, 0:1], 16384.0, A.is_gt, A.mult, ["IO16", "KF"], ["BT4"])
-        ts(T.W16[:], T.IOT[:, 0:144], T.G15[:, 0:1], T.WTF[:, 0:1], A.is_equal, A.mult, ["IOT", "G15", "WTF"], ["W16"])
-        ts(T.MULP[:], T.KF[:], 0.0, -15.0, A.is_equal, A.mult, ["KF"], ["MULP"])
-        ts(T.ADDP[:], T.KF[:], 0.0, float(P0), A.is_equal, A.mult, ["KF"], ["ADDP"])
-        ts(T.MULP[:], T.MULP[:], 16.0, None, A.add, None, ["MULP"], ["MULP"])
-        tt(T.ADDP[:], T.ADDP[:], T.KF[:], A.add, ["ADDP", "KF"], ["ADDP"])
-        tt(T.BT4[:], T.BT4[:], T.BO[:], A.mult, ["BT4", "BO"], ["BT4"])
-        cp(T.BOH[:], T.BO[:, 0:128:16], ["BO"], ["BOH"])
-        ts(T.LXT[:, 8:2056:8], T.IOT[:], T.MULP[:, 0:1], T.ADDP[:, 0:1], A.mult, A.add, ["IOT", "MULP", "ADDP"], ["LXT"])
-
-    def late_constants():
-        for name, c in (("N12M", -4096.0), ("N16M", -16.0), ("IDF", 1.0)):
-            act(T[name][:], T.ID[:], ["ID"], [name], scale=c)
-        act(T.KR[0:1, :], T.IO16[0:1, 0:128], ["IO16"], ["KR"])
-        act(T.I16B[0:1, :], T.IOT[0:1, 0:16], ["IOT"], ["I16B"], scale=16.0)
-        act(T.KC2[0:1, :], T.IO16[0:1, :], ["IO16"], ["KC2"], bias=30720.0, scale=-2048.0)
-        act(T.B32K[:], T.BO[:, 0:128:16], ["BO"], ["B32K"], scale=32768.0)
-
-    def last_constants():
-        for name, c in (("P16M", 65536.0), ("P20M", 1048576.0), ("N19M", -524288.0)):
-            act(T[name][:], T.ID[:], ["ID"], [name], scale=c)
-        act(T.BO4[:], T.BO[:], ["BO"], ["BO4"], scale=16384.0)
-        act(T.NDEL[:], T.DELB[:], ["DELB"], ["NDEL"], bias=1.0, scale=-1.0)
-        act(T.OFFD[:], T.DELB[:], ["DELB"], ["OFFD"], bias=-8388608.0, scale=8388608.0)
-        op("a", lambda: AC.activation(T.LB[:], T.IOT[:, 0:16], F.Identity, bias=T.KF[:, 0:1], scale=16.0), ["IOT", "KF"], ["LB"])
-        act(T.TP[:], T.LB[:], ["LB"], ["TP"], bias=float(TR))
-        act(T.TW[:], T.LB[:], ["LB"], ["TW"], bias=2048.0 + UP)
-
-    def one_hot_table():
-        dma("s", T.TOH[:, 0:256], T.DELB[:], "dt0", ["DELB", "CAP"], ["TOH"])
-        for j, s in enumerate((256, 512, 1024, 2048)):
-            dma("s", T.TOH[:, s:2 * s], T.TOH[:, 0:s], "dt%d" % (j + 1), ["TOH"], ["TOH"])
+    def table(j, b):
+        o, k, ft = T["B%d" % b][:], whole_bank[b], T.FT[:, half(j & 1, 512)]
+        mm(o, T.KR4[0:4, :], T.ROWS[0:4, half(j, 512)], True, True, ["KR4", "ROW0", "ROW1", "ROW2", "ROW3"], k)
+        act(ft, o, k, ["FT%d" % (j & 1)], bias=-0.499755859375, scale=1.0 / 2048)
+        mm(o, T.KR4[0:4, :], T.ROWS[0:4, half(j, 512)], True, False, ["KR4", "ROW0", "ROW1", "ROW2", "ROW3"], k)
+        mm(o, T.N11M[:], ft, False, True, ["N11M", "FT%d" % (j & 1)], k)
+        act(T.TAB[:, half(j, 512)], o, k, [tab[j]])
 
     def first_offsets():
         src = T.BRI[:, 0:2048:8]
@@ -283,294 +340,366 @@ def rank_program(g, core, T, topo):
         ts(T.B3[:, 0:256], src, 0.0, 4096.0, A.is_lt, A.mult, ["BRI"], ["B3.g"])
         ts(T.UI[:], src, 4095, None, A.bitwise_and, None, ["BRI"], ["UI"])
         ts(T.B4[:, 0:256], T.UU[:], 4096.0, 4096.0, A.is_lt, A.mult, ["UU"], ["B4.g"])
-        tt(T.KS[:], T.UI[:], T.B3[:, 0:256], A.max, ["B3.g", "UI"], ["KS"])
-        tt(T.CNS[:], T.KS[:], T.B4[:, 0:256], A.max, ["B4.g", "KS"], ["CNS"])
+        tt(T.KS[:], T.UI[:], T.B3[:, 0:256], A.max, ["B3.g", "UI"], ["KS0", "KS1"])
+        tt(T.CNS[:], T.KS[:], T.B4[:, 0:256], A.max, ["B4.g", "KS0", "KS1"], ["CNS"])
         ts(T.EO[:], T.CNS[:], float(ZC), None, A.min, None, ["CNS"], ["EO"])
 
     def k_part(out, key, t):
         act(out, T.WD[:, t - 1:2048:8], ["WD"], [key], bias=199.50390625, scale=1.0 / 65536)
 
-    def offsets_a(t):
+    def offsets(t):
         act(T.N12[:], T.WD[:, t - 1:2048:8], ["WD"], ["N12"], bias=219.5625, scale=1.0 / 4096)
         k_part(T.KN[:], "KN", t)
-        mm(T.B7[:, 256:512], T.ID[:], T.N12[:], True, False, ["ID", "N12"], ["B7.hi"])
-        mm(T.B7[:, 256:512], T.N16M[:], T.KN[:], False, True, ["N16M", "KN"], ["B7.hi"])
-
-    def offsets_b(t):
+        mm(T.B7[:, 0:256], T.ID[:], T.N12[:], True, False, ["ID", "N12"], ["B7.x"])
+        mm(T.B7[:, 0:256], T.N16M[:], T.KN[:], False, True, ["N16M", "KN"], ["B7.x"])
         act(T.BD2[:], T.KN[:], ["KN"], ["BD2"], F.Relu, bias=4096.0 * (201 - t), scale=-4096.0)
-        act(T.BD1[:], T.B7[:, 256:512], ["B7.hi"], ["BD1"], F.Relu, bias=4096.0 * (t - 2980), scale=-4096.0)
-        o = T.B5[:, 256:512]
-        mm(o, T.IDF[:], T.WD[:, t - 1:2048:8], True, False, ["IDF", "WD"], ["B5.off"])
-        mm(o, T.N12M[:], T.N12[:], False, False, ["N12M", "N12"], ["B5.off"])
-        mm(o, T.ID[:], T.BD2[:], False, False, ["ID", "BD2"], ["B5.off"])
-        mm(o, T.ID[:], T.BD1[:], False, True, ["ID", "BD1"], ["B5.off"])
+        act(T.BD1[:], T.B7[:, 0:256], ["B7.x"], ["BD1"], F.Relu, bias=4096.0 * (t - 2980), scale=-4096.0)
+        o = T.B7[:, 256:512]
+        mm(o, T.IDF[:], T.WD[:, t - 1:2048:8], True, False, ["IDF", "WD"], ["B7.hi"])
+        mm(o, T.N12M[:], T.N12[:], False, False, ["N12M", "N12"], ["B7.hi"])
+        mm(o, T.ID[:], T.BD2[:], False, False, ["ID", "BD2"], ["B7.hi"])
+        mm(o, T.ID[:], T.BD1[:], False, True, ["ID", "BD1"], ["B7.hi"])
+        ts(T.EO[:], o, 901120.0, float(ZC), A.add, A.min, ["B7.hi"], ["EO"])
 
-    def offsets_c():
-        ts(T.EO[:], T.B5[:, 256:512], 901120.0, float(ZC), A.add, A.min, ["B5.off"], ["EO"])
+    def pk(h):
+        return ["PK%d" % j for j in range(4 * h, 4 * h + 4)]
 
-    def rows(lo, hi, eng, key):
-        out, src = T.PK[:, 16 * lo:16 * hi], T.RES[:, 0:3344].indirect(T.EO[:, lo:hi])
-        (act if eng == "a" else cp)(out, src, ["RES", "RESG", "RESZ", "EO"], key)
+    def rows(q, j, m):
+        lo, hi = 32 * j, 32 * (j + m)
+        gather(q, T.PK[:, 16 * lo:16 * hi], T.RES[:, 0:3344], T.EO[:, lo:hi], ["RES", "RESG", "RESZ", "EO"], ["PK%d" % i for i in range(j, j + m)])
 
-    row0, aside = T.PK[:, 0:4096:16], T.PK[:, P0:P0 + Q]
-    pk = ["PK0", "PK1"]
+    def row0(h):
+        return T.PK[:, 2048 * h:2048 * h + 2048:16]
+
+    def aside(h):
+        return T.PK[:, P0 + H * h:P0 + H * h + H]
 
     def row0_aside():
-        act(aside, row0, pk + ["PKx"], ["P0"])
-        act(row0, T.ONES[:], ["ONES"], pk, scale=255.0)
+        act(T.PK[:, P0:P0 + Q], T.PK[:, 0:4096:16], pk(0) + pk(1), ["P00", "P01"])
+        act(T.PK[:, 0:4096:16], T.ONES[:], ["ONES"], pk(0) + pk(1), scale=255.0)
 
     def cap_wide(t, ks):
         cx = "CX%d" % (t & 1)
         for k in ks:
-            gcopy(T[cx][:, k:4096:16], T.CAP[:, t - 1:2048:8], Q, ["CAP"], [cx + "k%d" % k])
+            gcopy(T[cx][:, k:4096:16], T.CAP[:, t - 1:2048:8], ["CAP"], [cx + "k%d" % k])
 
-    def cap_room(t):
-        act(T.B0[:, 0:256], T.CAP[:, t - 1:2048:8], ["CAP"], ["B0.cap"])
-
-    def word_list():
-        return [
-            lambda: tt(T.LD[:], T.CNS[:, 15:256:16], T.TW[:], A.min, ["CNS", "TW"], ["LD"]),
-            lambda: tt(T.LC[:], T.LD[:], T.B0[:, 256:272], A.max, ["LD", "B0.lv"], ["LC"]),
-            lambda: ts(T.PW[:], T.LC[:], -float(UP), None, A.add, None, ["LC"], ["PW"]),
-        ]
-
-    def old_words():
-        tt(T.WOLD[:], T.WD[:, 0:2304].indirect(T.PW[:]), T.NDEL[:], A.mult, ["WD", "WDT", "PW", "NDEL"], ["WOLD"])
-
-    def set_words():
-        tt(T.WD[:, 0:2304].indirect(T.PW[:]), T.WOLD[:], T.NEW[:], A.add, ["WOLD", "NEW", "PW"], ["WD", "WDT"])
-
-    def marks():
-        act(T.OH[:], T.TOH[:].indirect(T.KL[:]), ["TOH", "KL"], ["OH"])
-        op("a", lambda: AC.activation(T.SGN[:], T.B3[:, 0:256], F.Sign, accum_out=T.SACC[:]), ["B3.g"], ["SGN", "SACC"])
-
-    def suspended_a(t):
-        z = T.B5[:, 256:512]
-        k_part(T.KP[:], "KP", t)
-        mm(z, T.P20M[:], T.OH[:], True, False, ["P20M", "OH"], ["B5.off"])
-        mm(z, T.N19M[:], T.SGN[:], False, False, ["N19M", "SGN"], ["B5.off"])
-        mm(z, T.P16M[:], T.KP[:], False, True, ["P16M", "KP"], ["B5.off"])
-        act(z, z, ["B5.off"], ["B5.off"], F.Relu, bias=65536.0 * (t + 8 - 200) - 1572864.0)
-
-    def suspended_b(t):
-        tt(T.WD[:, t - 1:2048:8], T.WD[:, t - 1:2048:8], T.B5[:, 256:512], A.subtract, ["WD", "B5.off"], ["WD"])
-
-    def new_words(t):
+    def words(t):
+        tt(T.LD[:], T.CNS[:, 15:256:16], T.TW[:], A.min, ["CNS", "TW"], ["LD"])
+        tt(T.LC[:], T.LD[:], T.B0[:, 288:304], A.max, ["LD", "B0.far0", "B0.far1"], ["LC"])
+        ts(T.PW[:], T.LC[:], -float(FAR), None, A.add, None, ["LC"], ["PW"])
         act(T.NEW[:], T.IOTM[:], ["IOTM"], ["NEW"], F.Relu, bias=2048.0 + 256.0 * (t - 1) + 4096.0 * (t + 2))
+        win = T.WD[:, 0:2304]
+        tt(T.WOLD[:], win.indirect(T.PW[:]), T.NDEL[:], A.mult, ["WD", "WDT", "PW", "NDEL"], ["WOLD"], GATHER)
+        tt(win.indirect(T.PW[:]), T.WOLD[:], T.NEW[:], A.add, ["WOLD", "NEW", "PW"], ["WD", "WDT"], SCATTER)
+
+    def suspended(t):
+        gather("a", T.OH[:], T.TOH[:], T.KL[:], ["TOH", "KL0", "KL1"], ["OH"])
+        z = T.B3[:, 256:512]
+        k_part(T.KP[:], "KP", t)
+        mm(z, T.P20M[:], T.OH[:], True, False, ["P20M", "OH"], ["B3.z"])
+        mm(z, T.N19M[:], T.SG[:], False, False, ["N19M", "SG0", "SG1"], ["B3.z"])
+        mm(z, T.P16M[:], T.KP[:], False, True, ["P16M", "KP"], ["B3.z"])
+        act(T.OH[:], z, ["B3.z"], ["OH"], F.Relu, bias=65536.0 * (t + 8 - 200) - 1572864.0)
+        mm(z, T.IDF[:], T.WD[:, t - 1:2048:8], True, False, ["IDF", "WD"], ["B3.z"])
+        mm(z, T.NID[:], T.OH[:], False, True, ["NID", "OH"], ["B3.z"])
+        act(T.WD[:, t - 1:2048:8], z, ["B3.z"], ["WD"])
 
     def parity():
-        o = T.B4[:, 256:257]
-        mm(o, T.PAR[:], T.SACC[:], True, True, ["PAR", "SACC"], ["B4.par"])
-        act(T.PB[:], o, ["B4.par"], ["PB"], bias=-0.25, scale=-0.015625)
-        act(T.PC[:], T.PB[:], ["PB"], ["PC"], bias=MAGIC)
-        act(T.PC[:], T.PC[:], ["PC"], ["PC"], bias=MAGIC, scale=-1.0)
-        op("a", lambda: AC.activation(T.ODD[:], T.PB[:], F.Identity, bias=T.PC[:, 0:1]), ["PB", "PC"], ["ODD"])
-        op("a", lambda: AC.activation(T.LIMT[:], T.EIGHT[:], F.Copy, bias=20.0, scale=T.ODD[:, 0:1]), ["EIGHT", "ODD"], ["LIMT"])
+        o = T.B0[:, 272:273]
+        for h in (0, 1):
+            mm(o, T.PAR[:], T.SACC[:, h:h + 1], h == 0, h == 1, ["PAR", "SACC%d" % h], ["B0.par"])
+        act(col("PB"), o, ["B0.par"], ["PB"], bias=-0.25, scale=-0.015625)
+        act(col("PC"), col("PB"), ["PB"], ["PC"], bias=MAGIC)
+        act(col("PC"), col("PC"), ["PC"], ["PC"], bias=MAGIC, scale=-1.0)
+        act(col("ODD"), col("PB"), ["PB", "PC"], ["ODD"], F.Identity, bias=col("PC"))
+        act(T.LIMT[:], T.EIGHT[:], ["EIGHT", "ODD"], ["LIMT"], bias=20.0, scale=col("ODD"))
 
-    more_constants()
-    late_constants()
-    last_constants()
-    cp(T.OFFC[:], T.IOT[:], ["IOT"], ["OFFC"])
-    first_offsets()
-    rows(0, GS, "a", pk)
-    rows(GS, Q, "v", ["PKx"])
-    cap_wide(1, (0, 1, 2))
-    left = [(T.B2, ["B2.k"]), (T.B3, ["B3.g"]), (T.B4, ["B4.g", "B4.par"]), (T.B7, ["B7.x", "B7.hi"])]
-    for j, (b, k) in enumerate(left):
-        mm(b[:], T.ID[:], T.CAP[:, half(j, 512)], True, False, ["ID", "CAP"], k)
-        mm(b[:], T.NID[:], T.RES[:, half(j, 512)], False, True, ["NID", "RES"], k)
-    for k in range(3, 16):
-        cp(T.CX1[:, k:4096:16], T.CAP[:, 0:2048:8], ["CAP"], ["CX1k%d" % k])
-    cap_wide(2, range(8))
-    iota(T.LXT[:], [[0, 2064]], 8192, 0, "LXT")
-    one_hot_table()
-    row0_aside()
+    BA, BG, BU = [T.B1, T.B2], [T.B3, T.B4], [T.B5, T.B6]
 
-    for t in range(1, NT + 1):
+    def one_round(t):
         c = t - 1
         cx = "CX%d" % (t & 1)
-        cxk = [cx + "k%d" % k for k in range(16)]
         L0 = c * Q
         dst = cores[(rank + 1 + c % (n - 1)) % n]
-        rid, pid, _s = topo.addr(dst)
-        land, lk = T.LAND[:, L0:L0 + Q], "LAND%d" % t
-        snd, sk = T.SND[:, L0:L0 + Q], "SND%d" % t
-        cap = T.CAP[:, c:2048:8]
-        ka, d = T.B1, T.B6[:, 256:512]
-        mm(ka[:, 0:256], T.ONES[0:1, 0:H], T.KC[0:1, :], True, False, ["KC", "ONES"], ["B1.k"])
-        for h in (0, 1):
-            mm(ka[:, H * h:H * h + H:16], T.CAP[:, c + 1024 * h:1024 * h + 1024:8], T.B16[:], False, False, ["B16", "CAP"], ["B1.k"])
-        mm(d, T.NID[:], cap, True, False, ["NID", "CAP"], ["B6.d"])
-        mm(d, T.ID[:], aside, False, True, ["ID", "P0"], ["B6.d"])
-        act(T.R0[:], d, ["B6.d"], ["R0"], F.Relu)
-        for h in (0, 1):
-            s = half(h, 2048)
-            scan(T.CM[:, s], T[cx][:, s], T.PK[:, s], A.min, A.max, cxk + ["PK%d" % h], ["CM%d" % h])
+        last = t == NT
+        land = [T.LAND[:, L0 + H * h:L0 + H * h + H] for h in (0, 1)]
+        snd = [T.SND[:, L0 + H * h:L0 + H * h + H] for h in (0, 1)]
+        cap = [T.CAP[:, c + 1024 * h:1024 * h + 1024:8] for h in (0, 1)]
+        lk = ["LAND%d%d" % (t, h) for h in (0, 1)]
+        sk = ["SND%d%d" % (t, h) for h in (0, 1)]
+
+        def low_bits(h, src, key, mask):
+            cp(T.XI[:, half(h, 8)], src, [key], ["XI%d" % h])
+            ts(T.XI2[:, half(h, 8)], T.XI[:, half(h, 8)], mask, None, A.bitwise_and, None, ["XI%d" % h], ["XJ%d" % h])
+
+        def largest_key(h, lo, mask, out, key):
+            scan(T.KS[:, half(h)], T.MB[:, 0:H], BA[h][:, lo:lo + H], A.min, A.max, ["MB", "B%d.k" % (1 + h)], ["KS%d" % h])
+            low_bits(h, T.KS[:, H * h + 15:H * h + H:16], "KS%d" % h, mask)
+            tt(out[:, half(h)], T.XI2[:, half(h, 8)].indirect(T.OFFC[:, 0:8]), T.DELB[:, 0:H], A.mult, ["XJ%d" % h, "OFFC", "DELB"], [key], GATHER)
+
+        def sums(h):
+            b, key = BA[h], "B%d.k" % (1 + h)
+            clip = [j for j in CLIP if j // 4 == h and t > 1]
+            cut = H - 32 * len(clip)
+            mm(b[:, 0:H], T.ONES[0:1, 0:H], T.KC[0:1, :], True, False, ["KC", "ONES"], [key])
+            mm(b[0:cut, 0:H:16], T.CAP[:, c + 1024 * h:1024 * h + 8 * cut:8], T.B16[:], False, False, ["B16", "CAP"], [key])
+            d, dk = BU[h][:, 384:512], "B%d.d" % (5 + h)
+            mm(d, T.NID[:], cap[h], True, False, ["NID", "CAP"], [dk])
+            mm(d, T.ID[:], aside(h), False, True, ["ID", "P0%d" % h], [dk])
+            act(T.R0[:, half(h)], d, [dk], ["R0%d" % h], F.Relu)
+            cxk, cmk = [cx + "k%d" % k for k in range(16)], ["CM%d" % j for j in range(4 * h, 4 * h + 4)]
+            s = slice(2048 * h, 2048 * h + 16 * cut)
+            scan(T.CM[:, s], T[cx][:, s], T.PK[:, s], A.min, A.max, cxk + pk(h)[:cut // 32], cmk[:cut // 32])
+            for j in clip:
+                bn = (3, 4)[7 - j]
+                o, ok = T["B%d" % bn][:], whole_bank[bn]
+                mm(o, T.NID[:], T[cx][:, half(j, 512)], True, False, ["NID"] + cxk, ok)
+                mm(o, T.ID[:], T.PK[:, half(j, 512)], False, True, ["ID", "PK%d" % j], ok)
+                act(T.CM[:, half(j, 512)], o, ok, ["CM%d" % j], F.Relu)
             for k in range(1, 16):
-                mm(ka[:, H * h + k:H * h + H:16], T.CM[:, 2048 * h + k:2048 * h + 2048:16], T.B16[:], False, False, ["B16", "CM%d" % h], ["B1.k"])
-        for h in (0, 1):
-            mm(ka[:, H * h:H * h + H:16], T.R0[:, half(h)], T.B16[:], False, h == 1, ["B16", "R0"], ["B1.k"])
-        cap_room(t)
-        if t > 1:
-            act(row0, aside, ["P0"], pk)
-            parity()
-            new_words(t - 1)
-            wl = word_list()
-            wl[0]()
-            wl[1]()
-        else:
-            for j, (b, k) in enumerate(left):
-                if j == 2:
-                    act(row0, aside, ["P0"], pk)
-                act(T.SL[:, half(j, 512)], b[:], k, ["SL"], F.Relu)
-            tt(T.IOTM[:], T.IOT[:], T.OFFD[:], A.add, ["IOT", "OFFD"], ["IOTM"])
-        scan(T.KS[:], T.MB[:], ka[:, 0:256], A.min, A.max, ["MB", "B1.k"], ["KS"])
-        if t > 1:
-            wl[2]()
-        cp(T.XI[:], T.KS[:, 15:256:16], ["KS"], ["XI"])
-        ts(T.XI2[:], T.XI[:], 15, None, A.bitwise_and, None, ["XI"], ["XJ"])
-        tt(T.XA[:], T.XI2[:].indirect(T.OFFC[:, 0:16]), T.DELB[:], A.mult, ["XJ", "OFFC", "DELB"], ["XA"])
-        o = ka[:, 256:272]
-        mm(o, T.KR16[0:1, :], T.ONES[0:1, 0:16], True, False, ["KR16", "ONES"], ["B1.kl"])
-        mm(o, T.ONES[0:1, 0:H], T.IO256[0:1, :], False, False, ["IO256", "ONES"], ["B1.kl"])
-        for h in (0, 1):
-            mm(ka[:, 256 + 8 * h:264 + 8 * h], T.XA[:, half(h)], T.NB8[:], False, h == 1, ["XA", "NB8"], ["B1.kl"])
-        if t == 1:
-            for j in range(0, 3):
-                table(j)
-        cp(T.KL[:], o, ["B1.kl"], ["KL"])
-        win = T.PK[:, 0:4096].indirect(T.KL[:])
-        cp(T.XS[:], win, pk + ["KL"], ["XS"])
-        cp(win, aside, ["P0", "KL"], pk)
-        cp(row0, T.XS[:], ["XS"], pk)
-        verdict = [(T.B3[:, 0:256], "B3.g"), (T.B4[:, 0:256], "B4.g")]
-        for o, key in verdict:
-            mm(o, T.LIMT[:], T.ONES[:], True, False, ["LIMT", "ONES"], [key])
-        for h in (0, 1):
+                mm(b[:, k:H:16], T.CM[:, 2048 * h + k:2048 * h + 2048:16], T.B16[:], False, False, ["B16"] + cmk, [key])
+            mm(b[:, 0:H:16], T.R0[:, half(h)], T.B16[:], False, True, ["B16", "R0%d" % h], [key])
+            act(row0(h), aside(h), ["P0%d" % h], pk(h))
+
+        def messages(h):
+            b, s = BA[h], half(h, 2048)
+            o, ok = b[:, 384:392], "B%d.kl" % (1 + h)
+            mm(o, T.KR16[0:1, :], T.ONES[0:1, 0:8], True, False, ["KR16", "ONES"], [ok])
+            mm(o, T.ONES[0:1, 0:H], T.IO256[0:1, 0:8], False, False, ["IO256", "ONES"], [ok])
+            largest_key(h, 0, 15, T.XA, "XA%d" % h)
+            mm(o, T.XA[:, half(h)], T.NB8[:], False, True, ["XA%d" % h, "NB8"], [ok])
+            kl = T.KL[:, half(h, 8)]
+            cp(kl, o, [ok], ["KL%d" % h])
+            gather("a", T.XS[:, half(h)], T.PK[:, s], kl, pk(h) + ["KL%d" % h], ["XS%d" % h])
+            scatter(T.PK[:, s], kl, aside(h), ["P0%d" % h, "KL%d" % h], pk(h))
+            act(row0(h), T.XS[:, half(h)], ["XS%d" % h], pk(h))
             lo = 2048 * h
             s = slice(lo + 2047, lo - 1 if lo else None, -1)
-            scan(T.FB[:, s], T.SEG[:], T.PK[:, s], A.mult, A.max, ["SEG", "PK%d" % h], ["FB%d" % h])
-        fb = ["FB0", "FB1"]
-        for j, cm in enumerate((T.CMP1, T.CMP2)):
-            tt(cm[:], T.FB[:, j:4096:16], T.B0[:, 0:256], A.is_gt, fb + ["B0.cap"], ["CMP%d" % j])
-            mm(verdict[j][0], T.NBO[:], cm[:], False, True, ["NBO", "CMP%d" % j], [verdict[j][1]])
-        mb = T.B5[:, 0:256]
-        act(mb, T.B3[:, 0:256], ["B3.g"], ["B5.m"], F.Relu)
-        tt(T.XS[:], T.FB[:, 1:4096:16], T.B4[:, 0:256], A.min, fb + ["B4.g"], ["XS"])
-        tt(mb, T.FB[:, 0:4096:16], mb, A.min, fb + ["B5.m"], ["B5.m"])
-        tt(snd, T.XS[:], mb, A.max, ["XS", "B5.m"], [sk])
-        wait_for("p", deps("p", [sk], []))
-        g.remote_dma(land, snd, T.sem["arr%d" % t], T.sem.loc, pid, rid, topo.mask(core, dst))
-        lastw[lk] = ("arr%d" % t, len(topo.engines(core, dst)), {})
-        if t == 1:
-            for j in range(3, 8):
-                table(j)
-        mm(d, T.ID[:], cap, True, False, ["ID", "CAP"], ["B6.d"])
-        mm(d, T.NID[:], snd, False, True, ["NID", sk], ["B6.d"])
-        act(T.SL[:, c:2048:8], d, ["B6.d"], ["SL"], F.Relu)
-        gcopy(T.RES[:, c:2048:8], snd, Q, [sk], ["RES"])
-        if t == NT:
-            dma("s", T.yr[:], T.RES[:, 0:2048], "dyr", ["RES"], ["yr"])
-        if t > 1:
-            suspended_b(t - 1)
-            old_words()
-            set_words()
-        else:
-            vector_constants()
-            cp(T.WD[:, 0:2048], T.BRI[:], ["BRI"], ["WD"])
-        ul = T.B2[:, 256:272]
-        mm(ul, T.KR[0:1, :], T.C37[0:1, 0:16], True, False, ["KR", "C37"], ["B2.u"])
-        mm(ul, T.C37[0:1, :], T.I16B[0:1, :], False, False, ["I16B", "C37"], ["B2.u"])
-        for r in range(16):
-            mm(ul, T.W16[:, 15 - r:143 - r], T.LAND[:, L0 + r:L0 + Q:16], False, r == 15, ["W16", lk], ["B2.u"])
-        if t < NT:
-            gcopy(T.RES[:, 2048 + L0:2048 + L0 + Q], land, Q, [lk], ["RESG"])
-        lo, hi = CH[-1]
-        for k in range(16):
-            gcopy(T.MX[:, 16 * lo + k:16 * hi:16], T.LAND[:, L0 + lo:L0 + hi], hi - lo, [lk], ["MXk%d" % k])
-        if t == 1:
-            cap_wide(2, range(8, 16))
-        if t + 2 <= NT:
-            cap_wide(t + 2, range(1, 16))
+            scan(T.FB[:, s], T.SEG[:], T.PK[:, s], A.mult, A.max, ["SEG"] + pk(h), ["FB%d" % h])
+            m = [T.FB[:, lo + j:lo + 2048:16] for j in (0, 1)]
+            cm, fb = T["CMP%d" % h], "FB%d" % h
+            if h == 0:
+                act(T.B0[:, 0:256], T.CAP[:, c:2048:8], ["CAP"], ["B0.cap"])
+            for j in (0, 1):
+                tt(cm[:, half(j)], m[j], T.B0[:, half(h)], A.is_gt, [fb, "B0.cap"], ["CMP%d%d" % (h, j)])
+            bu, mk, dk, gk, vk = BU[h], "B%d.m" % (5 + h), "B%d.d" % (5 + h), "B%d.g" % (3 + h), "B%d.v" % (1 + h)
+            v0, v1, d = BG[h][:, 0:H], b[:, 256:384], bu[:, 384:512]
+            for j, (o, ok) in enumerate(((v0, gk), (v1, vk))):
+                mm(o, T.LIMT[:], T.ONES[:, 0:H], True, False, ["LIMT", "ONES"], [ok])
+                mm(o, T.NBO[:], cm[:, half(j)], False, True, ["NBO", "CMP%d%d" % (h, j)], [ok])
+            act(bu[:, 0:H], v0, [gk], [mk], F.Relu)
+            tt(T.XS[:, half(h)], m[1], v1, A.min, [fb, vk], ["XS%d" % h])
+            tt(bu[:, 0:H], m[0], bu[:, 0:H], A.min, [fb, mk], [mk])
+            tt(snd[h], T.XS[:, half(h)], bu[:, 0:H], A.max, ["XS%d" % h, mk], [sk[h]])
+            act(T.SG[:, half(h)], v0, [gk], ["SG%d" % h, "SACC%d" % h], F.Sign, accum=T.SACC[:, h:h + 1])
+            mm(d, T.ID[:], cap[h], True, False, ["ID", "CAP"], [dk])
+            mm(d, T.NID[:], snd[h], False, True, ["NID", sk[h]], [dk])
+            calls.append(("p", (land[h], snd[h], "arr%d%d" % (t, h), dst), [sk[h]], [lk[h]], 300.0, FIRST if t == 1 and h == 0 else LAT))
+            act(T.SL[:, c + 1024 * h:1024 * h + 1024:8], d, [dk], ["SL%d" % h], F.Relu)
+
+        def candidates(h):
+            ul, key = BA[h][:, 392:400], "B%d.u" % (1 + h)
+            mm(ul, T.KR[0:1, :], T.C37[0:1, 0:8], True, False, ["KR", "C37"], [key])
+            mm(ul, T.C37[0:1, :], T.I16B[0:1, half(h, 8)], False, False, ["I16B", "C37"], [key])
+            for r in range(16):
+                mm(ul, T.W16[:, 15 - r:143 - r], T.LAND[:, L0 + H * h + r:L0 + H * h + H:16], False, r == 15, ["W16", lk[h]], [key])
+            low_bits(h, ul, key, 4095)
+            cp(T.UL[:, half(h, 8)], T.XI2[:, half(h, 8)], ["XJ%d" % h], ["UL%d" % h])
+            gather("v", T.P16[:, half(h)], T.TAB[:], T.UL[:, half(h, 8)], tab + ["UL%d" % h], ["P16%d" % h])
+            gather("a", T.PF[:, half(h)], T.TAB[:], T.UL[:, half(h, 8)], tab + ["UL%d" % h], ["PF%d" % h])
 
         def wide(j):
-            lo, hi = CH[j]
-            act(T.MX[:, 16 * lo:16 * hi], land.indirect(T.OFFC[:, lo:hi]), [lk, "OFFC"], ["MX%d" % j])
-        wide(0)
-        if t < NT:
-            offsets_a(t + 1)
-        wide(1)
-        cp(T.XI[:], ul, ["B2.u"], ["XI"])
-        ts(T.XI2[:], T.XI[:], 4095, None, A.bitwise_and, None, ["XI"], ["XJ"])
-        cp(T.UL[:], T.XI2[:], ["XJ"], ["UL"])
-        cp(T.P16[:], T.TAB[:].indirect(T.UL[:]), ["TAB", "UL"], ["P16"])
-        wide(2)
-        if t < NT:
-            offsets_b(t + 1)
-        wide(3)
-        kb = T.B2
-        for j in (0, 1, 2, 4, 3):
-            lo, hi = CH[j]
-            s = slice(16 * lo, 16 * hi)
-            mx = ["MX%d" % j] if j < len(CH) - 1 else ["MXk%d" % k for k in range(16)]
-            tt(T.SC[:, s], T.SL[:, 0:2048].indirect(T.P16[:, lo:hi]), T.MX[:, s], A.min, ["SL", "P16"] + mx, ["SC%d" % j])
-            if j == 0:
-                cp(T.PF[:], T.P16[:], ["P16"], ["PF"])
-                mm(kb[:, 0:256], T.ONES[:, 0:H], T.NEG[:], True, False, ["NEG", "ONES"], ["B2.k"])
-                mm(kb[:, 0:256], T.ONES[0:1, 0:H], T.KC2[0:1, :], False, False, ["KC2", "ONES"], ["B2.k"])
-                for h in (0, 1):
-                    mm(kb[:, half(h)], T.PF[:, half(h)], T.IDH[:], False, False, ["PF", "IDH"], ["B2.k"])
-            if j == 2 and t < NT:
-                offsets_c()
-            if j in (2, 3):
-                h = lo // H
+            m = min(x for x in list(WIDE) + list(SHARE) + [8] if x > j) - j
+            h, src, mx = j // 4, T.LAND[:, L0 + 32 * j:L0 + 32 * (j + m)], ["MX%d" % x for x in range(j, j + m)]
+            if WIDE[j] == "v":
+                cp(T.SP[:, 1024 * h:1024 * h + 512 * m:16], src, [lk[h]], ["SP%d" % h])
+                scan(T.MX[:, 512 * j:512 * (j + m)], T.SEG[:, 0:512 * m], T.SP[:, 1024 * h:1024 * h + 512 * m], A.mult, A.max, ["SEG", "SP%d" % h], mx)
+            elif WIDE[j] == "a":
+                gather("a", T.MX[:, 512 * j:512 * (j + m)], src, T.OFFC[:, 0:32 * m], [lk[h], "OFFC"], mx)
+            else:
+                for k in range(16):
+                    gcopy(T.MX[:, 512 * j + k:512 * (j + m):16], src, [lk[h]], ["MXk%d" % k])
+
+        def scores(j):
+            h, s = j // 4, half(j, 512)
+            sl, off, r = T.SL[:, 0:2048], T.P16[:, half(j, 32)], ["SL0", "SL1", "P16%d" % h]
+            if j in SHARE:
+                b = 3 + SHARE.index(j) % 2
+                o, k = T["B%d" % b], whole_bank[b]
                 for m in range(16):
-                    mm(kb[:, H * h + m:H * h + H:16], T.SC[:, 2048 * h + m:2048 * h + 2048:16], T.B32K[:], False, h == 1 and m == 15,
-                       ["B32K"] + ["SC%d" % i for i in ((0, 1, 2), (3, 4))[h]], ["B2.k"])
-        if t < NT:
-            rows(0, Q, "a", pk)
-            row0_aside()
-        marks()
-        if t == NT:
-            new_words(t)
-        lv = T.B0[:, 256:272]
-        mm(lv, T.CUP[0:1, :], T.ONES[0:1, 0:16], True, False, ["CUP", "ONES"], ["B0.lv"])
-        scan(T.KS[:], T.MB[:], kb[:, 0:256], A.min, A.max, ["MB", "B2.k"], ["KS"])
-        cp(T.XI[:], T.KS[:, 15:256:16], ["KS"], ["XI"])
-        ts(T.XI2[:], T.XI[:], 2047, None, A.bitwise_and, None, ["XI"], ["XJ"])
-        tt(T.XW[:], T.XI2[:].indirect(T.OFFC[:, 0:16]), T.DELB[:], A.mult, ["XJ", "OFFC", "DELB"], ["XW"])
+                    mm(o[:, m:512:16], T.ID[:], T.LAND[:, L0 + 32 * j:L0 + 32 * j + 32], m == 0, False, ["ID", lk[h]], k)
+                gather("a", T.MX[:, s], sl, off, r, ["MX%d" % j])
+                mm(o[:], T.NID[:], T.MX[:, s], False, True, ["NID", "MX%d" % j], k)
+                act(T.SC[:, s], o[:], k, ["SC%d" % j], F.Relu)
+                return
+            if WIDE.get(j, "p") != "p":
+                wide(j)
+            mx = ["MXk%d" % k for k in range(16)] if WIDE[max(x for x in WIDE if x <= j)] == "p" else ["MX%d" % j]
+            tt(T.SC[:, s], sl.indirect(off), T.MX[:, s], A.min, r + mx, ["SC%d" % j], GATHER)
+
+        def parents(h):
+            b, key = BA[h], "B%d.k" % (1 + h)
+            o = b[:, H:2 * H]
+            shared = [j for j in SHARE if j // 4 == h]
+
+            def nodes():
+                mm(o, T.PF[:, half(h)], T.IDF[:], False, bool(shared), ["PF%d" % h, "IDF"], [key])
+            mm(o, T.ONES[:, 0:H], T.NEG[:], True, False, ["NEG", "ONES"], [key])
+            mm(o, T.ONES[0:1, 0:H], T.KC2[0:1, :], False, False, ["KC2", "ONES"], [key])
+            if not shared:
+                nodes()
+                parts = [(0, H, T.B32K, "B32K")]
+            else:
+                lo = 32 * (shared[0] % 4)
+                hi = lo + 32 * len(shared)
+                mm(b[lo:hi, H:2 * H], T.LAND[:, L0 + H * h + lo:L0 + H * h + hi], T.BW32K[:], False, False, ["BW32K", lk[h]], [key])
+                parts = [x for x in ((0, lo, T.B32K, "B32K"), (hi, H, T.B32K, "B32K"), (lo, hi, T.NB32K, "NB32K")) if x[0] < x[1]]
+            for lo, hi, w, wk in parts:
+                for m in range(16):
+                    mm(b[lo:hi, H + m:2 * H:16], T.SC[:, 2048 * h + 16 * lo + m:2048 * h + 16 * hi:16], w[:], False, m == 15 and not shared,
+                       [wk] + ["SC%d" % j for j in range(4 * h + lo // 32, 4 * h + hi // 32)], [key])
+            if shared:
+                nodes()
+            largest_key(h, H, 2047, T.XW, "XW%d" % h)
+            lv, lvk, far, fk = T.B0[:, 256 + 8 * h:264 + 8 * h], "B0.lv%d" % h, T.B0[:, 288 + 8 * h:296 + 8 * h], "B0.far%d" % h
+            mm(lv, T.XW[:, half(h)], T.BOH[:], True, True, ["XW%d" % h, "BOH"], [lvk])
+            cp(T.LV[:, half(h, 8)], lv, [lvk], ["LV%d" % h])
+            gather("v", T.VB[:, half(h)], T.IO2K[:], T.LV[:, half(h, 8)], ["IO2K", "LV%d" % h], ["VB%d" % h])
+            mm(far, T.CFAR[0:1, :], T.ONES[0:1, 0:8], True, False, ["CFAR", "ONES"], [fk])
+            mm(far, T.XW[:, half(h)], T.BOH[:], False, True, ["XW%d" % h, "BOH"], [fk])
+            if not last:
+                act(T.LXW[:, half(h)], T.LXT[:].indirect(T.LV[:, half(h, 8)]), ["LXT", "LV%d" % h], ["LXW%d" % h], F.Abs, bias=-768.0 * t, rate=GATHER)
+
+        if t > 1:
+            parity()
+        sums(0)
+        sums(1)
+        messages(0)
+        if t == 1:
+            table(6, 7)
+            table(7, 3)
+        else:
+            words(t - 1)
+            if not last:
+                offsets(t + 1)
+        messages(1)
+        if t == 1:
+            cp(T.WD[:, 0:1024], T.BRI[:, 0:1024], ["BRI"], ["WD"])
+            cp(T.WD[:, 1024:2048], T.BRI[:, 1024:2048], ["BRI"], ["WD"])
         for h in (0, 1):
-            mm(T.B0[:, 256 + 8 * h:264 + 8 * h], T.XW[:, half(h)], T.BOH[:], False, h == 1, ["XW", "BOH"], ["B0.lv"])
-        mm(T.B7[:, 0:256], T.ID[:], T.OFFD[:], True, False, ["ID", "OFFD"], ["B7.x"])
-        ts(T.LV[:], lv, -float(UP), None, A.add, None, ["B0.lv"], ["LV"])
-        if t < NT:
-            ts(T.LV2[:], lv, 8.0 - t - UP, None, A.add, None, ["B0.lv"], ["LV2"])
-        cp(T.VB[:], T.IO2K[:].indirect(T.LV[:]), ["IO2K", "LV"], ["VB"])
-        if t < NT:
-            cp(T.LXW[:], T.LXT[:].indirect(T.LV2[:]), ["LXT", "LV2"], ["LXW"])
-            mm(T.B7[:, 0:256], T.IDF[:], T.LXW[:], False, False, ["IDF", "LXW"], ["B7.x"])
+            gcopy(T.RES[:, c + 1024 * h:1024 * h + 1024:8], snd[h], [sk[h]], ["RES"])
+        if last:
+            dma("s", T.yr[:], T.RES[:, 0:2048], "dyr", ["RES"], ["yr"], 512)
+        else:
+            if t == 1:
+                offsets(2)
+            for h in (0, 1):
+                act(T.RES[:, 2048 + L0 + H * h:2048 + L0 + H * h + H], land[h], [lk[h]], ["RESG"])
+        for j in WIDE:
+            if WIDE[j] == "p":
+                wide(j)
+        if t + 2 <= NT:
+            cap_wide(t + 2, range(1, 16))
+        mm(T.B7[:, 0:256], T.ID[:], T.OFFA[:], True, False, ["ID", "OFFA"], ["B7.x"])
+        for h in (0, 1):
+            candidates(h)
+            for j in range(4 * h, 4 * h + 4):
+                scores(j)
+        if not last:
+            for j in range(0, 8, 2):
+                rows("a", j, 2)
+            row0_aside()
+        suspended(t)
+        for h in (0, 1):
+            parents(h)
         for i in range(16):
-            ts(T.EQ[:, i, 0:256 - 16 * i], T.VB[:, 16 * i:256], T.B0[:, 256 + i:257 + i], None, A.is_equal, None, ["VB", "B0.lv"], ["EQ%d" % i])
+            ts(T.EQ[:, i, 0:256 - 16 * i], T.VB[:, 16 * i:256], T.B0[:, 256 + i:257 + i], None, A.is_equal, None,
+               ["VB0", "VB1", "B0.lv0", "B0.lv1"], ["EQ%d" % i])
             if i < 15:
                 mm(T.B7[:, 16 * i + 16:256], T.BO4[:], T.EQ[:, i, 16:256 - 16 * i], False, False, ["BO4", "EQ%d" % i], ["B7.x"])
+        if not last:
+            mm(T.B7[:, 0:256], T.MULD[:], T.LXW[:], False, False, ["MULD", "LXW0", "LXW1"], ["B7.x"])
         mm(T.B7[:, 0:256], T.BT4[:], T.EQ[:, :, 0:16], False, True, ["BT4"] + ["EQ%d" % i for i in range(16)], ["B7.x"])
-        suspended_a(t)
         scan(T.CNS[:], T.MB[:], T.B7[:, 0:256], A.min, A.max, ["MB", "B7.x"], ["CNS"])
-        if t < NT:
+        if not last:
             tt(T.LB[:], T.CNS[:, 15:256:16], T.TP[:], A.min, ["CNS", "TP"], ["LB"])
             cp(T.PL[:], T.LB[:], ["LB"], ["PL"])
-            cp(T.PK[:].indirect(T.PL[:]), land, ["PL", lk], pk + ["P0", "PKT"])
+            scatter(T.PK[:], T.PL[:], T.LAND[:, L0:L0 + Q], ["PL"] + lk, pk(0) + pk(1) + ["P00", "P01", "PKT"])
 
-    wl = word_list()
-    wl[0]()
-    suspended_b(NT)
-    wl[1]()
-    wl[2]()
-    old_words()
-    set_words()
-    dma("s", T.yb[:], T.WD[:, 0:2048], "dyb", ["WD"], ["yb"])
-    g.wait_ge(T.sem.loc, sum(len(topo.engines(core, cores[(rank + 1 + c % (n - 1)) % n])) for c in range(NT)))
-    for s, k in own.items():
-        g.wait_ge(T.sem[k], count[s])
+    table(0, 7)
+    table(1, 6)
+    first_offsets()
+    for j in range(8):
+        rows("a" if j < GS else "v", j, 1)
+    row0_aside()
+    cap_wide(1, range(GC))
+    for k in range(GC, 16):
+        cp(T.CX1[:, k:4096:16], T.CAP[:, 0:2048:8], ["CAP"], ["CX1k%d" % k])
+    cap_wide(2, range(16))
+    for j, b in enumerate((0, 3, 4, 7)):
+        o, k = T["B%d" % b][:], whole_bank[b]
+        mm(o, T.ID[:], T.CAP[:, half(j, 512)], True, False, ["ID", "CAP"], k)
+        mm(o, T.NID[:], T.RES[:, half(j, 512)], False, True, ["NID", "RES"], k)
+        act(T.SL[:, half(j, 512)], o, k, ["SL%d" % (j // 2)], F.Relu)
+    for j in range(2, 6):
+        table(j, (7, 4)[j & 1])
+    for t in range(1, NT + 1):
+        one_round(t)
+    words(NT)
+    dma("s", T.yb[:], T.WD[:, 0:2048], "dyb", ["WD"], ["yb"], 1024)
+
+    if len(calls) not in ORDERS:
+        ORDERS[len(calls)] = issue_order(calls)
+    queues = {"v": V, "t": PE, "a": AC, "p": g, "s": g.sync}
+    own = {"v": "cv", "t": "ct", "a": "ca", "p": "cp"}
+    count = {k: 0 for k in own}
+    known = {k: {} for k in queues}
+    lastw, readers, banks = {}, {}, {}
+    sent = 0
+    for i in ORDERS[len(calls)]:
+        q, f, r, w, _ns, lat = calls[i]
+        remote = q == "p" and lat > 0
+        if remote:
+            w, arrival = [], w[0]
+        toks = [lastw[k] for k in list(r) + list(w) if k in lastw]
+        for k in w:
+            toks += list(readers.get(k, {}).values())
+        for b in banks_of(list(r) + list(w)):
+            toks += [tok for e, tok in banks.get(b, {}).items() if e != q]
+        best = {}
+        for tok in toks:
+            if not (q == "t" and tok[0] == "ct") and (tok[0] not in best or best[tok[0]][1] < tok[1]):
+                best[tok[0]] = tok
+        kn = known[q]
+        for s, val, snap in sorted(best.values(), key=lambda x: -len(x[2])):
+            if kn.get(s, 0) < val:
+                queues[q].wait_ge(T.sem[s], val)
+                kn[s] = val
+                for s2, v2 in snap.items():
+                    kn[s2] = max(kn.get(s2, 0), v2)
+        if remote:
+            out, in_, sem, dst = f
+            rid, pid, _s = topo.addr(dst)
+            g.remote_dma(out, in_, T.sem[sem], T.sem.loc, pid, rid, topo.mask(core, dst))
+            lastw[arrival] = (sem, len(topo.engines(core, dst)), {})
+            sent += len(topo.engines(core, dst))
+            continue
+        if lat:
+            queues[q].dma_start(f[0], f[1]).then_inc(T.sem[f[2]], 16)
+            tok = (f[2], 16, dict(kn))
+        else:
+            count[q] += 1
+            tok = (own[q], count[q], dict(kn))
+            f().then_inc(T.sem[own[q]], 1)
+        for k in r:
+            readers.setdefault(k, {})[tok[0]] = tok
+        for k in w:
+            lastw[k] = tok
+            readers[k] = {}
+        for b in banks_of(list(r) + list(w)):
+            banks.setdefault(b, {})[q] = tok
+    g.wait_ge(T.sem.loc, sent)
+    for q, s in own.items():
+        g.wait_ge(T.sem[s], count[q])
     for s in DMAS:
         g.wait_ge(T.sem[s], 16)

@@ -6,15 +6,20 @@ H = 128
 ZC = 3328
 P0 = 4096
 TR = 4352
+WIN = 2080
 FAR = 131072
 MAGIC = 12582912.0
-GS = 4
-GC = 4
-CLIP = (6, 7)
-SHARE = (2, 3)
-WIDE = {0: "v", 4: "v", 6: "a", 7: "p"}
-CYCLE, GATHER, SCATTER = 0.83, 1.56, 4.0
-WAKE, DMA, LAT, FIRST = 75.0, 1700.0, 1500.0, 4200.0
+OPT = {
+    "gs": "v v a a a a a v", "as1": "vv",
+    "clip": [0, 2, 2, 2, 2, 2],
+    "score": ["ssvvvvvv"] * 5 + ["ssvvssvv"],
+    "vm": 2, "wm": 2, "rows": "aa aa aa aa", "pf": "a", "whole": True, "tail": 7, "clipw": "cx", "su": "a", "pm": 4,
+    "aside": "p", "restore": "vp", "pieces": 4, "xs": "a", "pack": "", "row0": "v", "ghost": "p", "kn": "a", "bd2": "a", "n12": "a", "bd1": "a", "kp": "a", "new": "v", "r0": "a",
+    "sl": "a", "ft": "aaaa", "const": "v", "tab0": 2, "cmp": "vv", "wold": "vvvvvv", "um": "vv", "sp": "v", "seg": "v", "own1": "", "own6": "",
+    "ona": "N11M NID N12M N16M IDF P12M P16M M16M NBO BO4",
+}
+CYCLE, PE_CYCLE, PE_CALL, GATHER, SCATTER, ACT = 0.83, 0.42, 8.0, 1.56, 4.0, 140.0
+WAKE, DMA, LAT, FIRST = 90.0, 1700.0, 2300.0, 5000.0
 PASSES, TOL, URG, RATIO = 6, 60, 100, 1.0
 SCRATCH = {
     "RES": ("sbuf", [128, 3344], "bfloat16"),
@@ -22,34 +27,49 @@ SCRATCH = {
     "BRI": ("sbuf", [128, 2048], "int32"),
     "PK": ("sbuf", [128, 4608], "bfloat16"),
     "EQ": ("sbuf", [128, 16, 256], "bfloat16"),
-    "SND": ("sbuf", [128, NT * Q], "bfloat16"),
-    "LAND": ("sbuf", [128, NT * Q], "bfloat16"),
+    "SND": ("sbuf", [128, NT * 2 * Q], "bfloat16"),
+    "LAND": ("sbuf", [128, NT * 2 * Q], "bfloat16"),
+    "NEW": ("sbuf", [128, NT * Q], "float32"),
     "IO2K": ("sbuf", [128, 2048], "float32"),
     "LXT": ("sbuf", [128, 2048], "float32"),
     "TAB": ("sbuf", [128, 4096], "float32"),
     "ROWS": ("sbuf", [128, 4096], "float16"),
-    "FT": ("sbuf", [128, 1024], "bfloat16"),
+    "OK0": ("sbuf", [128, 256], "bfloat16"),
+    "M0": ("sbuf", [128, 256], "bfloat16"),
+    "KC": ("sbuf", [128, 256], "bfloat16"),
+    "ALT": ("sbuf", [128, 256], "bfloat16"),
+    "FS": ("sbuf", [128, 2 * WIN], "bfloat16"),
+    "BS": ("sbuf", [128, 2 * WIN], "bfloat16"),
+    "SEG": ("sbuf", [128, 2064], "bfloat16"),
+    "KS": ("sbuf", [128, 512], "float32"),
+    "XF": ("sbuf", [128, 16], "float32"),
+    "B16": ("sbuf", [128, 16], "bfloat16"),
+    "TWO": ("sbuf", [128, 512], "bfloat16"),
+    "EQT": ("sbuf", [128, 512], "bfloat16"),
+    "MASK": ("sbuf", [128, 16], "bfloat16"),
+    "NSEL": ("sbuf", [128, 512], "float16"),
     "SACC": ("sbuf", [128, 2], "float32"),
     "K4": ("sbuf", [128, 4], "float16"),
     "XW": ("sbuf", [128, 256], "float16"),
+    "VB": ("sbuf", [128, 256], "float16"),
     "BOH": ("sbuf", [128, 8], "float16"),
     "W16": ("sbuf", [128, 144], "bfloat16"),
     "COL": ("sbuf", [128, 16], "float32"),
 }
-for _n in ("FB", "CM", "CX0", "CX1", "MX", "SC"):
+for _n in ("CM", "CX0", "CX1", "MX", "SC"):
     SCRATCH[_n] = ("sbuf", [128, 4096], "bfloat16")
-for _n in ("CAP", "SL", "SEG", "TOH", "SP"):
+for _n in ("CAP", "SL", "TOH", "SP", "FT"):
     SCRATCH[_n] = ("sbuf", [128, 2048], "bfloat16")
-for _n in ("ONES", "OFFD", "OFFA", "DELB", "N12", "KN", "KP", "BD1", "BD2", "R0", "XS", "XA", "OH", "SG", "LXW", "CMP0", "CMP1"):
+for _n in ("ONES", "OFFD", "OFFA", "DELB", "N12", "KN", "KP", "BD1", "BD2", "R0", "XS", "XA", "OH", "DW", "LXW", "CMP0", "CMP1"):
     SCRATCH[_n] = ("sbuf", [128, 256], "bfloat16")
-for _n in ("IOT", "IO16", "NDEL", "NEW", "MB", "KS", "CNS", "WOLD", "IOTM", "PF"):
+for _n in ("IOT", "IO16", "NDEL", "MB", "CNS", "WOLD", "IOTM", "PF"):
     SCRATCH[_n] = ("sbuf", [128, 256], "float32")
-for _n in ("BO", "NBO", "BO4", "BT4", "BW32K", "ID", "NID", "N11M", "N12M", "N16M", "P16M", "P20M", "N19M", "MULD", "C37", "CFAR", "NEG",
-           "KC", "KC2", "KR", "KR16", "EIGHT", "LIMT"):
+for _n in ("BO", "NBO", "BO4", "BT4", "BW32K", "ID", "NID", "N11M", "N12M", "P12M", "N16M", "P16M", "M16M", "MULD", "C37", "CFAR", "NEG",
+           "KC2", "KR", "KR16", "QRT", "LIM"):
     SCRATCH[_n] = ("sbuf", [128, 128], "bfloat16")
 for _n in ("IDH", "RH", "KR4"):
     SCRATCH[_n] = ("sbuf", [128, 128], "float16")
-for _n in ("B16", "B32K", "NB32K", "NB8"):
+for _n in ("B32K", "NB32K", "NB8"):
     SCRATCH[_n] = ("sbuf", [128, 8], "bfloat16")
 for _n in ("IO256", "I16B"):
     SCRATCH[_n] = ("sbuf", [128, 16], "bfloat16")
@@ -57,22 +77,69 @@ for _n in ("IOB", "PAR", "IDF"):
     SCRATCH[_n] = ("sbuf", [128, 128], "float32")
 for _n in ("UI", "UU"):
     SCRATCH[_n] = ("sbuf", [128, 256], "int32")
-for _n in ("EO", "P16", "VB", "OFFC"):
+for _n in ("EO", "P16", "OFFC"):
     SCRATCH[_n] = ("sbuf", [128, 256], "uint16")
 for _n in ("WTI", "KAI", "PI", "KI"):
     SCRATCH[_n] = ("sbuf", [128, 1], "int32")
 for _n in ("TP", "TW", "LB", "LC", "LD"):
     SCRATCH[_n] = ("sbuf", [128, 16], "float32")
 for _n in ("XI", "XI2"):
-    SCRATCH[_n] = ("sbuf", [128, 16], "int32")
+    SCRATCH[_n] = ("sbuf", [128, 48], "int32")
 for _n in ("KL", "PL", "PW", "LV", "UL"):
     SCRATCH[_n] = ("sbuf", [128, 16], "uint16")
-for _n in range(8):
-    SCRATCH["B%d" % _n] = ("psum", [128, 512], "float32")
+for _n, _c in (("B0", 512), ("B1", 512), ("B2", 512), ("B34", 1024), ("B56", 1024), ("B7", 512)):
+    SCRATCH[_n] = ("psum", [128, _c], "float32")
 DMAS = ["dbr", "dres", "dcap", "dwt", "dka", "dyr", "dyb"] + ["dr%d" % k for k in range(4)] + ["dt%d" % k for k in range(4)]
 SEMAPHORES = ["cv", "ct", "ca", "cp", "loc"] + DMAS + ["arr%d%d" % (t, h) for t in range(1, NT + 1) for h in (0, 1)]
-COLS = ("WTF", "PFL", "KF", "G16", "G15", "MULP", "ADDP", "PB", "PC", "ODD")
+COLS = ("WTF", "PFL", "KF", "G16", "G15", "MULP", "ADDP", "PC", "HALF")
 ORDERS = {}
+SEEN = {}
+TAG = [None]
+ROUND = """
+par1 r0a clipa kc0 kc1 cm0 r0b par2 clipb sli0 sli1 cm1 par3 sum0 klc0 rest0 ks0 ki0 sum1 klc1 rest1 kj0 ks1 kx0 ki1 kl0 kj1 cap0 xs0 kx1 lim0 sw0 kl1
+row0 xs1 fb0 sw1 cmp00 cmp01 ok0 row1 mn0 cap1 lim1 snd0 fb1 sla slb0 res0 uc0 cmp10 cmp11 ok1 mn1 snd1 uc1 slb1 sl res1 oh yr wdc0 wdc1 tb2a tb3a tb2b tb3b
+ld lc pw wold wd yb u0 gh0 shw0 shw1 shw2 shw3 sp0 sp1 sp2 sp3 wd0 wd1 wd2 wd3 ui0 uj0 ul0 p160 pf0 shg0 shg1 shg2 shg3 n12 kn t1 bd2 bd1 t2
+sc0 sc1 sc2 sc3 u1 gh1 pw4 pw5 pw6 pw7 shr0 shr1 shr2 shr3 shw4 shw5 shw6 shw7 ui1 uj1 ul1 sp4 sp5 p161 eo wd4 wd5 pf1 shg4 shg5 shg6 shg7 sp6 sp7
+wd6 wd7 offa pc0 ps0 ps1 ps2 ps3 pn0 sc4 sc5 shr4 shr5 shr6 shr7 rows0 sc6 sc7 as0 rows1 as1 rows2 as2 rows3 as3 qs0 qi0 qj0 qx0 lv0 vb0 lxw0
+pc1 ps4 ps5 ps6 ps7 pn1 eqm cx0 cx1 cx2 cx3 cx4 qs1 qi1 qj1 qx1 rows4 lv1 as4 vb1 lxw1 rows5 as5 eqt eq0 eq1 eq2 eqv eq3 eq4 eq5 rows6 as6
+eq6 eq7 eq8 eq9 eq10 eq11 eq12 eq13 eq14 eq15 rows7 as7 eqe far kp z su1 su2 cns lb pl patch
+"""
+
+
+OPT.update({
+    "score": ["ssvvsvvv"] * 6, "vm": 1, "pm": 2, "su": "a", "kp": "a", "wm": 4, "clip": [4] * 6, "clipw": "t", "cmp": "vv", "row0": "v",
+    "rows": "aa aa aa aa", "pf": "v", "gs": "v a v a a a a a", "ft": "aavv", "new": "a", "pack": "v",
+    "own1": "pk0 pk1 r0b r0c clipa0 clipa1 clipa2 clipa3 clipb0 clipb2 kc0 kc1 cm0 cm1 sum0 sum1 ks0 ki0 kj0 kx0 kl0 ks1 ki1 kj1 kx1 kl1 klc0 klc1 rest0 rest1 "
+            "xs0 xs1 sw0 sw1 row0 row1 fb0 fb1 cap0 cap1 lim0 lim1 cmp00 cmp01 cmp10 cmp11 ok0 ok1 mn0 mn1 snd0 snd1 sla n12 kn t1 bd1 bd2 t2 eo kp oh new "
+            "cx0 cx1 cx2 cx3 cx4 offa slb0 slb1 sl uc0 uc1 res0 res1"})
+ROUND = """
+BRI-- TOH0- TOH1 TOH2 RES-- CAP-- UI-- cx3_1+ IOT-- C37 cx2_1+ PI-- IOB-- IO256-- KC-- IO16-- BT4 LIM-- SP3-- I16B-- WDT SP1-- PKT KR16--
+SP0-- LXT0-- CY4 SP2-- KR-- res1_1 ONES-- CFAR-- CY0-- IO2K0-- NEG-- KC2 K42-- RI3-- KAI-- RI0-- RI1-- RI2-- RH-- PFL-- RESZ-- ID-- ROW3--
+ROW2-- ROW1-- KI-- KF-- ROW0-- N11M-- WTI-- N16M-- N12M-- sl_1 XIu0-- K43-- K40-- IDH-- G16-- K41-- BO-- NBO-- NID-- IDF-- B1.k-- KR4--
+tb0a-- tb1a-- tb0b-- kp_1 tb1b-- NB32K-- DELB-- SEG-- MB-- B16-- B32K-- FO1-- FO2-- WTF-- FO3-- G2-- G3-- G1-- G0-- SX0-- BOH-- NB8-- AS0--
+CX1h0-- cm0_1-- OFFC-- G4-- sli0-- r0b_1-- kc0_1-- sli1-- clipa1_1-- sum0_1-- kc1_1-- rest0_1-- OK00-- WDc0-- WDc1-- ks0_1-- ki0_1--
+clipa0_1-- G7-- G5-- G6-- klc0_1-- clipa2_1-- kj0_1-- G15-- kx0_1-- MULP-- kl0_1-- xs0_1-- AS4-- sw0_1-- row0_1-- clipb0_1-- clipa3_1--
+clipb2_1-- lim0_1-- r0c_1-- cap0_1-- sum1_1-- fb0_1-- cmp00_1-- cmp01_1-- ks1_1-- TOH-- n12_1-- ki1_1-- kj1_1-- klc1_1-- kx1_1-- mn0_1--
+kl1_1-- rest1_1-- cx1_1+ LXT1 ok0_1-- kn_1-- cx0_1+ snd0_1-- t1_1-- r0a sla_1-- cap1_1-- xs1_1-- bd1_1-- NDEL bd2_1-- r0b P16M- clipb2
+clipa1 clipb0 kc0 lim1_1-- sum0 ks0 sw1_1-- ki0 sla cap1 cap0 klc0 kc1 uc0_1 t2_1-- sum1 kj0 kx0 QRT+ kl0 ks1 ki1 rest0 rest1 cx0 res0_1--
+n12 kn BO4-- xs0 sw0 ADDP kj1 row0 eo_1 row1_1-- fb1_1-- cmp10_1-- cmp11_1-- IOTM ok1_1-- tb2b t1 P12M-- kp par1 par2 M16M-- par3 W16-- bd1
+klc1 lim0 kx1 fb0 kl1 tb3b xs1 cmp00 oh_1 ok0 bd2 mn1_1-- cmp01 mn0 OFFD-- snd1_1-- cx3 snd0 res0 lim1 t2 offa tb2a-- slb0 uc0 sw1 row1 fb1
+tb3a-- cmp10 slb0_1-- cmp11 eo oh LB new ok1 mn1 snd1 res1 gh0 gh1 CY2 cx2 LXT2 CY1 IO2K1 IO2K2 LXT3 IO2K3 slb1_1-- u0 slb1 uc1_1 uc1 shw0
+sp2 NSEL1 ui0 PAR uj0 MASK ul0 BW32K pf0 OFFA p160 sl wd2 sc2 shg0 sc3 pc0 pn0 pc1 offa_1 u1 rows4 shr0 ui1 sp5 uj1 WDc4 ul1 WDc3 pf1 wd5
+p161 MULD sc5 z shw4 pn1 ps2 ps0 shg4 sc6 new_1 shr4 ps5 ps6 ps4 sc7 ps7 NSEL0 WDc6 qs1 TP qi1 yb yr clipa3- clipa0- qj1 TW qx1 eqm WDc5 lv1
+vb1 eqt rows2 rows0 eq0 eq2 eq1 lxw1 far eqx eqv eq6 eq4 eq5 eq3 eq7 eqd eq8 eqe cx4 cx1 WDc2 cx4_1+ as4 as2 CY3 as0 rows6 as6 su1 su2
+clipa2- cns WDc7 ld- lb lc- pl pw- patch wold- cm0- wd-
+""".replace("snd0_1--", "snd0_1-- pk0_1--").replace("snd1_1--", "snd1_1-- pk1_1--").replace("snd0 ", "snd0 pk0 ").replace("snd1 ", "snd1 pk1 ")
+
+
+OPT.update({
+    "pf": "a", "pack": "", "pieces": 2,
+    "own1": "r0b r0c clipa0 clipa1 clipa2 clipa3 clipb0 clipb2 kc0 kc1 cm0 cm1 sum0 sum1 ks0 ki0 kx0 kl0 ks1 ki1 kx1 kl1 klc0 klc1 rest0 rest1 xs0 xs1 "
+            "m00 m01 m10 m11 bs00 bs01 bs02 bs03 bs10 bs11 bs12 bs13 fs00 fs01 fs02 fs03 fs10 fs11 fs12 fs13 lin0 lin1 cap0 cap1 lim0 lim1 "
+            "cmp00 cmp01 cmp10 cmp11 ok0 ok1 mn0 mn1 snd0 snd1 sla n12 kn t1 bd1 bd2 t2 eo kp oh new cx0 cx1 cx2 cx3 cx4 offa slb0 slb1 sl uc0 uc1 res0 res1"})
+ROUND = """
+TOH1 BRI-- TOH0- TOH2 RES-- CAP-- UI-- IOB-- PI-- IOT-- CY0 ENDS-- IO16-- LXT0-- SP2-- res0_1- KR-- ONES-- SP1-- CFAR-- IO256-- SP3-- KC2-- SP0-- KC-- KR16-- IO2K0-- RI3-- K43-- RI2-- RI0-- RI1-- PFL-- RH-- LIM-- KAI-- KI-- MB-- ID-- K42-- K41-- XIu0-- IDH-- K40-- ROW1-- ROW0-- new_1- ROW3-- ROW2-- KF-- RESZ-- G16-- B1.k-- KR4-- BO-- LB-- N16M-- WTI-- IDF-- NBO-- N11M-- NID-- tb0a-- SEG-- B16-- tb1a-- tb0b-- tb1b-- NB8-- FO1-- TW-- FO2-- DELB-- WDc1-- FO3-- G2-- G0-- SX0-- OFFD-- CX1h0-- G3-- G1-- AS0-- G15-- cm0_1-- G5-- sli0-- kc0_1-- r0b_1-- sli1-- clipa0_1-- WTF-- B32K-- OFFC-- bs00_1-- clipa1_1-- sum0_1-- bs01_1-- ks0_1-- rest0_1-- QRT-- G6-- G7-- G4-- clipa3_1-- clipa2_1-- klc0_1-- ki0_1-- fs01_1-- kc1_1-- clipb2_1-- kx0_1-- clipb0_1-- bs11_1-- cap0_1-- AS4-- kl0_1-- cap1_1-- bs10_1-- LXT1-- fs00_1-- xs0_1-- r0c_1-- sum1_1-- CY2- IO2K1-- ALT-- cx0_1+ IO2K2-- WDT-- rest1_1-- m00_1-- m01_1-- lim0_1-- cmp00_1-- kn_1-- TOH-- lin0_1-- lim1_1-- fs10_1-- sla_1-- cmp10_1-- m10_1-- ks1_1-- C37-- res1_1- PKT- I16B-- NEG-- BT4 uc0_1-- LXT2-- lin1_1-- klc1_1-- cx2_1-- LXT3-- BOH-- cmp01_1-- ki1_1-- fs11_1-- ok0_1-- kx1_1-- ok1_1-- n12_1-- t1_1-- NSEL0-- mn0_1-- kl1_1-- M16M-- xs1_1-- mn1_1-- WDc0-- snd0_1-- CY1-- cx1_1-- m11_1-- tb2a-- bd1_1-- bd2_1-- N12M-- t2_1-- cmp11_1-- slb0_1-- kc0 ADDP-- W16-- r0a NDEL-- su1+ P12M-- new PAR snd1_1-- cx4_1-- ld clipa2 NB32K clipa3 patch+ cm0 r0b bs01 bs00 bs10 clipb2 sum0 OFFA WDc4-- IOTM-- rest0 ks0 bs11 ki0 fs00 cx3 cx4 far+ clipa0 clipa1 clipb0 rest1 cap0 cx3_1-- cx1+ klc0 par1 su2+ MULP kx0 tb3a-- m00 fs01 par2 P16M-- kl0 xs0 par3 slb1_1-- cap1 kc1 sum1 lin1 lim0 fs11 cmp00 ks1 m10 ki1 NSEL1 WDc3 WDc6 m01 lin0 klc1 kx1 MASK uc1 sla cmp01 lim1 fs10 kl1 uc0 cmp10 MULD kp_1-- ok0 mn0 xs1 lc snd0 res0 ok1 m11 pw cmp11 mn1 wold snd1 cx0 slb0 slb1 u0 sl_1-- oh sl wd ui0 eo_1 sp2 uj0 BW32K TP ul0 wd2 p160 BO4-- n12 kn shw0 uc1_1-- u1 t1 kp offa_1 tb2b-- bd2 pf0 oh_1 tb3b-- bd1 ui1 sp5 uj1 wd5 ul1 sc3 shg0 pf1 p161 shg4 sc2 shw4 pc0 pc1 pn0 t2 offa sc5 eo shr0 pn1 sc6 shr4 ps2 ps5 ps0 sc7 ps4 WDc5 WDc7 ps6 ps7 qs1 qi1 z res1 yr yb gh0 cx2 gh1 rows2 CY3 IO2K3 as2 rows0 as0 CY4 rows4 as4 qj1 qx1 WDc2 eqm lv1 vb1 lxw1 eqt eq3 eq5 eq4 eq0 eqx eqv eq2 eq6 eq1 eq7 eqd eq8 eqe cns lb pl rows6 as6
+"""
 
 
 def banks_of(keys):
@@ -82,20 +149,45 @@ def banks_of(keys):
 def issue_order(calls):
     n = len(calls)
     before, after = [set() for _ in calls], [[] for _ in calls]
-    lastw, readers = {}, {}
-    for i, (q, _f, r, w, _ns, _lat) in enumerate(calls):
-        w = list(w) + (["T" + b for b in banks_of(list(r) + list(w))] if q == "t" else [])
-        for k in list(r) + w:
+    lastw, readers, in_bank = {}, {}, {}
+    for i, (q, _f, r, w, _ns, _lat, step, _grp) in enumerate(calls):
+        for k in list(r) + list(w):
             if k in lastw:
                 before[i].add(lastw[k])
         for k in w:
             before[i].update(readers.get(k, []))
+        for b in banks_of(list(r) + list(w)) if q == "t" else ():
+            seen = in_bank.setdefault(b, [])
+            if step is None:
+                before[i].update(seen)
+                seen[:] = [i]
+            else:
+                before[i].update(x for x in seen[:1] if calls[x][6] is None)
+                seen.append(i)
         before[i].discard(i)
         for k in r:
             readers.setdefault(k, []).append(i)
         for k in w:
             lastw[k] = i
             readers[k] = []
+    SEEN["calls"], SEEN["before"] = calls, [set(b) for b in before]
+    place = {x.rstrip("+-"): (x.count("+") - x.count("-"), j) for j, x in enumerate(ROUND.split())}
+    listed = sorted((i for i in range(n) if calls[i][6]), key=lambda i: (calls[i][6][0] + place[calls[i][6][1]][0], place[calls[i][6][1]][1], i))
+    spot = {i: x for x, i in enumerate(listed)}
+    for i in listed:
+        for p in before[i]:
+            assert spot.get(p, -1) < spot[i], (calls[p][6], calls[i][6])
+    last, soft = {}, set()
+    for i in listed:
+        p = last.get(calls[i][0])
+        if p is not None and p not in before[i]:
+            before[i].add(p)
+            soft.add((p, i))
+        last[calls[i][0]] = i
+        for b in banks_of(list(calls[i][2]) + list(calls[i][3])):
+            before[i].update(p for q, p in last.setdefault(b, {}).items() if q != calls[i][0])
+            last[b][calls[i][0]] = i
+    for i in range(n):
         for p in before[i]:
             after[p].append(i)
     banks = [banks_of(list(c[2]) + list(c[3])) for c in calls]
@@ -134,7 +226,7 @@ def issue_order(calls):
                 if pick is None or st[first] < pick[0]:
                     pick = (st[first], first)
             s, i = pick
-            q, _f, _r, _w, ns, lat = calls[i]
+            q, ns, lat = calls[i][0], calls[i][4], calls[i][5]
             ready[q].remove(i)
             held.discard(behind.get(i))
             order.append(i)
@@ -146,7 +238,10 @@ def issue_order(calls):
                 bank[b] = (q, s + ns)
             for j in next_of[i]:
                 late = calls[j][5] + (DMA if calls[j][5] and calls[j][0] != "p" else 0.0) if back else 0.0
-                at[j] = max(at[j], end[i] + late + (0.0 if q == calls[j][0] == "t" else WAKE))
+                if ((j, i) if back else (i, j)) in soft:
+                    at[j] = max(at[j], s + ns)
+                else:
+                    at[j] = max(at[j], end[i] + late + (0.0 if q == calls[j][0] == "t" else WAKE))
                 missing[j] -= 1
                 if not missing[j]:
                     ready[calls[j][0]].append(j)
@@ -162,6 +257,43 @@ def issue_order(calls):
     return best[1]
 
 
+def runs(blocks, most):
+    out = []
+    for j in blocks:
+        if out and out[-1][0] + out[-1][1] == j and j % 4 and out[-1][1] < most:
+            out[-1] = (out[-1][0], out[-1][1] + 1)
+        else:
+            out.append((j, 1))
+    return out
+
+
+def issue_order(calls):
+    n = len(calls)
+    before = [set() for _ in calls]
+    lastw, readers = {}, {}
+    for i, c in enumerate(calls):
+        r, w = c[2], c[3]
+        for k in list(r) + list(w):
+            if k in lastw:
+                before[i].add(lastw[k])
+        for k in w:
+            before[i].update(readers.get(k, []))
+        before[i].discard(i)
+        for k in r:
+            readers.setdefault(k, []).append(i)
+        for k in w:
+            lastw[k] = i
+            readers[k] = []
+    SEEN["calls"], SEEN["before"] = calls, before
+    place = {x.rstrip("+-"): (x.count("+") - x.count("-"), j) for j, x in enumerate(ROUND.split())}
+    order = sorted(range(n), key=lambda i: (calls[i][6][0] + place[calls[i][6][1]][0], place[calls[i][6][1]][1], i))
+    spot = {i: x for x, i in enumerate(order)}
+    for i in order:
+        for p in before[i]:
+            assert spot[p] < spot[i], (calls[p][6], calls[i][6])
+    return order
+
+
 def rank_program(g, core, T, topo):
     rank = T.rank_of(core)
     if rank is None:
@@ -170,6 +302,18 @@ def rank_program(g, core, T, topo):
     n = len(cores)
     V, PE, AC = g.vector, g.tensor, g.scalar
     calls = []
+    now = [1, None]
+
+    def step(name):
+        now[1] = name
+
+    def put(q, f, r, w, ns, lat=0.0, grp=None):
+        name = now[1] or w[0]
+        if now[0] == 1 and name in OPT["own1"].split():
+            name += "_1"
+        if now[0] >= NT and name in OPT["own6"].split():
+            name += "_6"
+        calls.append((q, f, r, w, ns, lat, (now[0], name), grp))
 
     def cols(ap):
         c = 1
@@ -181,25 +325,23 @@ def rank_program(g, core, T, topo):
         return all("16" in str(a.dtype) for a in aps)
 
     def vec(f, r, w, n_cols, rate):
-        calls.append(("v", f, r, w, 60.0 + max(64.0, n_cols * rate) * CYCLE, 0.0))
+        put("v", f, r, w, 60.0 + max(64.0, n_cols * rate) * CYCLE)
 
     def mm(out, lhs, rhs, st, sp, r, w):
-        ns = max(min(64, cols(lhs)), cols(rhs)) * CYCLE * (1 if narrow(lhs) else 4)
-        calls.append(("t", lambda: PE.matmul(out, lhs, rhs, st, sp), r, w, ns, 0.0))
+        ns = PE_CALL + max(min(64, cols(lhs)), cols(rhs)) * PE_CYCLE * (1 if narrow(lhs) else 4)
+        put("t", lambda: PE.matmul(out, lhs, rhs, st, sp), r, w, ns, 0.0, (st, sp))
 
     def act(out, in_, r, w, func=F.Copy, bias=0.0, scale=1.0, accum=None, rate=1.0):
-        calls.append(("a", lambda: AC.activation(out, in_, func, bias=bias, scale=scale, accum_out=accum), r, w,
-                      75.0 + max(64, cols(out)) * rate * CYCLE, 0.0))
+        put("a", lambda: AC.activation(out, in_, func, bias=bias, scale=scale, accum_out=accum), r, w,
+            (ACT if rate == 1.0 else 65.0) + max(64, cols(out)) * rate * CYCLE)
 
     def fill(ap, c, k):
-        vec(lambda: V.memset(ap, c), [], [k], cols(ap), 0.5 if narrow(ap) else 1.0)
+        vec(lambda: V.memset(ap, c), [], [k] if isinstance(k, str) else k, cols(ap), 0.5 if narrow(ap) else 1.0)
 
     def iota(ap, pattern, base, cm, k):
         small = "int" not in str(ap.dtype)
-        calls.append(("p", lambda: g.iota(ap, pattern, base, cm, allow_small_or_imprecise_dtypes=small), [], [k], 130.0 + 2 * cols(ap) * CYCLE, 0.0))
-
-    def gcopy(out, in_, r, w):
-        calls.append(("p", lambda: g.affine_select(out, in_, [[0, cols(out)]], A.is_ge, 0.0, 0, 0), r, w, 170.0 + 2 * cols(out) * CYCLE, 0.0))
+        put("p", lambda: g.iota(ap, pattern, base, cm, allow_small_or_imprecise_dtypes=small), [], [k] if isinstance(k, str) else k,
+            130.0 + 2 * cols(ap) * CYCLE)
 
     def ts(out, in0, s1, s2, o0, o1, r, w):
         rate = 0.5 if narrow(out, in0) else 1.0
@@ -211,8 +353,25 @@ def rank_program(g, core, T, topo):
     def tt(out, a, b, o, r, w, rate=None):
         vec(lambda: V.tensor_tensor(out, a, b, o), r, w, cols(b), rate or (1.0 if banks_of(r) else 2.0))
 
-    def cp(out, a, r, w):
-        vec(lambda: V.tensor_copy(out, a), r, w, cols(out), 0.5 if narrow(out, a) else 1.0)
+    def cp(out, a, r, w, q="v"):
+        if q == "v":
+            vec(lambda: V.tensor_copy(out, a), r, w, cols(out), 0.5 if narrow(out, a) else 1.0)
+        elif q == "a":
+            act(out, a, r, w)
+        else:
+            put("p", lambda: g.affine_select(out, a, [[0, cols(out)]], A.is_ge, 0.0, 0, 0), r, w, 170.0 + 2 * cols(out) * CYCLE)
+
+    def lin(q, out, in_, scale, bias, r, w):
+        if q == "a":
+            act(out, in_, r, w, bias=bias, scale=scale)
+        else:
+            ts(out, in_, scale, bias, A.mult, A.add, r, w)
+
+    def relu(q, out, in_, bias, r, w):
+        if q == "a":
+            act(out, in_, r, w, F.Relu, bias=bias)
+        else:
+            ts(out, in_, bias, 0.0, A.add, A.max, r, w)
 
     def gather(q, out, win, off, r, w):
         if q == "a":
@@ -227,7 +386,7 @@ def rank_program(g, core, T, topo):
         vec(lambda: V.tensor_tensor_scan(out, d0, d1, 0.0, o0, o1), r, w, cols(out), 0.5 if narrow(out, d0, d1) else 1.0)
 
     def dma(q, out, in_, sem, r, w, kib):
-        calls.append((q, (out, in_, sem), r, w, 100.0, 3.0 * kib + 1.0))
+        put(q, (out, in_, sem), r, w, 100.0, 3.0 * kib + 1.0)
 
     def half(h, size=H):
         return slice(size * h, size * h + size)
@@ -236,6 +395,18 @@ def rank_program(g, core, T, topo):
         j = COLS.index(name)
         return T.COL[:, j:j + 1]
 
+    def bank(b, lo, hi, by=1, rows=slice(0, 128)):
+        name, at = {3: ("B34", 0), 4: ("B34", 512), 5: ("B56", 0), 6: ("B56", 512)}.get(b, ("B%d" % b, 0))
+        return T[name][rows, at + lo:at + hi:by]
+
+    whole = {3: ["B3.g"], 4: ["B4.g"], 5: ["B5.c", "B5.v"], 6: ["B6.c", "B6.v"]}
+    first_tail = 16 - OPT["tail"]
+    tail = []
+    for b in range(first_tail, 16):
+        tail.append((b, sum(x[2] for x in tail), Q - 16 * b))
+    tail_cols = sum(x[2] for x in tail)
+
+    cq = OPT["const"]
     dma("s", T.BRI[:], T.br[:], "dbr", [], ["BRI"], 1024)
     dma("a", T.KAI[:], T.ka[:], "dka", [], ["KAI"], 1)
     dma("a", T.WTI[:], T.wt[:], "dwt", [], ["WTI"], 1)
@@ -246,13 +417,28 @@ def rank_program(g, core, T, topo):
     iota(T.IO16[:], [[0, 16], [1, 16]], 0, 0, "IO16")
     iota(T.IOB[:], [[16, 8], [0, 16]], 0, 0, "IOB")
     iota(T.ONES[:], [[0, 256]], 1, 0, "ONES")
-    for name, c in (("LIMT", 18), ("PAR", 1), ("EIGHT", 8), ("C37", 37), ("CFAR", FAR), ("NEG", -131072)):
+    for name, c in (("C37", 37), ("CFAR", FAR), ("NEG", -131072)):
         iota(T[name][:], [[0, 128]], c, 0, name)
-    for j in range(2):
-        iota(T.SP[:, half(j, 1024)], [[0, 1024]], 0, 0, "SP%d" % j)
+    iota(T.LIM[0:3, :], [[0, 128]], 9216, -6656, "LIM")
+    iota(T.LIM[0:1, :], [[0, 128]], -256, 0, "LIM")
+    if "a" in OPT["cmp"]:
+        fill(col("HALF"), -0.5, "HALF")
+    iota(T.KC[0:1, 0:H], [[0, 8], [-1, 16]], 15, 0, "KC")
+    iota(T.KC[0:1, H:2 * H], [[0, H]], 0, 0, "KC")
+    iota(T.ALT[0:2, :], [[0, H], [1, 2]], 0, 0, "ALT")
+    for name, pattern, base in (("KC2", [[0, 8], [-2048, 16]], 30720), ("KR16", [[0, 8], [16, 16]], 15),
+                                ("KR", [[0, 8], [1, 16]], 0), ("IO256", [[256, 16]], 0), ("I16B", [[16, 16]], 0)):
+        iota(T[name][0:1, :], pattern, base, 0, name)
     for j in range(4):
+        iota(T.SP[:, half(j, 512)], [[0, 512]], 0, 0, "SP%d" % j)
+    iota(T.FS[:, 0:2 * WIN:WIN], [[0, 2]], 0, 0, "ENDS")
+    iota(T.BS[:, 2063:2 * WIN:WIN], [[0, 2]], 0, 0, "ENDS")
+    for j in range(4):
+        step("IO2K%d" % j)
         iota(T.IO2K[:, half(j, 512)], [[1, 512]], 512 * j, 0, "IO2K")
+        step("LXT%d" % j)
         iota(T.LXT[:, half(j, 512)], [[1, 64], [768, 8]], 64 * j, 0, "LXT")
+    step(None)
     fill(T.UU[:, 96:128], 2048, "RI3")
     ts(T.UU[:, 0:32], u32, 2016, None, A.bitwise_and, None, ["UI"], ["RI0"])
     ts(T.UU[:, 32:64], u32, 31, None, A.bitwise_and, None, ["UI"], ["RI1"])
@@ -260,7 +446,7 @@ def rank_program(g, core, T, topo):
     ts(T.UU[:, 64:96], T.UU[:, 64:96], 5, 2047, A.arith_shift_right, A.bitwise_and, ["RI2"], ["RI2"])
     cp(T.RH[:], T.UU[:, 0:128], ["RI0", "RI1", "RI2", "RI3", "UU"], ["RH"])
     for k in range(4):
-        dma("s", T.ROWS[k:k + 1, :], T.RH[:, 32 * k:32 * k + 32], "dr%d" % k, ["RH"], ["ROW%d" % k], 8)
+        dma("a", T.ROWS[k:k + 1, :], T.RH[:, 32 * k:32 * k + 32], "dr%d" % k, ["RH"], ["ROW%d" % k], 8)
     dma("s", T.RES[:, 0:ZC], T.res[:], "dres", [], ["RES", "RESG"], 832)
     dma("s", T.CAP[:], T.cap[:], "dcap", [], ["CAP"], 512)
     fill(T.RES[:, ZC:ZC + 16], 0.0, "RESZ")
@@ -274,42 +460,49 @@ def rank_program(g, core, T, topo):
     cp(T.IDH[:], T.ID[:], ["ID"], ["IDH"])
     ts(T.DELB[:], T.IO16[:], col("KF"), None, A.is_equal, None, ["IO16", "KF"], ["DELB"])
     ts(T.BO[:], T.IOB[:], col("G16"), None, A.is_equal, None, ["IOB", "G16"], ["BO"])
-    ts(T.XI[:, 0:1], T.KAI[:], 63, None, A.bitwise_and, None, ["KAI"], ["XI0"])
+    ts(T.XI[:, 0:1], T.KAI[:], 63, None, A.bitwise_and, None, ["KAI"], ["XIu0"])
     cp(T.K4[:, 1:2], T.KAI[:], ["KAI"], ["K41"])
-    cp(T.K4[:, 0:1], T.XI[:, 0:1], ["XI0"], ["K40"])
+    cp(T.K4[:, 0:1], T.XI[:, 0:1], ["XIu0"], ["K40"])
     mm(T.B1[0:4, 0:128], T.K4[:], T.IDH[:], True, True, ["K40", "K41", "K42", "K43", "IDH"], ["B1.k"])
     cp(T.KR4[0:4, :], T.B1[0:4, 0:128], ["B1.k"], ["KR4"])
-    fill(T.SEG[:], 1.0, "SEG")
-    fill(T.SEG[:, 0:2048:16], 0.0, "SEG")
+    if OPT["seg"] == "v":
+        fill(T.SEG[:], 256.0, "SEG")
+        fill(T.SEG[:, 0:2064:16], 0.0, "SEG")
+    else:
+        for j in range(4):
+            step("SEG%d" % j)
+            iota(T.SEG[:, half(j, 512)], [[0, 32], [256, 16]], 0, 0, "SEG")
+        step(None)
     fill(T.MB[:], 1e9, "MB")
     fill(T.MB[:, 0:256:16], -1e9, "MB")
-    fill(T.PK[:, TR:TR + Q], 0.0, "PKT")
-    fill(T.WD[:, 2048:2304], 0.0, "WDT")
+    iota(T.PK[:, TR:TR + Q], [[0, Q]], 0, 0, "PKT")
+    iota(T.WD[:, 2048:2304], [[0, Q]], 0, 0, "WDT")
+    fill(T.PAR[:], 1.0 / 8192, "PAR")
+    fill(T.QRT[0:1, :], -0.25, "QRT")
     cp(T.OFFC[:], T.IOT[:], ["IOT"], ["OFFC"])
     cp(col("WTF"), T.WTI[:], ["WTI"], ["WTF"])
     ts(col("G15"), col("G16"), 15.0, None, A.add, None, ["G16"], ["G15"])
     ts(T.W16[:], T.IOT[:, 0:144], col("G15"), col("WTF"), A.is_equal, A.mult, ["IOT", "G15", "WTF"], ["W16"])
-    ts(T.BT4[:], T.IO16[:, 0:128], col("KF"), 2.0 * FAR, A.is_gt, A.mult, ["IO16", "KF"], ["BT4"])
-    tt(T.BT4[:], T.BT4[:], T.BO[:], A.mult, ["BT4", "BO"], ["BT4"])
     cp(T.BOH[:], T.BO[:, 0:128:16], ["BO"], ["BOH"])
-    for name, c in (("N11M", -2048.0), ("NID", -1.0), ("N12M", -4096.0), ("N16M", -16.0), ("IDF", 1.0), ("P16M", 65536.0), ("P20M", 1048576.0),
-                    ("N19M", -524288.0)):
-        act(T[name][:], T.ID[:], ["ID"], [name], scale=c)
-    for name, c in (("NBO", -512.0), ("BO4", 2.0 * FAR), ("BW32K", 32768.0)):
-        act(T[name][:], T.BO[:], ["BO"], [name], scale=c)
-    for name, c in (("B16", 16.0), ("NB8", -1.0), ("B32K", 32768.0), ("NB32K", -32768.0)):
-        act(T[name][:], T.BO[:, 0:128:16], ["BO"], [name], scale=c)
-    act(T.KC[0:1, :], T.IO16[0:1, 0:H], ["IO16"], ["KC"], bias=15.0, scale=-1.0)
-    act(T.KC2[0:1, :], T.IO16[0:1, 0:H], ["IO16"], ["KC2"], bias=30720.0, scale=-2048.0)
-    act(T.KR16[0:1, :], T.IO16[0:1, 0:H], ["IO16"], ["KR16"], bias=15.0, scale=16.0)
-    act(T.KR[0:1, :], T.IO16[0:1, 0:H], ["IO16"], ["KR"])
-    act(T.IO256[0:1, :], T.IOT[0:1, 0:16], ["IOT"], ["IO256"], scale=256.0)
-    act(T.I16B[0:1, :], T.IOT[0:1, 0:16], ["IOT"], ["I16B"], scale=16.0)
-    act(T.NDEL[:], T.DELB[:], ["DELB"], ["NDEL"], bias=1.0, scale=-1.0)
-    act(T.OFFD[:], T.DELB[:], ["DELB"], ["OFFD"], bias=-67108864.0, scale=67108864.0)
+    def who(name):
+        return "a" if name in OPT["ona"].split() else "v"
+    for name, c in (("N11M", -2048.0), ("NID", -1.0), ("N12M", -4096.0), ("P12M", 4096.0), ("N16M", -16.0), ("IDF", 1.0), ("P16M", 65536.0),
+                    ("M16M", -65536.0)):
+        lin(who(name), T[name][:], T.ID[:], c, 0.0, ["ID"], [name])
+    for name, c in (("NBO", -512.0), ("BO4", 2.0 * FAR), ("BW32K", 32768.0)) + ((("NBO2", -256.0),) if "a" in OPT["cmp"] else ()):
+        lin(who(name), T[name][:], T.BO[:], c, 0.0, ["BO"], [name])
+    for j in (0, 1):
+        lin("v", T.B16[:, half(j, 8)], T.BO[:, 0:128:16], 16.0, 0.0, ["BO"], ["B16"])
+    for name, c in (("NB8", -1.0), ("B32K", 32768.0), ("NB32K", -32768.0)):
+        lin(who(name), T[name][:], T.BO[:, 0:128:16], c, 0.0, ["BO"], [name])
+    lin("a", T.NDEL[:], T.DELB[:], -1.0, 1.0, ["DELB"], ["NDEL"])
+    put("p", lambda: g.affine_select(T.BT4[:], T.BO4[:], [[1, 128]], A.is_gt, 0.0, 0, -1), ["BO4"], ["BT4"], 382.0)
+    if "a" in OPT["um"]:
+        iota(T.FOUR[0:1, :], [[0, 8]], 4, 0, "FOUR")
+    lin(cq, T.OFFD[:], T.DELB[:], 67108864.0, -67108864.0, ["DELB"], ["OFFD"])
     act(T.LB[:], T.IOT[:, 0:16], ["IOT", "KF"], ["LB"], F.Identity, bias=col("KF"), scale=16.0)
-    act(T.TP[:], T.LB[:], ["LB"], ["TP"], bias=float(TR))
-    act(T.TW[:], T.LB[:], ["LB"], ["TW"], bias=2048.0 + FAR)
+    lin(cq, T.TP[:], T.LB[:], 1.0, float(TR), ["LB"], ["TP"])
+    lin(cq, T.TW[:], T.LB[:], 1.0, 2048.0 + FAR, ["LB"], ["TW"])
     tt(T.IOTM[:], T.IOT[:], T.OFFD[:], A.add, ["IOT", "OFFD"], ["IOTM"])
     ts(col("MULP"), col("KF"), 0.0, -15.0, A.is_equal, A.mult, ["KF"], ["MULP"])
     ts(col("ADDP"), col("KF"), 0.0, float(P0), A.is_equal, A.mult, ["KF"], ["ADDP"])
@@ -317,55 +510,91 @@ def rank_program(g, core, T, topo):
     tt(col("ADDP"), col("ADDP"), col("KF"), A.add, ["ADDP", "KF"], ["ADDP"])
     ts(T.MULD[:], T.ID[:], col("MULP"), None, A.mult, None, ["ID", "MULP"], ["MULD"])
     ts(T.OFFA[:], T.DELB[:], col("ADDP"), None, A.mult, None, ["DELB", "ADDP"], ["OFFA"])
-    tt(T.OFFA[:], T.OFFA[:], T.OFFD[:], A.add, ["OFFA", "OFFD"], ["OFFA"])
-    dma("s", T.TOH[:, 0:256], T.DELB[:], "dt0", ["DELB", "CAP"], ["TOH"], 64)
+    lin("a", T.TOH[:, 0:256], T.DELB[:], -16.0, 208.0, ["DELB"], ["TOH"])
     for j, s in enumerate((256, 512, 1024)):
+        step("TOH%d" % j)
         dma("s", T.TOH[:, s:2 * s], T.TOH[:, 0:s], "dt%d" % (j + 1), ["TOH"], ["TOH"], s // 4)
+    step(None)
+    if tail:
+        ts(T.MASK[:], T.IO16[:, 0:16], col("KF"), 4096.0, A.is_le, A.mult, ["IO16", "KF"], ["MASK"])
+    for b, lo, m in tail:
+        step("NSEL%d" % (b % 2))
+        ts(T.NSEL[:, lo:lo + m], T.ONES[:, 0:m], T.BO[:, 16 * (b - 8):16 * (b - 8) + 1], -1.0, A.mult, A.mult, ["ONES", "BO"], ["NSEL%d" % b])
+    step(None)
 
-    whole_bank = {0: ["B0.cap", "B0.lv0", "B0.lv1", "B0.par", "B0.far0", "B0.far1"], 3: ["B3.g", "B3.z"], 4: ["B4.g"],
-                  6: ["B6.m", "B6.d"], 7: ["B7.x", "B7.hi"]}
-    tab = ["TAB%d" % j for j in range(8)]
+    tab = ["TAB%d" % j for j in range(4)]
+    wdk = ["WDc%d" % j for j in range(8)]
 
-    def table(j, b):
-        o, k, ft = T["B%d" % b][:], whole_bank[b], T.FT[:, half(j & 1, 512)]
-        mm(o, T.KR4[0:4, :], T.ROWS[0:4, half(j, 512)], True, True, ["KR4", "ROW0", "ROW1", "ROW2", "ROW3"], k)
-        act(ft, o, k, ["FT%d" % (j & 1)], bias=-0.499755859375, scale=1.0 / 2048)
-        mm(o, T.KR4[0:4, :], T.ROWS[0:4, half(j, 512)], True, False, ["KR4", "ROW0", "ROW1", "ROW2", "ROW3"], k)
-        mm(o, T.N11M[:], ft, False, True, ["N11M", "FT%d" % (j & 1)], k)
-        act(T.TAB[:, half(j, 512)], o, k, [tab[j]])
+    def table(j):
+        b = (3, 5)[j & 1]
+        k, ft, rk = whole[b] + whole[b + 1], T.FT[:, half(j & 1, 1024)], ["KR4", "ROW0", "ROW1", "ROW2", "ROW3"]
+        step("tb%da" % j)
+        for x in (0, 1):
+            mm(bank(b + x, 0, 512), T.KR4[0:4, :], T.ROWS[0:4, half(2 * j + x, 512)], True, True, rk, whole[b + x])
+        lin(OPT["ft"][j], ft, bank(b, 0, 1024), 1.0 / 2048, -0.499755859375, k, ["FT%d" % (j & 1)])
+        step("tb%db" % j)
+        for x in (0, 1):
+            mm(bank(b + x, 0, 512), T.KR4[0:4, :], T.ROWS[0:4, half(2 * j + x, 512)], True, False, rk, whole[b + x])
+            mm(bank(b + x, 0, 512), T.N11M[:], T.FT[:, half(2 * (j & 1) + x, 512)], False, True, ["N11M", "FT%d" % (j & 1)], whole[b + x])
+        act(T.TAB[:, half(j, 1024)], bank(b, 0, 1024), k, [tab[j]])
+
+    def first_room(j):
+        b = (3, 5)[j]
+        step("sli%d" % j)
+        for x in (0, 1):
+            mm(bank(b + x, 0, 512), T.ID[:], T.CAP[:, half(2 * j + x, 512)], True, False, ["ID", "CAP"], whole[b + x])
+            mm(bank(b + x, 0, 512), T.NID[:], T.RES[:, half(2 * j + x, 512)], False, True, ["NID", "RES"], whole[b + x])
+        act(T.SL[:, half(j, 1024)], bank(b, 0, 1024), whole[b] + whole[b + 1], ["SL"], F.Relu)
 
     def first_offsets():
         src = T.BRI[:, 0:2048:8]
+        step("FO1")
         ts(T.UU[:], src, 65535, None, A.bitwise_and, None, ["BRI"], ["UU"])
-        ts(T.B3[:, 0:256], src, 0.0, 4096.0, A.is_lt, A.mult, ["BRI"], ["B3.g"])
+        ts(T.B7[:, 0:256], src, 0.0, 4096.0, A.is_lt, A.mult, ["BRI"], ["B7.x"])
         ts(T.UI[:], src, 4095, None, A.bitwise_and, None, ["BRI"], ["UI"])
-        ts(T.B4[:, 0:256], T.UU[:], 4096.0, 4096.0, A.is_lt, A.mult, ["UU"], ["B4.g"])
-        tt(T.KS[:], T.UI[:], T.B3[:, 0:256], A.max, ["B3.g", "UI"], ["KS0", "KS1"])
-        tt(T.CNS[:], T.KS[:], T.B4[:, 0:256], A.max, ["B4.g", "KS0", "KS1"], ["CNS"])
+        ts(T.B7[:, 256:512], T.UU[:], 4096.0, 4096.0, A.is_lt, A.mult, ["UU"], ["B7.hi"])
+        tt(T.KS[:, 0:Q], T.UI[:], T.B7[:, 0:256], A.max, ["B7.x", "UI"], ["KS0", "KS1"])
+        step("FO2")
+        tt(T.CNS[:], T.KS[:, 0:Q], T.B7[:, 256:512], A.max, ["B7.hi", "KS0", "KS1"], ["CNS"])
+        step("FO3")
         ts(T.EO[:], T.CNS[:], float(ZC), None, A.min, None, ["CNS"], ["EO"])
+        step(None)
 
-    def k_part(out, key, t):
-        act(out, T.WD[:, t - 1:2048:8], ["WD"], [key], bias=199.50390625, scale=1.0 / 65536)
+    def k_part(q, out, key, t, more):
+        lin(q, out, T.WD[:, t - 1:2048:8], 1.0 / 65536, 199.50390625 + more, [wdk[t - 1]], [key])
 
     def offsets(t):
-        act(T.N12[:], T.WD[:, t - 1:2048:8], ["WD"], ["N12"], bias=219.5625, scale=1.0 / 4096)
-        k_part(T.KN[:], "KN", t)
+        step("n12")
+        lin(OPT["n12"], T.N12[:], T.WD[:, t - 1:2048:8], 1.0 / 4096, 219.5625, [wdk[t - 1]], ["N12"])
+        step("kn")
+        k_part(OPT["kn"], T.KN[:], "KN", t, 0)
+        step("t1")
         mm(T.B7[:, 0:256], T.ID[:], T.N12[:], True, False, ["ID", "N12"], ["B7.x"])
         mm(T.B7[:, 0:256], T.N16M[:], T.KN[:], False, True, ["N16M", "KN"], ["B7.x"])
-        act(T.BD2[:], T.KN[:], ["KN"], ["BD2"], F.Relu, bias=4096.0 * (201 - t), scale=-4096.0)
-        act(T.BD1[:], T.B7[:, 0:256], ["B7.x"], ["BD1"], F.Relu, bias=4096.0 * (t - 2980), scale=-4096.0)
+        for name, src, sk, c in (("bd2", T.KN[:], "KN", 201.0 - t), ("bd1", T.B7[:, 0:256], "B7.x", t - 2980.0)):
+            step(name)
+            if OPT[name] == "a":
+                act(T[name.upper()][:], src, [sk], [name], F.Relu, bias=4096.0 * c, scale=-4096.0)
+            else:
+                ts(T[name.upper()][:], src, c, 4096.0, A.is_lt, A.mult, [sk], [name])
+        step("t2")
         o = T.B7[:, 256:512]
-        mm(o, T.IDF[:], T.WD[:, t - 1:2048:8], True, False, ["IDF", "WD"], ["B7.hi"])
+        mm(o, T.IDF[:], T.WD[:, t - 1:2048:8], True, False, ["IDF", wdk[t - 1]], ["B7.hi"])
         mm(o, T.N12M[:], T.N12[:], False, False, ["N12M", "N12"], ["B7.hi"])
-        mm(o, T.ID[:], T.BD2[:], False, False, ["ID", "BD2"], ["B7.hi"])
-        mm(o, T.ID[:], T.BD1[:], False, True, ["ID", "BD1"], ["B7.hi"])
+        mm(o, T.ID[:], T.BD2[:], False, False, ["ID", "bd2"], ["B7.hi"])
+        mm(o, T.ID[:], T.BD1[:], False, True, ["ID", "bd1"], ["B7.hi"])
+        step("eo")
         ts(T.EO[:], o, 901120.0, float(ZC), A.add, A.min, ["B7.hi"], ["EO"])
 
     def pk(h):
         return ["PK%d" % j for j in range(4 * h, 4 * h + 4)]
 
-    def rows(q, j, m):
+    def p0(h):
+        return ["P0%d" % j for j in range(4 * h, 4 * h + 4)]
+
+    def rows(q, j, m, name="rows"):
         lo, hi = 32 * j, 32 * (j + m)
+        step(name + str(j))
         gather(q, T.PK[:, 16 * lo:16 * hi], T.RES[:, 0:3344], T.EO[:, lo:hi], ["RES", "RESG", "RESZ", "EO"], ["PK%d" % i for i in range(j, j + m)])
 
     def row0(h):
@@ -374,279 +603,535 @@ def rank_program(g, core, T, topo):
     def aside(h):
         return T.PK[:, P0 + H * h:P0 + H * h + H]
 
-    def row0_aside():
-        act(T.PK[:, P0:P0 + Q], T.PK[:, 0:4096:16], pk(0) + pk(1), ["P00", "P01"])
-        act(T.PK[:, 0:4096:16], T.ONES[:], ["ONES"], pk(0) + pk(1), scale=255.0)
+    def row0_aside(q, t, j, m, name="as"):
+        lo, hi, keys = 32 * j, 32 * (j + m), ["PK%d" % x for x in range(j, j + m)]
+        step(name + str(j))
+        cp(T.PK[:, P0 + lo:P0 + hi], T.PK[:, 16 * lo:16 * hi:16], keys, ["P0%d" % x for x in range(j, j + m)], q)
+        hi = min(hi, Q - 32 * OPT["clip"][t - 1])
+        if hi > lo:
+            if q == "p":
+                iota(T.PK[:, 16 * lo:16 * hi:16], [[0, hi - lo]], 255, 0, keys)
+            elif q == "a":
+                act(T.PK[:, 16 * lo:16 * hi:16], T.ONES[:, 0:hi - lo], ["ONES"], keys, scale=255.0)
+            else:
+                fill(T.PK[:, 16 * lo:16 * hi:16], 255.0, keys)
 
-    def cap_wide(t, ks):
-        cx = "CX%d" % (t & 1)
+    def cap_wide(t, ks, name="cx"):
+        cx, cut = "CX%d" % (t & 1), Q - (32 * OPT["clip"][t - 1] if OPT["clipw"] == "t" else 0)
         for k in ks:
-            gcopy(T[cx][:, k:4096:16], T.CAP[:, t - 1:2048:8], ["CAP"], [cx + "k%d" % k])
+            step(name + str(max(k - 1, 0) // 3))
+            cp(T[cx][:, k:16 * cut:16], T.CAP[:, t - 1:8 * cut:8], ["CAP"], [cx + "k%d" % k], "p")
 
     def words(t):
+        step("ld")
         tt(T.LD[:], T.CNS[:, 15:256:16], T.TW[:], A.min, ["CNS", "TW"], ["LD"])
-        tt(T.LC[:], T.LD[:], T.B0[:, 288:304], A.max, ["LD", "B0.far0", "B0.far1"], ["LC"])
+        step("lc")
+        tt(T.LC[:], T.LD[:], bank(2, 400, 416), A.max, ["LD", "B2.far"], ["LC"])
+        step("pw")
         ts(T.PW[:], T.LC[:], -float(FAR), None, A.add, None, ["LC"], ["PW"])
-        act(T.NEW[:], T.IOTM[:], ["IOTM"], ["NEW"], F.Relu, bias=2048.0 + 256.0 * (t - 1) + 4096.0 * (t + 2))
         win = T.WD[:, 0:2304]
-        tt(T.WOLD[:], win.indirect(T.PW[:]), T.NDEL[:], A.mult, ["WD", "WDT", "PW", "NDEL"], ["WOLD"], GATHER)
-        tt(win.indirect(T.PW[:]), T.WOLD[:], T.NEW[:], A.add, ["WOLD", "NEW", "PW"], ["WD", "WDT"], SCATTER)
+        step("wold")
+        tt(T.WOLD[:], win.indirect(T.PW[:]), T.NDEL[:], A.mult, wdk + ["WDT", "PW", "NDEL"], ["WOLD"], GATHER)
+        step("wd")
+        tt(win.indirect(T.PW[:]), T.WOLD[:], T.NEW[:, half(t - 1, Q)], A.add, ["WOLD", "NEW%d" % t, "PW"], wdk + ["WDT"], SCATTER)
 
     def suspended(t):
+        step("oh")
         gather("a", T.OH[:], T.TOH[:], T.KL[:], ["TOH", "KL0", "KL1"], ["OH"])
-        z = T.B3[:, 256:512]
-        k_part(T.KP[:], "KP", t)
-        mm(z, T.P20M[:], T.OH[:], True, False, ["P20M", "OH"], ["B3.z"])
-        mm(z, T.N19M[:], T.SG[:], False, False, ["N19M", "SG0", "SG1"], ["B3.z"])
-        mm(z, T.P16M[:], T.KP[:], False, True, ["P16M", "KP"], ["B3.z"])
-        act(T.OH[:], z, ["B3.z"], ["OH"], F.Relu, bias=65536.0 * (t + 8 - 200) - 1572864.0)
-        mm(z, T.IDF[:], T.WD[:, t - 1:2048:8], True, False, ["IDF", "WD"], ["B3.z"])
-        mm(z, T.NID[:], T.OH[:], False, True, ["NID", "OH"], ["B3.z"])
-        act(T.WD[:, t - 1:2048:8], z, ["B3.z"], ["WD"])
+        z, wd = T.B0[:, 256:512], T.WD[:, t - 1:2048:8]
+        step("kp")
+        k_part(OPT["kp"], T.KP[:], "KP", t, t)
+        step("z")
+        mm(z, T.P16M[:], T.OH[:], True, False, ["P16M", "OH"], ["B0.z"])
+        mm(z, T.M16M[:], T.KP[:], False, False, ["M16M", "KP"], ["B0.z"])
+        mm(z, T.P12M[:], T.OK0[:], False, OPT["su"] == "a", ["P12M", "OK00", "OK01"], ["B0.z"])
+        if OPT["su"] == "a":
+            step("su1")
+            act(T.DW[:], z, ["B0.z"], ["DW"], F.Relu, scale=-1.0)
+            step("su2")
+            mm(z, T.IDF[:], wd, True, False, ["IDF", wdk[t - 1]], ["B0.z"])
+            mm(z, T.NID[:], T.DW[:], False, True, ["NID", "DW"], ["B0.z"])
+            act(wd, z, ["B0.z"], [wdk[t - 1]])
+        else:
+            mm(z, T.IDF[:], wd, False, True, ["IDF", wdk[t - 1]], ["B0.z"])
+            step("su1")
+            tt(wd, wd, z, A.min, [wdk[t - 1], "B0.z"], [wdk[t - 1]])
 
     def parity():
-        o = T.B0[:, 272:273]
+        o, pc = T.B7[0:1, 256:384], T.COL[0:1, 7:8]
+        step("par1")
+        mm(o, T.QRT[0:1, 0:1], T.ONES[0:1, 0:H], True, False, ["QRT", "ONES"], ["B7.hi"])
         for h in (0, 1):
-            mm(o, T.PAR[:], T.SACC[:, h:h + 1], h == 0, h == 1, ["PAR", "SACC%d" % h], ["B0.par"])
-        act(col("PB"), o, ["B0.par"], ["PB"], bias=-0.25, scale=-0.015625)
-        act(col("PC"), col("PB"), ["PB"], ["PC"], bias=MAGIC)
-        act(col("PC"), col("PC"), ["PC"], ["PC"], bias=MAGIC, scale=-1.0)
-        act(col("ODD"), col("PB"), ["PB", "PC"], ["ODD"], F.Identity, bias=col("PC"))
-        act(T.LIMT[:], T.EIGHT[:], ["EIGHT", "ODD"], ["LIMT"], bias=20.0, scale=col("ODD"))
+            mm(o, T.SACC[:, h:h + 1], T.PAR[:], False, h == 1, ["PAR", "SACC%d" % h], ["B7.hi"])
+        act(pc, T.B7[0:1, 256:257], ["B7.hi"], ["PC"], bias=MAGIC)
+        step("par2")
+        act(pc, pc, ["PC"], ["PC"], bias=1024.0 * MAGIC, scale=-1024.0)
+        step("par3")
+        act(T.LIM[0:1, :], o, ["B7.hi", "PC"], ["LIM"], F.Identity, bias=pc, scale=1024.0)
 
-    BA, BG, BU = [T.B1, T.B2], [T.B3, T.B4], [T.B5, T.B6]
+    BA = [T.B1, T.B2]
 
     def one_round(t):
         c = t - 1
         cx = "CX%d" % (t & 1)
-        L0 = c * Q
+        L0 = 2 * c * Q
         dst = cores[(rank + 1 + c % (n - 1)) % n]
         last = t == NT
-        land = [T.LAND[:, L0 + H * h:L0 + H * h + H] for h in (0, 1)]
-        snd = [T.SND[:, L0 + H * h:L0 + H * h + H] for h in (0, 1)]
+        plan = OPT["score"][c]
+        share = [j for j in range(8) if plan[j] == "s"]
         cap = [T.CAP[:, c + 1024 * h:1024 * h + 1024:8] for h in (0, 1)]
         lk = ["LAND%d%d" % (t, h) for h in (0, 1)]
         sk = ["SND%d%d" % (t, h) for h in (0, 1)]
 
-        def low_bits(h, src, key, mask):
-            cp(T.XI[:, half(h, 8)], src, [key], ["XI%d" % h])
-            ts(T.XI2[:, half(h, 8)], T.XI[:, half(h, 8)], mask, None, A.bitwise_and, None, ["XI%d" % h], ["XJ%d" % h])
+        def msg(buf, lo, hi, by=1):
+            if OPT["pack"]:
+                return buf[:, L0 + lo:L0 + hi:by]
+            return buf[:, L0 + 2 * lo + 1:L0 + 2 * hi:2 * by]
 
-        def largest_key(h, lo, mask, out, key):
-            scan(T.KS[:, half(h)], T.MB[:, 0:H], BA[h][:, lo:lo + H], A.min, A.max, ["MB", "B%d.k" % (1 + h)], ["KS%d" % h])
-            low_bits(h, T.KS[:, H * h + 15:H * h + H:16], "KS%d" % h, mask)
-            tt(out[:, half(h)], T.XI2[:, half(h, 8)].indirect(T.OFFC[:, 0:8]), T.DELB[:, 0:H], A.mult, ["XJ%d" % h, "OFFC", "DELB"], [key], GATHER)
+        land = [msg(T.LAND, H * h, H * h + H) for h in (0, 1)]
+        snd = [msg(T.SND, H * h, H * h + H) for h in (0, 1)]
+
+        def low_bits(at, m, name, src, keys, mask):
+            step(name[0] + "i" + name[1])
+            cp(T.XI[:, at:at + m], src, keys, ["XI" + name])
+            step(name[0] + "j" + name[1])
+            ts(T.XI2[:, at:at + m], T.XI[:, at:at + m], mask, None, A.bitwise_and, None, ["XI" + name], ["XJ" + name])
+
+        def largest_key(hs, src, keys, at, name, mask, out, ok):
+            lo, hi, m, ks = H * hs[0], H * hs[-1] + H, 8 * len(hs), ["KS%d" % h for h in hs]
+            step(name[0] + "s" + name[1])
+            scan(T.KS[:, lo:hi], T.MB[:, 0:hi - lo], src, A.min, A.max, ["MB"] + keys, ks)
+            low_bits(at, m, name, T.KS[:, lo + 15:hi:16], ks, mask)
+            step(name[0] + "x" + name[1])
+            tt(out[:, lo:hi], T.XI2[:, at:at + m].indirect(T.OFFC[:, 0:m]), T.DELB[:, 0:hi - lo], A.mult, ["XJ" + name, "OFFC", "DELB"], ok, GATHER)
+
+        def first_rows():
+            d = T.B0[:, 0:256]
+            if t == 1:
+                for h in (0, 1):
+                    step("r0" + "bc"[h])
+                    mm(T.B0[:, half(h)], T.NID[:], cap[h], True, False, ["NID", "CAP"], ["B0.d"])
+                    mm(T.B0[:, half(h)], T.ID[:], aside(h), False, True, ["ID"] + p0(h), ["B0.d"])
+                    relu(OPT["r0"], T.R0[:, half(h)], T.B0[:, half(h)], 0.0, ["B0.d"], ["R0%d" % h])
+                return
+            step("r0a")
+            mm(d, T.NID[:], T.CAP[:, c:2048:8], True, False, ["NID", "CAP"], ["B0.d"])
+            step("r0b")
+            mm(d, T.ID[:], T.PK[:, P0:P0 + Q], False, True, ["ID"] + p0(0) + p0(1), ["B0.d"])
+            relu(OPT["r0"], T.R0[:], d, 0.0, ["B0.d"], ["R00", "R01"])
 
         def sums(h):
             b, key = BA[h], "B%d.k" % (1 + h)
-            clip = [j for j in CLIP if j // 4 == h and t > 1]
+            clip = [j for j in range(8 - OPT["clip"][c], 8) if j // 4 == h]
             cut = H - 32 * len(clip)
-            mm(b[:, 0:H], T.ONES[0:1, 0:H], T.KC[0:1, :], True, False, ["KC", "ONES"], [key])
-            mm(b[0:cut, 0:H:16], T.CAP[:, c + 1024 * h:1024 * h + 8 * cut:8], T.B16[:], False, False, ["B16", "CAP"], [key])
-            d, dk = BU[h][:, 384:512], "B%d.d" % (5 + h)
-            mm(d, T.NID[:], cap[h], True, False, ["NID", "CAP"], [dk])
-            mm(d, T.ID[:], aside(h), False, True, ["ID", "P0%d" % h], [dk])
-            act(T.R0[:, half(h)], d, [dk], ["R0%d" % h], F.Relu)
-            cxk, cmk = [cx + "k%d" % k for k in range(16)], ["CM%d" % j for j in range(4 * h, 4 * h + 4)]
-            s = slice(2048 * h, 2048 * h + 16 * cut)
-            scan(T.CM[:, s], T[cx][:, s], T.PK[:, s], A.min, A.max, cxk + pk(h)[:cut // 32], cmk[:cut // 32])
-            for j in clip:
-                bn = (3, 4)[7 - j]
-                o, ok = T["B%d" % bn][:], whole_bank[bn]
-                mm(o, T.NID[:], T[cx][:, half(j, 512)], True, False, ["NID"] + cxk, ok)
-                mm(o, T.ID[:], T.PK[:, half(j, 512)], False, True, ["ID", "PK%d" % j], ok)
-                act(T.CM[:, half(j, 512)], o, ok, ["CM%d" % j], F.Relu)
+            step("kc%d" % h)
+            mm(b[:, 0:2 * H], T.ONES[0:1, 0:H], T.KC[0:1, :], True, False, ["KC", "ONES"], [key])
+            cxk, cmk = [cx + "k%d" % k for k in range(16)] + [cx + "h%d" % h], ["CM%d" % j for j in range(4 * h, 4 * h + 4)]
+            if cut:
+                mm(b[0:cut, 0:2 * H:16], T.CAP[:, c + 1024 * h:1024 * h + 8 * cut:8], T.B16[:], False, False, ["B16", "CAP"], [key])
+                s = slice(2048 * h, 2048 * h + 16 * cut)
+                step("cm%d" % h)
+                scan(T.CM[:, s], T[cx][:, s], T.PK[:, s], A.min, A.max, cxk + pk(h)[:cut // 32], cmk[:cut // 32])
+            if clip:
+                for y, j in enumerate(clip):
+                    step("clipa%d" % y)
+                    if OPT["clipw"] == "cx":
+                        mm(bank(3 + y, 0, 512), T.NID[:], T[cx][:, half(j, 512)], True, False, ["NID"] + cxk, whole[3 + y])
+                    else:
+                        for k in range(16):
+                            mm(bank(3 + y, k, 512, 16), T.NID[:], T.CAP[:, c + 256 * j:256 * (j + 1):8], k == 0, False, ["NID", "CAP"], whole[3 + y])
+                for x in range(0, len(clip), 2):
+                    step("clipb%d" % x)
+                    two = list(enumerate(clip))[x:x + 2]
+                    for y, j in two:
+                        mm(bank(3 + y, 0, 512), T.ID[:], T.PK[:, half(j, 512)], False, True, ["ID", "PK%d" % j], whole[3 + y])
+                    act(T.CM[:, 512 * two[0][1]:512 * (two[-1][1] + 1)], bank(3 + x, 0, 512 * len(two)), sum((whole[3 + y] for y, j in two), []),
+                        ["CM%d" % j for y, j in two], F.Relu)
+            step("sum%d" % h)
             for k in range(1, 16):
-                mm(b[:, k:H:16], T.CM[:, 2048 * h + k:2048 * h + 2048:16], T.B16[:], False, False, ["B16"] + cmk, [key])
-            mm(b[:, 0:H:16], T.R0[:, half(h)], T.B16[:], False, True, ["B16", "R0%d" % h], [key])
-            act(row0(h), aside(h), ["P0%d" % h], pk(h))
+                mm(b[:, k:2 * H:16], T.CM[:, 2048 * h + k:2048 * h + 2048:16], T.B16[:], False, False, ["B16"] + cmk, [key])
+            mm(b[:, 0:2 * H:16], T.R0[:, half(h)], T.B16[:], False, True, ["B16", "R0%d" % h], [key])
+
+        def running(h):
+            m, lo, at = 2048 // OPT["pieces"], 2048 * h, WIN * h
+            for x in range(OPT["pieces"]):
+                a, z = m * x, m * x + m
+                step("bs%d%d" % (h, x))
+                scan(T.BS[:, at + 14 + z:at + 14 + a:-1], T.PK[:, lo + z - 1:(lo + a - 1 if lo + a else None):-1], T.SEG[:, 1:m + 1], A.max, A.min,
+                     ["SEG"] + pk(h)[a // 512:(z + 511) // 512], ["BS%d%d" % (h, x)])
+            step("rest%d" % h)
+            cp(row0(h), aside(h), p0(h), pk(h), OPT["restore"][h])
+            for x in range(OPT["pieces"]):
+                a, z = m * x, m * x + m
+                step("fs%d%d" % (h, x))
+                scan(T.FS[:, at + 1 + a:at + 1 + z], T.PK[:, lo + a:lo + z], T.SEG[:, 1:m + 1], A.max, A.min,
+                     ["SEG"] + pk(h)[a // 512:(z + 511) // 512], ["FS%d%d" % (h, x)])
 
         def messages(h):
-            b, s = BA[h], half(h, 2048)
+            b, at = BA[h], WIN * h
+            fs, bs = (["%s%d%d" % (x, h, y) for y in range(OPT["pieces"])] + ["ENDS"] for x in ("FS", "BS"))
+            cm, ck, gk, vk, y0, y1 = T["CMP%d" % h], "B%d.c" % (5 + h), "B%d.g" % (3 + h), "B%d.v" % (5 + h), "Y0%d" % h, "Y1%d" % h
+            room, v0, v1 = bank(5 + h, 0, H), bank(3 + h, 0, H), bank(5 + h, H, 3 * H)
+            ya, yb = (T.TWO[:, 256 * h + j:256 * h + 256:2] for j in (0, 1))
+            step("cap%d" % h)
+            mm(room, T.ID[:], cap[h], True, False, ["ID", "CAP"], [ck])
+            mm(bank(5 + h, 3 * H, 4 * H), T.ID[:], aside(h), False, True, ["ID"] + p0(h), [ck])
+            step("m0%d" % h)
+            tt(T.M0[:, half(h)], T.BS[:, at + 16:at + 2064:16], bank(5 + h, 3 * H, 4 * H), A.max, bs + [ck], ["M0%d" % h])
+            step("lim%d" % h)
+            mm(v0, T.LIM[0:2, :], T.ONES[0:2, 0:H], True, False, ["LIM", "ONES"], [gk])
+            step("cmp%d0" % h)
+            tt(cm[:, 0:H], T.M0[:, half(h)], room, A.is_gt, ["M0%d" % h, ck], ["CMP%d0" % h])
+            mm(v0, T.NBO[:], cm[:, 0:H], False, True, ["NBO", "CMP%d0" % h], [gk])
+            step("ok%d" % h)
+            act(T.OK0[:, half(h)], v0, [gk], ["OK0%d" % h, "SACC%d" % h], F.Relu, accum=T.SACC[:, h:h + 1])
+            act(v0, v0, [gk], [gk], F.Relu)
+            step("mn%d" % h)
+            tt(yb, T.M0[:, half(h)], v0, A.min, ["M0%d" % h, gk], [y1])
             o, ok = b[:, 384:392], "B%d.kl" % (1 + h)
+            step("klc%d" % h)
             mm(o, T.KR16[0:1, :], T.ONES[0:1, 0:8], True, False, ["KR16", "ONES"], [ok])
             mm(o, T.ONES[0:1, 0:H], T.IO256[0:1, 0:8], False, False, ["IO256", "ONES"], [ok])
-            largest_key(h, 0, 15, T.XA, "XA%d" % h)
+            ks = 256 * h
+            step("ks%d" % h)
+            scan(T.KS[:, ks:ks + 256], T.MB[:], b[:, 0:256], A.min, A.max, ["MB", "B%d.k" % (1 + h)], ["KS%d" % h])
+            step("ki%d" % h)
+            tt(T.XF[:, half(h, 8)], T.KS[:, ks + 15:ks + H:16], T.KS[:, ks + H + 15:ks + 256:16], A.subtract, ["KS%d" % h], ["XF%d" % h])
+            step("kx%d" % h)
+            tt(T.XA[:, half(h)], T.XF[:, half(h, 8)].indirect(T.OFFC[:, 0:8]), T.DELB[:, 0:H], A.mult, ["XF%d" % h, "OFFC", "DELB"], ["XA%d" % h], GATHER)
             mm(o, T.XA[:, half(h)], T.NB8[:], False, True, ["XA%d" % h, "NB8"], [ok])
             kl = T.KL[:, half(h, 8)]
+            step("kl%d" % h)
             cp(kl, o, [ok], ["KL%d" % h])
+            step("xs%d" % h)
+            gather(OPT["xs"], T.XS[:, half(h)], T.FS[:, at:at + 2048], kl, fs + ["KL%d" % h], ["XS%d" % h])
+            step("m1%d" % h)
+            tt(ya, T.BS[:, at + 16:at + 2064].indirect(kl), T.XS[:, half(h)], A.max, bs + ["KL%d" % h, "XS%d" % h], [y0], GATHER)
+            step("lin%d" % h)
+            mm(v1, T.LIM[0:2, :], T.ALT[0:2, :], True, False, ["LIM", "ALT"], [vk])
+            step("cmp%d1" % h)
+            tt(cm[:, H:2 * H], ya, room, A.is_gt, [y0, ck], ["CMP%d1" % h])
+            mm(bank(5 + h, H + 1, 3 * H, 2), T.NBO[:], cm[:, H:2 * H], False, True, ["NBO", "CMP%d1" % h], [vk])
+            out = slice(L0 + 256 * h, L0 + 256 * h + 256)
+            step("snd%d" % h)
+            scan(T.SND[:, out], v1, T.TWO[:, half(h, 256)], A.min, A.max, [vk, y0, y1], [sk[h]])
+            put("p", (T.LAND[:, out], T.SND[:, out], "arr%d%d" % (t, h), dst), [sk[h]], [lk[h]], 300.0, FIRST if t == 1 and h == 0 else LAT)
+
+        def messages_old(h):
+            b, s = BA[h], half(h, 2048)
+            o, ok = b[:, 384:392], "B%d.kl" % (1 + h)
+            step("klc%d" % h)
+            mm(o, T.KR16[0:1, :], T.ONES[0:1, 0:8], True, False, ["KR16", "ONES"], [ok])
+            mm(o, T.ONES[0:1, 0:H], T.IO256[0:1, 0:8], False, False, ["IO256", "ONES"], [ok])
+            largest_key([h], b[:, 0:H], ["B%d.k" % (1 + h)], 16 + 8 * h, "k%d" % h, 15, T.XA, ["XA%d" % h])
+            mm(o, T.XA[:, half(h)], T.NB8[:], False, True, ["XA%d" % h, "NB8"], [ok])
+            kl = T.KL[:, half(h, 8)]
+            step("kl%d" % h)
+            cp(kl, o, [ok], ["KL%d" % h])
+            step("xs%d" % h)
             gather("a", T.XS[:, half(h)], T.PK[:, s], kl, pk(h) + ["KL%d" % h], ["XS%d" % h])
-            scatter(T.PK[:, s], kl, aside(h), ["P0%d" % h, "KL%d" % h], pk(h))
-            act(row0(h), T.XS[:, half(h)], ["XS%d" % h], pk(h))
+            step("sw%d" % h)
+            scatter(T.PK[:, s], kl, aside(h), p0(h) + ["KL%d" % h], pk(h))
+            step("row%d" % h)
+            cp(row0(h), T.XS[:, half(h)], ["XS%d" % h], pk(h), OPT["row0"])
             lo = 2048 * h
-            s = slice(lo + 2047, lo - 1 if lo else None, -1)
-            scan(T.FB[:, s], T.SEG[:], T.PK[:, s], A.mult, A.max, ["SEG"] + pk(h), ["FB%d" % h])
+            fb, s = "FB%d" % h, slice(lo + 2047, lo - 1 if lo else None, -1)
+            step("fb%d" % h)
+            scan(T.FB[:, s], T.SEG[:], T.PK[:, s], A.min, A.max, ["SEG"] + pk(h), [fb])
             m = [T.FB[:, lo + j:lo + 2048:16] for j in (0, 1)]
-            cm, fb = T["CMP%d" % h], "FB%d" % h
-            if h == 0:
-                act(T.B0[:, 0:256], T.CAP[:, c:2048:8], ["CAP"], ["B0.cap"])
-            for j in (0, 1):
-                tt(cm[:, half(j)], m[j], T.B0[:, half(h)], A.is_gt, [fb, "B0.cap"], ["CMP%d%d" % (h, j)])
-            bu, mk, dk, gk, vk = BU[h], "B%d.m" % (5 + h), "B%d.d" % (5 + h), "B%d.g" % (3 + h), "B%d.v" % (1 + h)
-            v0, v1, d = BG[h][:, 0:H], b[:, 256:384], bu[:, 384:512]
-            for j, (o, ok) in enumerate(((v0, gk), (v1, vk))):
-                mm(o, T.LIMT[:], T.ONES[:, 0:H], True, False, ["LIMT", "ONES"], [ok])
-                mm(o, T.NBO[:], cm[:, half(j)], False, True, ["NBO", "CMP%d%d" % (h, j)], [ok])
-            act(bu[:, 0:H], v0, [gk], [mk], F.Relu)
-            tt(T.XS[:, half(h)], m[1], v1, A.min, [fb, vk], ["XS%d" % h])
-            tt(bu[:, 0:H], m[0], bu[:, 0:H], A.min, [fb, mk], [mk])
-            tt(snd[h], T.XS[:, half(h)], bu[:, 0:H], A.max, ["XS%d" % h, mk], [sk[h]])
-            act(T.SG[:, half(h)], v0, [gk], ["SG%d" % h, "SACC%d" % h], F.Sign, accum=T.SACC[:, h:h + 1])
-            mm(d, T.ID[:], cap[h], True, False, ["ID", "CAP"], [dk])
-            mm(d, T.NID[:], snd[h], False, True, ["NID", sk[h]], [dk])
-            calls.append(("p", (land[h], snd[h], "arr%d%d" % (t, h), dst), [sk[h]], [lk[h]], 300.0, FIRST if t == 1 and h == 0 else LAT))
-            act(T.SL[:, c + 1024 * h:1024 * h + 1024:8], d, [dk], ["SL%d" % h], F.Relu)
+            cm, ck, gk, vk = T["CMP%d" % h], "B%d.c" % (5 + h), "B%d.g" % (3 + h), "B%d.v" % (1 + h)
+            signs = OPT["cmp"][h] == "a"
+            step("cap%d" % h)
+            if signs:
+                for j in (0, 1):
+                    mm(bank(5 + h, H * j, H * j + H), T.NID[:], cap[h], j == 0, False, ["NID", "CAP"], [ck])
+            else:
+                mm(bank(5 + h, 0, H), T.ID[:], cap[h], True, True, ["ID", "CAP"], [ck])
+            verdicts = ((bank(3 + h, 0, H), gk), (b[:, 256:384], vk))
+            step("lim%d" % h)
+            for o, ok in verdicts:
+                mm(o, T.LIM[0:3 if signs else 2, :], T.ONES[0:3 if signs else 2, 0:H], True, False, ["LIM", "ONES"], [ok])
+            if signs:
+                step("cmp%d0" % h)
+                for j in (0, 1):
+                    mm(bank(5 + h, H * j, H * j + H), T.ID[:], m[j], False, j == 1, ["ID", fb], [ck])
+                act(cm[:], bank(5 + h, 0, 256), [ck, "HALF"], ["CMP%d0" % h, "CMP%d1" % h], F.Sign, bias=col("HALF"))
+            for j, (o, ok) in enumerate(verdicts):
+                step("cmp%d%d" % (h, 1 if signs else j))
+                if not signs:
+                    tt(cm[:, half(j)], m[j], bank(5 + h, 0, H), A.is_gt, [fb, ck], ["CMP%d%d" % (h, j)])
+                mm(o, T["NBO2" if signs else "NBO"][:], cm[:, half(j)], False, True, ["NBO", "NBO2", "CMP%d%d" % (h, j)], [ok])
+            step("ok%d" % h)
+            act(T.OK0[:, 256 * h + 1:256 * h + 256:2], verdicts[0][0], [gk], ["OK0%d" % h, "SACC%d" % h], F.Relu, accum=T.SACC[:, h:h + 1])
+            step("mn%d" % h)
+            tt(T.FB[:, lo + 8:lo + 2048:16], m[1], verdicts[1][0], A.min, [fb, vk], [fb])
+            out = slice(L0 + 256 * h, L0 + 256 * h + 256)
+            step("snd%d" % h)
+            if OPT["pack"]:
+                out = slice(L0 + H * h, L0 + H * h + H)
+                scan(T.TWO[:, half(h, 256)], T.OK0[:, half(h, 256)], T.FB[:, lo:lo + 2048:8], A.min, A.max, [fb, "OK0%d" % h], ["TWO%d" % h])
+                step("pk%d" % h)
+                cp(T.SND[:, out], T.TWO[:, 256 * h + 1:256 * h + 256:2], ["TWO%d" % h], [sk[h]], OPT["pack"])
+            else:
+                scan(T.SND[:, out], T.OK0[:, half(h, 256)], T.FB[:, lo:lo + 2048:8], A.min, A.max, [fb, "OK0%d" % h], [sk[h]])
+            put("p", (T.LAND[:, out], T.SND[:, out], "arr%d%d" % (t, h), dst), [sk[h]], [lk[h]], 300.0, FIRST if t == 1 and h == 0 else LAT)
+
+        def room_left():
+            step("sla")
+            mm(T.B0[:, 0:256], T.ID[:], T.CAP[:, c:2048:8], True, False, ["ID", "CAP"], ["B0.d"])
+            for h in (0, 1):
+                step("slb%d" % h)
+                mm(T.B0[:, half(h)], T.NID[:], snd[h], False, h == 1, ["NID", sk[h]], ["B0.d"])
+            step("sl")
+            relu(OPT["sl"], T.SL[:, c:2048:8], T.B0[:, 0:256], 0.0, ["B0.d"], ["SL"])
 
         def candidates(h):
             ul, key = BA[h][:, 392:400], "B%d.u" % (1 + h)
+            step("uc%d" % h)
             mm(ul, T.KR[0:1, :], T.C37[0:1, 0:8], True, False, ["KR", "C37"], [key])
             mm(ul, T.C37[0:1, :], T.I16B[0:1, half(h, 8)], False, False, ["I16B", "C37"], [key])
+            step("u%d" % h)
             for r in range(16):
-                mm(ul, T.W16[:, 15 - r:143 - r], T.LAND[:, L0 + H * h + r:L0 + H * h + H:16], False, r == 15, ["W16", lk[h]], [key])
-            low_bits(h, ul, key, 4095)
-            cp(T.UL[:, half(h, 8)], T.XI2[:, half(h, 8)], ["XJ%d" % h], ["UL%d" % h])
+                mm(ul, T.W16[:, 15 - r:143 - r], msg(T.LAND, H * h + r, H * h + H, 16), False, r == 15, ["W16", lk[h]], [key])
+            if OPT["um"][h] == "a":
+                step("ui%d" % h)
+                act(T.UH[:], ul, [key], ["UH"], bias=127.5001220703125, scale=1.0 / 4096)
+                o = bank(6, 0, 8)
+                step("ud%d" % h)
+                mm(o, T.KR[0:1, :], T.C37[0:1, 0:8], True, False, ["KR", "C37"], ["B6.c"])
+                mm(o, T.C37[0:1, :], T.I16B[0:1, half(h, 8)], False, False, ["I16B", "C37"], ["B6.c"])
+                mm(o, T.CFAR[0:1, :], T.FOUR[0:1, :], False, False, ["CFAR", "FOUR"], ["B6.c"])
+                step("ue%d" % h)
+                for r in range(16):
+                    mm(o, T.W16[:, 15 - r:143 - r], msg(T.LAND, H * h + r, H * h + H, 16), False, False, ["W16", lk[h]], ["B6.c"])
+                step("uj%d" % h)
+                mm(o, T.N12M[:], T.UH[:], False, True, ["N12M", "UH"], ["B6.c"])
+                step("ul%d" % h)
+                cp(T.UL[:, half(h, 8)], o, ["B6.c"], ["UL%d" % h])
+            else:
+                low_bits(8 * h, 8, "u%d" % h, ul, [key], 4095)
+                step("ul%d" % h)
+                cp(T.UL[:, half(h, 8)], T.XI2[:, half(h, 8)], ["XJu%d" % h], ["UL%d" % h])
+            if OPT["pf"] == "v":
+                step("pf%d" % h)
+                gather("v", T.PH[:, half(h)], T.TAB[:], T.UL[:, half(h, 8)], tab + ["UL%d" % h], ["PF%d" % h])
+                step("p16%d" % h)
+                cp(T.P16[:, half(h)], T.PH[:, half(h)], ["PF%d" % h], ["P16%d" % h])
+                return
+            step("p16%d" % h)
             gather("v", T.P16[:, half(h)], T.TAB[:], T.UL[:, half(h, 8)], tab + ["UL%d" % h], ["P16%d" % h])
+            step("pf%d" % h)
             gather("a", T.PF[:, half(h)], T.TAB[:], T.UL[:, half(h, 8)], tab + ["UL%d" % h], ["PF%d" % h])
 
-        def wide(j):
-            m = min(x for x in list(WIDE) + list(SHARE) + [8] if x > j) - j
-            h, src, mx = j // 4, T.LAND[:, L0 + 32 * j:L0 + 32 * (j + m)], ["MX%d" % x for x in range(j, j + m)]
-            if WIDE[j] == "v":
-                cp(T.SP[:, 1024 * h:1024 * h + 512 * m:16], src, [lk[h]], ["SP%d" % h])
-                scan(T.MX[:, 512 * j:512 * (j + m)], T.SEG[:, 0:512 * m], T.SP[:, 1024 * h:1024 * h + 512 * m], A.mult, A.max, ["SEG", "SP%d" % h], mx)
-            elif WIDE[j] == "a":
-                gather("a", T.MX[:, 512 * j:512 * (j + m)], src, T.OFFC[:, 0:32 * m], [lk[h], "OFFC"], mx)
-            else:
+        def scores(h):
+            sl, mine = T.SL[:, 0:2048], range(4 * h, 4 * h + 4)
+            for j, m in runs([j for j in mine if plan[j] == "s"], 2):
+                bn, s = (3, 5)[[x[0] for x in runs(share, 2)].index(j) & 1], slice(512 * j, 512 * (j + m))
+                mx = ["MX%d" % (j + y) for y in range(m)]
+                step("shw%d" % j)
+                for y in range(m):
+                    for k in range(16):
+                        mm(bank(bn + y, k, 512, 16), T.ID[:], msg(T.LAND, 32 * (j + y), 32 * (j + y + 1)), k == 0, False, ["ID", lk[h]], whole[bn + y])
+                step("shg%d" % j)
+                gather("a", T.MX[:, s], sl, T.P16[:, 32 * j:32 * (j + m)], ["SL", "P16%d" % h], mx)
+                step("shr%d" % j)
+                for y in range(m):
+                    mm(bank(bn + y, 0, 512), T.NID[:], T.MX[:, half(j + y, 512)], False, True, ["NID", mx[y]], whole[bn + y])
+                act(T.SC[:, s], bank(bn, 0, 512 * m), sum((whole[bn + y] for y in range(m)), []), ["SC%d" % (j + y) for y in range(m)], F.Relu)
+            for j, m in runs([j for j in mine if plan[j] == "v"], OPT["wm"]):
+                lo, sp = 512 * (j % 4), ["SP%d" % ((j + y) % 4) for y in range(m)]
+                step("sp%d" % j)
+                cp(T.SP[:, lo:lo + 512 * m:16], msg(T.LAND, 32 * j, 32 * (j + m)), [lk[h]], sp, OPT["sp"])
+                step("wd%d" % j)
+                scan(T.MX[:, 512 * j:512 * (j + m)], T.SEG[:, 0:512 * m], T.SP[:, lo:lo + 512 * m], A.min, A.max, ["SEG"] + sp,
+                     ["MX%d" % (j + y) for y in range(m)])
+            for j, m in runs([j for j in mine if plan[j] == "p"], 4):
                 for k in range(16):
-                    gcopy(T.MX[:, 512 * j + k:512 * (j + m):16], src, [lk[h]], ["MXk%d" % k])
+                    step("gw%d%s" % (j, "abcd"[k // 4]))
+                    cp(T.MX[:, 512 * j + k:512 * (j + m):16], msg(T.LAND, 32 * j, 32 * (j + m)), [lk[h]], ["MX%dk%d" % (j + y, k) for y in range(m)], "p")
+            for j, m in runs([j for j in mine if plan[j] != "s"], OPT["vm"]):
+                s = slice(512 * j, 512 * (j + m))
+                mx = sum((["MX%d" % x] + ["MX%dk%d" % (x, k) for k in range(16)] for x in range(j, j + m)), [])
+                step("sc%d" % j)
+                tt(T.SC[:, s], sl.indirect(T.P16[:, 32 * j:32 * (j + m)]), T.MX[:, s], A.min, ["SL", "P16%d" % h] + mx,
+                   ["SC%d" % (j + y) for y in range(m)], GATHER)
 
-        def scores(j):
-            h, s = j // 4, half(j, 512)
-            sl, off, r = T.SL[:, 0:2048], T.P16[:, half(j, 32)], ["SL0", "SL1", "P16%d" % h]
-            if j in SHARE:
-                b = 3 + SHARE.index(j) % 2
-                o, k = T["B%d" % b], whole_bank[b]
-                for m in range(16):
-                    mm(o[:, m:512:16], T.ID[:], T.LAND[:, L0 + 32 * j:L0 + 32 * j + 32], m == 0, False, ["ID", lk[h]], k)
-                gather("a", T.MX[:, s], sl, off, r, ["MX%d" % j])
-                mm(o[:], T.NID[:], T.MX[:, s], False, True, ["NID", "MX%d" % j], k)
-                act(T.SC[:, s], o[:], k, ["SC%d" % j], F.Relu)
-                return
-            if WIDE.get(j, "p") != "p":
-                wide(j)
-            mx = ["MXk%d" % k for k in range(16)] if WIDE[max(x for x in WIDE if x <= j)] == "p" else ["MX%d" % j]
-            tt(T.SC[:, s], sl.indirect(off), T.MX[:, s], A.min, r + mx, ["SC%d" % j], GATHER)
+        def keys(h, b, at, key, first, final):
+            o = b[:, at:at + H]
+            every = key + [x + "s%d" % y for x in key[:2] for y in range(4)]
+            parts = []
+            for kind in (True, False):
+                for j, m in runs([j for j in range(4 * h, 4 * h + 4) if (plan[j] == "s") == kind], OPT["pm"]):
+                    j %= 4
+                    parts += [(j, m, kind)] if j == 0 or m == 1 or j == 2 else [(j, 1, kind), (j + 1, m - 1, kind)]
+            pf, ident, ik = (T.PH, T.IDH, "IDH") if OPT["pf"] == "v" else (T.PF, T.IDF, "IDF")
 
-        def parents(h):
-            b, key = BA[h], "B%d.k" % (1 + h)
-            o = b[:, H:2 * H]
-            shared = [j for j in SHARE if j // 4 == h]
+            def nodes(j, m, end):
+                mm(b[32 * j:32 * (j + m), at:at + H], pf[:, H * h + 32 * j:H * h + 32 * (j + m)], ident[:], False, end, ["PF%d" % h, ik], key if end else key[:1])
+            step("pc%d" % h)
+            mm(o, T.ONES[:, 0:H], T.NEG[:], first, False, ["NEG", "ONES"], key if first else key[:1])
+            mm(o, T.ONES[0:1, 0:H], T.KC2[0:1, :], False, False, ["KC2", "ONES"], key[:1])
+            for j, m, kind in parts:
+                if kind:
+                    mm(b[32 * j:32 * (j + m), at:at + H], msg(T.LAND, H * h + 32 * j, H * h + 32 * (j + m)), T.BW32K[:], False, False, ["BW32K", lk[h]], key[:1])
+            step("pn%d" % h)
+            plain = [j for j in range(4) if plan[4 * h + j] != "s"]
+            for j, m in runs(plain, 4):
+                for x in ([(j, m)] if j == 0 or m == 1 or j == 2 else [(j, 1), (j + 1, m - 1)]):
+                    nodes(x[0], x[1], False)
+            for x, (j, m, kind) in enumerate(parts):
+                lo, hi = 32 * j, 32 * (j + m)
+                wk, sk2 = "NB32K" if kind else "B32K", [key[0] + "s%d" % y for y in range(j, j + m)]
+                step("ps%d" % (4 * h + j))
+                for k in range(16):
+                    mm(b[lo:hi, at + k:at + H:16], T.SC[:, 2048 * h + 16 * lo + k:2048 * h + 16 * hi:16], T[wk][:], False, False,
+                       [wk, key[0]] + ["SC%d" % y for y in range(4 * h + j, 4 * h + j + m)], sk2)
+                if kind:
+                    mm(b[lo:hi, at:at + H], pf[:, H * h + lo:H * h + hi], ident[:], False, False, ["PF%d" % h, ik, key[0]], sk2)
+            if final:
+                mm(b[:, at:at + 2], T.ONES[0:1, 0:H], T.KC[0:1, H:H + 2], False, True, ["ONES", "KC"], every)
 
-            def nodes():
-                mm(o, T.PF[:, half(h)], T.IDF[:], False, bool(shared), ["PF%d" % h, "IDF"], [key])
-            mm(o, T.ONES[:, 0:H], T.NEG[:], True, False, ["NEG", "ONES"], [key])
-            mm(o, T.ONES[0:1, 0:H], T.KC2[0:1, :], False, False, ["KC2", "ONES"], [key])
-            if not shared:
-                nodes()
-                parts = [(0, H, T.B32K, "B32K")]
+        def parents(hs):
+            if len(hs) == 2:
+                key = ["B1.p0", "B1.p1", "B1.k"]
+                keys(0, T.B1, H, key, True, False)
+                keys(1, T.B1, 2 * H, key[1::-1], False, True)
+                src = T.B1[:, H:3 * H]
             else:
-                lo = 32 * (shared[0] % 4)
-                hi = lo + 32 * len(shared)
-                mm(b[lo:hi, H:2 * H], T.LAND[:, L0 + H * h + lo:L0 + H * h + hi], T.BW32K[:], False, False, ["BW32K", lk[h]], [key])
-                parts = [x for x in ((0, lo, T.B32K, "B32K"), (hi, H, T.B32K, "B32K"), (lo, hi, T.NB32K, "NB32K")) if x[0] < x[1]]
-            for lo, hi, w, wk in parts:
-                for m in range(16):
-                    mm(b[lo:hi, H + m:2 * H:16], T.SC[:, 2048 * h + 16 * lo + m:2048 * h + 16 * hi:16], w[:], False, m == 15 and not shared,
-                       [wk] + ["SC%d" % j for j in range(4 * h + lo // 32, 4 * h + hi // 32)], [key])
-            if shared:
-                nodes()
-            largest_key(h, H, 2047, T.XW, "XW%d" % h)
-            lv, lvk, far, fk = T.B0[:, 256 + 8 * h:264 + 8 * h], "B0.lv%d" % h, T.B0[:, 288 + 8 * h:296 + 8 * h], "B0.far%d" % h
-            mm(lv, T.XW[:, half(h)], T.BOH[:], True, True, ["XW%d" % h, "BOH"], [lvk])
-            cp(T.LV[:, half(h, 8)], lv, [lvk], ["LV%d" % h])
-            gather("v", T.VB[:, half(h)], T.IO2K[:], T.LV[:, half(h, 8)], ["IO2K", "LV%d" % h], ["VB%d" % h])
-            mm(far, T.CFAR[0:1, :], T.ONES[0:1, 0:8], True, False, ["CFAR", "ONES"], [fk])
-            mm(far, T.XW[:, half(h)], T.BOH[:], False, True, ["XW%d" % h, "BOH"], [fk])
+                key = ["B%d.p" % (1 + hs[0]), "B%d.k" % (1 + hs[0])]
+                keys(hs[0], BA[hs[0]], H, key, True, True)
+                src = BA[hs[0]][:, H:2 * H]
+            xw, lvk, lo, hi, z = ["XW%d" % h for h in hs], ["B2.lv%d" % h for h in hs], 8 * hs[0], 8 * hs[-1] + 8, hs[-1]
+            largest_key(hs, src, key, 32 + lo, "q%d" % z, 2047, T.XW, xw)
+            for h in hs:
+                mm(bank(2, 416 + 8 * h, 424 + 8 * h), T.XW[:, half(h)], T.BOH[:], True, True, ["XW%d" % h, "BOH"], ["B2.lv%d" % h])
+            lv, lk2 = T.LV[:, lo:hi], ["LV%d" % h for h in hs]
+            step("lv%d" % z)
+            cp(lv, bank(2, 416 + lo, 416 + hi), lvk, lk2)
+            step("vb%d" % z)
+            gather("v", T.VB[:, 16 * lo:16 * hi], T.IO2K[:], lv, ["IO2K"] + lk2, ["VB%d" % h for h in hs])
             if not last:
-                act(T.LXW[:, half(h)], T.LXT[:].indirect(T.LV[:, half(h, 8)]), ["LXT", "LV%d" % h], ["LXW%d" % h], F.Abs, bias=-768.0 * t, rate=GATHER)
+                step("lxw%d" % z)
+                act(T.LXW[:, 16 * lo:16 * hi], T.LXT[:].indirect(lv), ["LXT"] + lk2, ["LXW%d" % h for h in hs], F.Abs, bias=-768.0 * t, rate=GATHER)
 
+        now[0] = t
         if t > 1:
             parity()
+        else:
+            for j in range(OPT["tab0"]):
+                table(j)
+            first_room(0)
+            first_room(1)
+        first_rows()
         sums(0)
         sums(1)
+        running(0)
+        running(1)
         messages(0)
-        if t == 1:
-            table(6, 7)
-            table(7, 3)
-        else:
-            words(t - 1)
-            if not last:
-                offsets(t + 1)
         messages(1)
-        if t == 1:
-            cp(T.WD[:, 0:1024], T.BRI[:, 0:1024], ["BRI"], ["WD"])
-            cp(T.WD[:, 1024:2048], T.BRI[:, 1024:2048], ["BRI"], ["WD"])
+        room_left()
+        if t > 1:
+            words(t - 1)
+        else:
+            for j in range(OPT["tab0"], 4):
+                table(j)
+        if not last:
+            offsets(t + 1)
         for h in (0, 1):
-            gcopy(T.RES[:, c + 1024 * h:1024 * h + 1024:8], snd[h], [sk[h]], ["RES"])
+            step("res%d" % h)
+            cp(T.RES[:, c + 1024 * h:1024 * h + 1024:8], snd[h], [sk[h]], ["RES"], "p")
         if last:
+            step("yr")
             dma("s", T.yr[:], T.RES[:, 0:2048], "dyr", ["RES"], ["yr"], 512)
         else:
-            if t == 1:
-                offsets(2)
             for h in (0, 1):
-                act(T.RES[:, 2048 + L0 + H * h:2048 + L0 + H * h + H], land[h], [lk[h]], ["RESG"])
-        for j in WIDE:
-            if WIDE[j] == "p":
-                wide(j)
+                step("gh%d" % h)
+                cp(T.RES[:, 2048 + c * Q + H * h:2048 + c * Q + H * h + H], land[h], [lk[h]], ["RESG"], OPT["ghost"])
         if t + 2 <= NT:
             cap_wide(t + 2, range(1, 16))
-        mm(T.B7[:, 0:256], T.ID[:], T.OFFA[:], True, False, ["ID", "OFFA"], ["B7.x"])
+        step("offa")
+        mm(T.B7[:, 0:256], T.ID[:], T.OFFD[:], True, False, ["ID", "OFFD"], ["B7.x"])
+        mm(T.B7[:, 0:256], T.ID[:], T.OFFA[:], False, False, ["ID", "OFFA"], ["B7.x"])
         for h in (0, 1):
             candidates(h)
-            for j in range(4 * h, 4 * h + 4):
-                scores(j)
+            scores(h)
         if not last:
-            for j in range(0, 8, 2):
-                rows("a", j, 2)
-            row0_aside()
+            j = 0
+            for x in OPT["rows"].split():
+                rows(x[0], j, len(x))
+                row0_aside(OPT["aside"], t + 1, j, len(x))
+                j += len(x)
         suspended(t)
-        for h in (0, 1):
-            parents(h)
-        for i in range(16):
-            ts(T.EQ[:, i, 0:256 - 16 * i], T.VB[:, 16 * i:256], T.B0[:, 256 + i:257 + i], None, A.is_equal, None,
-               ["VB0", "VB1", "B0.lv0", "B0.lv1"], ["EQ%d" % i])
+        step("new")
+        relu(OPT["new"], T.NEW[:, half(c, Q)], T.IOTM[:], 2048.0 + 256.0 * c + 4096.0 * (t + 2), ["IOTM"], ["NEW%d" % t])
+        for hs in ([[0, 1]] if OPT["whole"] else [[0], [1]]):
+            parents(hs)
+        if tail:
+            step("eqm")
+            mm(bank(5, 0, tail_cols), T.XW[:, half(1)], T.NSEL[:, 0:tail_cols], True, False, ["XW1"] + ["NSEL%d" % x[0] for x in tail], whole[5])
+            for b, lo, m in tail:
+                mm(bank(5, lo, lo + 16), T.ID[:], T.MASK[:], False, False, ["ID", "MASK"], ["B5.c"])
+            step("eqt")
+            for b, lo, m in tail:
+                mm(bank(5, lo, lo + m), T.IDH[:], T.VB[:, 16 * b:Q], False, b == 15, ["IDH", "VB1"], ["B5.c"])
+            step("eqv")
+            ts(T.EQT[:, 0:tail_cols], bank(5, 0, tail_cols), 0.0, None, A.is_equal, None, whole[5], ["EQT"])
+            for b, lo, m in tail:
+                mm(T.B7[:, 16 * b:Q], T.BO4[:], T.EQT[:, lo:lo + m], False, False, ["BO4", "EQT", "B7.x"], ["B7.x%d" % b])
+        for i in range(first_tail):
+            step("eq%d" % i)
+            ts(T.EQ[:, i, 0:256 - 16 * i], T.VB[:, 16 * i:256], bank(2, 416 + i, 417 + i), None, A.is_equal, None,
+               ["VB0", "VB1", "B2.lv0", "B2.lv1"], ["EQ%d" % i])
             if i < 15:
-                mm(T.B7[:, 16 * i + 16:256], T.BO4[:], T.EQ[:, i, 16:256 - 16 * i], False, False, ["BO4", "EQ%d" % i], ["B7.x"])
+                mm(T.B7[:, 16 * i + 16:256], T.BO4[:], T.EQ[:, i, 16:256 - 16 * i], False, False, ["BO4", "EQ%d" % i, "B7.x"], ["B7.x%d" % i])
         if not last:
-            mm(T.B7[:, 0:256], T.MULD[:], T.LXW[:], False, False, ["MULD", "LXW0", "LXW1"], ["B7.x"])
-        mm(T.B7[:, 0:256], T.BT4[:], T.EQ[:, :, 0:16], False, True, ["BT4"] + ["EQ%d" % i for i in range(16)], ["B7.x"])
+            step("eqx")
+            mm(T.B7[:, 0:256], T.MULD[:], T.LXW[:], False, False, ["MULD", "LXW0", "LXW1", "B7.x"], ["B7.xm"])
+        e = first_tail - 2
+        step("eqd")
+        mm(T.B7[:, 0:16 * e], T.BT4[:], T.EQ[:, 0:e, 0:16], False, False, ["BT4", "B7.x"] + ["EQ%d" % i for i in range(e)], ["B7.xd"])
+        step("eqe")
+        mm(T.B7[:, 16 * e:16 * e + 32], T.BT4[:], T.EQ[:, e:e + 2, 0:16], False, True, ["BT4", "EQ%d" % e, "EQ%d" % (e + 1)],
+           ["B7.x", "B7.xm", "B7.xd"] + ["B7.x%d" % i for i in range(16)])
+        step("far")
+        mm(bank(2, 400, 416), T.CFAR[0:1, :], T.ONES[0:1, 0:16], True, False, ["CFAR", "ONES"], ["B2.far"])
+        for h in (0, 1):
+            mm(bank(2, 400 + 8 * h, 408 + 8 * h), T.XW[:, half(h)], T.BOH[:], False, h == 1, ["XW%d" % h, "BOH"], ["B2.far"])
+        step("cns")
         scan(T.CNS[:], T.MB[:], T.B7[:, 0:256], A.min, A.max, ["MB", "B7.x"], ["CNS"])
         if not last:
+            step("lb")
             tt(T.LB[:], T.CNS[:, 15:256:16], T.TP[:], A.min, ["CNS", "TP"], ["LB"])
+            step("pl")
             cp(T.PL[:], T.LB[:], ["LB"], ["PL"])
-            scatter(T.PK[:], T.PL[:], T.LAND[:, L0:L0 + Q], ["PL"] + lk, pk(0) + pk(1) + ["P00", "P01", "PKT"])
+            step("patch")
+            scatter(T.PK[:], T.PL[:], msg(T.LAND, 0, Q), ["PL"] + lk, pk(0) + pk(1) + p0(0) + p0(1) + ["PKT"])
 
-    table(0, 7)
-    table(1, 6)
     first_offsets()
     for j in range(8):
-        rows("a" if j < GS else "v", j, 1)
-    row0_aside()
-    cap_wide(1, range(GC))
-    for k in range(GC, 16):
-        cp(T.CX1[:, k:4096:16], T.CAP[:, 0:2048:8], ["CAP"], ["CX1k%d" % k])
-    cap_wide(2, range(16))
-    for j, b in enumerate((0, 3, 4, 7)):
-        o, k = T["B%d" % b][:], whole_bank[b]
-        mm(o, T.ID[:], T.CAP[:, half(j, 512)], True, False, ["ID", "CAP"], k)
-        mm(o, T.NID[:], T.RES[:, half(j, 512)], False, True, ["NID", "RES"], k)
-        act(T.SL[:, half(j, 512)], o, k, ["SL%d" % (j // 2)], F.Relu)
-    for j in range(2, 6):
-        table(j, (7, 4)[j & 1])
+        cp(T.WD[:, j:2048:8], T.BRI[:, j:2048:8], ["BRI"], ["WDc%d" % j])
+    j = 0
+    for x in OPT["gs"].split():
+        rows(x[0], j, len(x), "G")
+        j += len(x)
+    for h in (0, 1):
+        row0_aside(OPT["as1"][h], 1, 4 * h, 4, "AS")
+    step(None)
+    cut1 = Q - (32 * OPT["clip"][0] if OPT["clipw"] == "t" else 0)
+    for lo in range(0, cut1, H):
+        m, sp = min(H, cut1 - lo), ["SP%d" % j for j in range(4)]
+        step("SX%d" % (lo // H))
+        cp(T.SP[:, 0:16 * m:16], T.CAP[:, 8 * lo:8 * (lo + m):8], ["CAP"], sp)
+        step(None)
+        scan(T.CX1[:, 16 * lo:16 * (lo + m)], T.SEG[:, 0:16 * m], T.SP[:, 0:16 * m], A.min, A.max, ["SEG"] + sp, ["CX1h%d" % (lo // H)])
+    cap_wide(2, range(16), "CY")
+    step(None)
     for t in range(1, NT + 1):
         one_round(t)
+    now[0] = NT + 1
     words(NT)
-    dma("s", T.yb[:], T.WD[:, 0:2048], "dyb", ["WD"], ["yb"], 1024)
+    step("yb")
+    dma("s", T.yb[:], T.WD[:, 0:2048], "dyb", wdk, ["yb"], 1024)
 
     if len(calls) not in ORDERS:
         ORDERS[len(calls)] = issue_order(calls)
@@ -656,8 +1141,10 @@ def rank_program(g, core, T, topo):
     known = {k: {} for k in queues}
     lastw, readers, banks = {}, {}, {}
     sent = 0
+    used = []
     for i in ORDERS[len(calls)]:
-        q, f, r, w, _ns, lat = calls[i]
+        q, f, r, w, _ns, lat = calls[i][:6]
+        TAG[0] = i
         remote = q == "p" and lat > 0
         if remote:
             w, arrival = [], w[0]
@@ -686,6 +1173,7 @@ def rank_program(g, core, T, topo):
             continue
         if lat:
             queues[q].dma_start(f[0], f[1]).then_inc(T.sem[f[2]], 16)
+            used.append(f[2])
             tok = (f[2], 16, dict(kn))
         else:
             count[q] += 1
@@ -701,5 +1189,5 @@ def rank_program(g, core, T, topo):
     g.wait_ge(T.sem.loc, sent)
     for q, s in own.items():
         g.wait_ge(T.sem[s], count[q])
-    for s in DMAS:
+    for s in used:
         g.wait_ge(T.sem[s], 16)

@@ -10,78 +10,72 @@ WIN = 2080
 FAR = 131072
 MAGIC = 12582912.0
 OPT = {
-    "gs": "v v a a a a a v", "as1": "vv",
-    "clip": [0, 2, 2, 2, 2, 2],
-    "score": ["ssvvvvvv"] * 5 + ["ssvvssvv"],
-    "vm": 2, "wm": 2, "rows": "aa aa aa aa", "pf": "a", "whole": True, "tail": 7, "clipw": "cx", "su": "a", "pm": 4,
-    "aside": "p", "restore": "vp", "pieces": 4, "xs": "a", "pack": "", "row0": "v", "ghost": "p", "kn": "a", "bd2": "a", "n12": "a", "bd1": "a", "kp": "a", "new": "v", "r0": "a",
-    "sl": "a", "ft": "aaaa", "const": "v", "tab0": 2, "cmp": "vv", "wold": "vvvvvv", "um": "vv", "sp": "v", "seg": "v", "own1": "", "own6": "",
-    "ona": "N11M NID N12M N16M IDF P12M P16M M16M NBO BO4",
+    "gs": "v a v a v a a a", "as1": "vv",
+    "clip": [0, 0, 0, 0, 0, 0],
+    "score": ["ssvvvvvs"] * 6,
+    "vm": 1, "wm": 4, "pm": 2, "rows": ["aa aa aa a v"] * 6, "tail": 5, "restore": "pp", "pieces": 1, "cmp": 1, "cnt": 2, "fb": "zz", "xf": "a", "xs": "aa", "wp": 1, "rp": 4, "scp": "11221111", "cy": "pv", "su": "v", "bd1": "v", "bd2": "v", "two": "aa", "as": "p02 p22 p42 p61 v71", "pf": "a",
+    "ft": "34aa - 56aa - 56aa - 5vv 6va", "sli": "7777",
+    "early": "t0 t2", "late": "t4 s0 s1 t6 t7 s2 s3",
+    "ona": "ONES WDT N11M NID N15M NBO NBO2 BO4", "onp": "N12M P12M N16M IDF P16M M16M",
+    "own1": "", "own6": "",
 }
-CYCLE, PE_CYCLE, PE_CALL, GATHER, SCATTER, ACT = 0.83, 0.42, 8.0, 1.56, 4.0, 140.0
-WAKE, DMA, LAT, FIRST = 90.0, 1700.0, 2300.0, 5000.0
-PASSES, TOL, URG, RATIO = 6, 60, 100, 1.0
+CYCLE, PE_CYCLE, PE_CALL, GATHER, SCATTER, ACT = 0.83, 0.42, 4.0, 1.56, 3.8, 110.0
+WAKE, DMA, LAT, FIRST = 80.0, 1700.0, 2000.0, 3000.0
 SCRATCH = {
     "RES": ("sbuf", [128, 3344], "bfloat16"),
     "WD": ("sbuf", [128, 2304], "float32"),
     "BRI": ("sbuf", [128, 2048], "int32"),
     "PK": ("sbuf", [128, 4608], "bfloat16"),
     "EQ": ("sbuf", [128, 16, 256], "bfloat16"),
-    "SND": ("sbuf", [128, NT * 2 * Q], "bfloat16"),
-    "LAND": ("sbuf", [128, NT * 2 * Q], "bfloat16"),
+    "SND": ("sbuf", [128, NT * 3 * Q], "bfloat16"),
+    "LAND": ("sbuf", [128, NT * 3 * Q], "bfloat16"),
     "NEW": ("sbuf", [128, NT * Q], "float32"),
     "IO2K": ("sbuf", [128, 2048], "float32"),
     "LXT": ("sbuf", [128, 2048], "float32"),
     "TAB": ("sbuf", [128, 4096], "float32"),
     "ROWS": ("sbuf", [128, 4096], "float16"),
-    "OK0": ("sbuf", [128, 256], "bfloat16"),
-    "M0": ("sbuf", [128, 256], "bfloat16"),
-    "KC": ("sbuf", [128, 256], "bfloat16"),
-    "ALT": ("sbuf", [128, 256], "bfloat16"),
-    "FS": ("sbuf", [128, 2 * WIN], "bfloat16"),
-    "BS": ("sbuf", [128, 2 * WIN], "bfloat16"),
-    "SEG": ("sbuf", [128, 2064], "bfloat16"),
+    "BOH": ("sbuf", [128, 8], "float16"),
     "KS": ("sbuf", [128, 512], "float32"),
-    "XF": ("sbuf", [128, 16], "float32"),
-    "B16": ("sbuf", [128, 16], "bfloat16"),
-    "TWO": ("sbuf", [128, 512], "bfloat16"),
+    "XF": ("sbuf", [128, 32], "float32"),
+    "TRI": ("sbuf", [128, 3 * Q], "bfloat16"),
     "EQT": ("sbuf", [128, 512], "bfloat16"),
-    "MASK": ("sbuf", [128, 16], "bfloat16"),
+    "KC2": ("sbuf", [128, 512], "bfloat16"),
     "NSEL": ("sbuf", [128, 512], "float16"),
     "SACC": ("sbuf", [128, 2], "float32"),
     "K4": ("sbuf", [128, 4], "float16"),
-    "XW": ("sbuf", [128, 256], "float16"),
-    "VB": ("sbuf", [128, 256], "float16"),
-    "BOH": ("sbuf", [128, 8], "float16"),
-    "W16": ("sbuf", [128, 144], "bfloat16"),
+    "W16": ("sbuf", [128, 145], "bfloat16"),
     "COL": ("sbuf", [128, 16], "float32"),
 }
 for _n in ("CM", "CX0", "CX1", "MX", "SC"):
     SCRATCH[_n] = ("sbuf", [128, 4096], "bfloat16")
-for _n in ("CAP", "SL", "TOH", "SP", "FT"):
+for _n in ("CAP", "SL", "SP", "FT", "TOH"):
     SCRATCH[_n] = ("sbuf", [128, 2048], "bfloat16")
-for _n in ("ONES", "OFFD", "OFFA", "DELB", "N12", "KN", "KP", "BD1", "BD2", "R0", "XS", "XA", "OH", "DW", "LXW", "CMP0", "CMP1"):
+for _n, _c in (("SEG", 2064), ("FS", 2 * WIN), ("BS", 2 * WIN)):
+    SCRATCH[_n] = ("sbuf", [128, _c], "bfloat16")
+for _n in ("XS", "M63", "ONES", "OFFD", "OFFA", "DELB", "N12", "KN", "KP", "BD1", "BD2", "R0", "SG", "OH", "OK0", "DW", "LXW", "CMP", "KC", "BW32K"):
     SCRATCH[_n] = ("sbuf", [128, 256], "bfloat16")
-for _n in ("IOT", "IO16", "NDEL", "MB", "CNS", "WOLD", "IOTM", "PF"):
+for _n in ("XA", "XW", "VB", "PH"):
+    SCRATCH[_n] = ("sbuf", [128, 256], "float16")
+for _n in ("IOT", "IO16", "NDEL", "NMB", "MTP", "CNS", "CNW", "WOLD", "IOTM", "PF"):
     SCRATCH[_n] = ("sbuf", [128, 256], "float32")
-for _n in ("BO", "NBO", "BO4", "BT4", "BW32K", "ID", "NID", "N11M", "N12M", "P12M", "N16M", "P16M", "M16M", "MULD", "C37", "CFAR", "NEG",
-           "KC2", "KR", "KR16", "QRT", "LIM"):
+for _n in ("MB", "QS"):
+    SCRATCH[_n] = ("sbuf", [128, 512], "float32")
+for _n in ("BO", "NBO", "NBO2", "BO4", "BT4", "ID", "NID", "N11M", "N12M", "P12M", "N15M", "N16M", "P16M", "M16M", "MULD", "CFAR",
+           "ZERO", "LIM", "NODE"):
     SCRATCH[_n] = ("sbuf", [128, 128], "bfloat16")
 for _n in ("IDH", "RH", "KR4"):
     SCRATCH[_n] = ("sbuf", [128, 128], "float16")
-for _n in ("B32K", "NB32K", "NB8"):
-    SCRATCH[_n] = ("sbuf", [128, 8], "bfloat16")
-for _n in ("IO256", "I16B"):
+for _n in ("B16", "MASK", "B32K", "NB32K"):
     SCRATCH[_n] = ("sbuf", [128, 16], "bfloat16")
 for _n in ("IOB", "PAR", "IDF"):
     SCRATCH[_n] = ("sbuf", [128, 128], "float32")
-for _n in ("UI", "UU"):
-    SCRATCH[_n] = ("sbuf", [128, 256], "int32")
+for _n, _c in (("UI", 128), ("UU", 128), ("FO", 256)):
+    SCRATCH[_n] = ("sbuf", [128, _c], "int32")
 for _n in ("EO", "P16", "OFFC"):
     SCRATCH[_n] = ("sbuf", [128, 256], "uint16")
-for _n in ("WTI", "KAI", "PI", "KI"):
+for _n in ("WTI", "KAI", "PI"):
     SCRATCH[_n] = ("sbuf", [128, 1], "int32")
-for _n in ("TP", "TW", "LB", "LC", "LD"):
+for _n in ("LB", "LC", "QF", "C37"):
     SCRATCH[_n] = ("sbuf", [128, 16], "float32")
 for _n in ("XI", "XI2"):
     SCRATCH[_n] = ("sbuf", [128, 48], "int32")
@@ -89,172 +83,19 @@ for _n in ("KL", "PL", "PW", "LV", "UL"):
     SCRATCH[_n] = ("sbuf", [128, 16], "uint16")
 for _n, _c in (("B0", 512), ("B1", 512), ("B2", 512), ("B34", 1024), ("B56", 1024), ("B7", 512)):
     SCRATCH[_n] = ("psum", [128, _c], "float32")
-DMAS = ["dbr", "dres", "dcap", "dwt", "dka", "dyr", "dyb"] + ["dr%d" % k for k in range(4)] + ["dt%d" % k for k in range(4)]
+DMAS = ["dbr0", "dbr1", "dres", "dcap0", "dcap1", "dwt", "dka", "dyr", "dyb", "drow"] + ["dt%d" % k for k in range(4)]
 SEMAPHORES = ["cv", "ct", "ca", "cp", "loc"] + DMAS + ["arr%d%d" % (t, h) for t in range(1, NT + 1) for h in (0, 1)]
-COLS = ("WTF", "PFL", "KF", "G16", "G15", "MULP", "ADDP", "PC", "HALF")
+COLS = ("WTF", "PFL", "KF", "G16", "G15", "MULP", "ADDP", "PC")
 ORDERS = {}
 SEEN = {}
 TAG = [None]
 ROUND = """
-par1 r0a clipa kc0 kc1 cm0 r0b par2 clipb sli0 sli1 cm1 par3 sum0 klc0 rest0 ks0 ki0 sum1 klc1 rest1 kj0 ks1 kx0 ki1 kl0 kj1 cap0 xs0 kx1 lim0 sw0 kl1
-row0 xs1 fb0 sw1 cmp00 cmp01 ok0 row1 mn0 cap1 lim1 snd0 fb1 sla slb0 res0 uc0 cmp10 cmp11 ok1 mn1 snd1 uc1 slb1 sl res1 oh yr wdc0 wdc1 tb2a tb3a tb2b tb3b
-ld lc pw wold wd yb u0 gh0 shw0 shw1 shw2 shw3 sp0 sp1 sp2 sp3 wd0 wd1 wd2 wd3 ui0 uj0 ul0 p160 pf0 shg0 shg1 shg2 shg3 n12 kn t1 bd2 bd1 t2
-sc0 sc1 sc2 sc3 u1 gh1 pw4 pw5 pw6 pw7 shr0 shr1 shr2 shr3 shw4 shw5 shw6 shw7 ui1 uj1 ul1 sp4 sp5 p161 eo wd4 wd5 pf1 shg4 shg5 shg6 shg7 sp6 sp7
-wd6 wd7 offa pc0 ps0 ps1 ps2 ps3 pn0 sc4 sc5 shr4 shr5 shr6 shr7 rows0 sc6 sc7 as0 rows1 as1 rows2 as2 rows3 as3 qs0 qi0 qj0 qx0 lv0 vb0 lxw0
-pc1 ps4 ps5 ps6 ps7 pn1 eqm cx0 cx1 cx2 cx3 cx4 qs1 qi1 qj1 qx1 rows4 lv1 as4 vb1 lxw1 rows5 as5 eqt eq0 eq1 eq2 eqv eq3 eq4 eq5 rows6 as6
-eq6 eq7 eq8 eq9 eq10 eq11 eq12 eq13 eq14 eq15 rows7 as7 eqe far kp z su1 su2 cns lb pl patch
-"""
-
-
-OPT.update({
-    "score": ["ssvvsvvv"] * 6, "vm": 1, "pm": 2, "su": "a", "kp": "a", "wm": 4, "clip": [4] * 6, "clipw": "t", "cmp": "vv", "row0": "v",
-    "rows": "aa aa aa aa", "pf": "v", "gs": "v a v a a a a a", "ft": "aavv", "new": "a", "pack": "v",
-    "own1": "pk0 pk1 r0b r0c clipa0 clipa1 clipa2 clipa3 clipb0 clipb2 kc0 kc1 cm0 cm1 sum0 sum1 ks0 ki0 kj0 kx0 kl0 ks1 ki1 kj1 kx1 kl1 klc0 klc1 rest0 rest1 "
-            "xs0 xs1 sw0 sw1 row0 row1 fb0 fb1 cap0 cap1 lim0 lim1 cmp00 cmp01 cmp10 cmp11 ok0 ok1 mn0 mn1 snd0 snd1 sla n12 kn t1 bd1 bd2 t2 eo kp oh new "
-            "cx0 cx1 cx2 cx3 cx4 offa slb0 slb1 sl uc0 uc1 res0 res1"})
-ROUND = """
-BRI-- TOH0- TOH1 TOH2 RES-- CAP-- UI-- cx3_1+ IOT-- C37 cx2_1+ PI-- IOB-- IO256-- KC-- IO16-- BT4 LIM-- SP3-- I16B-- WDT SP1-- PKT KR16--
-SP0-- LXT0-- CY4 SP2-- KR-- res1_1 ONES-- CFAR-- CY0-- IO2K0-- NEG-- KC2 K42-- RI3-- KAI-- RI0-- RI1-- RI2-- RH-- PFL-- RESZ-- ID-- ROW3--
-ROW2-- ROW1-- KI-- KF-- ROW0-- N11M-- WTI-- N16M-- N12M-- sl_1 XIu0-- K43-- K40-- IDH-- G16-- K41-- BO-- NBO-- NID-- IDF-- B1.k-- KR4--
-tb0a-- tb1a-- tb0b-- kp_1 tb1b-- NB32K-- DELB-- SEG-- MB-- B16-- B32K-- FO1-- FO2-- WTF-- FO3-- G2-- G3-- G1-- G0-- SX0-- BOH-- NB8-- AS0--
-CX1h0-- cm0_1-- OFFC-- G4-- sli0-- r0b_1-- kc0_1-- sli1-- clipa1_1-- sum0_1-- kc1_1-- rest0_1-- OK00-- WDc0-- WDc1-- ks0_1-- ki0_1--
-clipa0_1-- G7-- G5-- G6-- klc0_1-- clipa2_1-- kj0_1-- G15-- kx0_1-- MULP-- kl0_1-- xs0_1-- AS4-- sw0_1-- row0_1-- clipb0_1-- clipa3_1--
-clipb2_1-- lim0_1-- r0c_1-- cap0_1-- sum1_1-- fb0_1-- cmp00_1-- cmp01_1-- ks1_1-- TOH-- n12_1-- ki1_1-- kj1_1-- klc1_1-- kx1_1-- mn0_1--
-kl1_1-- rest1_1-- cx1_1+ LXT1 ok0_1-- kn_1-- cx0_1+ snd0_1-- t1_1-- r0a sla_1-- cap1_1-- xs1_1-- bd1_1-- NDEL bd2_1-- r0b P16M- clipb2
-clipa1 clipb0 kc0 lim1_1-- sum0 ks0 sw1_1-- ki0 sla cap1 cap0 klc0 kc1 uc0_1 t2_1-- sum1 kj0 kx0 QRT+ kl0 ks1 ki1 rest0 rest1 cx0 res0_1--
-n12 kn BO4-- xs0 sw0 ADDP kj1 row0 eo_1 row1_1-- fb1_1-- cmp10_1-- cmp11_1-- IOTM ok1_1-- tb2b t1 P12M-- kp par1 par2 M16M-- par3 W16-- bd1
-klc1 lim0 kx1 fb0 kl1 tb3b xs1 cmp00 oh_1 ok0 bd2 mn1_1-- cmp01 mn0 OFFD-- snd1_1-- cx3 snd0 res0 lim1 t2 offa tb2a-- slb0 uc0 sw1 row1 fb1
-tb3a-- cmp10 slb0_1-- cmp11 eo oh LB new ok1 mn1 snd1 res1 gh0 gh1 CY2 cx2 LXT2 CY1 IO2K1 IO2K2 LXT3 IO2K3 slb1_1-- u0 slb1 uc1_1 uc1 shw0
-sp2 NSEL1 ui0 PAR uj0 MASK ul0 BW32K pf0 OFFA p160 sl wd2 sc2 shg0 sc3 pc0 pn0 pc1 offa_1 u1 rows4 shr0 ui1 sp5 uj1 WDc4 ul1 WDc3 pf1 wd5
-p161 MULD sc5 z shw4 pn1 ps2 ps0 shg4 sc6 new_1 shr4 ps5 ps6 ps4 sc7 ps7 NSEL0 WDc6 qs1 TP qi1 yb yr clipa3- clipa0- qj1 TW qx1 eqm WDc5 lv1
-vb1 eqt rows2 rows0 eq0 eq2 eq1 lxw1 far eqx eqv eq6 eq4 eq5 eq3 eq7 eqd eq8 eqe cx4 cx1 WDc2 cx4_1+ as4 as2 CY3 as0 rows6 as6 su1 su2
-clipa2- cns WDc7 ld- lb lc- pl pw- patch wold- cm0- wd-
-""".replace("snd0_1--", "snd0_1-- pk0_1--").replace("snd1_1--", "snd1_1-- pk1_1--").replace("snd0 ", "snd0 pk0 ").replace("snd1 ", "snd1 pk1 ")
-
-
-OPT.update({
-    "pf": "a", "pack": "", "pieces": 2,
-    "own1": "r0b r0c clipa0 clipa1 clipa2 clipa3 clipb0 clipb2 kc0 kc1 cm0 cm1 sum0 sum1 ks0 ki0 kx0 kl0 ks1 ki1 kx1 kl1 klc0 klc1 rest0 rest1 xs0 xs1 "
-            "m00 m01 m10 m11 bs00 bs01 bs02 bs03 bs10 bs11 bs12 bs13 fs00 fs01 fs02 fs03 fs10 fs11 fs12 fs13 lin0 lin1 cap0 cap1 lim0 lim1 "
-            "cmp00 cmp01 cmp10 cmp11 ok0 ok1 mn0 mn1 snd0 snd1 sla n12 kn t1 bd1 bd2 t2 eo kp oh new cx0 cx1 cx2 cx3 cx4 offa slb0 slb1 sl uc0 uc1 res0 res1"})
-ROUND = """
-TOH1 BRI-- TOH0- TOH2 RES-- CAP-- UI-- IOB-- PI-- IOT-- CY0 ENDS-- IO16-- LXT0-- SP2-- res0_1- KR-- ONES-- SP1-- CFAR-- IO256-- SP3-- KC2-- SP0-- KC-- KR16-- IO2K0-- RI3-- K43-- RI2-- RI0-- RI1-- PFL-- RH-- LIM-- KAI-- KI-- MB-- ID-- K42-- K41-- XIu0-- IDH-- K40-- ROW1-- ROW0-- new_1- ROW3-- ROW2-- KF-- RESZ-- G16-- B1.k-- KR4-- BO-- LB-- N16M-- WTI-- IDF-- NBO-- N11M-- NID-- tb0a-- SEG-- B16-- tb1a-- tb0b-- tb1b-- NB8-- FO1-- TW-- FO2-- DELB-- WDc1-- FO3-- G2-- G0-- SX0-- OFFD-- CX1h0-- G3-- G1-- AS0-- G15-- cm0_1-- G5-- sli0-- kc0_1-- r0b_1-- sli1-- clipa0_1-- WTF-- B32K-- OFFC-- bs00_1-- clipa1_1-- sum0_1-- bs01_1-- ks0_1-- rest0_1-- QRT-- G6-- G7-- G4-- clipa3_1-- clipa2_1-- klc0_1-- ki0_1-- fs01_1-- kc1_1-- clipb2_1-- kx0_1-- clipb0_1-- bs11_1-- cap0_1-- AS4-- kl0_1-- cap1_1-- bs10_1-- LXT1-- fs00_1-- xs0_1-- r0c_1-- sum1_1-- CY2- IO2K1-- ALT-- cx0_1+ IO2K2-- WDT-- rest1_1-- m00_1-- m01_1-- lim0_1-- cmp00_1-- kn_1-- TOH-- lin0_1-- lim1_1-- fs10_1-- sla_1-- cmp10_1-- m10_1-- ks1_1-- C37-- res1_1- PKT- I16B-- NEG-- BT4 uc0_1-- LXT2-- lin1_1-- klc1_1-- cx2_1-- LXT3-- BOH-- cmp01_1-- ki1_1-- fs11_1-- ok0_1-- kx1_1-- ok1_1-- n12_1-- t1_1-- NSEL0-- mn0_1-- kl1_1-- M16M-- xs1_1-- mn1_1-- WDc0-- snd0_1-- CY1-- cx1_1-- m11_1-- tb2a-- bd1_1-- bd2_1-- N12M-- t2_1-- cmp11_1-- slb0_1-- kc0 ADDP-- W16-- r0a NDEL-- su1+ P12M-- new PAR snd1_1-- cx4_1-- ld clipa2 NB32K clipa3 patch+ cm0 r0b bs01 bs00 bs10 clipb2 sum0 OFFA WDc4-- IOTM-- rest0 ks0 bs11 ki0 fs00 cx3 cx4 far+ clipa0 clipa1 clipb0 rest1 cap0 cx3_1-- cx1+ klc0 par1 su2+ MULP kx0 tb3a-- m00 fs01 par2 P16M-- kl0 xs0 par3 slb1_1-- cap1 kc1 sum1 lin1 lim0 fs11 cmp00 ks1 m10 ki1 NSEL1 WDc3 WDc6 m01 lin0 klc1 kx1 MASK uc1 sla cmp01 lim1 fs10 kl1 uc0 cmp10 MULD kp_1-- ok0 mn0 xs1 lc snd0 res0 ok1 m11 pw cmp11 mn1 wold snd1 cx0 slb0 slb1 u0 sl_1-- oh sl wd ui0 eo_1 sp2 uj0 BW32K TP ul0 wd2 p160 BO4-- n12 kn shw0 uc1_1-- u1 t1 kp offa_1 tb2b-- bd2 pf0 oh_1 tb3b-- bd1 ui1 sp5 uj1 wd5 ul1 sc3 shg0 pf1 p161 shg4 sc2 shw4 pc0 pc1 pn0 t2 offa sc5 eo shr0 pn1 sc6 shr4 ps2 ps5 ps0 sc7 ps4 WDc5 WDc7 ps6 ps7 qs1 qi1 z res1 yr yb gh0 cx2 gh1 rows2 CY3 IO2K3 as2 rows0 as0 CY4 rows4 as4 qj1 qx1 WDc2 eqm lv1 vb1 lxw1 eqt eq3 eq5 eq4 eq0 eqx eqv eq2 eq6 eq1 eq7 eqd eq8 eqe cns lb pl rows6 as6
+FOa1 kp_6+ as0+ AS0 CY12+ eq5+ ps4_6+ kc0_1 rows7b_1+ IO2K3 eqt+ qi_1+ FOb1 CY11+ eq0+ ok_6+ WDc0 WDc2+ tb2d eq1+ eq2+ rows4_1+ ps7_6+ SX11 qx_1+ cnc0_1 eq5T+ r0b_1 FOc1 P16M+ eqv+ cm00_1 ps6_6+ eq0T+ kp+ rows7c_1+ LXT0 as2_1+ eq1T+ pe_6+ z_6+ rows7d_1+ eq3+ qxT_1+ eq2T+ r0bA_1 qs_6+ as6+ lv_1+ eq4+ MASK+ PKT+ eqx+ G6 CX1h1 eqm_1+ eq6+ vb_1+ as0_1+ NEW1+ ok+ sum0_1 far_1+ LXT1 TW+ MULD+ lxw_1+ eqvT+ offa_6+ G5 cnt00_1 eq5_1+ eqt_1+ eq7+ qx_6+ eq1_1+ offa_1+ qi_6+ ks0_1 eq9_1+ as4_1+ rows6_1+ eq0_1+ eq8+ cnt01_1 eq5T_1+ eq2_1+ ADDP eq3_1+ eq9T_1+ eq1T_1+ eqv_1+ G7 eq0T_1+ LXT2 eq3T+ eq2T_1+ ki0_1 eq4_1+ eq3T_1+ tb4a G4 eq9+ eqx_1+ kp_1+ eq6_1+ eq8_1+ eqvT_1+ eq7_1+ eq10_1+ eq4T+ as6_1+ as7_1+ eq4T_1+ eq6T_1+ cnc1_1 ok_1+ eq10+ NBO2 eq8T_1+ kc1_1 eqd_1+ eq7T_1+ MTW+ kx0_1 eq10T_1+ WDc7+ eqe_1+ NBO NEW3++ as7+ LXT3 oh_1+ eq6T+ NB32K AS4 cx2_1+ cns_1+ eq7T+ NEW4+++ kx0T_1 qxT_6+ sli0 eq8T+ WDT+ cnw_1+ eqm_6+ B32K eqd+ rest0_1 kl0_1 z_1+ pl_1+ cx14+ lv_6+ QRT+ eq9T+ cm10_1 cx1_1+ NEW2+ r0c xs0_1 patch_1+ eq10T+ KC3 vb_6+ eqe+ r0cA z+ cns+ NEW5+++ cx12_1+ tb4b cx15_1++ cx15+ pl+ cnw+ r0a zero0_1 patch+ WDc6+ eq7_6+ par1 cnt10_1 eq0_6+ eqt_6+ cm00 cx5_1+ r0b CY2 MULP kc0 r0bA cx8_1+ eq1_6+ NDEL+ cm10 sum1_1 sum0 rest0P_6 eq3_6+ eq7T_6+ eq0T_6+ fs00_1 kc1 cx6_1 LB NEW6+++ eq4_6+ ks0 cx1 eqx_6+ sum1 lin0_1 eqv_6+ rest1P_6 par2 ki0 eq1T_6+ cnt11_1 par3 kx0 eq3T_6+ CY4 rest0P eq9_6+ sg0_1 eq5_6+ ks1 ld ks1_1 eq4T_6+ eq2_6+ kx0T CY15 eqvT_6+ rest1_1 two0_1 eq6_6+ cmp0_1 v10_1 rest1P cnt00 eq8_6+ kl0 ki1_1 eq10_6+ NMB ki1 WDc3 eq9T_6+ eq5T_6+ su_1+ su+ cmp0T_1 eq2T_6+ kx1_1 cx6 eq6T_6+ cnt01 eqd_6+ sli0A xs0 eq8T_6+ snd0_1 kx1 eq10T_6+ eqe_6+ cx3 zero0 kx1T_1 tb4c kx1T cnc1 cns_6+ sg0 kl1_1 cnt10 PAR snd0P_1 lc kl1 cnt11 WTF cx5 WDc1 PW fs00 xs1_1 xs1 lin1 lin0 NSEL1 cx2 sg1_1 zero1 two0 WOLD SX21 cx4 cmp0 zero1_1 sg1 pw pw_6 tb4d fs10 oh lin1_1 WD v11 lim WDc5 v10 sli1 cmp0T v0 sla snd0 two1 cmp1 fs10_1 wolda snd0P two1_6 cmp1T cx3_1+ v11_1 cmp1_6 slb0 snd1 wolda_6 wda sli1A slb1 snd1P cx7 cmp1T_6 sl tb6a res0_6 u0 WDc4 tb7a m630 n12 snd1_6 cmp1_1 two1_1 res0 lim_1 shw0 tb6b ui0 sp2 wda_6 kn n12_1 gh0 cmp1T_1 uj0 slb1_6 sli2 snd1P_6 u1 G15 res1_6 wd2 C37 snd1_1 sl_6 cx8 tb6c u0_6 t1 ul0 tb7b m637 sli2A oh_6 bd2 snd1P_1 sp4 pf0 N16M W16 p160 CX0h1 ui0_6 cx10_1+ tb7c kn_1 yb cx9 IDF sp2_6 IOT- SEG- u1_6 shw7 ui1 BO4 sli3 uj0_6 cx4_1 bd1 tb7d UI- wd2_6 tb6d shg0 u0_1 ONES- PI- pc CY0 KAI- m630_1 IO16- uj1 sli3A BW32K1 v0_1 sp2_1 sc3 ul0_6 bd2_1 sla_1 m637_6 slb0_1 res0_1 ui0_1 cx10 slb1_1 SP0- m637_1 u1_1 NSEL0 ui1_6 pn0 IOB- TOH uj0_1 wd2_1 cx7_1 p160_6 RI2- RI0- pf0_6 RI1- t1_1 ul1 shw7_6 NODE- PFL- sl_1 RI3- shw7_1 K42- pc0 ul0_1 RH- uj1_6 ui1_1 OFFA ID- BT4 sp4_6 sc2 sp4_1 BRI0- XIu0- pf0_1 p160_1 m630_6 K41- pc_1 KI- bd1_1 t2 IDH- res1_1 shw0_1 FOa0- res1 sc2_6 shg0_6 KC- K40- uj1_1 shg0_1 K43- sc2_1 KF- p161 Y2- CY1 shw0_6 FOb0- pn0_1 wd4 CAP0- B1.k- NID- G16- ul1_1 ul1_6 ZERO- sc3_1 TOH0 t2_1 cx13 RESZ- CY5 sc3_6 KR4- N11M- pf1 ROWS- BO- pc_6 p161_1 shg7 OFFC- yr N15M- CY3 shr0 sc3b_1 sc3b tb2a- DELB- LIM- t3_1 shg7_1 pc0_1 gh1 KC2- M16M wd4_1 p161_6 t3 tb0a- shr0_1 pn1 BOH- B160- pn0_6 B161- tb2b- OFFD- sc2b gh0_1 wd4_6 sc3b_6 shr0A FOc0- cx11 pf1_1 pc0_6 BW32K0- pc1 MB- sc2b_1 shr7 N12M- pf1_6 eo TOH1 gh1_1 sc4 shr7_1 shr0A_1 cx12 shg7_6 sc5_1 CFAR- shr0_6 ps2 CY6 pn1_1 shr7A sc5 tb0b- ps0 SX10- IO2K0- ps2_1 IOTM- rows2 sc6 cx11_1+ CY8 pn1_6 RES- ps7 eo_1 sc2b_6 shr7A_1 ps4 pc1_1 sc4_1 CY7 cx9_1+ G2- rows7a shr0A_6 ps0_1 rows7b ps6 rows4 CY10 sc4_6 G1- pc1_6 IO2K1- rows2_1 shr7_6 rows7c pe sc6_1 G0- cx13_1+ tb0c- offa TOH2 CY14 qs ps4_1 cx14_1+ qi sc5_6 rows0 qx G3- ps2_6 BRI1- CY13 as4 rows7d rows7a_1 ps7_1 WTI- CX1h0- qxT IO2K2- eqm MTP ps6_1 shr7A_6 tb2c- CY9 lv as2 pe_1 rows0_1 far tb0d- ps0_6 vb P12M lxw qs_1 sc6_6 cnc0- CAP1- rows6
 """
 
 
 def banks_of(keys):
     return set(x.split(".")[0] for x in keys if "." in x)
-
-
-def issue_order(calls):
-    n = len(calls)
-    before, after = [set() for _ in calls], [[] for _ in calls]
-    lastw, readers, in_bank = {}, {}, {}
-    for i, (q, _f, r, w, _ns, _lat, step, _grp) in enumerate(calls):
-        for k in list(r) + list(w):
-            if k in lastw:
-                before[i].add(lastw[k])
-        for k in w:
-            before[i].update(readers.get(k, []))
-        for b in banks_of(list(r) + list(w)) if q == "t" else ():
-            seen = in_bank.setdefault(b, [])
-            if step is None:
-                before[i].update(seen)
-                seen[:] = [i]
-            else:
-                before[i].update(x for x in seen[:1] if calls[x][6] is None)
-                seen.append(i)
-        before[i].discard(i)
-        for k in r:
-            readers.setdefault(k, []).append(i)
-        for k in w:
-            lastw[k] = i
-            readers[k] = []
-    SEEN["calls"], SEEN["before"] = calls, [set(b) for b in before]
-    place = {x.rstrip("+-"): (x.count("+") - x.count("-"), j) for j, x in enumerate(ROUND.split())}
-    listed = sorted((i for i in range(n) if calls[i][6]), key=lambda i: (calls[i][6][0] + place[calls[i][6][1]][0], place[calls[i][6][1]][1], i))
-    spot = {i: x for x, i in enumerate(listed)}
-    for i in listed:
-        for p in before[i]:
-            assert spot.get(p, -1) < spot[i], (calls[p][6], calls[i][6])
-    last, soft = {}, set()
-    for i in listed:
-        p = last.get(calls[i][0])
-        if p is not None and p not in before[i]:
-            before[i].add(p)
-            soft.add((p, i))
-        last[calls[i][0]] = i
-        for b in banks_of(list(calls[i][2]) + list(calls[i][3])):
-            before[i].update(p for q, p in last.setdefault(b, {}).items() if q != calls[i][0])
-            last[b][calls[i][0]] = i
-    for i in range(n):
-        for p in before[i]:
-            after[p].append(i)
-    banks = [banks_of(list(c[2]) + list(c[3])) for c in calls]
-    loads = [i for i in range(n) if calls[i][0] == "s"]
-    behind = dict(zip(loads, loads[1:]))
-
-    def run(way, first_of, next_of, back):
-        missing = [len(b) for b in first_of]
-        held = set() if back else set(behind.values())
-        ready = {q: [] for q in "vatps"}
-        at, end, free, bank, dmas = [0.0] * n, [0.0] * n, {q: 0.0 for q in ready}, {}, 0.0
-        for i in range(n):
-            if not missing[i]:
-                ready[calls[i][0]].append(i)
-        order = []
-
-        def start(i):
-            q = calls[i][0]
-            s = max(free[q], at[i])
-            for b in banks[i]:
-                if b in bank and bank[b][0] != q:
-                    s = max(s, bank[b][1] + WAKE)
-            return s
-
-        while len(order) < n:
-            pick = None
-            for q, cand in ready.items():
-                st = {i: start(i) for i in cand if i not in held}
-                if not st:
-                    continue
-                soon = min(st.values())
-                first = max([i for i in st if st[i] <= soon + TOL], key=lambda i: (way[i], -i))
-                for i in st:
-                    if way[i] > way[first] + URG and st[first] + calls[first][4] - st[i] > RATIO * (st[i] - st[first]):
-                        first = i
-                if pick is None or st[first] < pick[0]:
-                    pick = (st[first], first)
-            s, i = pick
-            q, ns, lat = calls[i][0], calls[i][4], calls[i][5]
-            ready[q].remove(i)
-            held.discard(behind.get(i))
-            order.append(i)
-            free[q] = s + ns
-            end[i] = s + ns + (0.0 if back else lat)
-            if lat and q != "p" and not back:
-                end[i] = dmas = max(s + DMA, dmas) + lat
-            for b in banks[i]:
-                bank[b] = (q, s + ns)
-            for j in next_of[i]:
-                late = calls[j][5] + (DMA if calls[j][5] and calls[j][0] != "p" else 0.0) if back else 0.0
-                if ((j, i) if back else (i, j)) in soft:
-                    at[j] = max(at[j], s + ns)
-                else:
-                    at[j] = max(at[j], end[i] + late + (0.0 if q == calls[j][0] == "t" else WAKE))
-                missing[j] -= 1
-                if not missing[j]:
-                    ready[calls[j][0]].append(j)
-        return order, end
-
-    way = [-50.0 * i for i in range(n)]
-    best = None
-    for _ in range(PASSES):
-        order, end = run(way, before, after, False)
-        if best is None or max(end) < best[0]:
-            best = (max(end), order, way)
-        way = run(end, after, before, True)[1]
-    return best[1]
 
 
 def runs(blocks, most):
@@ -267,30 +108,59 @@ def runs(blocks, most):
     return out
 
 
-def issue_order(calls):
-    n = len(calls)
+def depends(calls):
     before = [set() for _ in calls]
-    lastw, readers = {}, {}
+    lastw, readers, closed = {}, {}, {}
     for i, c in enumerate(calls):
-        r, w = c[2], c[3]
+        r, w, grp = c[2], c[3], c[7]
         for k in list(r) + list(w):
             if k in lastw:
                 before[i].add(lastw[k])
         for k in w:
             before[i].update(readers.get(k, []))
+        for b in banks_of(w) if grp else ():
+            if grp[0] and b in closed:
+                before[i].add(closed[b])
+            if grp[1]:
+                closed[b] = i
         before[i].discard(i)
         for k in r:
             readers.setdefault(k, []).append(i)
         for k in w:
             lastw[k] = i
             readers[k] = []
+    return before
+
+
+def issue_order(calls):
+    before = depends(calls)
     SEEN["calls"], SEEN["before"] = calls, before
     place = {x.rstrip("+-"): (x.count("+") - x.count("-"), j) for j, x in enumerate(ROUND.split())}
-    order = sorted(range(n), key=lambda i: (calls[i][6][0] + place[calls[i][6][1]][0], place[calls[i][6][1]][1], i))
-    spot = {i: x for x, i in enumerate(order)}
-    for i in order:
-        for p in before[i]:
-            assert spot[p] < spot[i], (calls[p][6], calls[i][6])
+    unit, members = [], []
+    for i, c in enumerate(calls):
+        if i and c[0] == "t" == calls[i - 1][0] and c[6] == calls[i - 1][6]:
+            members[-1].append(i)
+        else:
+            members.append([i])
+        unit.append(len(members) - 1)
+    rank, missing, after = [], [], [[] for _ in members]
+    for u, m in enumerate(members):
+        t, name = calls[m[0]][6]
+        rank.append((t + place.get(name, (0, 0))[0], place.get(name, (0, 0))[1], u))
+        first = set(unit[p] for i in m for p in before[i]) - {u}
+        missing.append(len(first))
+        for p in first:
+            after[p].append(u)
+    ready = [rank[u] for u in range(len(members)) if not missing[u]]
+    order = []
+    while ready:
+        first = min(ready)
+        ready.remove(first)
+        order += members[first[2]]
+        for x in after[first[2]]:
+            missing[x] -= 1
+            if not missing[x]:
+                ready.append(rank[x])
     return order
 
 
@@ -302,18 +172,23 @@ def rank_program(g, core, T, topo):
     n = len(cores)
     V, PE, AC = g.vector, g.tensor, g.scalar
     calls = []
-    now = [1, None]
+    now = [1, None, None]
+    first_queue = {}
+    named = set(x.rstrip("+-") for x in ROUND.split())
 
-    def step(name):
-        now[1] = name
+    def step(name, pieces=None):
+        now[1], now[2] = name, pieces and (now[0], pieces)
 
     def put(q, f, r, w, ns, lat=0.0, grp=None):
         name = now[1] or w[0]
-        if now[0] == 1 and name in OPT["own1"].split():
+        r = sum(([k + "0", k + "1"] if k in ("CAP", "BRI", "B16", "BW32K") else [k] for k in r), [])
+        if first_queue.setdefault(name, q) != q:
+            name += q.upper()
+        if now[0] == 1 and (name + "_1" in named or name in OPT["own1"].split()):
             name += "_1"
-        if now[0] >= NT and name in OPT["own6"].split():
+        if now[0] >= NT and (name + "_6" in named or name in OPT["own6"].split()):
             name += "_6"
-        calls.append((q, f, r, w, ns, lat, (now[0], name), grp))
+        calls.append((q, f, r, w, ns, lat, (now[0], name), grp, now[2]))
 
     def cols(ap):
         c = 1
@@ -325,7 +200,7 @@ def rank_program(g, core, T, topo):
         return all("16" in str(a.dtype) for a in aps)
 
     def vec(f, r, w, n_cols, rate):
-        put("v", f, r, w, 60.0 + max(64.0, n_cols * rate) * CYCLE)
+        put("v", f, r, w, 55.0 + max(64.0, n_cols * rate) * CYCLE)
 
     def mm(out, lhs, rhs, st, sp, r, w):
         ns = PE_CALL + max(min(64, cols(lhs)), cols(rhs)) * PE_CYCLE * (1 if narrow(lhs) else 4)
@@ -367,15 +242,9 @@ def rank_program(g, core, T, topo):
         else:
             ts(out, in_, scale, bias, A.mult, A.add, r, w)
 
-    def relu(q, out, in_, bias, r, w):
+    def gather(q, out, win, off, r, w, bias=0.0):
         if q == "a":
-            act(out, in_, r, w, F.Relu, bias=bias)
-        else:
-            ts(out, in_, bias, 0.0, A.add, A.max, r, w)
-
-    def gather(q, out, win, off, r, w):
-        if q == "a":
-            act(out, win.indirect(off), r, w, rate=GATHER)
+            act(out, win.indirect(off), r, w, bias=bias, rate=GATHER)
         else:
             vec(lambda: V.tensor_copy(out, win.indirect(off)), r, w, cols(out), GATHER)
 
@@ -386,7 +255,7 @@ def rank_program(g, core, T, topo):
         vec(lambda: V.tensor_tensor_scan(out, d0, d1, 0.0, o0, o1), r, w, cols(out), 0.5 if narrow(out, d0, d1) else 1.0)
 
     def dma(q, out, in_, sem, r, w, kib):
-        put(q, (out, in_, sem), r, w, 100.0, 3.0 * kib + 1.0)
+        put(q, (out, in_, sem), r, w, 100.0, DMA + 3.0 * kib)
 
     def half(h, size=H):
         return slice(size * h, size * h + size)
@@ -395,66 +264,68 @@ def rank_program(g, core, T, topo):
         j = COLS.index(name)
         return T.COL[:, j:j + 1]
 
-    def bank(b, lo, hi, by=1, rows=slice(0, 128)):
+    def bank(b, lo, hi, by=1):
         name, at = {3: ("B34", 0), 4: ("B34", 512), 5: ("B56", 0), 6: ("B56", 512)}.get(b, ("B%d" % b, 0))
-        return T[name][rows, at + lo:at + hi:by]
+        return T[name][:, at + lo:at + hi:by]
 
-    whole = {3: ["B3.g"], 4: ["B4.g"], 5: ["B5.c", "B5.v"], 6: ["B6.c", "B6.v"]}
+    def rw(lo, hi, by=1):
+        return T.PK[:, lo:hi:by]
+
+    whole = {3: ["B3.n", "B3.v"], 4: ["B4.n", "B4.v"], 5: ["B5.c"], 6: ["B6.c"], 7: ["B7.x", "B7.hi"]}
     first_tail = 16 - OPT["tail"]
     tail = []
     for b in range(first_tail, 16):
         tail.append((b, sum(x[2] for x in tail), Q - 16 * b))
     tail_cols = sum(x[2] for x in tail)
 
-    cq = OPT["const"]
-    dma("s", T.BRI[:], T.br[:], "dbr", [], ["BRI"], 1024)
-    dma("a", T.KAI[:], T.ka[:], "dka", [], ["KAI"], 1)
-    dma("a", T.WTI[:], T.wt[:], "dwt", [], ["WTI"], 1)
-    u32 = T.UI[:, 0:32]
-    iota(u32, [[1, 32]], 0, 32, "UI")
+    dma("s", T.KAI[:], T.ka[:], "dka", [], ["KAI"], 1)
+    dma("s", T.WTI[:], T.wt[:], "dwt", [], ["WTI"], 1)
+    dma("s", T.RES[:, 0:ZC], T.res[:], "dres", [], ["RES", "RESG"], 832)
+    for h in (0, 1):
+        dma("s", T.BRI[:, half(h, 1024)], T.br[:, half(h, 1024)], "dbr%d" % h, [], ["BRI%d" % h], 512)
+        dma("s", T.CAP[:, half(h, 1024)], T.cap[:, half(h, 1024)], "dcap%d" % h, [], ["CAP%d" % h], 256)
+    iota(T.UI[0:96, :], [[1, 128]], 0, 128, "UI")
     iota(T.PI[:], [[0, 1]], 0, 1, "PI")
     iota(T.IOT[:], [[1, 256]], 0, 0, "IOT")
     iota(T.IO16[:], [[0, 16], [1, 16]], 0, 0, "IO16")
     iota(T.IOB[:], [[16, 8], [0, 16]], 0, 0, "IOB")
-    iota(T.ONES[:], [[0, 256]], 1, 0, "ONES")
-    for name, c in (("C37", 37), ("CFAR", FAR), ("NEG", -131072)):
-        iota(T[name][:], [[0, 128]], c, 0, name)
+    for ap, c, key in ((T.ONES[:], 1.0, "ONES"), (T.ZERO[:], 0.0, "ZERO"), (T.TRI[:, 2:3 * Q:3], 0.0, "Y2"), (rw(TR, TR + Q), 0.0, "PKT"),
+                       (T.WD[:, 2048:2304], 0.0, "WDT")):
+        if key in OPT["ona"].split():
+            act(ap, T.IOT[:, 0:cols(ap)], ["IOT"], [key], scale=0.0, bias=c)
+        else:
+            fill(ap, c, key)
+    iota(T.CFAR[0:1, :], [[0, 128]], FAR, 0, "CFAR")
     iota(T.LIM[0:3, :], [[0, 128]], 9216, -6656, "LIM")
     iota(T.LIM[0:1, :], [[0, 128]], -256, 0, "LIM")
-    if "a" in OPT["cmp"]:
-        fill(col("HALF"), -0.5, "HALF")
-    iota(T.KC[0:1, 0:H], [[0, 8], [-1, 16]], 15, 0, "KC")
-    iota(T.KC[0:1, H:2 * H], [[0, H]], 0, 0, "KC")
-    iota(T.ALT[0:2, :], [[0, H], [1, 2]], 0, 0, "ALT")
-    for name, pattern, base in (("KC2", [[0, 8], [-2048, 16]], 30720), ("KR16", [[0, 8], [16, 16]], 15),
-                                ("KR", [[0, 8], [1, 16]], 0), ("IO256", [[256, 16]], 0), ("I16B", [[16, 16]], 0)):
-        iota(T[name][0:1, :], pattern, base, 0, name)
+    iota(T.NODE[0:2, :], [[-16, H]], 1008, 0, "NODE")
+    iota(T.NODE[0:1, :], [[0, H]], 1, 0, "NODE")
+    iota(T.KC[0:2, :], [[-1, 2], [0, H]], 1, 0, "KC")
+    iota(T.KC[0:1, 0:H], [[0, 8], [-1, 16]], 16, 0, "KC")
+    fill(T.KC2[0:2, :], -16777216.0, "KC2")
+    step("KC3")
+    iota(T.KC2[0:1, :], [[0, 32], [-2048, 16]], 30720, 0, "KC2")
+    step(None)
+
     for j in range(4):
-        iota(T.SP[:, half(j, 512)], [[0, 512]], 0, 0, "SP%d" % j)
-    iota(T.FS[:, 0:2 * WIN:WIN], [[0, 2]], 0, 0, "ENDS")
-    iota(T.BS[:, 2063:2 * WIN:WIN], [[0, 2]], 0, 0, "ENDS")
-    for j in range(4):
-        step("IO2K%d" % j)
+        step("IO2K%d" % j, "IO2K")
         iota(T.IO2K[:, half(j, 512)], [[1, 512]], 512 * j, 0, "IO2K")
-        step("LXT%d" % j)
+        step("LXT%d" % j, "LXT")
         iota(T.LXT[:, half(j, 512)], [[1, 64], [768, 8]], 64 * j, 0, "LXT")
     step(None)
-    fill(T.UU[:, 96:128], 2048, "RI3")
-    ts(T.UU[:, 0:32], u32, 2016, None, A.bitwise_and, None, ["UI"], ["RI0"])
-    ts(T.UU[:, 32:64], u32, 31, None, A.bitwise_and, None, ["UI"], ["RI1"])
-    tt(T.UU[:, 64:96], u32, u32, A.mult, ["UI"], ["RI2"])
-    ts(T.UU[:, 64:96], T.UU[:, 64:96], 5, 2047, A.arith_shift_right, A.bitwise_and, ["RI2"], ["RI2"])
-    cp(T.RH[:], T.UU[:, 0:128], ["RI0", "RI1", "RI2", "RI3", "UU"], ["RH"])
-    for k in range(4):
-        dma("a", T.ROWS[k:k + 1, :], T.RH[:, 32 * k:32 * k + 32], "dr%d" % k, ["RH"], ["ROW%d" % k], 8)
-    dma("s", T.RES[:, 0:ZC], T.res[:], "dres", [], ["RES", "RESG"], 832)
-    dma("s", T.CAP[:], T.cap[:], "dcap", [], ["CAP"], 512)
+    fill(T.RH[96:128, :], 2048.0, "RI3")
+    tt(T.UU[0:32, :], T.UI[0:32, :], T.UI[0:32, :], A.mult, ["UI"], ["RI0"])
+    ts(T.UU[0:32, :], T.UU[0:32, :], 5, 2047, A.arith_shift_right, A.bitwise_and, ["RI0"], ["RI0"])
+    ts(T.UU[32:64, :], T.UI[32:64, :], 31, None, A.bitwise_and, None, ["UI"], ["RI1"])
+    ts(T.UU[64:96, :], T.UI[64:96, :], 2016, None, A.bitwise_and, None, ["UI"], ["RI2"])
+    cp(T.RH[0:96, :], T.UU[0:96, :], ["RI0", "RI1", "RI2"], ["RH"])
+    dma("s", T.ROWS[0:4, :], T.RH[:], "drow", ["RH", "RI3"], ["ROWS"], 32)
     fill(T.RES[:, ZC:ZC + 16], 0.0, "RESZ")
-    fill(T.K4[:, 2:3], 1.0, "K42")
+    fill(T.K4[:, 0:1], 1.0, "K42")
     fill(T.K4[:, 3:4], 130.0, "K43")
-    ts(T.KI[:], T.PI[:], 15, None, A.bitwise_and, None, ["PI"], ["KI"])
+    ts(T.XI2[:, 40:41], T.PI[:], 15, None, A.bitwise_and, None, ["PI"], ["KI"])
     cp(col("PFL"), T.PI[:], ["PI"], ["PFL"])
-    cp(col("KF"), T.KI[:], ["KI"], ["KF"])
+    cp(col("KF"), T.XI2[:, 40:41], ["KI"], ["KF"])
     ts(T.ID[:], T.IOT[:, 0:128], col("PFL"), None, A.is_equal, None, ["IOT", "PFL"], ["ID"])
     tt(col("G16"), col("PFL"), col("KF"), A.subtract, ["PFL", "KF"], ["G16"])
     cp(T.IDH[:], T.ID[:], ["ID"], ["IDH"])
@@ -462,48 +333,52 @@ def rank_program(g, core, T, topo):
     ts(T.BO[:], T.IOB[:], col("G16"), None, A.is_equal, None, ["IOB", "G16"], ["BO"])
     ts(T.XI[:, 0:1], T.KAI[:], 63, None, A.bitwise_and, None, ["KAI"], ["XIu0"])
     cp(T.K4[:, 1:2], T.KAI[:], ["KAI"], ["K41"])
-    cp(T.K4[:, 0:1], T.XI[:, 0:1], ["XIu0"], ["K40"])
+    cp(T.K4[:, 2:3], T.XI[:, 0:1], ["XIu0"], ["K40"])
     mm(T.B1[0:4, 0:128], T.K4[:], T.IDH[:], True, True, ["K40", "K41", "K42", "K43", "IDH"], ["B1.k"])
     cp(T.KR4[0:4, :], T.B1[0:4, 0:128], ["B1.k"], ["KR4"])
-    if OPT["seg"] == "v":
-        fill(T.SEG[:], 256.0, "SEG")
-        fill(T.SEG[:, 0:2064:16], 0.0, "SEG")
-    else:
-        for j in range(4):
-            step("SEG%d" % j)
-            iota(T.SEG[:, half(j, 512)], [[0, 32], [256, 16]], 0, 0, "SEG")
-        step(None)
+    fill(T.SEG[:], 256.0, "SEG")
+    fill(T.SEG[:, 0:2064:16], 0.0, "SEG")
     fill(T.MB[:], 1e9, "MB")
-    fill(T.MB[:, 0:256:16], -1e9, "MB")
-    iota(T.PK[:, TR:TR + Q], [[0, Q]], 0, 0, "PKT")
-    iota(T.WD[:, 2048:2304], [[0, Q]], 0, 0, "WDT")
+    fill(T.MB[:, 0:512:16], -1e9, "MB")
+    if "f" in OPT["fb"]:
+        iota(T.FS[:, 0:2 * WIN:WIN], [[0, 2]], 0, 0, "ENDS")
+        iota(T.BS[:, 2063:2 * WIN:WIN], [[0, 2]], 0, 0, "ENDS")
+    act(T.SP[:], T.SEG[:, 0:2048], ["SEG"], ["SP%d" % j for j in range(4)], scale=0.0)
     fill(T.PAR[:], 1.0 / 8192, "PAR")
-    fill(T.QRT[0:1, :], -0.25, "QRT")
+    fill(T.W16[0:1, 144:145], -0.25, "QRT")
     cp(T.OFFC[:], T.IOT[:], ["IOT"], ["OFFC"])
     cp(col("WTF"), T.WTI[:], ["WTI"], ["WTF"])
     ts(col("G15"), col("G16"), 15.0, None, A.add, None, ["G16"], ["G15"])
-    ts(T.W16[:], T.IOT[:, 0:144], col("G15"), col("WTF"), A.is_equal, A.mult, ["IOT", "G15", "WTF"], ["W16"])
+    ts(T.W16[:, 0:144], T.IOT[:, 0:144], col("G15"), col("WTF"), A.is_equal, A.mult, ["IOT", "G15", "WTF"], ["W16"])
     cp(T.BOH[:], T.BO[:, 0:128:16], ["BO"], ["BOH"])
+
     def who(name):
         return "a" if name in OPT["ona"].split() else "v"
-    for name, c in (("N11M", -2048.0), ("NID", -1.0), ("N12M", -4096.0), ("P12M", 4096.0), ("N16M", -16.0), ("IDF", 1.0), ("P16M", 65536.0),
-                    ("M16M", -65536.0)):
-        lin(who(name), T[name][:], T.ID[:], c, 0.0, ["ID"], [name])
-    for name, c in (("NBO", -512.0), ("BO4", 2.0 * FAR), ("BW32K", 32768.0)) + ((("NBO2", -256.0),) if "a" in OPT["cmp"] else ()):
+    for name, c in (("N11M", -2048.0), ("NID", -1.0), ("N12M", -4096.0), ("P12M", 4096.0), ("N15M", -15.0), ("N16M", -16.0), ("IDF", 1.0),
+                    ("P16M", 65536.0), ("M16M", -65536.0)):
+        if name in OPT["onp"].split():
+            put("p", lambda name=name, c=c: g.affine_select(T[name][:], T.ZERO[:], [[-1, 128]], A.not_equal, c, 0, 1), ["ZERO"], [name], 382.0)
+        else:
+            lin(who(name), T[name][:], T.ID[:], c, 0.0, ["ID"], [name])
+    for name, c in (("NBO", -512.0), ("NBO2", -256.0), ("BO4", 2.0 * FAR)):
         lin(who(name), T[name][:], T.BO[:], c, 0.0, ["BO"], [name])
     for j in (0, 1):
-        lin("v", T.B16[:, half(j, 8)], T.BO[:, 0:128:16], 16.0, 0.0, ["BO"], ["B16"])
-    for name, c in (("NB8", -1.0), ("B32K", 32768.0), ("NB32K", -32768.0)):
-        lin(who(name), T[name][:], T.BO[:, 0:128:16], c, 0.0, ["BO"], [name])
+        lin("v", T.B16[:, half(j, 8)], T.BO[:, 0:128:16], 16.0, 0.0, ["BO"], ["B16%d" % j])
+        lin("v", T.BW32K[:, half(j)], T.BO[:], 32768.0, 0.0, ["BO"], ["BW32K%d" % j])
+    for name, c in (("B32K", 2048.0), ("NB32K", -2048.0)):
+        lin("v", T[name][:], T.B16[:], c, 0.0, ["B16"], [name])
     lin("a", T.NDEL[:], T.DELB[:], -1.0, 1.0, ["DELB"], ["NDEL"])
     put("p", lambda: g.affine_select(T.BT4[:], T.BO4[:], [[1, 128]], A.is_gt, 0.0, 0, -1), ["BO4"], ["BT4"], 382.0)
-    if "a" in OPT["um"]:
-        iota(T.FOUR[0:1, :], [[0, 8]], 4, 0, "FOUR")
-    lin(cq, T.OFFD[:], T.DELB[:], 67108864.0, -67108864.0, ["DELB"], ["OFFD"])
+    lin("v", T.OFFD[:], T.DELB[:], 67108864.0, -67108864.0, ["DELB"], ["OFFD"])
     act(T.LB[:], T.IOT[:, 0:16], ["IOT", "KF"], ["LB"], F.Identity, bias=col("KF"), scale=16.0)
-    lin(cq, T.TP[:], T.LB[:], 1.0, float(TR), ["LB"], ["TP"])
-    lin(cq, T.TW[:], T.LB[:], 1.0, 2048.0 + FAR, ["LB"], ["TW"])
+    lin("a", T.C37[:], T.LB[:], 37.0, 0.0, ["LB"], ["C37"])
+    lin("a", T.NMB[:], T.MB[:, 0:Q], -1.0, 0.0, ["MB"], ["NMB"])
+    fill(T.MTP[:], -1e9, "MTP")
+    lin("v", T.MTP[:, 0:Q:16], T.LB[:], 1.0, float(TR), ["LB"], ["MTP"])
+    lin("v", T.LB[:], T.LB[:], 1.0, 2048.0 + FAR, ["LB"], ["TW", "LB"])
     tt(T.IOTM[:], T.IOT[:], T.OFFD[:], A.add, ["IOT", "OFFD"], ["IOTM"])
+    for t in range(1, NT + 1):
+        act(T.NEW[:, half(t - 1, Q)], T.IOTM[:], ["IOTM"], ["NEW%d" % t], F.Relu, bias=2048.0 + 256.0 * (t - 1) + 4096.0 * (t + 2))
     ts(col("MULP"), col("KF"), 0.0, -15.0, A.is_equal, A.mult, ["KF"], ["MULP"])
     ts(col("ADDP"), col("KF"), 0.0, float(P0), A.is_equal, A.mult, ["KF"], ["ADDP"])
     ts(col("MULP"), col("MULP"), 16.0, None, A.add, None, ["MULP"], ["MULP"])
@@ -515,59 +390,61 @@ def rank_program(g, core, T, topo):
         step("TOH%d" % j)
         dma("s", T.TOH[:, s:2 * s], T.TOH[:, 0:s], "dt%d" % (j + 1), ["TOH"], ["TOH"], s // 4)
     step(None)
-    if tail:
-        ts(T.MASK[:], T.IO16[:, 0:16], col("KF"), 4096.0, A.is_le, A.mult, ["IO16", "KF"], ["MASK"])
+    ts(T.MASK[:], T.IO16[:, 0:16], col("KF"), 4096.0, A.is_le, A.mult, ["IO16", "KF"], ["MASK"])
     for b, lo, m in tail:
         step("NSEL%d" % (b % 2))
         ts(T.NSEL[:, lo:lo + m], T.ONES[:, 0:m], T.BO[:, 16 * (b - 8):16 * (b - 8) + 1], -1.0, A.mult, A.mult, ["ONES", "BO"], ["NSEL%d" % b])
     step(None)
 
-    tab = ["TAB%d" % j for j in range(4)]
+    tab = ["TAB%d" % j for j in range(8)]
     wdk = ["WDc%d" % j for j in range(8)]
 
     def table(j):
-        b = (3, 5)[j & 1]
-        k, ft, rk = whole[b] + whole[b + 1], T.FT[:, half(j & 1, 1024)], ["KR4", "ROW0", "ROW1", "ROW2", "ROW3"]
+        spec = OPT["ft"].split()[j]
+        bs, q = [int(x) for x in spec[:-2]], spec[-2:]
+        both, rk, fk = sum((whole[b] for b in bs), []), ["KR4", "ROWS"], ["FT%d" % ((j + y) % 4) for y in range(len(bs))]
+        lo, m = 512 * (j % 4), 512 * len(bs)
         step("tb%da" % j)
-        for x in (0, 1):
-            mm(bank(b + x, 0, 512), T.KR4[0:4, :], T.ROWS[0:4, half(2 * j + x, 512)], True, True, rk, whole[b + x])
-        lin(OPT["ft"][j], ft, bank(b, 0, 1024), 1.0 / 2048, -0.499755859375, k, ["FT%d" % (j & 1)])
+        for y, b in enumerate(bs):
+            mm(bank(b, 0, 512), T.KR4[0:4, :], T.ROWS[0:4, half(j + y, 512)], True, True, rk, whole[b])
         step("tb%db" % j)
-        for x in (0, 1):
-            mm(bank(b + x, 0, 512), T.KR4[0:4, :], T.ROWS[0:4, half(2 * j + x, 512)], True, False, rk, whole[b + x])
-            mm(bank(b + x, 0, 512), T.N11M[:], T.FT[:, half(2 * (j & 1) + x, 512)], False, True, ["N11M", "FT%d" % (j & 1)], whole[b + x])
-        act(T.TAB[:, half(j, 1024)], bank(b, 0, 1024), k, [tab[j]])
+        lin(q[0], T.FT[:, lo:lo + m], bank(bs[0], 0, m), 1.0 / 2048, -0.499755859375, both, fk)
+        step("tb%dc" % j)
+        for y, b in enumerate(bs):
+            mm(bank(b, 0, 512), T.KR4[0:4, :], T.ROWS[0:4, half(j + y, 512)], True, False, rk, whole[b])
+            mm(bank(b, 0, 512), T.N11M[:], T.FT[:, lo + 512 * y:lo + 512 * y + 512], False, True, ["N11M", fk[y]], whole[b])
+        step("tb%dd" % j)
+        cp(T.TAB[:, 512 * j:512 * j + m], bank(bs[0], 0, m), both, tab[j:j + len(bs)], q[1])
 
     def first_room(j):
-        b = (3, 5)[j]
+        b = int(OPT["sli"][j])
         step("sli%d" % j)
-        for x in (0, 1):
-            mm(bank(b + x, 0, 512), T.ID[:], T.CAP[:, half(2 * j + x, 512)], True, False, ["ID", "CAP"], whole[b + x])
-            mm(bank(b + x, 0, 512), T.NID[:], T.RES[:, half(2 * j + x, 512)], False, True, ["NID", "RES"], whole[b + x])
-        act(T.SL[:, half(j, 1024)], bank(b, 0, 1024), whole[b] + whole[b + 1], ["SL"], F.Relu)
+        mm(bank(b, 0, 512), T.ID[:], T.CAP[:, half(j, 512)], True, False, ["ID", "CAP%d" % (j // 2)], whole[b])
+        mm(bank(b, 0, 512), T.NID[:], T.RES[:, half(j, 512)], False, True, ["NID", "RES"], whole[b])
+        act(T.SL[:, half(j, 512)], bank(b, 0, 512), whole[b], ["SL"], F.Relu)
 
-    def first_offsets():
-        src = T.BRI[:, 0:2048:8]
-        step("FO1")
-        ts(T.UU[:], src, 65535, None, A.bitwise_and, None, ["BRI"], ["UU"])
-        ts(T.B7[:, 0:256], src, 0.0, 4096.0, A.is_lt, A.mult, ["BRI"], ["B7.x"])
-        ts(T.UI[:], src, 4095, None, A.bitwise_and, None, ["BRI"], ["UI"])
-        ts(T.B7[:, 256:512], T.UU[:], 4096.0, 4096.0, A.is_lt, A.mult, ["UU"], ["B7.hi"])
-        tt(T.KS[:, 0:Q], T.UI[:], T.B7[:, 0:256], A.max, ["B7.x", "UI"], ["KS0", "KS1"])
-        step("FO2")
-        tt(T.CNS[:], T.KS[:, 0:Q], T.B7[:, 256:512], A.max, ["B7.hi", "KS0", "KS1"], ["CNS"])
-        step("FO3")
-        ts(T.EO[:], T.CNS[:], float(ZC), None, A.min, None, ["CNS"], ["EO"])
+    def first_pieces(names):
+        for x in names.split():
+            (table if x[0] == "t" else first_room)(int(x[1]))
+
+    def first_offsets(h):
+        fo, key = T.FO[:, half(h)], "FO%d" % h
+        step("FOa%d" % h)
+        ts(fo, T.BRI[:, 1024 * h:1024 * h + 1024:8], 4095.0, None, A.max, None, ["BRI%d" % h], [key])
+        step("FOb%d" % h)
+        ts(fo, fo, 4095, None, A.bitwise_and, None, [key], [key])
+        step("FOc%d" % h)
+        ts(T.EO[:, half(h)], fo, float(ZC), None, A.min, None, [key], ["EO%d" % h])
         step(None)
 
-    def k_part(q, out, key, t, more):
-        lin(q, out, T.WD[:, t - 1:2048:8], 1.0 / 65536, 199.50390625 + more, [wdk[t - 1]], [key])
+    def k_part(out, key, t, more):
+        lin("a", out, T.WD[:, t - 1:2048:8], 1.0 / 65536, 199.50390625 + more, [wdk[t - 1]], [key])
 
     def offsets(t):
         step("n12")
-        lin(OPT["n12"], T.N12[:], T.WD[:, t - 1:2048:8], 1.0 / 4096, 219.5625, [wdk[t - 1]], ["N12"])
+        lin("a", T.N12[:], T.WD[:, t - 1:2048:8], 1.0 / 4096, 219.5625, [wdk[t - 1]], ["N12"])
         step("kn")
-        k_part(OPT["kn"], T.KN[:], "KN", t, 0)
+        k_part(T.KN[:], "KN", t, 0)
         step("t1")
         mm(T.B7[:, 0:256], T.ID[:], T.N12[:], True, False, ["ID", "N12"], ["B7.x"])
         mm(T.B7[:, 0:256], T.N16M[:], T.KN[:], False, True, ["N16M", "KN"], ["B7.x"])
@@ -582,9 +459,10 @@ def rank_program(g, core, T, topo):
         mm(o, T.IDF[:], T.WD[:, t - 1:2048:8], True, False, ["IDF", wdk[t - 1]], ["B7.hi"])
         mm(o, T.N12M[:], T.N12[:], False, False, ["N12M", "N12"], ["B7.hi"])
         mm(o, T.ID[:], T.BD2[:], False, False, ["ID", "bd2"], ["B7.hi"])
+        step("t3")
         mm(o, T.ID[:], T.BD1[:], False, True, ["ID", "bd1"], ["B7.hi"])
         step("eo")
-        ts(T.EO[:], o, 901120.0, float(ZC), A.add, A.min, ["B7.hi"], ["EO"])
+        ts(T.EO[:], o, 901120.0, float(ZC), A.add, A.min, ["B7.hi"], ["EO0", "EO1"])
 
     def pk(h):
         return ["PK%d" % j for j in range(4 * h, 4 * h + 4)]
@@ -594,87 +472,99 @@ def rank_program(g, core, T, topo):
 
     def rows(q, j, m, name="rows"):
         lo, hi = 32 * j, 32 * (j + m)
+        if q == "v" and name == "rows":
+            by = 32 // OPT["rp"]
+            for x in range(lo, hi, by):
+                step(name + str(x // 32) + "abcd"[x % 32 // by], name)
+                gather(q, rw(16 * x, 16 * (x + by)), T.RES[:, 0:3344], T.EO[:, x:x + by], ["RES", "RESG", "RESZ", "EO%d" % (j // 4)], ["PK%d" % (x // 32)])
+            return
         step(name + str(j))
-        gather(q, T.PK[:, 16 * lo:16 * hi], T.RES[:, 0:3344], T.EO[:, lo:hi], ["RES", "RESG", "RESZ", "EO"], ["PK%d" % i for i in range(j, j + m)])
-
-    def row0(h):
-        return T.PK[:, 2048 * h:2048 * h + 2048:16]
+        gather(q, rw(16 * lo, 16 * hi), T.RES[:, 0:3344], T.EO[:, lo:hi], ["RES", "RESG", "RESZ", "EO%d" % (j // 4)], ["PK%d" % i for i in range(j, j + m)])
 
     def aside(h):
-        return T.PK[:, P0 + H * h:P0 + H * h + H]
+        return rw(P0 + H * h, P0 + H * h + H)
 
     def row0_aside(q, t, j, m, name="as"):
         lo, hi, keys = 32 * j, 32 * (j + m), ["PK%d" % x for x in range(j, j + m)]
         step(name + str(j))
-        cp(T.PK[:, P0 + lo:P0 + hi], T.PK[:, 16 * lo:16 * hi:16], keys, ["P0%d" % x for x in range(j, j + m)], q)
+        cp(rw(P0 + lo, P0 + hi), rw(16 * lo, 16 * hi, 16), keys, ["P0%d" % x for x in range(j, j + m)], q)
         hi = min(hi, Q - 32 * OPT["clip"][t - 1])
         if hi > lo:
             if q == "p":
-                iota(T.PK[:, 16 * lo:16 * hi:16], [[0, hi - lo]], 255, 0, keys)
-            elif q == "a":
-                act(T.PK[:, 16 * lo:16 * hi:16], T.ONES[:, 0:hi - lo], ["ONES"], keys, scale=255.0)
+                iota(rw(16 * lo, 16 * hi, 16), [[0, hi - lo]], 255, 0, keys)
             else:
-                fill(T.PK[:, 16 * lo:16 * hi:16], 255.0, keys)
+                fill(rw(16 * lo, 16 * hi, 16), 255.0, keys)
 
     def cap_wide(t, ks, name="cx"):
-        cx, cut = "CX%d" % (t & 1), Q - (32 * OPT["clip"][t - 1] if OPT["clipw"] == "t" else 0)
+        cx, cut = "CX%d" % (t & 1), Q - 32 * OPT["clip"][t - 1]
         for k in ks:
-            step(name + str(max(k - 1, 0) // 3))
+            step(name + str(k))
             cp(T[cx][:, k:16 * cut:16], T.CAP[:, t - 1:8 * cut:8], ["CAP"], [cx + "k%d" % k], "p")
 
     def words(t):
+        win = T.WD[:, 0:2304]
+        if t == NT:
+            step("PW")
+            cp(T.PW[:], T.CNS[:, 15:256:16], ["CNS"], ["PW"])
+            step("WOLD")
+            tt(T.WOLD[:], win.indirect(T.PW[:]), T.NDEL[:], A.mult, wdk + ["WDT", "PW", "NDEL"], ["WOLD0", "WOLD1"], GATHER)
+            step("WD")
+            tt(win.indirect(T.PW[:]), T.WOLD[:], T.NEW[:, half(t - 1, Q)], A.add, ["WOLD0", "WOLD1", "NEW%d" % t, "PW"], wdk + ["WDT"], SCATTER)
+            return
         step("ld")
-        tt(T.LD[:], T.CNS[:, 15:256:16], T.TW[:], A.min, ["CNS", "TW"], ["LD"])
+        tt(T.XF[:, 16:32], T.CNW[:, 15:256:16], T.LB[:], A.min, ["CNW", "TW"], ["LD"])
         step("lc")
-        tt(T.LC[:], T.LD[:], bank(2, 400, 416), A.max, ["LD", "B2.far"], ["LC"])
+        tt(T.LC[:], T.XF[:, 16:32], bank(2, 400, 416), A.max, ["LD", "B2.far"], ["LC"])
         step("pw")
         ts(T.PW[:], T.LC[:], -float(FAR), None, A.add, None, ["LC"], ["PW"])
-        win = T.WD[:, 0:2304]
-        step("wold")
-        tt(T.WOLD[:], win.indirect(T.PW[:]), T.NDEL[:], A.mult, wdk + ["WDT", "PW", "NDEL"], ["WOLD"], GATHER)
-        step("wd")
-        tt(win.indirect(T.PW[:]), T.WOLD[:], T.NEW[:, half(t - 1, Q)], A.add, ["WOLD", "NEW%d" % t, "PW"], wdk + ["WDT"], SCATTER)
+        n, m = OPT["wp"], Q // OPT["wp"]
+        for x in range(n):
+            step("wold" + "abcd"[x])
+            tt(T.WOLD[:, half(x, m)], win.indirect(T.PW[:, half(x, m // 16)]), T.NDEL[:, 0:m], A.mult, wdk + ["WDT", "PW", "NDEL"], ["WOLD%d" % x], GATHER)
+        for x in range(n):
+            step("wd" + "abcd"[x])
+            at = Q * (t - 1) + m * x
+            tt(win.indirect(T.PW[:, half(x, m // 16)]), T.WOLD[:, half(x, m)], T.NEW[:, at:at + m], A.add, ["WOLD%d" % x, "NEW%d" % t, "PW"],
+               wdk + ["WDT"], SCATTER)
 
     def suspended(t):
+        z, wd = T.B0[:, 256:512], T.WD[:, t - 1:2048:8]
         step("oh")
         gather("a", T.OH[:], T.TOH[:], T.KL[:], ["TOH", "KL0", "KL1"], ["OH"])
-        z, wd = T.B0[:, 256:512], T.WD[:, t - 1:2048:8]
         step("kp")
-        k_part(OPT["kp"], T.KP[:], "KP", t, t)
+        k_part(T.KP[:], "KP", t, t)
         step("z")
         mm(z, T.P16M[:], T.OH[:], True, False, ["P16M", "OH"], ["B0.z"])
-        mm(z, T.M16M[:], T.KP[:], False, False, ["M16M", "KP"], ["B0.z"])
-        mm(z, T.P12M[:], T.OK0[:], False, OPT["su"] == "a", ["P12M", "OK00", "OK01"], ["B0.z"])
-        if OPT["su"] == "a":
-            step("su1")
-            act(T.DW[:], z, ["B0.z"], ["DW"], F.Relu, scale=-1.0)
-            step("su2")
-            mm(z, T.IDF[:], wd, True, False, ["IDF", wdk[t - 1]], ["B0.z"])
-            mm(z, T.NID[:], T.DW[:], False, True, ["NID", "DW"], ["B0.z"])
-            act(wd, z, ["B0.z"], [wdk[t - 1]])
-        else:
+        mm(z, T.P12M[:], T.OK0[:], False, False, ["P12M", "OK0"], ["B0.z"])
+        mm(z, T.M16M[:], T.KP[:], False, OPT["su"] == "a", ["M16M", "KP"], ["B0.z"])
+        if OPT["su"] == "v":
             mm(z, T.IDF[:], wd, False, True, ["IDF", wdk[t - 1]], ["B0.z"])
-            step("su1")
+            step("su")
             tt(wd, wd, z, A.min, [wdk[t - 1], "B0.z"], [wdk[t - 1]])
+            return
+        step("su1")
+        act(T.DW[:], z, ["B0.z"], ["DW"], F.Relu, scale=-1.0)
+        step("su2")
+        mm(z, T.IDF[:], wd, True, False, ["IDF", wdk[t - 1]], ["B0.z"])
+        mm(z, T.NID[:], T.DW[:], False, True, ["NID", "DW"], ["B0.z"])
+        act(wd, z, ["B0.z"], [wdk[t - 1]])
 
     def parity():
         o, pc = T.B7[0:1, 256:384], T.COL[0:1, 7:8]
         step("par1")
-        mm(o, T.QRT[0:1, 0:1], T.ONES[0:1, 0:H], True, False, ["QRT", "ONES"], ["B7.hi"])
-        for h in (0, 1):
-            mm(o, T.SACC[:, h:h + 1], T.PAR[:], False, h == 1, ["PAR", "SACC%d" % h], ["B7.hi"])
-        act(pc, T.B7[0:1, 256:257], ["B7.hi"], ["PC"], bias=MAGIC)
+        mm(o, T.W16[0:1, 144:145], T.ONES[0:1, 0:H], True, False, ["QRT", "ONES"], ["B7.hi"])
+        mm(o, T.SACC[:, 0:1], T.PAR[:], False, True, ["PAR", "SACC"], ["B7.hi"])
         step("par2")
-        act(pc, pc, ["PC"], ["PC"], bias=1024.0 * MAGIC, scale=-1024.0)
+        ts(pc, T.B7[0:1, 256:257], MAGIC, -MAGIC, A.add, A.add, ["B7.hi"], ["PC"])
         step("par3")
-        act(T.LIM[0:1, :], o, ["B7.hi", "PC"], ["LIM"], F.Identity, bias=pc, scale=1024.0)
+        ts(T.LIM[0:1, :], o, pc, 1024.0, A.subtract, A.mult, ["B7.hi", "PC"], ["LIM"])
 
     BA = [T.B1, T.B2]
 
     def one_round(t):
         c = t - 1
         cx = "CX%d" % (t & 1)
-        L0 = 2 * c * Q
+        L0 = 3 * c * Q
         dst = cores[(rank + 1 + c % (n - 1)) % n]
         last = t == NT
         plan = OPT["score"][c]
@@ -684,197 +574,143 @@ def rank_program(g, core, T, topo):
         sk = ["SND%d%d" % (t, h) for h in (0, 1)]
 
         def msg(buf, lo, hi, by=1):
-            if OPT["pack"]:
-                return buf[:, L0 + lo:L0 + hi:by]
-            return buf[:, L0 + 2 * lo + 1:L0 + 2 * hi:2 * by]
+            return buf[:, L0 + 3 * lo + 2:L0 + 3 * hi:3 * by]
 
         land = [msg(T.LAND, H * h, H * h + H) for h in (0, 1)]
         snd = [msg(T.SND, H * h, H * h + H) for h in (0, 1)]
-
-        def low_bits(at, m, name, src, keys, mask):
-            step(name[0] + "i" + name[1])
-            cp(T.XI[:, at:at + m], src, keys, ["XI" + name])
-            step(name[0] + "j" + name[1])
-            ts(T.XI2[:, at:at + m], T.XI[:, at:at + m], mask, None, A.bitwise_and, None, ["XI" + name], ["XJ" + name])
-
-        def largest_key(hs, src, keys, at, name, mask, out, ok):
-            lo, hi, m, ks = H * hs[0], H * hs[-1] + H, 8 * len(hs), ["KS%d" % h for h in hs]
-            step(name[0] + "s" + name[1])
-            scan(T.KS[:, lo:hi], T.MB[:, 0:hi - lo], src, A.min, A.max, ["MB"] + keys, ks)
-            low_bits(at, m, name, T.KS[:, lo + 15:hi:16], ks, mask)
-            step(name[0] + "x" + name[1])
-            tt(out[:, lo:hi], T.XI2[:, at:at + m].indirect(T.OFFC[:, 0:m]), T.DELB[:, 0:hi - lo], A.mult, ["XJ" + name, "OFFC", "DELB"], ok, GATHER)
 
         def first_rows():
             d = T.B0[:, 0:256]
             if t == 1:
                 for h in (0, 1):
                     step("r0" + "bc"[h])
-                    mm(T.B0[:, half(h)], T.NID[:], cap[h], True, False, ["NID", "CAP"], ["B0.d"])
+                    mm(T.B0[:, half(h)], T.NID[:], cap[h], True, False, ["NID", "CAP%d" % h], ["B0.d"])
                     mm(T.B0[:, half(h)], T.ID[:], aside(h), False, True, ["ID"] + p0(h), ["B0.d"])
-                    relu(OPT["r0"], T.R0[:, half(h)], T.B0[:, half(h)], 0.0, ["B0.d"], ["R0%d" % h])
+                    act(T.R0[:, half(h)], T.B0[:, half(h)], ["B0.d"], ["R0%d" % h], F.Relu)
                 return
             step("r0a")
             mm(d, T.NID[:], T.CAP[:, c:2048:8], True, False, ["NID", "CAP"], ["B0.d"])
             step("r0b")
-            mm(d, T.ID[:], T.PK[:, P0:P0 + Q], False, True, ["ID"] + p0(0) + p0(1), ["B0.d"])
-            relu(OPT["r0"], T.R0[:], d, 0.0, ["B0.d"], ["R00", "R01"])
+            mm(d, T.ID[:], rw(P0, P0 + Q), False, True, ["ID"] + p0(0) + p0(1), ["B0.d"])
+            act(T.R0[:], d, ["B0.d"], ["R00", "R01"], F.Relu)
 
-        def sums(h):
-            b, key = BA[h], "B%d.k" % (1 + h)
+        def worst(h):
+            b, key, nk = BA[h], "B%d.k" % (1 + h), "B%d.n" % (3 + h)
             clip = [j for j in range(8 - OPT["clip"][c], 8) if j // 4 == h]
             cut = H - 32 * len(clip)
+            over = bank(3 + h, 0, H)
             step("kc%d" % h)
-            mm(b[:, 0:2 * H], T.ONES[0:1, 0:H], T.KC[0:1, :], True, False, ["KC", "ONES"], [key])
+            mm(b[:, 0:2 * H], T.NODE[0:2, :], T.KC[0:2, :], True, False, ["KC", "NODE"], [key])
+            mm(b[:, 2 * H:3 * H], T.ID[:], cap[h], False, False, ["ID", "CAP%d" % h], [key])
             cxk, cmk = [cx + "k%d" % k for k in range(16)] + [cx + "h%d" % h], ["CM%d" % j for j in range(4 * h, 4 * h + 4)]
             if cut:
-                mm(b[0:cut, 0:2 * H:16], T.CAP[:, c + 1024 * h:1024 * h + 8 * cut:8], T.B16[:], False, False, ["B16", "CAP"], [key])
-                s = slice(2048 * h, 2048 * h + 16 * cut)
-                step("cm%d" % h)
-                scan(T.CM[:, s], T[cx][:, s], T.PK[:, s], A.min, A.max, cxk + pk(h)[:cut // 32], cmk[:cut // 32])
-            if clip:
-                for y, j in enumerate(clip):
-                    step("clipa%d" % y)
-                    if OPT["clipw"] == "cx":
-                        mm(bank(3 + y, 0, 512), T.NID[:], T[cx][:, half(j, 512)], True, False, ["NID"] + cxk, whole[3 + y])
-                    else:
-                        for k in range(16):
-                            mm(bank(3 + y, k, 512, 16), T.NID[:], T.CAP[:, c + 256 * j:256 * (j + 1):8], k == 0, False, ["NID", "CAP"], whole[3 + y])
-                for x in range(0, len(clip), 2):
-                    step("clipb%d" % x)
-                    two = list(enumerate(clip))[x:x + 2]
-                    for y, j in two:
-                        mm(bank(3 + y, 0, 512), T.ID[:], T.PK[:, half(j, 512)], False, True, ["ID", "PK%d" % j], whole[3 + y])
-                    act(T.CM[:, 512 * two[0][1]:512 * (two[-1][1] + 1)], bank(3 + x, 0, 512 * len(two)), sum((whole[3 + y] for y, j in two), []),
-                        ["CM%d" % j for y, j in two], F.Relu)
+                room = T.CAP[:, c + 1024 * h:1024 * h + 8 * cut:8]
+                mm(b[0:cut, 0:2 * H:16], room, T.B16[:], False, False, ["B16", "CAP%d" % h], [key])
+                step("cnc%d" % h)
+                mm(bank(3 + h, 0, cut), T.N15M[:], room, True, False, ["N15M", "CAP%d" % h], whole[3 + h])
+                if cut < H:
+                    mm(bank(3 + h, cut, H), T.ZERO[0:1, :], T.ONES[0:1, cut:H], False, False, ["ZERO", "ONES"], whole[3 + h])
+                m = 16 * cut // OPT["cmp"]
+                for x in range(OPT["cmp"]):
+                    lo = 2048 * h + m * x
+                    step("cm%d%d" % (h, x))
+                    scan(T.CM[:, lo:lo + m], T[cx][:, lo:lo + m], rw(lo, lo + m), A.min, A.max, cxk + pk(h)[m * x // 512:m * (x + 1) // 512],
+                         cmk[m * x // 512:m * (x + 1) // 512])
+            for x in range(0, len(clip), 2):
+                two = clip[x:x + 2]
+                step("clipa%d" % x)
+                for y, j in enumerate(two):
+                    for k in range(16):
+                        mm(bank(5 + y, k, 512, 16), T.NID[:], T.CAP[:, c + 256 * j:256 * (j + 1):8], k == 0, False, ["NID", "CAP"], whole[5 + y])
+                step("clipb%d" % x)
+                for y, j in enumerate(two):
+                    mm(bank(5 + y, 0, 512), T.ID[:], rw(512 * j, 512 * j + 512), False, True, ["ID", "PK%d" % j], whole[5 + y])
+                act(T.CM[:, 512 * two[0]:512 * (two[-1] + 1)], bank(5, 0, 512 * len(two)), whole[5] + whole[6], ["CM%d" % j for j in two], F.Relu)
             step("sum%d" % h)
             for k in range(1, 16):
                 mm(b[:, k:2 * H:16], T.CM[:, 2048 * h + k:2048 * h + 2048:16], T.B16[:], False, False, ["B16"] + cmk, [key])
             mm(b[:, 0:2 * H:16], T.R0[:, half(h)], T.B16[:], False, True, ["B16", "R0%d" % h], [key])
-
-        def running(h):
-            m, lo, at = 2048 // OPT["pieces"], 2048 * h, WIN * h
-            for x in range(OPT["pieces"]):
-                a, z = m * x, m * x + m
-                step("bs%d%d" % (h, x))
-                scan(T.BS[:, at + 14 + z:at + 14 + a:-1], T.PK[:, lo + z - 1:(lo + a - 1 if lo + a else None):-1], T.SEG[:, 1:m + 1], A.max, A.min,
-                     ["SEG"] + pk(h)[a // 512:(z + 511) // 512], ["BS%d%d" % (h, x)])
-            step("rest%d" % h)
-            cp(row0(h), aside(h), p0(h), pk(h), OPT["restore"][h])
-            for x in range(OPT["pieces"]):
-                a, z = m * x, m * x + m
-                step("fs%d%d" % (h, x))
-                scan(T.FS[:, at + 1 + a:at + 1 + z], T.PK[:, lo + a:lo + z], T.SEG[:, 1:m + 1], A.max, A.min,
-                     ["SEG"] + pk(h)[a // 512:(z + 511) // 512], ["FS%d%d" % (h, x)])
-
-        def messages(h):
-            b, at = BA[h], WIN * h
-            fs, bs = (["%s%d%d" % (x, h, y) for y in range(OPT["pieces"])] + ["ENDS"] for x in ("FS", "BS"))
-            cm, ck, gk, vk, y0, y1 = T["CMP%d" % h], "B%d.c" % (5 + h), "B%d.g" % (3 + h), "B%d.v" % (5 + h), "Y0%d" % h, "Y1%d" % h
-            room, v0, v1 = bank(5 + h, 0, H), bank(3 + h, 0, H), bank(5 + h, H, 3 * H)
-            ya, yb = (T.TWO[:, 256 * h + j:256 * h + 256:2] for j in (0, 1))
-            step("cap%d" % h)
-            mm(room, T.ID[:], cap[h], True, False, ["ID", "CAP"], [ck])
-            mm(bank(5 + h, 3 * H, 4 * H), T.ID[:], aside(h), False, True, ["ID"] + p0(h), [ck])
-            step("m0%d" % h)
-            tt(T.M0[:, half(h)], T.BS[:, at + 16:at + 2064:16], bank(5 + h, 3 * H, 4 * H), A.max, bs + [ck], ["M0%d" % h])
-            step("lim%d" % h)
-            mm(v0, T.LIM[0:2, :], T.ONES[0:2, 0:H], True, False, ["LIM", "ONES"], [gk])
-            step("cmp%d0" % h)
-            tt(cm[:, 0:H], T.M0[:, half(h)], room, A.is_gt, ["M0%d" % h, ck], ["CMP%d0" % h])
-            mm(v0, T.NBO[:], cm[:, 0:H], False, True, ["NBO", "CMP%d0" % h], [gk])
-            step("ok%d" % h)
-            act(T.OK0[:, half(h)], v0, [gk], ["OK0%d" % h, "SACC%d" % h], F.Relu, accum=T.SACC[:, h:h + 1])
-            act(v0, v0, [gk], [gk], F.Relu)
-            step("mn%d" % h)
-            tt(yb, T.M0[:, half(h)], v0, A.min, ["M0%d" % h, gk], [y1])
-            o, ok = b[:, 384:392], "B%d.kl" % (1 + h)
-            step("klc%d" % h)
-            mm(o, T.KR16[0:1, :], T.ONES[0:1, 0:8], True, False, ["KR16", "ONES"], [ok])
-            mm(o, T.ONES[0:1, 0:H], T.IO256[0:1, 0:8], False, False, ["IO256", "ONES"], [ok])
-            ks = 256 * h
+            for k in range(1, 16):
+                step("cnt%d%d" % (h, k * OPT["cnt"] // 16))
+                mm(over, T.ID[:], T.CM[:, 2048 * h + k:2048 * h + 2048:16], k == 1 and not cut, False, ["ID"] + cmk, whole[3 + h] if k == 1 else [nk])
+            mm(over, T.ID[:], T.R0[:, half(h)], False, True, ["ID", "R0%d" % h], [nk])
+            step("sg%d" % h)
+            act(T.SG[:, half(h)], over, [nk], ["SG%d" % h], F.Sign, bias=-0.5)
+            o, ok, ks = b[:, 384:392], "B%d.kl" % (1 + h), 2 * H * h
             step("ks%d" % h)
-            scan(T.KS[:, ks:ks + 256], T.MB[:], b[:, 0:256], A.min, A.max, ["MB", "B%d.k" % (1 + h)], ["KS%d" % h])
+            scan(T.KS[:, ks:ks + 2 * H], T.MB[:, 0:2 * H], b[:, 0:2 * H], A.min, A.max, ["MB", key], ["KS%d" % h])
             step("ki%d" % h)
-            tt(T.XF[:, half(h, 8)], T.KS[:, ks + 15:ks + H:16], T.KS[:, ks + H + 15:ks + 256:16], A.subtract, ["KS%d" % h], ["XF%d" % h])
+            tt(T.XF[:, half(h, 8)], T.KS[:, ks + 15:ks + H:16], T.KS[:, ks + H + 15:ks + 2 * H:16], A.subtract, ["KS%d" % h], ["XF%d" % h])
             step("kx%d" % h)
             tt(T.XA[:, half(h)], T.XF[:, half(h, 8)].indirect(T.OFFC[:, 0:8]), T.DELB[:, 0:H], A.mult, ["XF%d" % h, "OFFC", "DELB"], ["XA%d" % h], GATHER)
-            mm(o, T.XA[:, half(h)], T.NB8[:], False, True, ["XA%d" % h, "NB8"], [ok])
-            kl = T.KL[:, half(h, 8)]
+            mm(o, T.XA[:, half(h)], T.BOH[:], True, True, ["XA%d" % h, "BOH"], [ok])
             step("kl%d" % h)
-            cp(kl, o, [ok], ["KL%d" % h])
-            step("xs%d" % h)
-            gather(OPT["xs"], T.XS[:, half(h)], T.FS[:, at:at + 2048], kl, fs + ["KL%d" % h], ["XS%d" % h])
-            step("m1%d" % h)
-            tt(ya, T.BS[:, at + 16:at + 2064].indirect(kl), T.XS[:, half(h)], A.max, bs + ["KL%d" % h, "XS%d" % h], [y0], GATHER)
-            step("lin%d" % h)
-            mm(v1, T.LIM[0:2, :], T.ALT[0:2, :], True, False, ["LIM", "ALT"], [vk])
-            step("cmp%d1" % h)
-            tt(cm[:, H:2 * H], ya, room, A.is_gt, [y0, ck], ["CMP%d1" % h])
-            mm(bank(5 + h, H + 1, 3 * H, 2), T.NBO[:], cm[:, H:2 * H], False, True, ["NBO", "CMP%d1" % h], [vk])
-            out = slice(L0 + 256 * h, L0 + 256 * h + 256)
-            step("snd%d" % h)
-            scan(T.SND[:, out], v1, T.TWO[:, half(h, 256)], A.min, A.max, [vk, y0, y1], [sk[h]])
-            put("p", (T.LAND[:, out], T.SND[:, out], "arr%d%d" % (t, h), dst), [sk[h]], [lk[h]], 300.0, FIRST if t == 1 and h == 0 else LAT)
+            ts(T.KL[:, half(h, 8)], o, -1.0, 1024.0, A.mult, A.add, [ok], ["KL%d" % h])
 
-        def messages_old(h):
-            b, s = BA[h], half(h, 2048)
-            o, ok = b[:, 384:392], "B%d.kl" % (1 + h)
-            step("klc%d" % h)
-            mm(o, T.KR16[0:1, :], T.ONES[0:1, 0:8], True, False, ["KR16", "ONES"], [ok])
-            mm(o, T.ONES[0:1, 0:H], T.IO256[0:1, 0:8], False, False, ["IO256", "ONES"], [ok])
-            largest_key([h], b[:, 0:H], ["B%d.k" % (1 + h)], 16 + 8 * h, "k%d" % h, 15, T.XA, ["XA%d" % h])
-            mm(o, T.XA[:, half(h)], T.NB8[:], False, True, ["XA%d" % h, "NB8"], [ok])
-            kl = T.KL[:, half(h, 8)]
-            step("kl%d" % h)
-            cp(kl, o, [ok], ["KL%d" % h])
+        def kept():
+            o = T.B0[:, 256:512]
+            step("lim")
+            mm(o, T.LIM[0:3, :], T.ONES[0:3, :], True, False, ["LIM", "ONES"], ["B0.z"])
+            step("v0")
+            mm(o, T.NBO2[:], T.SG[:], False, True, ["NBO2", "SG0", "SG1"], ["B0.z"])
+            step("ok")
+            act(T.OK0[:], o, ["B0.z"], ["OK0", "SACC"], F.Relu, accum=T.SACC[:, 0:1])
+
+        def messages(h):
+            lo, kl = 2048 * h, T.KL[:, half(h, 8)]
+            cmk = ["SC%d" % j for j in range(4 * h, 4 * h + 4)]
+            ck, vk, sg = "B%d.k" % (1 + h), "B%d.v" % (3 + h), T.SG[:, half(h)]
+            tri = [T.TRI[:, 3 * H * h + j:3 * H * h + 3 * H:3] for j in (0, 1)]
+            v = [bank(3 + h, H + j, 4 * H, 3) for j in range(3)]
+            if OPT["fb"][h] == "f":
+                m, at = 2048 // OPT["pieces"], WIN * h
+                for x in range(OPT["pieces"]):
+                    a, z = m * x, m * x + m
+                    step("bs%d%d" % (h, x))
+                    scan(T.BS[:, at + 14 + z:at + 14 + a:-1], T.PK[:, lo + z - 1:(lo + a - 1 if lo + a else None):-1], T.SEG[:, 1:m + 1], A.max, A.min,
+                         ["SEG"] + pk(h)[a // 512:z // 512], ["BS%d%d" % (h, x)])
+            if OPT["clip"][c] < 4 or h == 0:
+                step("rest%d" % h)
+                cp(rw(lo, lo + 2048, 16), aside(h), p0(h), pk(h), "v" if t == 1 else OPT["restore"][h])
+            m = 2048 // OPT["pieces"]
+            if OPT["fb"][h] == "f":
+                at = WIN * h
+                fs, bs = (["%s%d%d" % (x, h, y) for y in range(OPT["pieces"])] + ["ENDS"] for x in ("FS", "BS"))
+                for x in range(OPT["pieces"]):
+                    a, z = m * x, m * x + m
+                    step("fs%d%d" % (h, x))
+                    scan(T.FS[:, at + 1 + a:at + 1 + z], rw(lo + a, lo + z), T.SEG[:, 1:m + 1], A.max, A.min, ["SEG"] + pk(h)[a // 512:z // 512], [fs[x]])
+                step("xf%d" % h)
+                gather(OPT["xf"], T.XS[:, half(h)], T.FS[:, at:at + 2048], kl, fs + ["KL%d" % h], ["XS%d" % h])
+                step("m1%d" % h)
+                tt(tri[1], T.BS[:, at + 16:at + 2064].indirect(kl), T.XS[:, half(h)], A.max, bs + ["KL%d" % h, "XS%d" % h], ["Y1%d" % h], GATHER)
+                most, cmk = tri[1], ["Y1%d" % h]
             step("xs%d" % h)
-            gather("a", T.XS[:, half(h)], T.PK[:, s], kl, pk(h) + ["KL%d" % h], ["XS%d" % h])
-            step("sw%d" % h)
-            scatter(T.PK[:, s], kl, aside(h), p0(h) + ["KL%d" % h], pk(h))
-            step("row%d" % h)
-            cp(row0(h), T.XS[:, half(h)], ["XS%d" % h], pk(h), OPT["row0"])
-            lo = 2048 * h
-            fb, s = "FB%d" % h, slice(lo + 2047, lo - 1 if lo else None, -1)
-            step("fb%d" % h)
-            scan(T.FB[:, s], T.SEG[:], T.PK[:, s], A.min, A.max, ["SEG"] + pk(h), [fb])
-            m = [T.FB[:, lo + j:lo + 2048:16] for j in (0, 1)]
-            cm, ck, gk, vk = T["CMP%d" % h], "B%d.c" % (5 + h), "B%d.g" % (3 + h), "B%d.v" % (1 + h)
-            signs = OPT["cmp"][h] == "a"
-            step("cap%d" % h)
-            if signs:
-                for j in (0, 1):
-                    mm(bank(5 + h, H * j, H * j + H), T.NID[:], cap[h], j == 0, False, ["NID", "CAP"], [ck])
-            else:
-                mm(bank(5 + h, 0, H), T.ID[:], cap[h], True, True, ["ID", "CAP"], [ck])
-            verdicts = ((bank(3 + h, 0, H), gk), (b[:, 256:384], vk))
-            step("lim%d" % h)
-            for o, ok in verdicts:
-                mm(o, T.LIM[0:3 if signs else 2, :], T.ONES[0:3 if signs else 2, 0:H], True, False, ["LIM", "ONES"], [ok])
-            if signs:
-                step("cmp%d0" % h)
-                for j in (0, 1):
-                    mm(bank(5 + h, H * j, H * j + H), T.ID[:], m[j], False, j == 1, ["ID", fb], [ck])
-                act(cm[:], bank(5 + h, 0, 256), [ck, "HALF"], ["CMP%d0" % h, "CMP%d1" % h], F.Sign, bias=col("HALF"))
-            for j, (o, ok) in enumerate(verdicts):
-                step("cmp%d%d" % (h, 1 if signs else j))
-                if not signs:
-                    tt(cm[:, half(j)], m[j], bank(5 + h, 0, H), A.is_gt, [fb, ck], ["CMP%d%d" % (h, j)])
-                mm(o, T["NBO2" if signs else "NBO"][:], cm[:, half(j)], False, True, ["NBO", "NBO2", "CMP%d%d" % (h, j)], [ok])
-            step("ok%d" % h)
-            act(T.OK0[:, 256 * h + 1:256 * h + 256:2], verdicts[0][0], [gk], ["OK0%d" % h, "SACC%d" % h], F.Relu, accum=T.SACC[:, h:h + 1])
-            step("mn%d" % h)
-            tt(T.FB[:, lo + 8:lo + 2048:16], m[1], verdicts[1][0], A.min, [fb, vk], [fb])
-            out = slice(L0 + 256 * h, L0 + 256 * h + 256)
+            gather(OPT["xs"][h], tri[0], rw(lo, lo + 2048), kl, pk(h) + ["KL%d" % h], ["Y0%d" % h])
+            if OPT["fb"][h] != "f":
+                step("zero%d" % h)
+                scatter(rw(lo, lo + 2048), kl, T.ZERO[:], ["ZERO", "KL%d" % h], pk(h))
+                for x in range(OPT["pieces"]):
+                    a, z = m * x, m * x + m
+                    step("fs%d%d" % (h, x))
+                    scan(T.SC[:, lo + a:lo + z], T.SEG[:, 0:m], rw(lo + a, lo + z), A.min, A.max, ["SEG"] + pk(h)[a // 512:z // 512], cmk[a // 512:z // 512])
+                most = T.SC[:, lo + 15:lo + 2048:16]
+                step("two%d" % h)
+                cp(tri[1], most, cmk, ["Y1%d" % h], OPT["two"][h])
+            step("lin%d" % h)
+            mm(v[0], T.ZERO[0:1, :], T.ONES[0:1, 0:H], True, False, ["ZERO", "ONES"], [vk])
+            mm(v[1], T.LIM[0:3, :], T.ONES[0:3, 0:H], False, False, ["LIM", "ONES"], [vk])
+            mm(v[2], T.LIM[0:2, :], T.ONES[0:2, 0:H], False, False, ["LIM", "ONES"], [vk])
+            step("v1%d" % h)
+            mm(v[1], T.NBO2[:], sg, False, False, ["NBO2", "SG%d" % h], [vk])
+            step("cmp%d" % h)
+            tt(T.CMP[:, half(h)], most, BA[h][:, 2 * H:3 * H], A.is_gt, cmk + [ck], ["CMP%d" % h])
+            mm(v[2], T.NBO[:], T.CMP[:, half(h)], False, True, ["NBO", "CMP%d" % h], [vk])
+            out = slice(L0 + 3 * H * h, L0 + 3 * H * h + 3 * H)
             step("snd%d" % h)
-            if OPT["pack"]:
-                out = slice(L0 + H * h, L0 + H * h + H)
-                scan(T.TWO[:, half(h, 256)], T.OK0[:, half(h, 256)], T.FB[:, lo:lo + 2048:8], A.min, A.max, [fb, "OK0%d" % h], ["TWO%d" % h])
-                step("pk%d" % h)
-                cp(T.SND[:, out], T.TWO[:, 256 * h + 1:256 * h + 256:2], ["TWO%d" % h], [sk[h]], OPT["pack"])
-            else:
-                scan(T.SND[:, out], T.OK0[:, half(h, 256)], T.FB[:, lo:lo + 2048:8], A.min, A.max, [fb, "OK0%d" % h], [sk[h]])
-            put("p", (T.LAND[:, out], T.SND[:, out], "arr%d%d" % (t, h), dst), [sk[h]], [lk[h]], 300.0, FIRST if t == 1 and h == 0 else LAT)
+            scan(T.SND[:, out], bank(3 + h, H, 4 * H), T.TRI[:, half(h, 3 * H)], A.min, A.max, [vk, "Y0%d" % h, "Y1%d" % h, "Y2"], [sk[h]])
+            first = t == 1 and h == 0
+            put("p", (T.LAND[:, out], T.SND[:, out], "arr%d%d" % (t, h), dst), [sk[h]], [lk[h]], 300.0 + (FIRST if first else 0.0), LAT)
 
         def room_left():
             step("sla")
@@ -883,35 +719,19 @@ def rank_program(g, core, T, topo):
                 step("slb%d" % h)
                 mm(T.B0[:, half(h)], T.NID[:], snd[h], False, h == 1, ["NID", sk[h]], ["B0.d"])
             step("sl")
-            relu(OPT["sl"], T.SL[:, c:2048:8], T.B0[:, 0:256], 0.0, ["B0.d"], ["SL"])
+            act(T.SL[:, c:2048:8], T.B0[:, 0:256], ["B0.d"], ["SL"], F.Relu)
 
         def candidates(h):
-            ul, key = BA[h][:, 392:400], "B%d.u" % (1 + h)
-            step("uc%d" % h)
-            mm(ul, T.KR[0:1, :], T.C37[0:1, 0:8], True, False, ["KR", "C37"], [key])
-            mm(ul, T.C37[0:1, :], T.I16B[0:1, half(h, 8)], False, False, ["I16B", "C37"], [key])
+            ul, key = (T.B2[:, 440:448], "B2.u") if h == 0 else (T.B1[:, 0:8], "B1.k")
             step("u%d" % h)
             for r in range(16):
-                mm(ul, T.W16[:, 15 - r:143 - r], msg(T.LAND, H * h + r, H * h + H, 16), False, r == 15, ["W16", lk[h]], [key])
-            if OPT["um"][h] == "a":
-                step("ui%d" % h)
-                act(T.UH[:], ul, [key], ["UH"], bias=127.5001220703125, scale=1.0 / 4096)
-                o = bank(6, 0, 8)
-                step("ud%d" % h)
-                mm(o, T.KR[0:1, :], T.C37[0:1, 0:8], True, False, ["KR", "C37"], ["B6.c"])
-                mm(o, T.C37[0:1, :], T.I16B[0:1, half(h, 8)], False, False, ["I16B", "C37"], ["B6.c"])
-                mm(o, T.CFAR[0:1, :], T.FOUR[0:1, :], False, False, ["CFAR", "FOUR"], ["B6.c"])
-                step("ue%d" % h)
-                for r in range(16):
-                    mm(o, T.W16[:, 15 - r:143 - r], msg(T.LAND, H * h + r, H * h + H, 16), False, False, ["W16", lk[h]], ["B6.c"])
-                step("uj%d" % h)
-                mm(o, T.N12M[:], T.UH[:], False, True, ["N12M", "UH"], ["B6.c"])
-                step("ul%d" % h)
-                cp(T.UL[:, half(h, 8)], o, ["B6.c"], ["UL%d" % h])
-            else:
-                low_bits(8 * h, 8, "u%d" % h, ul, [key], 4095)
-                step("ul%d" % h)
-                cp(T.UL[:, half(h, 8)], T.XI2[:, half(h, 8)], ["XJu%d" % h], ["UL%d" % h])
+                mm(ul, T.W16[:, 15 - r:143 - r], msg(T.LAND, H * h + r, H * h + H, 16), r == 0, r == 15, ["W16", lk[h]], [key])
+            step("ui%d" % h)
+            tt(T.XI[:, half(h, 8)], ul, T.C37[:, half(h, 8)], A.add, [key, "C37"], ["XIu%d" % h])
+            step("uj%d" % h)
+            ts(T.XI2[:, half(h, 8)], T.XI[:, half(h, 8)], 4095, None, A.bitwise_and, None, ["XIu%d" % h], ["XJu%d" % h])
+            step("ul%d" % h)
+            cp(T.UL[:, half(h, 8)], T.XI2[:, half(h, 8)], ["XJu%d" % h], ["UL%d" % h])
             if OPT["pf"] == "v":
                 step("pf%d" % h)
                 gather("v", T.PH[:, half(h)], T.TAB[:], T.UL[:, half(h, 8)], tab + ["UL%d" % h], ["PF%d" % h])
@@ -928,186 +748,178 @@ def rank_program(g, core, T, topo):
             for j, m in runs([j for j in mine if plan[j] == "s"], 2):
                 bn, s = (3, 5)[[x[0] for x in runs(share, 2)].index(j) & 1], slice(512 * j, 512 * (j + m))
                 mx = ["MX%d" % (j + y) for y in range(m)]
+                w, per = 32 * m, 16 // m
+                step("m63%d" % j)
+                ts(T.M63[:, 32 * j:32 * j + w], msg(T.LAND, 32 * j, 32 * j + w), 63.0, None, A.min, None, [lk[h]], ["M63%d" % j])
                 step("shw%d" % j)
-                for y in range(m):
-                    for k in range(16):
-                        mm(bank(bn + y, k, 512, 16), T.ID[:], msg(T.LAND, 32 * (j + y), 32 * (j + y + 1)), k == 0, False, ["ID", lk[h]], whole[bn + y])
+                for k in range(16):
+                    mm(bank(bn, w * k, w * k + w), T.ID[:], T.M63[:, 32 * j:32 * j + w], k % per == 0, False, ["ID", "M63%d" % j], whole[bn + k // per])
                 step("shg%d" % j)
                 gather("a", T.MX[:, s], sl, T.P16[:, 32 * j:32 * (j + m)], ["SL", "P16%d" % h], mx)
                 step("shr%d" % j)
-                for y in range(m):
-                    mm(bank(bn + y, 0, 512), T.NID[:], T.MX[:, half(j + y, 512)], False, True, ["NID", mx[y]], whole[bn + y])
+                for k in range(16):
+                    mm(bank(bn, w * k, w * k + w), T.NID[:], T.MX[:, 512 * j + k:512 * (j + m):16], False, k % per == per - 1, ["NID"] + mx,
+                       whole[bn + k // per])
                 act(T.SC[:, s], bank(bn, 0, 512 * m), sum((whole[bn + y] for y in range(m)), []), ["SC%d" % (j + y) for y in range(m)], F.Relu)
             for j, m in runs([j for j in mine if plan[j] == "v"], OPT["wm"]):
                 lo, sp = 512 * (j % 4), ["SP%d" % ((j + y) % 4) for y in range(m)]
                 step("sp%d" % j)
-                cp(T.SP[:, lo:lo + 512 * m:16], msg(T.LAND, 32 * j, 32 * (j + m)), [lk[h]], sp, OPT["sp"])
+                cp(T.SP[:, lo:lo + 512 * m:16], msg(T.LAND, 32 * j, 32 * (j + m)), [lk[h]], sp)
                 step("wd%d" % j)
                 scan(T.MX[:, 512 * j:512 * (j + m)], T.SEG[:, 0:512 * m], T.SP[:, lo:lo + 512 * m], A.min, A.max, ["SEG"] + sp,
                      ["MX%d" % (j + y) for y in range(m)])
-            for j, m in runs([j for j in mine if plan[j] == "p"], 4):
-                for k in range(16):
-                    step("gw%d%s" % (j, "abcd"[k // 4]))
-                    cp(T.MX[:, 512 * j + k:512 * (j + m):16], msg(T.LAND, 32 * j, 32 * (j + m)), [lk[h]], ["MX%dk%d" % (j + y, k) for y in range(m)], "p")
             for j, m in runs([j for j in mine if plan[j] != "s"], OPT["vm"]):
-                s = slice(512 * j, 512 * (j + m))
-                mx = sum((["MX%d" % x] + ["MX%dk%d" % (x, k) for k in range(16)] for x in range(j, j + m)), [])
-                step("sc%d" % j)
-                tt(T.SC[:, s], sl.indirect(T.P16[:, 32 * j:32 * (j + m)]), T.MX[:, s], A.min, ["SL", "P16%d" % h] + mx,
-                   ["SC%d" % (j + y) for y in range(m)], GATHER)
+                n = int(OPT["scp"][j])
+                for y in range(n):
+                    lo, hi = 32 * j + 32 * m * y // n, 32 * j + 32 * m * (y + 1) // n
+                    step("sc%d" % j + ("", "b")[y], "sc")
+                    tt(T.SC[:, 16 * lo:16 * hi], sl.indirect(T.P16[:, lo:hi]), T.MX[:, 16 * lo:16 * hi], A.min,
+                       ["SL", "P16%d" % h] + ["MX%d" % x for x in range(j, j + m)], ["SC%d" % x for x in range(j, j + m)], GATHER)
 
-        def keys(h, b, at, key, first, final):
-            o = b[:, at:at + H]
-            every = key + [x + "s%d" % y for x in key[:2] for y in range(4)]
+        def keys(h):
+            b, at = T.B1, 2 * H * h
             parts = []
             for kind in (True, False):
-                for j, m in runs([j for j in range(4 * h, 4 * h + 4) if (plan[j] == "s") == kind], OPT["pm"]):
+                for j, m in runs([j for j in range(4 * h, 4 * h + 4) if (plan[j] == "s") == kind], 2 if kind else OPT["pm"]):
                     j %= 4
                     parts += [(j, m, kind)] if j == 0 or m == 1 or j == 2 else [(j, 1, kind), (j + 1, m - 1, kind)]
-            pf, ident, ik = (T.PH, T.IDH, "IDH") if OPT["pf"] == "v" else (T.PF, T.IDF, "IDF")
 
-            def nodes(j, m, end):
-                mm(b[32 * j:32 * (j + m), at:at + H], pf[:, H * h + 32 * j:H * h + 32 * (j + m)], ident[:], False, end, ["PF%d" % h, ik], key if end else key[:1])
+            def nodes(j, m, key):
+                pf, ident = ("PF", "IDF") if OPT["pf"] == "a" else ("PH", "IDH")
+                mm(b[32 * j:32 * (j + m), at:at + H], T[pf][:, H * h + 32 * j:H * h + 32 * (j + m)], T[ident][:], False, False, ["PF%d" % h, ident, "B1.p"], key)
+            step("pn%d" % h)
+            nodes(0, 4, ["B1.p%d" % z for z in range(4 * h, 4 * h + 4)])
             step("pc%d" % h)
-            mm(o, T.ONES[:, 0:H], T.NEG[:], first, False, ["NEG", "ONES"], key if first else key[:1])
-            mm(o, T.ONES[0:1, 0:H], T.KC2[0:1, :], False, False, ["KC2", "ONES"], key[:1])
             for j, m, kind in parts:
                 if kind:
-                    mm(b[32 * j:32 * (j + m), at:at + H], msg(T.LAND, H * h + 32 * j, H * h + 32 * (j + m)), T.BW32K[:], False, False, ["BW32K", lk[h]], key[:1])
-            step("pn%d" % h)
-            plain = [j for j in range(4) if plan[4 * h + j] != "s"]
-            for j, m in runs(plain, 4):
-                for x in ([(j, m)] if j == 0 or m == 1 or j == 2 else [(j, 1), (j + 1, m - 1)]):
-                    nodes(x[0], x[1], False)
-            for x, (j, m, kind) in enumerate(parts):
+                    mm(b[32 * j:32 * (j + m), at:at + 2 * H], T.M63[:, H * h + 32 * j:H * h + 32 * (j + m)], T.BW32K[:], False, False,
+                       ["BW32K", "M63%d" % (4 * h + j), "B1.p"], ["B1.p%d" % y for y in range(4 * h + j, 4 * h + j + m)])
+            for j, m, kind in parts:
                 lo, hi = 32 * j, 32 * (j + m)
-                wk, sk2 = "NB32K" if kind else "B32K", [key[0] + "s%d" % y for y in range(j, j + m)]
+                wk, key = "NB32K" if kind else "B32K", ["B1.p%d" % y for y in range(4 * h + j, 4 * h + j + m)]
                 step("ps%d" % (4 * h + j))
+                first = 2048 * h + 16 * lo
                 for k in range(16):
-                    mm(b[lo:hi, at + k:at + H:16], T.SC[:, 2048 * h + 16 * lo + k:2048 * h + 16 * hi:16], T[wk][:], False, False,
-                       [wk, key[0]] + ["SC%d" % y for y in range(4 * h + j, 4 * h + j + m)], sk2)
-                if kind:
-                    mm(b[lo:hi, at:at + H], pf[:, H * h + lo:H * h + hi], ident[:], False, False, ["PF%d" % h, ik, key[0]], sk2)
-            if final:
-                mm(b[:, at:at + 2], T.ONES[0:1, 0:H], T.KC[0:1, H:H + 2], False, True, ["ONES", "KC"], every)
+                    sc = T.SC[:, first + (hi - lo) * k:first + (hi - lo) * (k + 1)] if kind else T.SC[:, first + k:2048 * h + 16 * hi:16]
+                    mm(b[lo:hi, at + k:at + 2 * H:16], sc, T[wk][:], False, False, [wk, "B1.p"] + ["SC%d" % y for y in range(4 * h + j, 4 * h + j + m)], key)
 
-        def parents(hs):
-            if len(hs) == 2:
-                key = ["B1.p0", "B1.p1", "B1.k"]
-                keys(0, T.B1, H, key, True, False)
-                keys(1, T.B1, 2 * H, key[1::-1], False, True)
-                src = T.B1[:, H:3 * H]
-            else:
-                key = ["B%d.p" % (1 + hs[0]), "B%d.k" % (1 + hs[0])]
-                keys(hs[0], BA[hs[0]], H, key, True, True)
-                src = BA[hs[0]][:, H:2 * H]
-            xw, lvk, lo, hi, z = ["XW%d" % h for h in hs], ["B2.lv%d" % h for h in hs], 8 * hs[0], 8 * hs[-1] + 8, hs[-1]
-            largest_key(hs, src, key, 32 + lo, "q%d" % z, 2047, T.XW, xw)
-            for h in hs:
-                mm(bank(2, 416 + 8 * h, 424 + 8 * h), T.XW[:, half(h)], T.BOH[:], True, True, ["XW%d" % h, "BOH"], ["B2.lv%d" % h])
-            lv, lk2 = T.LV[:, lo:hi], ["LV%d" % h for h in hs]
-            step("lv%d" % z)
-            cp(lv, bank(2, 416 + lo, 416 + hi), lvk, lk2)
-            step("vb%d" % z)
-            gather("v", T.VB[:, 16 * lo:16 * hi], T.IO2K[:], lv, ["IO2K"] + lk2, ["VB%d" % h for h in hs])
+        def parents():
+            every = ["B1.p"] + ["B1.p%d" % j for j in range(8)]
+            step("pc")
+            mm(T.B1[:], T.ONES[0:2, 0:H], T.KC2[0:2, :], True, False, ["KC2", "ONES"], every + ["B1.k", "B1.kl"])
+            keys(0)
+            keys(1)
+            step("pe")
+            mm(T.B1[:, H:H + 2], T.ONES[0:1, 0:H], T.ZERO[0:1, 0:2], False, True, ["ONES", "ZERO"], every + ["B1.k", "B1.kl"])
+            step("qs")
+            scan(T.QS[:], T.MB[:], T.B1[:], A.min, A.max, ["MB", "B1.p", "B1.k", "B1.kl"], ["QS"])
+            step("qi")
+            for h in (0, 1):
+                at = 2 * H * h
+                tt(T.QF[:, half(h, 8)], T.QS[:, at + 15:at + H:16], T.QS[:, at + H + 15:at + 2 * H:16], A.subtract, ["QS"], ["QF%d" % h])
+            step("qx")
+            tt(T.XW[:], T.QF[:].indirect(T.OFFC[:, 0:16]), T.DELB[:], A.mult, ["QF0", "QF1", "OFFC", "DELB"], ["XW"], GATHER)
+            for h in (0, 1):
+                mm(bank(2, 416 + 8 * h, 424 + 8 * h), T.XW[:, half(h)], T.BOH[:], h == 0, h == 1, ["XW", "BOH"], ["B2.lv"])
+            step("lv")
+            cp(T.LV[:], bank(2, 416, 432), ["B2.lv"], ["LV"])
+            step("vb")
+            gather("v", T.VB[:], T.IO2K[:], T.LV[:], ["IO2K", "LV"], ["VB"])
             if not last:
-                step("lxw%d" % z)
-                act(T.LXW[:, 16 * lo:16 * hi], T.LXT[:].indirect(lv), ["LXT"] + lk2, ["LXW%d" % h for h in hs], F.Abs, bias=-768.0 * t, rate=GATHER)
+                step("lxw")
+                act(T.LXW[:], T.LXT[:].indirect(T.LV[:]), ["LXT", "LV"], ["LXW"], F.Abs, bias=-768.0 * t, rate=GATHER)
 
         now[0] = t
         if t > 1:
             parity()
         else:
-            for j in range(OPT["tab0"]):
-                table(j)
-            first_room(0)
-            first_room(1)
+            first_pieces(OPT["early"])
         first_rows()
-        sums(0)
-        sums(1)
-        running(0)
-        running(1)
+        worst(0)
+        worst(1)
+        if t == 1:
+            first_pieces(OPT["late"])
+        kept()
         messages(0)
         messages(1)
-        room_left()
         if t > 1:
             words(t - 1)
-        else:
-            for j in range(OPT["tab0"], 4):
-                table(j)
         if not last:
             offsets(t + 1)
+        room_left()
+        suspended(t)
         for h in (0, 1):
-            step("res%d" % h)
+            step("res%d" % h, "res")
             cp(T.RES[:, c + 1024 * h:1024 * h + 1024:8], snd[h], [sk[h]], ["RES"], "p")
         if last:
             step("yr")
             dma("s", T.yr[:], T.RES[:, 0:2048], "dyr", ["RES"], ["yr"], 512)
         else:
             for h in (0, 1):
-                step("gh%d" % h)
-                cp(T.RES[:, 2048 + c * Q + H * h:2048 + c * Q + H * h + H], land[h], [lk[h]], ["RESG"], OPT["ghost"])
+                step("gh%d" % h, "gh")
+                cp(T.RES[:, 2048 + c * Q + H * h:2048 + c * Q + H * h + H], land[h], [lk[h]], ["RESG"], "p")
         if t + 2 <= NT:
-            cap_wide(t + 2, range(1, 16))
+            cap_wide(t + 2, range(0 if OPT["clip"][t + 1] < OPT["clip"][t - 1] else 1, 16))
         step("offa")
-        mm(T.B7[:, 0:256], T.ID[:], T.OFFD[:], True, False, ["ID", "OFFD"], ["B7.x"])
-        mm(T.B7[:, 0:256], T.ID[:], T.OFFA[:], False, False, ["ID", "OFFA"], ["B7.x"])
+        mm(T.B7[:, 0:256], T.NID[:], T.OFFD[:], True, False, ["NID", "OFFD"], ["B7.x"])
+        if not last:
+            mm(T.B7[:, 0:256], T.ID[:], T.OFFA[:], False, False, ["ID", "OFFA"], ["B7.x"])
         for h in (0, 1):
             candidates(h)
             scores(h)
         if not last:
             j = 0
-            for x in OPT["rows"].split():
+            for x in OPT["rows"][c].split():
                 rows(x[0], j, len(x))
-                row0_aside(OPT["aside"], t + 1, j, len(x))
                 j += len(x)
-        suspended(t)
-        step("new")
-        relu(OPT["new"], T.NEW[:, half(c, Q)], T.IOTM[:], 2048.0 + 256.0 * c + 4096.0 * (t + 2), ["IOTM"], ["NEW%d" % t])
-        for hs in ([[0, 1]] if OPT["whole"] else [[0], [1]]):
-            parents(hs)
-        if tail:
-            step("eqm")
-            mm(bank(5, 0, tail_cols), T.XW[:, half(1)], T.NSEL[:, 0:tail_cols], True, False, ["XW1"] + ["NSEL%d" % x[0] for x in tail], whole[5])
-            for b, lo, m in tail:
-                mm(bank(5, lo, lo + 16), T.ID[:], T.MASK[:], False, False, ["ID", "MASK"], ["B5.c"])
-            step("eqt")
-            for b, lo, m in tail:
-                mm(bank(5, lo, lo + m), T.IDH[:], T.VB[:, 16 * b:Q], False, b == 15, ["IDH", "VB1"], ["B5.c"])
-            step("eqv")
-            ts(T.EQT[:, 0:tail_cols], bank(5, 0, tail_cols), 0.0, None, A.is_equal, None, whole[5], ["EQT"])
-            for b, lo, m in tail:
-                mm(T.B7[:, 16 * b:Q], T.BO4[:], T.EQT[:, lo:lo + m], False, False, ["BO4", "EQT", "B7.x"], ["B7.x%d" % b])
+            for x in OPT["as"].split():
+                row0_aside(x[0], t + 1, int(x[1]), int(x[2]))
+        parents()
+        step("eqm")
+        mm(bank(5, 0, tail_cols), T.XW[:, half(1)], T.NSEL[:, 0:tail_cols], True, False, ["XW"] + ["NSEL%d" % x[0] for x in tail], whole[5])
+        for b, lo, m in tail:
+            mm(bank(5, lo, lo + 16), T.ID[:], T.MASK[:], False, False, ["ID", "MASK"], ["B5.c"])
+        step("eqt")
+        for b, lo, m in tail:
+            mm(bank(5, lo, lo + m), T.IDH[:], T.VB[:, 16 * b:Q], False, b == 15, ["IDH", "VB"], ["B5.c"])
+        step("eqv")
+        ts(T.EQT[:, 0:tail_cols], bank(5, 0, tail_cols), 0.0, None, A.is_equal, None, whole[5], ["EQT"])
+        for b, lo, m in tail:
+            mm(T.B7[:, 16 * b:Q], T.BO4[:], T.EQT[:, lo:lo + m], False, False, ["BO4", "EQT", "B7.x"], ["B7.x%d" % b])
         for i in range(first_tail):
             step("eq%d" % i)
-            ts(T.EQ[:, i, 0:256 - 16 * i], T.VB[:, 16 * i:256], bank(2, 416 + i, 417 + i), None, A.is_equal, None,
-               ["VB0", "VB1", "B2.lv0", "B2.lv1"], ["EQ%d" % i])
-            if i < 15:
-                mm(T.B7[:, 16 * i + 16:256], T.BO4[:], T.EQ[:, i, 16:256 - 16 * i], False, False, ["BO4", "EQ%d" % i, "B7.x"], ["B7.x%d" % i])
+            ts(T.EQ[:, i, 0:256 - 16 * i], T.VB[:, 16 * i:256], bank(2, 416 + i, 417 + i), None, A.is_equal, None, ["VB", "B2.lv"], ["EQ%d" % i])
+            mm(T.B7[:, 16 * i + 16:256], T.BO4[:], T.EQ[:, i, 16:256 - 16 * i], False, False, ["BO4", "EQ%d" % i, "B7.x"], ["B7.x%d" % i])
+        step("eqx")
         if not last:
-            step("eqx")
-            mm(T.B7[:, 0:256], T.MULD[:], T.LXW[:], False, False, ["MULD", "LXW0", "LXW1", "B7.x"], ["B7.xm"])
+            mm(T.B7[:, 0:256], T.MULD[:], T.LXW[:], False, False, ["MULD", "LXW", "B7.x"], ["B7.xm"])
+        else:
+            mm(T.B7[:, 0:256], T.IDH[:], T.VB[:], False, False, ["IDH", "VB", "B7.x"], ["B7.xm"])
         e = first_tail - 2
         step("eqd")
         mm(T.B7[:, 0:16 * e], T.BT4[:], T.EQ[:, 0:e, 0:16], False, False, ["BT4", "B7.x"] + ["EQ%d" % i for i in range(e)], ["B7.xd"])
         step("eqe")
         mm(T.B7[:, 16 * e:16 * e + 32], T.BT4[:], T.EQ[:, e:e + 2, 0:16], False, True, ["BT4", "EQ%d" % e, "EQ%d" % (e + 1)],
            ["B7.x", "B7.xm", "B7.xd"] + ["B7.x%d" % i for i in range(16)])
-        step("far")
-        mm(bank(2, 400, 416), T.CFAR[0:1, :], T.ONES[0:1, 0:16], True, False, ["CFAR", "ONES"], ["B2.far"])
-        for h in (0, 1):
-            mm(bank(2, 400 + 8 * h, 408 + 8 * h), T.XW[:, half(h)], T.BOH[:], False, h == 1, ["XW%d" % h, "BOH"], ["B2.far"])
+        if last:
+            step("MTW")
+            lin("v", T.MTP[:, 0:Q:16], T.LB[:], 1.0, -float(FAR), ["TW"], ["MTP"])
         step("cns")
-        scan(T.CNS[:], T.MB[:], T.B7[:, 0:256], A.min, A.max, ["MB", "B7.x"], ["CNS"])
+        scan(T.CNS[:], T.MTP[:], T.B7[:, 0:256], A.max, A.min, ["MTP", "B7.x"], ["CNS"])
         if not last:
-            step("lb")
-            tt(T.LB[:], T.CNS[:, 15:256:16], T.TP[:], A.min, ["CNS", "TP"], ["LB"])
+            step("far")
+            mm(bank(2, 400, 416), T.CFAR[0:1, :], T.ONES[0:1, 0:16], True, False, ["CFAR", "ONES"], ["B2.far"])
+            for h in (0, 1):
+                mm(bank(2, 400 + 8 * h, 408 + 8 * h), T.XW[:, half(h)], T.BOH[:], False, h == 1, ["XW", "BOH"], ["B2.far"])
             step("pl")
-            cp(T.PL[:], T.LB[:], ["LB"], ["PL"])
+            cp(T.PL[:], T.CNS[:, 15:256:16], ["CNS"], ["PL"])
+            step("cnw")
+            scan(T.CNW[:], T.NMB[:], T.B7[:, 0:256], A.max, A.min, ["NMB", "B7.x"], ["CNW"])
             step("patch")
-            scatter(T.PK[:], T.PL[:], msg(T.LAND, 0, Q), ["PL"] + lk, pk(0) + pk(1) + p0(0) + p0(1) + ["PKT"])
+            scatter(rw(0, 4608), T.PL[:], msg(T.LAND, 0, Q), ["PL"] + lk, pk(0) + pk(1) + p0(0) + p0(1) + ["PKT"])
 
-    first_offsets()
+    first_offsets(0)
+    first_offsets(1)
     for j in range(8):
         cp(T.WD[:, j:2048:8], T.BRI[:, j:2048:8], ["BRI"], ["WDc%d" % j])
     j = 0
@@ -1117,15 +929,19 @@ def rank_program(g, core, T, topo):
     for h in (0, 1):
         row0_aside(OPT["as1"][h], 1, 4 * h, 4, "AS")
     step(None)
-    cut1 = Q - (32 * OPT["clip"][0] if OPT["clipw"] == "t" else 0)
-    for lo in range(0, cut1, H):
-        m, sp = min(H, cut1 - lo), ["SP%d" % j for j in range(4)]
-        step("SX%d" % (lo // H))
-        cp(T.SP[:, 0:16 * m:16], T.CAP[:, 8 * lo:8 * (lo + m):8], ["CAP"], sp)
-        step(None)
-        scan(T.CX1[:, 16 * lo:16 * (lo + m)], T.SEG[:, 0:16 * m], T.SP[:, 0:16 * m], A.min, A.max, ["SEG"] + sp, ["CX1h%d" % (lo // H)])
-    cap_wide(2, range(16), "CY")
-    step(None)
+    for t in (1, 2):
+        cut, cx = Q - 32 * OPT["clip"][t - 1], "CX%d" % (t & 1)
+        for lo in range(0, cut, H):
+            m, sp = min(H, cut - lo), ["SP%d" % j for j in range(4)]
+            if t == 2 and OPT["cy"][lo // H] == "p":
+                for k in range(16):
+                    step("CY%d" % k)
+                    cp(T[cx][:, 16 * lo + k:16 * (lo + m):16], T.CAP[:, t - 1 + 8 * lo:8 * (lo + m):8], ["CAP%d" % (lo // H)], [cx + "k%d" % k], "p")
+                continue
+            step("SX%d%d" % (t, lo // H))
+            cp(T.SP[:, 0:16 * m:16], T.CAP[:, t - 1 + 8 * lo:8 * (lo + m):8], ["CAP%d" % (lo // H)], sp)
+            step(None)
+            scan(T[cx][:, 16 * lo:16 * (lo + m)], T.SEG[:, 0:16 * m], T.SP[:, 0:16 * m], A.min, A.max, ["SEG"] + sp, [cx + "h%d" % (lo // H)])
     for t in range(1, NT + 1):
         one_round(t)
     now[0] = NT + 1
@@ -1139,7 +955,7 @@ def rank_program(g, core, T, topo):
     own = {"v": "cv", "t": "ct", "a": "ca", "p": "cp"}
     count = {k: 0 for k in own}
     known = {k: {} for k in queues}
-    lastw, readers, banks = {}, {}, {}
+    lastw, readers, banks, pieces = {}, {}, {}, {}
     sent = 0
     used = []
     for i in ORDERS[len(calls)]:
@@ -1148,9 +964,12 @@ def rank_program(g, core, T, topo):
         remote = q == "p" and lat > 0
         if remote:
             w, arrival = [], w[0]
-        toks = [lastw[k] for k in list(r) + list(w) if k in lastw]
+        piece = calls[i][8]
+        toks = [lastw[k] for k in w if k in lastw and not (piece and pieces.get(k) == (q, piece))]
         for k in w:
             toks += list(readers.get(k, {}).values())
+            pieces[k] = (q, piece)
+        toks += [lastw[k] for k in r if k in lastw]
         for b in banks_of(list(r) + list(w)):
             toks += [tok for e, tok in banks.get(b, {}).items() if e != q]
         best = {}

from concourse.mybir import AluOpType as A, ActivationFunctionType as F

NT = 6
Q = 256
H = 128
ZC = 3328
P0 = 4096
TR = 4352
WIN = 2080
FAR = 131072
MAGIC = 12582912.0
OPT = {
    "gs": "v a v a v a a a", "as1": "vv",
    "clip": [0, 0, 0, 0, 0, 0],
    "score": ["ssvvvvvs"] * 6,
    "vm": 1, "wm": 4, "pm": 2, "rows": ["aa aa aa a v"] * 6, "tail": 5, "restore": "pp", "pieces": 1, "cmp": 1, "cnt": 2, "fb": "zz", "xf": "a", "xs": "aa", "wp": 1, "rp": 4, "scp": "11221111", "cy": "pv", "su": "v", "bd1": "v", "bd2": "v", "two": "aa", "as": "p02 p22 p42 p61 v71", "pf": "a",
    "ft": "34aa - 56aa - 56aa - 5vv 6va", "sli": "7777",
    "early": "t0 t2", "late": "t4 s0 s1 t6 t7 s2 s3",
    "ona": "ONES WDT N11M NID N15M NBO NBO2 BO4", "onp": "N12M P12M N16M IDF P16M M16M",
    "own1": "", "own6": "",
}
CYCLE, PE_CYCLE, PE_CALL, GATHER, SCATTER, ACT = 0.83, 0.42, 4.0, 1.56, 3.8, 110.0
WAKE, DMA, LAT, FIRST = 80.0, 1700.0, 2000.0, 3000.0
SCRATCH = {
    "RES": ("sbuf", [128, 3344], "bfloat16"),
    "WD": ("sbuf", [128, 2304], "float32"),
    "BRI": ("sbuf", [128, 2048], "int32"),
    "PK": ("sbuf", [128, 4608], "bfloat16"),
    "EQ": ("sbuf", [128, 16, 256], "bfloat16"),
    "SND": ("sbuf", [128, NT * 3 * Q], "bfloat16"),
    "LAND": ("sbuf", [128, NT * 3 * Q], "bfloat16"),
    "NEW": ("sbuf", [128, NT * Q], "float32"),
    "IO2K": ("sbuf", [128, 2048], "float32"),
    "LXT": ("sbuf", [128, 2048], "float32"),
    "TAB": ("sbuf", [128, 4096], "float32"),
    "ROWS": ("sbuf", [128, 4096], "float16"),
    "BOH": ("sbuf", [128, 8], "float16"),
    "KS": ("sbuf", [128, 512], "float32"),
    "XF": ("sbuf", [128, 32], "float32"),
    "TRI": ("sbuf", [128, 3 * Q], "bfloat16"),
    "EQT": ("sbuf", [128, 512], "bfloat16"),
    "KC2": ("sbuf", [128, 512], "bfloat16"),
    "NSEL": ("sbuf", [128, 512], "float16"),
    "SACC": ("sbuf", [128, 2], "float32"),
    "K4": ("sbuf", [128, 4], "float16"),
    "W16": ("sbuf", [128, 145], "bfloat16"),
    "COL": ("sbuf", [128, 16], "float32"),
}
for _n in ("CM", "CX0", "CX1", "MX", "SC"):
    SCRATCH[_n] = ("sbuf", [128, 4096], "bfloat16")
for _n in ("CAP", "SL", "SP", "FT", "TOH"):
    SCRATCH[_n] = ("sbuf", [128, 2048], "bfloat16")
for _n, _c in (("SEG", 2064), ("FS", 2 * WIN), ("BS", 2 * WIN)):
    SCRATCH[_n] = ("sbuf", [128, _c], "bfloat16")
for _n in ("XS", "M63", "ONES", "OFFD", "OFFA", "DELB", "N12", "KN", "KP", "BD1", "BD2", "R0", "SG", "OH", "OK0", "DW", "LXW", "CMP", "KC", "BW32K"):
    SCRATCH[_n] = ("sbuf", [128, 256], "bfloat16")
for _n in ("XA", "XW", "VB", "PH"):
    SCRATCH[_n] = ("sbuf", [128, 256], "float16")
for _n in ("IOT", "IO16", "NDEL", "NMB", "MTP", "CNS", "CNW", "WOLD", "IOTM", "PF"):
    SCRATCH[_n] = ("sbuf", [128, 256], "float32")
for _n in ("MB", "QS"):
    SCRATCH[_n] = ("sbuf", [128, 512], "float32")
for _n in ("BO", "NBO", "NBO2", "BO4", "BT4", "ID", "NID", "N11M", "N12M", "P12M", "N15M", "N16M", "P16M", "M16M", "MULD", "CFAR",
           "ZERO", "LIM", "NODE"):
    SCRATCH[_n] = ("sbuf", [128, 128], "bfloat16")
for _n in ("IDH", "RH", "KR4"):
    SCRATCH[_n] = ("sbuf", [128, 128], "float16")
for _n in ("B16", "MASK", "B32K", "NB32K"):
    SCRATCH[_n] = ("sbuf", [128, 16], "bfloat16")
for _n in ("IOB", "PAR", "IDF"):
    SCRATCH[_n] = ("sbuf", [128, 128], "float32")
for _n, _c in (("UI", 128), ("UU", 128), ("FO", 256)):
    SCRATCH[_n] = ("sbuf", [128, _c], "int32")
for _n in ("EO", "P16", "OFFC"):
    SCRATCH[_n] = ("sbuf", [128, 256], "uint16")
for _n in ("WTI", "KAI", "PI"):
    SCRATCH[_n] = ("sbuf", [128, 1], "int32")
for _n in ("LB", "LC", "QF", "C37"):
    SCRATCH[_n] = ("sbuf", [128, 16], "float32")
for _n in ("XI", "XI2"):
    SCRATCH[_n] = ("sbuf", [128, 48], "int32")
for _n in ("KL", "PL", "PW", "LV", "UL"):
    SCRATCH[_n] = ("sbuf", [128, 16], "uint16")
for _n, _c in (("B0", 512), ("B1", 512), ("B2", 512), ("B34", 1024), ("B56", 1024), ("B7", 512)):
    SCRATCH[_n] = ("psum", [128, _c], "float32")
DMAS = ["dbr0", "dbr1", "dres", "dcap0", "dcap1", "dwt", "dka", "dyr", "dyb", "drow"] + ["dt%d" % k for k in range(4)]
SEMAPHORES = ["cv", "ct", "ca", "cp", "loc"] + DMAS + ["arr%d%d" % (t, h) for t in range(1, NT + 1) for h in (0, 1)]
COLS = ("WTF", "PFL", "KF", "G16", "G15", "MULP", "ADDP", "PC")
ORDERS = {}
SEEN = {}
TAG = [None]
ROUND = """
FOa1 kp_6+ as0+ AS0 CY12+ eq5+ ps4_6+ kc0_1 rows7b_1+ IO2K3 eqt+ qi_1+ FOb1 CY11+ eq0+ ok_6+ WDc0 WDc2+ tb2d eq1+ eq2+ rows4_1+ ps7_6+ SX11 qx_1+ cnc0_1 eq5T+ r0b_1 FOc1 P16M+ eqv+ cm00_1 ps6_6+ eq0T+ kp+ rows7c_1+ LXT0 as2_1+ eq1T+ pe_6+ z_6+ rows7d_1+ eq3+ qxT_1+ eq2T+ r0bA_1 qs_6+ as6+ lv_1+ eq4+ MASK+ PKT+ eqx+ G6 CX1h1 eqm_1+ eq6+ vb_1+ as0_1+ NEW1+ ok+ sum0_1 far_1+ LXT1 TW+ MULD+ lxw_1+ eqvT+ offa_6+ G5 cnt00_1 eq5_1+ eqt_1+ eq7+ qx_6+ eq1_1+ offa_1+ qi_6+ ks0_1 eq9_1+ as4_1+ rows6_1+ eq0_1+ eq8+ cnt01_1 eq5T_1+ eq2_1+ ADDP eq3_1+ eq9T_1+ eq1T_1+ eqv_1+ G7 eq0T_1+ LXT2 eq3T+ eq2T_1+ ki0_1 eq4_1+ eq3T_1+ tb4a G4 eq9+ eqx_1+ kp_1+ eq6_1+ eq8_1+ eqvT_1+ eq7_1+ eq10_1+ eq4T+ as6_1+ as7_1+ eq4T_1+ eq6T_1+ cnc1_1 ok_1+ eq10+ NBO2 eq8T_1+ kc1_1 eqd_1+ eq7T_1+ MTW+ kx0_1 eq10T_1+ WDc7+ eqe_1+ NBO NEW3++ as7+ LXT3 oh_1+ eq6T+ NB32K AS4 cx2_1+ cns_1+ eq7T+ NEW4+++ kx0T_1 qxT_6+ sli0 eq8T+ WDT+ cnw_1+ eqm_6+ B32K eqd+ rest0_1 kl0_1 z_1+ pl_1+ cx14+ lv_6+ QRT+ eq9T+ cm10_1 cx1_1+ NEW2+ r0c xs0_1 patch_1+ eq10T+ KC3 vb_6+ eqe+ r0cA z+ cns+ NEW5+++ cx12_1+ tb4b cx15_1++ cx15+ pl+ cnw+ r0a zero0_1 patch+ WDc6+ eq7_6+ par1 cnt10_1 eq0_6+ eqt_6+ cm00 cx5_1+ r0b CY2 MULP kc0 r0bA cx8_1+ eq1_6+ NDEL+ cm10 sum1_1 sum0 rest0P_6 eq3_6+ eq7T_6+ eq0T_6+ fs00_1 kc1 cx6_1 LB NEW6+++ eq4_6+ ks0 cx1 eqx_6+ sum1 lin0_1 eqv_6+ rest1P_6 par2 ki0 eq1T_6+ cnt11_1 par3 kx0 eq3T_6+ CY4 rest0P eq9_6+ sg0_1 eq5_6+ ks1 ld ks1_1 eq4T_6+ eq2_6+ kx0T CY15 eqvT_6+ rest1_1 two0_1 eq6_6+ cmp0_1 v10_1 rest1P cnt00 eq8_6+ kl0 ki1_1 eq10_6+ NMB ki1 WDc3 eq9T_6+ eq5T_6+ su_1+ su+ cmp0T_1 eq2T_6+ kx1_1 cx6 eq6T_6+ cnt01 eqd_6+ sli0A xs0 eq8T_6+ snd0_1 kx1 eq10T_6+ eqe_6+ cx3 zero0 kx1T_1 tb4c kx1T cnc1 cns_6+ sg0 kl1_1 cnt10 PAR snd0P_1 lc kl1 cnt11 WTF cx5 WDc1 PW fs00 xs1_1 xs1 lin1 lin0 NSEL1 cx2 sg1_1 zero1 two0 WOLD SX21 cx4 cmp0 zero1_1 sg1 pw pw_6 tb4d fs10 oh lin1_1 WD v11 lim WDc5 v10 sli1 cmp0T v0 sla snd0 two1 cmp1 fs10_1 wolda snd0P two1_6 cmp1T cx3_1+ v11_1 cmp1_6 slb0 snd1 wolda_6 wda sli1A slb1 snd1P cx7 cmp1T_6 sl tb6a res0_6 u0 WDc4 tb7a m630 n12 snd1_6 cmp1_1 two1_1 res0 lim_1 shw0 tb6b ui0 sp2 wda_6 kn n12_1 gh0 cmp1T_1 uj0 slb1_6 sli2 snd1P_6 u1 G15 res1_6 wd2 C37 snd1_1 sl_6 cx8 tb6c u0_6 t1 ul0 tb7b m637 sli2A oh_6 bd2 snd1P_1 sp4 pf0 N16M W16 p160 CX0h1 ui0_6 cx10_1+ tb7c kn_1 yb cx9 IDF sp2_6 IOT- SEG- u1_6 shw7 ui1 BO4 sli3 uj0_6 cx4_1 bd1 tb7d UI- wd2_6 tb6d shg0 u0_1 ONES- PI- pc CY0 KAI- m630_1 IO16- uj1 sli3A BW32K1 v0_1 sp2_1 sc3 ul0_6 bd2_1 sla_1 m637_6 slb0_1 res0_1 ui0_1 cx10 slb1_1 SP0- m637_1 u1_1 NSEL0 ui1_6 pn0 IOB- TOH uj0_1 wd2_1 cx7_1 p160_6 RI2- RI0- pf0_6 RI1- t1_1 ul1 shw7_6 NODE- PFL- sl_1 RI3- shw7_1 K42- pc0 ul0_1 RH- uj1_6 ui1_1 OFFA ID- BT4 sp4_6 sc2 sp4_1 BRI0- XIu0- pf0_1 p160_1 m630_6 K41- pc_1 KI- bd1_1 t2 IDH- res1_1 shw0_1 FOa0- res1 sc2_6 shg0_6 KC- K40- uj1_1 shg0_1 K43- sc2_1 KF- p161 Y2- CY1 shw0_6 FOb0- pn0_1 wd4 CAP0- B1.k- NID- G16- ul1_1 ul1_6 ZERO- sc3_1 TOH0 t2_1 cx13 RESZ- CY5 sc3_6 KR4- N11M- pf1 ROWS- BO- pc_6 p161_1 shg7 OFFC- yr N15M- CY3 shr0 sc3b_1 sc3b tb2a- DELB- LIM- t3_1 shg7_1 pc0_1 gh1 KC2- M16M wd4_1 p161_6 t3 tb0a- shr0_1 pn1 BOH- B160- pn0_6 B161- tb2b- OFFD- sc2b gh0_1 wd4_6 sc3b_6 shr0A FOc0- cx11 pf1_1 pc0_6 BW32K0- pc1 MB- sc2b_1 shr7 N12M- pf1_6 eo TOH1 gh1_1 sc4 shr7_1 shr0A_1 cx12 shg7_6 sc5_1 CFAR- shr0_6 ps2 CY6 pn1_1 shr7A sc5 tb0b- ps0 SX10- IO2K0- ps2_1 IOTM- rows2 sc6 cx11_1+ CY8 pn1_6 RES- ps7 eo_1 sc2b_6 shr7A_1 ps4 pc1_1 sc4_1 CY7 cx9_1+ G2- rows7a shr0A_6 ps0_1 rows7b ps6 rows4 CY10 sc4_6 G1- pc1_6 IO2K1- rows2_1 shr7_6 rows7c pe sc6_1 G0- cx13_1+ tb0c- offa TOH2 CY14 qs ps4_1 cx14_1+ qi sc5_6 rows0 qx G3- ps2_6 BRI1- CY13 as4 rows7d rows7a_1 ps7_1 WTI- CX1h0- qxT IO2K2- eqm MTP ps6_1 shr7A_6 tb2c- CY9 lv as2 pe_1 rows0_1 far tb0d- ps0_6 vb P12M lxw qs_1 sc6_6 cnc0- CAP1- rows6
"""


def banks_of(keys):
    return set(x.split(".")[0] for x in keys if "." in x)


def runs(blocks, most):
    out = []
    for j in blocks:
        if out and out[-1][0] + out[-1][1] == j and j % 4 and out[-1][1] < most:
            out[-1] = (out[-1][0], out[-1][1] + 1)
        else:
            out.append((j, 1))
    return out


def depends(calls):
    before = [set() for _ in calls]
    lastw, readers, closed = {}, {}, {}
    for i, c in enumerate(calls):
        r, w, grp = c[2], c[3], c[7]
        for k in list(r) + list(w):
            if k in lastw:
                before[i].add(lastw[k])
        for k in w:
            before[i].update(readers.get(k, []))
        for b in banks_of(w) if grp else ():
            if grp[0] and b in closed:
                before[i].add(closed[b])
            if grp[1]:
                closed[b] = i
        before[i].discard(i)
        for k in r:
            readers.setdefault(k, []).append(i)
        for k in w:
            lastw[k] = i
            readers[k] = []
    return before


def issue_order(calls):
    before = depends(calls)
    SEEN["calls"], SEEN["before"] = calls, before
    place = {x.rstrip("+-"): (x.count("+") - x.count("-"), j) for j, x in enumerate(ROUND.split())}
    unit, members = [], []
    for i, c in enumerate(calls):
        if i and c[0] == "t" == calls[i - 1][0] and c[6] == calls[i - 1][6]:
            members[-1].append(i)
        else:
            members.append([i])
        unit.append(len(members) - 1)
    rank, missing, after = [], [], [[] for _ in members]
    for u, m in enumerate(members):
        t, name = calls[m[0]][6]
        rank.append((t + place.get(name, (0, 0))[0], place.get(name, (0, 0))[1], u))
        first = set(unit[p] for i in m for p in before[i]) - {u}
        missing.append(len(first))
        for p in first:
            after[p].append(u)
    ready = [rank[u] for u in range(len(members)) if not missing[u]]
    order = []
    while ready:
        first = min(ready)
        ready.remove(first)
        order += members[first[2]]
        for x in after[first[2]]:
            missing[x] -= 1
            if not missing[x]:
                ready.append(rank[x])
    return order


def rank_program(g, core, T, topo):
    rank = T.rank_of(core)
    if rank is None:
        return
    cores = T.cores
    n = len(cores)
    V, PE, AC = g.vector, g.tensor, g.scalar
    calls = []
    now = [1, None, None]
    first_queue = {}
    named = set(x.rstrip("+-") for x in ROUND.split())

    def step(name, pieces=None):
        now[1], now[2] = name, pieces and (now[0], pieces)

    def put(q, f, r, w, ns, lat=0.0, grp=None):
        name = now[1] or w[0]
        r = sum(([k + "0", k + "1"] if k in ("CAP", "BRI", "B16", "BW32K") else [k] for k in r), [])
        if first_queue.setdefault(name, q) != q:
            name += q.upper()
        if now[0] == 1 and (name + "_1" in named or name in OPT["own1"].split()):
            name += "_1"
        if now[0] >= NT and (name + "_6" in named or name in OPT["own6"].split()):
            name += "_6"
        calls.append((q, f, r, w, ns, lat, (now[0], name), grp, now[2]))

    def cols(ap):
        c = 1
        for x in ap.shape[1:]:
            c *= x
        return c

    def narrow(*aps):
        return all("16" in str(a.dtype) for a in aps)

    def vec(f, r, w, n_cols, rate):
        put("v", f, r, w, 55.0 + max(64.0, n_cols * rate) * CYCLE)

    def mm(out, lhs, rhs, st, sp, r, w):
        ns = PE_CALL + max(min(64, cols(lhs)), cols(rhs)) * PE_CYCLE * (1 if narrow(lhs) else 4)
        put("t", lambda: PE.matmul(out, lhs, rhs, st, sp), r, w, ns, 0.0, (st, sp))

    def act(out, in_, r, w, func=F.Copy, bias=0.0, scale=1.0, accum=None, rate=1.0):
        put("a", lambda: AC.activation(out, in_, func, bias=bias, scale=scale, accum_out=accum), r, w,
            (ACT if rate == 1.0 else 65.0) + max(64, cols(out)) * rate * CYCLE)

    def fill(ap, c, k):
        vec(lambda: V.memset(ap, c), [], [k] if isinstance(k, str) else k, cols(ap), 0.5 if narrow(ap) else 1.0)

    def iota(ap, pattern, base, cm, k):
        small = "int" not in str(ap.dtype)
        put("p", lambda: g.iota(ap, pattern, base, cm, allow_small_or_imprecise_dtypes=small), [], [k] if isinstance(k, str) else k,
            130.0 + 2 * cols(ap) * CYCLE)

    def ts(out, in0, s1, s2, o0, o1, r, w):
        rate = 0.5 if narrow(out, in0) else 1.0
        if o1 is None:
            vec(lambda: V.tensor_scalar(out, in0, s1, None, o0), r, w, cols(out), rate)
        else:
            vec(lambda: V.tensor_scalar(out, in0, s1, s2, o0, o1), r, w, cols(out), rate)

    def tt(out, a, b, o, r, w, rate=None):
        vec(lambda: V.tensor_tensor(out, a, b, o), r, w, cols(b), rate or (1.0 if banks_of(r) else 2.0))

    def cp(out, a, r, w, q="v"):
        if q == "v":
            vec(lambda: V.tensor_copy(out, a), r, w, cols(out), 0.5 if narrow(out, a) else 1.0)
        elif q == "a":
            act(out, a, r, w)
        else:
            put("p", lambda: g.affine_select(out, a, [[0, cols(out)]], A.is_ge, 0.0, 0, 0), r, w, 170.0 + 2 * cols(out) * CYCLE)

    def lin(q, out, in_, scale, bias, r, w):
        if q == "a":
            act(out, in_, r, w, bias=bias, scale=scale)
        else:
            ts(out, in_, scale, bias, A.mult, A.add, r, w)

    def gather(q, out, win, off, r, w, bias=0.0):
        if q == "a":
            act(out, win.indirect(off), r, w, bias=bias, rate=GATHER)
        else:
            vec(lambda: V.tensor_copy(out, win.indirect(off)), r, w, cols(out), GATHER)

    def scatter(win, off, src, r, w):
        vec(lambda: V.tensor_copy(win.indirect(off), src), r, w, cols(src), SCATTER)

    def scan(out, d0, d1, o0, o1, r, w):
        vec(lambda: V.tensor_tensor_scan(out, d0, d1, 0.0, o0, o1), r, w, cols(out), 0.5 if narrow(out, d0, d1) else 1.0)

    def dma(q, out, in_, sem, r, w, kib):
        put(q, (out, in_, sem), r, w, 100.0, DMA + 3.0 * kib)

    def half(h, size=H):
        return slice(size * h, size * h + size)

    def col(name):
        j = COLS.index(name)
        return T.COL[:, j:j + 1]

    def bank(b, lo, hi, by=1):
        name, at = {3: ("B34", 0), 4: ("B34", 512), 5: ("B56", 0), 6: ("B56", 512)}.get(b, ("B%d" % b, 0))
        return T[name][:, at + lo:at + hi:by]

    def rw(lo, hi, by=1):
        return T.PK[:, lo:hi:by]

    whole = {3: ["B3.n", "B3.v"], 4: ["B4.n", "B4.v"], 5: ["B5.c"], 6: ["B6.c"], 7: ["B7.x", "B7.hi"]}
    first_tail = 16 - OPT["tail"]
    tail = []
    for b in range(first_tail, 16):
        tail.append((b, sum(x[2] for x in tail), Q - 16 * b))
    tail_cols = sum(x[2] for x in tail)

    dma("s", T.KAI[:], T.ka[:], "dka", [], ["KAI"], 1)
    dma("s", T.WTI[:], T.wt[:], "dwt", [], ["WTI"], 1)
    dma("s", T.RES[:, 0:ZC], T.res[:], "dres", [], ["RES", "RESG"], 832)
    for h in (0, 1):
        dma("s", T.BRI[:, half(h, 1024)], T.br[:, half(h, 1024)], "dbr%d" % h, [], ["BRI%d" % h], 512)
        dma("s", T.CAP[:, half(h, 1024)], T.cap[:, half(h, 1024)], "dcap%d" % h, [], ["CAP%d" % h], 256)
    iota(T.UI[0:96, :], [[1, 128]], 0, 128, "UI")
    iota(T.PI[:], [[0, 1]], 0, 1, "PI")
    iota(T.IOT[:], [[1, 256]], 0, 0, "IOT")
    iota(T.IO16[:], [[0, 16], [1, 16]], 0, 0, "IO16")
    iota(T.IOB[:], [[16, 8], [0, 16]], 0, 0, "IOB")
    for ap, c, key in ((T.ONES[:], 1.0, "ONES"), (T.ZERO[:], 0.0, "ZERO"), (T.TRI[:, 2:3 * Q:3], 0.0, "Y2"), (rw(TR, TR + Q), 0.0, "PKT"),
                       (T.WD[:, 2048:2304], 0.0, "WDT")):
        if key in OPT["ona"].split():
            act(ap, T.IOT[:, 0:cols(ap)], ["IOT"], [key], scale=0.0, bias=c)
        else:
            fill(ap, c, key)
    iota(T.CFAR[0:1, :], [[0, 128]], FAR, 0, "CFAR")
    iota(T.LIM[0:3, :], [[0, 128]], 9216, -6656, "LIM")
    iota(T.LIM[0:1, :], [[0, 128]], -256, 0, "LIM")
    iota(T.NODE[0:2, :], [[-16, H]], 1008, 0, "NODE")
    iota(T.NODE[0:1, :], [[0, H]], 1, 0, "NODE")
    iota(T.KC[0:2, :], [[-1, 2], [0, H]], 1, 0, "KC")
    iota(T.KC[0:1, 0:H], [[0, 8], [-1, 16]], 16, 0, "KC")
    fill(T.KC2[0:2, :], -16777216.0, "KC2")
    step("KC3")
    iota(T.KC2[0:1, :], [[0, 32], [-2048, 16]], 30720, 0, "KC2")
    step(None)

    for j in range(4):
        step("IO2K%d" % j, "IO2K")
        iota(T.IO2K[:, half(j, 512)], [[1, 512]], 512 * j, 0, "IO2K")
        step("LXT%d" % j, "LXT")
        iota(T.LXT[:, half(j, 512)], [[1, 64], [768, 8]], 64 * j, 0, "LXT")
    step(None)
    fill(T.RH[96:128, :], 2048.0, "RI3")
    tt(T.UU[0:32, :], T.UI[0:32, :], T.UI[0:32, :], A.mult, ["UI"], ["RI0"])
    ts(T.UU[0:32, :], T.UU[0:32, :], 5, 2047, A.arith_shift_right, A.bitwise_and, ["RI0"], ["RI0"])
    ts(T.UU[32:64, :], T.UI[32:64, :], 31, None, A.bitwise_and, None, ["UI"], ["RI1"])
    ts(T.UU[64:96, :], T.UI[64:96, :], 2016, None, A.bitwise_and, None, ["UI"], ["RI2"])
    cp(T.RH[0:96, :], T.UU[0:96, :], ["RI0", "RI1", "RI2"], ["RH"])
    dma("s", T.ROWS[0:4, :], T.RH[:], "drow", ["RH", "RI3"], ["ROWS"], 32)
    fill(T.RES[:, ZC:ZC + 16], 0.0, "RESZ")
    fill(T.K4[:, 0:1], 1.0, "K42")
    fill(T.K4[:, 3:4], 130.0, "K43")
    ts(T.XI2[:, 40:41], T.PI[:], 15, None, A.bitwise_and, None, ["PI"], ["KI"])
    cp(col("PFL"), T.PI[:], ["PI"], ["PFL"])
    cp(col("KF"), T.XI2[:, 40:41], ["KI"], ["KF"])
    ts(T.ID[:], T.IOT[:, 0:128], col("PFL"), None, A.is_equal, None, ["IOT", "PFL"], ["ID"])
    tt(col("G16"), col("PFL"), col("KF"), A.subtract, ["PFL", "KF"], ["G16"])
    cp(T.IDH[:], T.ID[:], ["ID"], ["IDH"])
    ts(T.DELB[:], T.IO16[:], col("KF"), None, A.is_equal, None, ["IO16", "KF"], ["DELB"])
    ts(T.BO[:], T.IOB[:], col("G16"), None, A.is_equal, None, ["IOB", "G16"], ["BO"])
    ts(T.XI[:, 0:1], T.KAI[:], 63, None, A.bitwise_and, None, ["KAI"], ["XIu0"])
    cp(T.K4[:, 1:2], T.KAI[:], ["KAI"], ["K41"])
    cp(T.K4[:, 2:3], T.XI[:, 0:1], ["XIu0"], ["K40"])
    mm(T.B1[0:4, 0:128], T.K4[:], T.IDH[:], True, True, ["K40", "K41", "K42", "K43", "IDH"], ["B1.k"])
    cp(T.KR4[0:4, :], T.B1[0:4, 0:128], ["B1.k"], ["KR4"])
    fill(T.SEG[:], 256.0, "SEG")
    fill(T.SEG[:, 0:2064:16], 0.0, "SEG")
    fill(T.MB[:], 1e9, "MB")
    fill(T.MB[:, 0:512:16], -1e9, "MB")
    if "f" in OPT["fb"]:
        iota(T.FS[:, 0:2 * WIN:WIN], [[0, 2]], 0, 0, "ENDS")
        iota(T.BS[:, 2063:2 * WIN:WIN], [[0, 2]], 0, 0, "ENDS")
    act(T.SP[:], T.SEG[:, 0:2048], ["SEG"], ["SP%d" % j for j in range(4)], scale=0.0)
    fill(T.PAR[:], 1.0 / 8192, "PAR")
    fill(T.W16[0:1, 144:145], -0.25, "QRT")
    cp(T.OFFC[:], T.IOT[:], ["IOT"], ["OFFC"])
    cp(col("WTF"), T.WTI[:], ["WTI"], ["WTF"])
    ts(col("G15"), col("G16"), 15.0, None, A.add, None, ["G16"], ["G15"])
    ts(T.W16[:, 0:144], T.IOT[:, 0:144], col("G15"), col("WTF"), A.is_equal, A.mult, ["IOT", "G15", "WTF"], ["W16"])
    cp(T.BOH[:], T.BO[:, 0:128:16], ["BO"], ["BOH"])

    def who(name):
        return "a" if name in OPT["ona"].split() else "v"
    for name, c in (("N11M", -2048.0), ("NID", -1.0), ("N12M", -4096.0), ("P12M", 4096.0), ("N15M", -15.0), ("N16M", -16.0), ("IDF", 1.0),
                    ("P16M", 65536.0), ("M16M", -65536.0)):
        if name in OPT["onp"].split():
            put("p", lambda name=name, c=c: g.affine_select(T[name][:], T.ZERO[:], [[-1, 128]], A.not_equal, c, 0, 1), ["ZERO"], [name], 382.0)
        else:
            lin(who(name), T[name][:], T.ID[:], c, 0.0, ["ID"], [name])
    for name, c in (("NBO", -512.0), ("NBO2", -256.0), ("BO4", 2.0 * FAR)):
        lin(who(name), T[name][:], T.BO[:], c, 0.0, ["BO"], [name])
    for j in (0, 1):
        lin("v", T.B16[:, half(j, 8)], T.BO[:, 0:128:16], 16.0, 0.0, ["BO"], ["B16%d" % j])
        lin("v", T.BW32K[:, half(j)], T.BO[:], 32768.0, 0.0, ["BO"], ["BW32K%d" % j])
    for name, c in (("B32K", 2048.0), ("NB32K", -2048.0)):
        lin("v", T[name][:], T.B16[:], c, 0.0, ["B16"], [name])
    lin("a", T.NDEL[:], T.DELB[:], -1.0, 1.0, ["DELB"], ["NDEL"])
    put("p", lambda: g.affine_select(T.BT4[:], T.BO4[:], [[1, 128]], A.is_gt, 0.0, 0, -1), ["BO4"], ["BT4"], 382.0)
    lin("v", T.OFFD[:], T.DELB[:], 67108864.0, -67108864.0, ["DELB"], ["OFFD"])
    act(T.LB[:], T.IOT[:, 0:16], ["IOT", "KF"], ["LB"], F.Identity, bias=col("KF"), scale=16.0)
    lin("a", T.C37[:], T.LB[:], 37.0, 0.0, ["LB"], ["C37"])
    lin("a", T.NMB[:], T.MB[:, 0:Q], -1.0, 0.0, ["MB"], ["NMB"])
    fill(T.MTP[:], -1e9, "MTP")
    lin("v", T.MTP[:, 0:Q:16], T.LB[:], 1.0, float(TR), ["LB"], ["MTP"])
    lin("v", T.LB[:], T.LB[:], 1.0, 2048.0 + FAR, ["LB"], ["TW", "LB"])
    tt(T.IOTM[:], T.IOT[:], T.OFFD[:], A.add, ["IOT", "OFFD"], ["IOTM"])
    for t in range(1, NT + 1):
        act(T.NEW[:, half(t - 1, Q)], T.IOTM[:], ["IOTM"], ["NEW%d" % t], F.Relu, bias=2048.0 + 256.0 * (t - 1) + 4096.0 * (t + 2))
    ts(col("MULP"), col("KF"), 0.0, -15.0, A.is_equal, A.mult, ["KF"], ["MULP"])
    ts(col("ADDP"), col("KF"), 0.0, float(P0), A.is_equal, A.mult, ["KF"], ["ADDP"])
    ts(col("MULP"), col("MULP"), 16.0, None, A.add, None, ["MULP"], ["MULP"])
    tt(col("ADDP"), col("ADDP"), col("KF"), A.add, ["ADDP", "KF"], ["ADDP"])
    ts(T.MULD[:], T.ID[:], col("MULP"), None, A.mult, None, ["ID", "MULP"], ["MULD"])
    ts(T.OFFA[:], T.DELB[:], col("ADDP"), None, A.mult, None, ["DELB", "ADDP"], ["OFFA"])
    lin("a", T.TOH[:, 0:256], T.DELB[:], -16.0, 208.0, ["DELB"], ["TOH"])
    for j, s in enumerate((256, 512, 1024)):
        step("TOH%d" % j)
        dma("s", T.TOH[:, s:2 * s], T.TOH[:, 0:s], "dt%d" % (j + 1), ["TOH"], ["TOH"], s // 4)
    step(None)
    ts(T.MASK[:], T.IO16[:, 0:16], col("KF"), 4096.0, A.is_le, A.mult, ["IO16", "KF"], ["MASK"])
    for b, lo, m in tail:
        step("NSEL%d" % (b % 2))
        ts(T.NSEL[:, lo:lo + m], T.ONES[:, 0:m], T.BO[:, 16 * (b - 8):16 * (b - 8) + 1], -1.0, A.mult, A.mult, ["ONES", "BO"], ["NSEL%d" % b])
    step(None)

    tab = ["TAB%d" % j for j in range(8)]
    wdk = ["WDc%d" % j for j in range(8)]

    def table(j):
        spec = OPT["ft"].split()[j]
        bs, q = [int(x) for x in spec[:-2]], spec[-2:]
        both, rk, fk = sum((whole[b] for b in bs), []), ["KR4", "ROWS"], ["FT%d" % ((j + y) % 4) for y in range(len(bs))]
        lo, m = 512 * (j % 4), 512 * len(bs)
        step("tb%da" % j)
        for y, b in enumerate(bs):
            mm(bank(b, 0, 512), T.KR4[0:4, :], T.ROWS[0:4, half(j + y, 512)], True, True, rk, whole[b])
        step("tb%db" % j)
        lin(q[0], T.FT[:, lo:lo + m], bank(bs[0], 0, m), 1.0 / 2048, -0.499755859375, both, fk)
        step("tb%dc" % j)
        for y, b in enumerate(bs):
            mm(bank(b, 0, 512), T.KR4[0:4, :], T.ROWS[0:4, half(j + y, 512)], True, False, rk, whole[b])
            mm(bank(b, 0, 512), T.N11M[:], T.FT[:, lo + 512 * y:lo + 512 * y + 512], False, True, ["N11M", fk[y]], whole[b])
        step("tb%dd" % j)
        cp(T.TAB[:, 512 * j:512 * j + m], bank(bs[0], 0, m), both, tab[j:j + len(bs)], q[1])

    def first_room(j):
        b = int(OPT["sli"][j])
        step("sli%d" % j)
        mm(bank(b, 0, 512), T.ID[:], T.CAP[:, half(j, 512)], True, False, ["ID", "CAP%d" % (j // 2)], whole[b])
        mm(bank(b, 0, 512), T.NID[:], T.RES[:, half(j, 512)], False, True, ["NID", "RES"], whole[b])
        act(T.SL[:, half(j, 512)], bank(b, 0, 512), whole[b], ["SL"], F.Relu)

    def first_pieces(names):
        for x in names.split():
            (table if x[0] == "t" else first_room)(int(x[1]))

    def first_offsets(h):
        fo, key = T.FO[:, half(h)], "FO%d" % h
        step("FOa%d" % h)
        ts(fo, T.BRI[:, 1024 * h:1024 * h + 1024:8], 4095.0, None, A.max, None, ["BRI%d" % h], [key])
        step("FOb%d" % h)
        ts(fo, fo, 4095, None, A.bitwise_and, None, [key], [key])
        step("FOc%d" % h)
        ts(T.EO[:, half(h)], fo, float(ZC), None, A.min, None, [key], ["EO%d" % h])
        step(None)

    def k_part(out, key, t, more):
        lin("a", out, T.WD[:, t - 1:2048:8], 1.0 / 65536, 199.50390625 + more, [wdk[t - 1]], [key])

    def offsets(t):
        step("n12")
        lin("a", T.N12[:], T.WD[:, t - 1:2048:8], 1.0 / 4096, 219.5625, [wdk[t - 1]], ["N12"])
        step("kn")
        k_part(T.KN[:], "KN", t, 0)
        step("t1")
        mm(T.B7[:, 0:256], T.ID[:], T.N12[:], True, False, ["ID", "N12"], ["B7.x"])
        mm(T.B7[:, 0:256], T.N16M[:], T.KN[:], False, True, ["N16M", "KN"], ["B7.x"])
        for name, src, sk, c in (("bd2", T.KN[:], "KN", 201.0 - t), ("bd1", T.B7[:, 0:256], "B7.x", t - 2980.0)):
            step(name)
            if OPT[name] == "a":
                act(T[name.upper()][:], src, [sk], [name], F.Relu, bias=4096.0 * c, scale=-4096.0)
            else:
                ts(T[name.upper()][:], src, c, 4096.0, A.is_lt, A.mult, [sk], [name])
        step("t2")
        o = T.B7[:, 256:512]
        mm(o, T.IDF[:], T.WD[:, t - 1:2048:8], True, False, ["IDF", wdk[t - 1]], ["B7.hi"])
        mm(o, T.N12M[:], T.N12[:], False, False, ["N12M", "N12"], ["B7.hi"])
        mm(o, T.ID[:], T.BD2[:], False, False, ["ID", "bd2"], ["B7.hi"])
        step("t3")
        mm(o, T.ID[:], T.BD1[:], False, True, ["ID", "bd1"], ["B7.hi"])
        step("eo")
        ts(T.EO[:], o, 901120.0, float(ZC), A.add, A.min, ["B7.hi"], ["EO0", "EO1"])

    def pk(h):
        return ["PK%d" % j for j in range(4 * h, 4 * h + 4)]

    def p0(h):
        return ["P0%d" % j for j in range(4 * h, 4 * h + 4)]

    def rows(q, j, m, name="rows"):
        lo, hi = 32 * j, 32 * (j + m)
        if q == "v" and name == "rows":
            by = 32 // OPT["rp"]
            for x in range(lo, hi, by):
                step(name + str(x // 32) + "abcd"[x % 32 // by], name)
                gather(q, rw(16 * x, 16 * (x + by)), T.RES[:, 0:3344], T.EO[:, x:x + by], ["RES", "RESG", "RESZ", "EO%d" % (j // 4)], ["PK%d" % (x // 32)])
            return
        step(name + str(j))
        gather(q, rw(16 * lo, 16 * hi), T.RES[:, 0:3344], T.EO[:, lo:hi], ["RES", "RESG", "RESZ", "EO%d" % (j // 4)], ["PK%d" % i for i in range(j, j + m)])

    def aside(h):
        return rw(P0 + H * h, P0 + H * h + H)

    def row0_aside(q, t, j, m, name="as"):
        lo, hi, keys = 32 * j, 32 * (j + m), ["PK%d" % x for x in range(j, j + m)]
        step(name + str(j))
        cp(rw(P0 + lo, P0 + hi), rw(16 * lo, 16 * hi, 16), keys, ["P0%d" % x for x in range(j, j + m)], q)
        hi = min(hi, Q - 32 * OPT["clip"][t - 1])
        if hi > lo:
            if q == "p":
                iota(rw(16 * lo, 16 * hi, 16), [[0, hi - lo]], 255, 0, keys)
            else:
                fill(rw(16 * lo, 16 * hi, 16), 255.0, keys)

    def cap_wide(t, ks, name="cx"):
        cx, cut = "CX%d" % (t & 1), Q - 32 * OPT["clip"][t - 1]
        for k in ks:
            step(name + str(k))
            cp(T[cx][:, k:16 * cut:16], T.CAP[:, t - 1:8 * cut:8], ["CAP"], [cx + "k%d" % k], "p")

    def words(t):
        win = T.WD[:, 0:2304]
        if t == NT:
            step("PW")
            cp(T.PW[:], T.CNS[:, 15:256:16], ["CNS"], ["PW"])
            step("WOLD")
            tt(T.WOLD[:], win.indirect(T.PW[:]), T.NDEL[:], A.mult, wdk + ["WDT", "PW", "NDEL"], ["WOLD0", "WOLD1"], GATHER)
            step("WD")
            tt(win.indirect(T.PW[:]), T.WOLD[:], T.NEW[:, half(t - 1, Q)], A.add, ["WOLD0", "WOLD1", "NEW%d" % t, "PW"], wdk + ["WDT"], SCATTER)
            return
        step("ld")
        tt(T.XF[:, 16:32], T.CNW[:, 15:256:16], T.LB[:], A.min, ["CNW", "TW"], ["LD"])
        step("lc")
        tt(T.LC[:], T.XF[:, 16:32], bank(2, 400, 416), A.max, ["LD", "B2.far"], ["LC"])
        step("pw")
        ts(T.PW[:], T.LC[:], -float(FAR), None, A.add, None, ["LC"], ["PW"])
        n, m = OPT["wp"], Q // OPT["wp"]
        for x in range(n):
            step("wold" + "abcd"[x])
            tt(T.WOLD[:, half(x, m)], win.indirect(T.PW[:, half(x, m // 16)]), T.NDEL[:, 0:m], A.mult, wdk + ["WDT", "PW", "NDEL"], ["WOLD%d" % x], GATHER)
        for x in range(n):
            step("wd" + "abcd"[x])
            at = Q * (t - 1) + m * x
            tt(win.indirect(T.PW[:, half(x, m // 16)]), T.WOLD[:, half(x, m)], T.NEW[:, at:at + m], A.add, ["WOLD%d" % x, "NEW%d" % t, "PW"],
               wdk + ["WDT"], SCATTER)

    def suspended(t):
        z, wd = T.B0[:, 256:512], T.WD[:, t - 1:2048:8]
        step("oh")
        gather("a", T.OH[:], T.TOH[:], T.KL[:], ["TOH", "KL0", "KL1"], ["OH"])
        step("kp")
        k_part(T.KP[:], "KP", t, t)
        step("z")
        mm(z, T.P16M[:], T.OH[:], True, False, ["P16M", "OH"], ["B0.z"])
        mm(z, T.P12M[:], T.OK0[:], False, False, ["P12M", "OK0"], ["B0.z"])
        mm(z, T.M16M[:], T.KP[:], False, OPT["su"] == "a", ["M16M", "KP"], ["B0.z"])
        if OPT["su"] == "v":
            mm(z, T.IDF[:], wd, False, True, ["IDF", wdk[t - 1]], ["B0.z"])
            step("su")
            tt(wd, wd, z, A.min, [wdk[t - 1], "B0.z"], [wdk[t - 1]])
            return
        step("su1")
        act(T.DW[:], z, ["B0.z"], ["DW"], F.Relu, scale=-1.0)
        step("su2")
        mm(z, T.IDF[:], wd, True, False, ["IDF", wdk[t - 1]], ["B0.z"])
        mm(z, T.NID[:], T.DW[:], False, True, ["NID", "DW"], ["B0.z"])
        act(wd, z, ["B0.z"], [wdk[t - 1]])

    def parity():
        o, pc = T.B7[0:1, 256:384], T.COL[0:1, 7:8]
        step("par1")
        mm(o, T.W16[0:1, 144:145], T.ONES[0:1, 0:H], True, False, ["QRT", "ONES"], ["B7.hi"])
        mm(o, T.SACC[:, 0:1], T.PAR[:], False, True, ["PAR", "SACC"], ["B7.hi"])
        step("par2")
        ts(pc, T.B7[0:1, 256:257], MAGIC, -MAGIC, A.add, A.add, ["B7.hi"], ["PC"])
        step("par3")
        ts(T.LIM[0:1, :], o, pc, 1024.0, A.subtract, A.mult, ["B7.hi", "PC"], ["LIM"])

    BA = [T.B1, T.B2]

    def one_round(t):
        c = t - 1
        cx = "CX%d" % (t & 1)
        L0 = 3 * c * Q
        dst = cores[(rank + 1 + c % (n - 1)) % n]
        last = t == NT
        plan = OPT["score"][c]
        share = [j for j in range(8) if plan[j] == "s"]
        cap = [T.CAP[:, c + 1024 * h:1024 * h + 1024:8] for h in (0, 1)]
        lk = ["LAND%d%d" % (t, h) for h in (0, 1)]
        sk = ["SND%d%d" % (t, h) for h in (0, 1)]

        def msg(buf, lo, hi, by=1):
            return buf[:, L0 + 3 * lo + 2:L0 + 3 * hi:3 * by]

        land = [msg(T.LAND, H * h, H * h + H) for h in (0, 1)]
        snd = [msg(T.SND, H * h, H * h + H) for h in (0, 1)]

        def first_rows():
            d = T.B0[:, 0:256]
            if t == 1:
                for h in (0, 1):
                    step("r0" + "bc"[h])
                    mm(T.B0[:, half(h)], T.NID[:], cap[h], True, False, ["NID", "CAP%d" % h], ["B0.d"])
                    mm(T.B0[:, half(h)], T.ID[:], aside(h), False, True, ["ID"] + p0(h), ["B0.d"])
                    act(T.R0[:, half(h)], T.B0[:, half(h)], ["B0.d"], ["R0%d" % h], F.Relu)
                return
            step("r0a")
            mm(d, T.NID[:], T.CAP[:, c:2048:8], True, False, ["NID", "CAP"], ["B0.d"])
            step("r0b")
            mm(d, T.ID[:], rw(P0, P0 + Q), False, True, ["ID"] + p0(0) + p0(1), ["B0.d"])
            act(T.R0[:], d, ["B0.d"], ["R00", "R01"], F.Relu)

        def worst(h):
            b, key, nk = BA[h], "B%d.k" % (1 + h), "B%d.n" % (3 + h)
            clip = [j for j in range(8 - OPT["clip"][c], 8) if j // 4 == h]
            cut = H - 32 * len(clip)
            over = bank(3 + h, 0, H)
            step("kc%d" % h)
            mm(b[:, 0:2 * H], T.NODE[0:2, :], T.KC[0:2, :], True, False, ["KC", "NODE"], [key])
            mm(b[:, 2 * H:3 * H], T.ID[:], cap[h], False, False, ["ID", "CAP%d" % h], [key])
            cxk, cmk = [cx + "k%d" % k for k in range(16)] + [cx + "h%d" % h], ["CM%d" % j for j in range(4 * h, 4 * h + 4)]
            if cut:
                room = T.CAP[:, c + 1024 * h:1024 * h + 8 * cut:8]
                mm(b[0:cut, 0:2 * H:16], room, T.B16[:], False, False, ["B16", "CAP%d" % h], [key])
                step("cnc%d" % h)
                mm(bank(3 + h, 0, cut), T.N15M[:], room, True, False, ["N15M", "CAP%d" % h], whole[3 + h])
                if cut < H:
                    mm(bank(3 + h, cut, H), T.ZERO[0:1, :], T.ONES[0:1, cut:H], False, False, ["ZERO", "ONES"], whole[3 + h])
                m = 16 * cut // OPT["cmp"]
                for x in range(OPT["cmp"]):
                    lo = 2048 * h + m * x
                    step("cm%d%d" % (h, x))
                    scan(T.CM[:, lo:lo + m], T[cx][:, lo:lo + m], rw(lo, lo + m), A.min, A.max, cxk + pk(h)[m * x // 512:m * (x + 1) // 512],
                         cmk[m * x // 512:m * (x + 1) // 512])
            for x in range(0, len(clip), 2):
                two = clip[x:x + 2]
                step("clipa%d" % x)
                for y, j in enumerate(two):
                    for k in range(16):
                        mm(bank(5 + y, k, 512, 16), T.NID[:], T.CAP[:, c + 256 * j:256 * (j + 1):8], k == 0, False, ["NID", "CAP"], whole[5 + y])
                step("clipb%d" % x)
                for y, j in enumerate(two):
                    mm(bank(5 + y, 0, 512), T.ID[:], rw(512 * j, 512 * j + 512), False, True, ["ID", "PK%d" % j], whole[5 + y])
                act(T.CM[:, 512 * two[0]:512 * (two[-1] + 1)], bank(5, 0, 512 * len(two)), whole[5] + whole[6], ["CM%d" % j for j in two], F.Relu)
            step("sum%d" % h)
            for k in range(1, 16):
                mm(b[:, k:2 * H:16], T.CM[:, 2048 * h + k:2048 * h + 2048:16], T.B16[:], False, False, ["B16"] + cmk, [key])
            mm(b[:, 0:2 * H:16], T.R0[:, half(h)], T.B16[:], False, True, ["B16", "R0%d" % h], [key])
            for k in range(1, 16):
                step("cnt%d%d" % (h, k * OPT["cnt"] // 16))
                mm(over, T.ID[:], T.CM[:, 2048 * h + k:2048 * h + 2048:16], k == 1 and not cut, False, ["ID"] + cmk, whole[3 + h] if k == 1 else [nk])
            mm(over, T.ID[:], T.R0[:, half(h)], False, True, ["ID", "R0%d" % h], [nk])
            step("sg%d" % h)
            act(T.SG[:, half(h)], over, [nk], ["SG%d" % h], F.Sign, bias=-0.5)
            o, ok, ks = b[:, 384:392], "B%d.kl" % (1 + h), 2 * H * h
            step("ks%d" % h)
            scan(T.KS[:, ks:ks + 2 * H], T.MB[:, 0:2 * H], b[:, 0:2 * H], A.min, A.max, ["MB", key], ["KS%d" % h])
            step("ki%d" % h)
            tt(T.XF[:, half(h, 8)], T.KS[:, ks + 15:ks + H:16], T.KS[:, ks + H + 15:ks + 2 * H:16], A.subtract, ["KS%d" % h], ["XF%d" % h])
            step("kx%d" % h)
            tt(T.XA[:, half(h)], T.XF[:, half(h, 8)].indirect(T.OFFC[:, 0:8]), T.DELB[:, 0:H], A.mult, ["XF%d" % h, "OFFC", "DELB"], ["XA%d" % h], GATHER)
            mm(o, T.XA[:, half(h)], T.BOH[:], True, True, ["XA%d" % h, "BOH"], [ok])
            step("kl%d" % h)
            ts(T.KL[:, half(h, 8)], o, -1.0, 1024.0, A.mult, A.add, [ok], ["KL%d" % h])

        def kept():
            o = T.B0[:, 256:512]
            step("lim")
            mm(o, T.LIM[0:3, :], T.ONES[0:3, :], True, False, ["LIM", "ONES"], ["B0.z"])
            step("v0")
            mm(o, T.NBO2[:], T.SG[:], False, True, ["NBO2", "SG0", "SG1"], ["B0.z"])
            step("ok")
            act(T.OK0[:], o, ["B0.z"], ["OK0", "SACC"], F.Relu, accum=T.SACC[:, 0:1])

        def messages(h):
            lo, kl = 2048 * h, T.KL[:, half(h, 8)]
            cmk = ["SC%d" % j for j in range(4 * h, 4 * h + 4)]
            ck, vk, sg = "B%d.k" % (1 + h), "B%d.v" % (3 + h), T.SG[:, half(h)]
            tri = [T.TRI[:, 3 * H * h + j:3 * H * h + 3 * H:3] for j in (0, 1)]
            v = [bank(3 + h, H + j, 4 * H, 3) for j in range(3)]
            if OPT["fb"][h] == "f":
                m, at = 2048 // OPT["pieces"], WIN * h
                for x in range(OPT["pieces"]):
                    a, z = m * x, m * x + m
                    step("bs%d%d" % (h, x))
                    scan(T.BS[:, at + 14 + z:at + 14 + a:-1], T.PK[:, lo + z - 1:(lo + a - 1 if lo + a else None):-1], T.SEG[:, 1:m + 1], A.max, A.min,
                         ["SEG"] + pk(h)[a // 512:z // 512], ["BS%d%d" % (h, x)])
            if OPT["clip"][c] < 4 or h == 0:
                step("rest%d" % h)
                cp(rw(lo, lo + 2048, 16), aside(h), p0(h), pk(h), "v" if t == 1 else OPT["restore"][h])
            m = 2048 // OPT["pieces"]
            if OPT["fb"][h] == "f":
                at = WIN * h
                fs, bs = (["%s%d%d" % (x, h, y) for y in range(OPT["pieces"])] + ["ENDS"] for x in ("FS", "BS"))
                for x in range(OPT["pieces"]):
                    a, z = m * x, m * x + m
                    step("fs%d%d" % (h, x))
                    scan(T.FS[:, at + 1 + a:at + 1 + z], rw(lo + a, lo + z), T.SEG[:, 1:m + 1], A.max, A.min, ["SEG"] + pk(h)[a // 512:z // 512], [fs[x]])
                step("xf%d" % h)
                gather(OPT["xf"], T.XS[:, half(h)], T.FS[:, at:at + 2048], kl, fs + ["KL%d" % h], ["XS%d" % h])
                step("m1%d" % h)
                tt(tri[1], T.BS[:, at + 16:at + 2064].indirect(kl), T.XS[:, half(h)], A.max, bs + ["KL%d" % h, "XS%d" % h], ["Y1%d" % h], GATHER)
                most, cmk = tri[1], ["Y1%d" % h]
            step("xs%d" % h)
            gather(OPT["xs"][h], tri[0], rw(lo, lo + 2048), kl, pk(h) + ["KL%d" % h], ["Y0%d" % h])
            if OPT["fb"][h] != "f":
                step("zero%d" % h)
                scatter(rw(lo, lo + 2048), kl, T.ZERO[:], ["ZERO", "KL%d" % h], pk(h))
                for x in range(OPT["pieces"]):
                    a, z = m * x, m * x + m
                    step("fs%d%d" % (h, x))
                    scan(T.SC[:, lo + a:lo + z], T.SEG[:, 0:m], rw(lo + a, lo + z), A.min, A.max, ["SEG"] + pk(h)[a // 512:z // 512], cmk[a // 512:z // 512])
                most = T.SC[:, lo + 15:lo + 2048:16]
                step("two%d" % h)
                cp(tri[1], most, cmk, ["Y1%d" % h], OPT["two"][h])
            step("lin%d" % h)
            mm(v[0], T.ZERO[0:1, :], T.ONES[0:1, 0:H], True, False, ["ZERO", "ONES"], [vk])
            mm(v[1], T.LIM[0:3, :], T.ONES[0:3, 0:H], False, False, ["LIM", "ONES"], [vk])
            mm(v[2], T.LIM[0:2, :], T.ONES[0:2, 0:H], False, False, ["LIM", "ONES"], [vk])
            step("v1%d" % h)
            mm(v[1], T.NBO2[:], sg, False, False, ["NBO2", "SG%d" % h], [vk])
            step("cmp%d" % h)
            tt(T.CMP[:, half(h)], most, BA[h][:, 2 * H:3 * H], A.is_gt, cmk + [ck], ["CMP%d" % h])
            mm(v[2], T.NBO[:], T.CMP[:, half(h)], False, True, ["NBO", "CMP%d" % h], [vk])
            out = slice(L0 + 3 * H * h, L0 + 3 * H * h + 3 * H)
            step("snd%d" % h)
            scan(T.SND[:, out], bank(3 + h, H, 4 * H), T.TRI[:, half(h, 3 * H)], A.min, A.max, [vk, "Y0%d" % h, "Y1%d" % h, "Y2"], [sk[h]])
            first = t == 1 and h == 0
            put("p", (T.LAND[:, out], T.SND[:, out], "arr%d%d" % (t, h), dst), [sk[h]], [lk[h]], 300.0 + (FIRST if first else 0.0), LAT)

        def room_left():
            step("sla")
            mm(T.B0[:, 0:256], T.ID[:], T.CAP[:, c:2048:8], True, False, ["ID", "CAP"], ["B0.d"])
            for h in (0, 1):
                step("slb%d" % h)
                mm(T.B0[:, half(h)], T.NID[:], snd[h], False, h == 1, ["NID", sk[h]], ["B0.d"])
            step("sl")
            act(T.SL[:, c:2048:8], T.B0[:, 0:256], ["B0.d"], ["SL"], F.Relu)

        def candidates(h):
            ul, key = (T.B2[:, 440:448], "B2.u") if h == 0 else (T.B1[:, 0:8], "B1.k")
            step("u%d" % h)
            for r in range(16):
                mm(ul, T.W16[:, 15 - r:143 - r], msg(T.LAND, H * h + r, H * h + H, 16), r == 0, r == 15, ["W16", lk[h]], [key])
            step("ui%d" % h)
            tt(T.XI[:, half(h, 8)], ul, T.C37[:, half(h, 8)], A.add, [key, "C37"], ["XIu%d" % h])
            step("uj%d" % h)
            ts(T.XI2[:, half(h, 8)], T.XI[:, half(h, 8)], 4095, None, A.bitwise_and, None, ["XIu%d" % h], ["XJu%d" % h])
            step("ul%d" % h)
            cp(T.UL[:, half(h, 8)], T.XI2[:, half(h, 8)], ["XJu%d" % h], ["UL%d" % h])
            if OPT["pf"] == "v":
                step("pf%d" % h)
                gather("v", T.PH[:, half(h)], T.TAB[:], T.UL[:, half(h, 8)], tab + ["UL%d" % h], ["PF%d" % h])
                step("p16%d" % h)
                cp(T.P16[:, half(h)], T.PH[:, half(h)], ["PF%d" % h], ["P16%d" % h])
                return
            step("p16%d" % h)
            gather("v", T.P16[:, half(h)], T.TAB[:], T.UL[:, half(h, 8)], tab + ["UL%d" % h], ["P16%d" % h])
            step("pf%d" % h)
            gather("a", T.PF[:, half(h)], T.TAB[:], T.UL[:, half(h, 8)], tab + ["UL%d" % h], ["PF%d" % h])

        def scores(h):
            sl, mine = T.SL[:, 0:2048], range(4 * h, 4 * h + 4)
            for j, m in runs([j for j in mine if plan[j] == "s"], 2):
                bn, s = (3, 5)[[x[0] for x in runs(share, 2)].index(j) & 1], slice(512 * j, 512 * (j + m))
                mx = ["MX%d" % (j + y) for y in range(m)]
                w, per = 32 * m, 16 // m
                step("m63%d" % j)
                ts(T.M63[:, 32 * j:32 * j + w], msg(T.LAND, 32 * j, 32 * j + w), 63.0, None, A.min, None, [lk[h]], ["M63%d" % j])
                step("shw%d" % j)
                for k in range(16):
                    mm(bank(bn, w * k, w * k + w), T.ID[:], T.M63[:, 32 * j:32 * j + w], k % per == 0, False, ["ID", "M63%d" % j], whole[bn + k // per])
                step("shg%d" % j)
                gather("a", T.MX[:, s], sl, T.P16[:, 32 * j:32 * (j + m)], ["SL", "P16%d" % h], mx)
                step("shr%d" % j)
                for k in range(16):
                    mm(bank(bn, w * k, w * k + w), T.NID[:], T.MX[:, 512 * j + k:512 * (j + m):16], False, k % per == per - 1, ["NID"] + mx,
                       whole[bn + k // per])
                act(T.SC[:, s], bank(bn, 0, 512 * m), sum((whole[bn + y] for y in range(m)), []), ["SC%d" % (j + y) for y in range(m)], F.Relu)
            for j, m in runs([j for j in mine if plan[j] == "v"], OPT["wm"]):
                lo, sp = 512 * (j % 4), ["SP%d" % ((j + y) % 4) for y in range(m)]
                step("sp%d" % j)
                cp(T.SP[:, lo:lo + 512 * m:16], msg(T.LAND, 32 * j, 32 * (j + m)), [lk[h]], sp)
                step("wd%d" % j)
                scan(T.MX[:, 512 * j:512 * (j + m)], T.SEG[:, 0:512 * m], T.SP[:, lo:lo + 512 * m], A.min, A.max, ["SEG"] + sp,
                     ["MX%d" % (j + y) for y in range(m)])
            for j, m in runs([j for j in mine if plan[j] != "s"], OPT["vm"]):
                n = int(OPT["scp"][j])
                for y in range(n):
                    lo, hi = 32 * j + 32 * m * y // n, 32 * j + 32 * m * (y + 1) // n
                    step("sc%d" % j + ("", "b")[y], "sc")
                    tt(T.SC[:, 16 * lo:16 * hi], sl.indirect(T.P16[:, lo:hi]), T.MX[:, 16 * lo:16 * hi], A.min,
                       ["SL", "P16%d" % h] + ["MX%d" % x for x in range(j, j + m)], ["SC%d" % x for x in range(j, j + m)], GATHER)

        def keys(h):
            b, at = T.B1, 2 * H * h
            parts = []
            for kind in (True, False):
                for j, m in runs([j for j in range(4 * h, 4 * h + 4) if (plan[j] == "s") == kind], 2 if kind else OPT["pm"]):
                    j %= 4
                    parts += [(j, m, kind)] if j == 0 or m == 1 or j == 2 else [(j, 1, kind), (j + 1, m - 1, kind)]

            def nodes(j, m, key):
                pf, ident = ("PF", "IDF") if OPT["pf"] == "a" else ("PH", "IDH")
                mm(b[32 * j:32 * (j + m), at:at + H], T[pf][:, H * h + 32 * j:H * h + 32 * (j + m)], T[ident][:], False, False, ["PF%d" % h, ident, "B1.p"], key)
            step("pn%d" % h)
            nodes(0, 4, ["B1.p%d" % z for z in range(4 * h, 4 * h + 4)])
            step("pc%d" % h)
            for j, m, kind in parts:
                if kind:
                    mm(b[32 * j:32 * (j + m), at:at + 2 * H], T.M63[:, H * h + 32 * j:H * h + 32 * (j + m)], T.BW32K[:], False, False,
                       ["BW32K", "M63%d" % (4 * h + j), "B1.p"], ["B1.p%d" % y for y in range(4 * h + j, 4 * h + j + m)])
            for j, m, kind in parts:
                lo, hi = 32 * j, 32 * (j + m)
                wk, key = "NB32K" if kind else "B32K", ["B1.p%d" % y for y in range(4 * h + j, 4 * h + j + m)]
                step("ps%d" % (4 * h + j))
                first = 2048 * h + 16 * lo
                for k in range(16):
                    sc = T.SC[:, first + (hi - lo) * k:first + (hi - lo) * (k + 1)] if kind else T.SC[:, first + k:2048 * h + 16 * hi:16]
                    mm(b[lo:hi, at + k:at + 2 * H:16], sc, T[wk][:], False, False, [wk, "B1.p"] + ["SC%d" % y for y in range(4 * h + j, 4 * h + j + m)], key)

        def parents():
            every = ["B1.p"] + ["B1.p%d" % j for j in range(8)]
            step("pc")
            mm(T.B1[:], T.ONES[0:2, 0:H], T.KC2[0:2, :], True, False, ["KC2", "ONES"], every + ["B1.k", "B1.kl"])
            keys(0)
            keys(1)
            step("pe")
            mm(T.B1[:, H:H + 2], T.ONES[0:1, 0:H], T.ZERO[0:1, 0:2], False, True, ["ONES", "ZERO"], every + ["B1.k", "B1.kl"])
            step("qs")
            scan(T.QS[:], T.MB[:], T.B1[:], A.min, A.max, ["MB", "B1.p", "B1.k", "B1.kl"], ["QS"])
            step("qi")
            for h in (0, 1):
                at = 2 * H * h
                tt(T.QF[:, half(h, 8)], T.QS[:, at + 15:at + H:16], T.QS[:, at + H + 15:at + 2 * H:16], A.subtract, ["QS"], ["QF%d" % h])
            step("qx")
            tt(T.XW[:], T.QF[:].indirect(T.OFFC[:, 0:16]), T.DELB[:], A.mult, ["QF0", "QF1", "OFFC", "DELB"], ["XW"], GATHER)
            for h in (0, 1):
                mm(bank(2, 416 + 8 * h, 424 + 8 * h), T.XW[:, half(h)], T.BOH[:], h == 0, h == 1, ["XW", "BOH"], ["B2.lv"])
            step("lv")
            cp(T.LV[:], bank(2, 416, 432), ["B2.lv"], ["LV"])
            step("vb")
            gather("v", T.VB[:], T.IO2K[:], T.LV[:], ["IO2K", "LV"], ["VB"])
            if not last:
                step("lxw")
                act(T.LXW[:], T.LXT[:].indirect(T.LV[:]), ["LXT", "LV"], ["LXW"], F.Abs, bias=-768.0 * t, rate=GATHER)

        now[0] = t
        if t > 1:
            parity()
        else:
            first_pieces(OPT["early"])
        first_rows()
        worst(0)
        worst(1)
        if t == 1:
            first_pieces(OPT["late"])
        kept()
        messages(0)
        messages(1)
        if t > 1:
            words(t - 1)
        if not last:
            offsets(t + 1)
        room_left()
        suspended(t)
        for h in (0, 1):
            step("res%d" % h, "res")
            cp(T.RES[:, c + 1024 * h:1024 * h + 1024:8], snd[h], [sk[h]], ["RES"], "p")
        if last:
            step("yr")
            dma("s", T.yr[:], T.RES[:, 0:2048], "dyr", ["RES"], ["yr"], 512)
        else:
            for h in (0, 1):
                step("gh%d" % h, "gh")
                cp(T.RES[:, 2048 + c * Q + H * h:2048 + c * Q + H * h + H], land[h], [lk[h]], ["RESG"], "p")
        if t + 2 <= NT:
            cap_wide(t + 2, range(0 if OPT["clip"][t + 1] < OPT["clip"][t - 1] else 1, 16))
        step("offa")
        mm(T.B7[:, 0:256], T.NID[:], T.OFFD[:], True, False, ["NID", "OFFD"], ["B7.x"])
        if not last:
            mm(T.B7[:, 0:256], T.ID[:], T.OFFA[:], False, False, ["ID", "OFFA"], ["B7.x"])
        for h in (0, 1):
            candidates(h)
            scores(h)
        if not last:
            j = 0
            for x in OPT["rows"][c].split():
                rows(x[0], j, len(x))
                j += len(x)
            for x in OPT["as"].split():
                row0_aside(x[0], t + 1, int(x[1]), int(x[2]))
        parents()
        step("eqm")
        mm(bank(5, 0, tail_cols), T.XW[:, half(1)], T.NSEL[:, 0:tail_cols], True, False, ["XW"] + ["NSEL%d" % x[0] for x in tail], whole[5])
        for b, lo, m in tail:
            mm(bank(5, lo, lo + 16), T.ID[:], T.MASK[:], False, False, ["ID", "MASK"], ["B5.c"])
        step("eqt")
        for b, lo, m in tail:
            mm(bank(5, lo, lo + m), T.IDH[:], T.VB[:, 16 * b:Q], False, b == 15, ["IDH", "VB"], ["B5.c"])
        step("eqv")
        ts(T.EQT[:, 0:tail_cols], bank(5, 0, tail_cols), 0.0, None, A.is_equal, None, whole[5], ["EQT"])
        for b, lo, m in tail:
            mm(T.B7[:, 16 * b:Q], T.BO4[:], T.EQT[:, lo:lo + m], False, False, ["BO4", "EQT", "B7.x"], ["B7.x%d" % b])
        for i in range(first_tail):
            step("eq%d" % i)
            ts(T.EQ[:, i, 0:256 - 16 * i], T.VB[:, 16 * i:256], bank(2, 416 + i, 417 + i), None, A.is_equal, None, ["VB", "B2.lv"], ["EQ%d" % i])
            mm(T.B7[:, 16 * i + 16:256], T.BO4[:], T.EQ[:, i, 16:256 - 16 * i], False, False, ["BO4", "EQ%d" % i, "B7.x"], ["B7.x%d" % i])
        step("eqx")
        if not last:
            mm(T.B7[:, 0:256], T.MULD[:], T.LXW[:], False, False, ["MULD", "LXW", "B7.x"], ["B7.xm"])
        else:
            mm(T.B7[:, 0:256], T.IDH[:], T.VB[:], False, False, ["IDH", "VB", "B7.x"], ["B7.xm"])
        e = first_tail - 2
        step("eqd")
        mm(T.B7[:, 0:16 * e], T.BT4[:], T.EQ[:, 0:e, 0:16], False, False, ["BT4", "B7.x"] + ["EQ%d" % i for i in range(e)], ["B7.xd"])
        step("eqe")
        mm(T.B7[:, 16 * e:16 * e + 32], T.BT4[:], T.EQ[:, e:e + 2, 0:16], False, True, ["BT4", "EQ%d" % e, "EQ%d" % (e + 1)],
           ["B7.x", "B7.xm", "B7.xd"] + ["B7.x%d" % i for i in range(16)])
        if last:
            step("MTW")
            lin("v", T.MTP[:, 0:Q:16], T.LB[:], 1.0, -float(FAR), ["TW"], ["MTP"])
        step("cns")
        scan(T.CNS[:], T.MTP[:], T.B7[:, 0:256], A.max, A.min, ["MTP", "B7.x"], ["CNS"])
        if not last:
            step("far")
            mm(bank(2, 400, 416), T.CFAR[0:1, :], T.ONES[0:1, 0:16], True, False, ["CFAR", "ONES"], ["B2.far"])
            for h in (0, 1):
                mm(bank(2, 400 + 8 * h, 408 + 8 * h), T.XW[:, half(h)], T.BOH[:], False, h == 1, ["XW", "BOH"], ["B2.far"])
            step("pl")
            cp(T.PL[:], T.CNS[:, 15:256:16], ["CNS"], ["PL"])
            step("cnw")
            scan(T.CNW[:], T.NMB[:], T.B7[:, 0:256], A.max, A.min, ["NMB", "B7.x"], ["CNW"])
            step("patch")
            scatter(rw(0, 4608), T.PL[:], msg(T.LAND, 0, Q), ["PL"] + lk, pk(0) + pk(1) + p0(0) + p0(1) + ["PKT"])

    first_offsets(0)
    first_offsets(1)
    for j in range(8):
        cp(T.WD[:, j:2048:8], T.BRI[:, j:2048:8], ["BRI"], ["WDc%d" % j])
    j = 0
    for x in OPT["gs"].split():
        rows(x[0], j, len(x), "G")
        j += len(x)
    for h in (0, 1):
        row0_aside(OPT["as1"][h], 1, 4 * h, 4, "AS")
    step(None)
    for t in (1, 2):
        cut, cx = Q - 32 * OPT["clip"][t - 1], "CX%d" % (t & 1)
        for lo in range(0, cut, H):
            m, sp = min(H, cut - lo), ["SP%d" % j for j in range(4)]
            if t == 2 and OPT["cy"][lo // H] == "p":
                for k in range(16):
                    step("CY%d" % k)
                    cp(T[cx][:, 16 * lo + k:16 * (lo + m):16], T.CAP[:, t - 1 + 8 * lo:8 * (lo + m):8], ["CAP%d" % (lo // H)], [cx + "k%d" % k], "p")
                continue
            step("SX%d%d" % (t, lo // H))
            cp(T.SP[:, 0:16 * m:16], T.CAP[:, t - 1 + 8 * lo:8 * (lo + m):8], ["CAP%d" % (lo // H)], sp)
            step(None)
            scan(T[cx][:, 16 * lo:16 * (lo + m)], T.SEG[:, 0:16 * m], T.SP[:, 0:16 * m], A.min, A.max, ["SEG"] + sp, [cx + "h%d" % (lo // H)])
    for t in range(1, NT + 1):
        one_round(t)
    now[0] = NT + 1
    words(NT)
    step("yb")
    dma("s", T.yb[:], T.WD[:, 0:2048], "dyb", wdk, ["yb"], 1024)

    if len(calls) not in ORDERS:
        ORDERS[len(calls)] = issue_order(calls)
    queues = {"v": V, "t": PE, "a": AC, "p": g, "s": g.sync}
    own = {"v": "cv", "t": "ct", "a": "ca", "p": "cp"}
    count = {k: 0 for k in own}
    known = {k: {} for k in queues}
    lastw, readers, banks, pieces = {}, {}, {}, {}
    sent = 0
    used = []
    for i in ORDERS[len(calls)]:
        q, f, r, w, _ns, lat = calls[i][:6]
        TAG[0] = i
        remote = q == "p" and lat > 0
        if remote:
            w, arrival = [], w[0]
        piece = calls[i][8]
        toks = [lastw[k] for k in w if k in lastw and not (piece and pieces.get(k) == (q, piece))]
        for k in w:
            toks += list(readers.get(k, {}).values())
            pieces[k] = (q, piece)
        toks += [lastw[k] for k in r if k in lastw]
        for b in banks_of(list(r) + list(w)):
            toks += [tok for e, tok in banks.get(b, {}).items() if e != q]
        best = {}
        for tok in toks:
            if not (q == "t" and tok[0] == "ct") and (tok[0] not in best or best[tok[0]][1] < tok[1]):
                best[tok[0]] = tok
        kn = known[q]
        for s, val, snap in sorted(best.values(), key=lambda x: -len(x[2])):
            if kn.get(s, 0) < val:
                queues[q].wait_ge(T.sem[s], val)
                kn[s] = val
                for s2, v2 in snap.items():
                    kn[s2] = max(kn.get(s2, 0), v2)
        if remote:
            out, in_, sem, dst = f
            rid, pid, _s = topo.addr(dst)
            g.remote_dma(out, in_, T.sem[sem], T.sem.loc, pid, rid, topo.mask(core, dst))
            lastw[arrival] = (sem, len(topo.engines(core, dst)), {})
            sent += len(topo.engines(core, dst))
            continue
        if lat:
            queues[q].dma_start(f[0], f[1]).then_inc(T.sem[f[2]], 16)
            used.append(f[2])
            tok = (f[2], 16, dict(kn))
        else:
            count[q] += 1
            tok = (own[q], count[q], dict(kn))
            f().then_inc(T.sem[own[q]], 1)
        for k in r:
            readers.setdefault(k, {})[tok[0]] = tok
        for k in w:
            lastw[k] = tok
            readers[k] = {}
        for b in banks_of(list(r) + list(w)):
            banks.setdefault(b, {})[q] = tok
    g.wait_ge(T.sem.loc, sent)
    for q, s in own.items():
        g.wait_ge(T.sem[s], count[q])
    for s in used:
        g.wait_ge(T.sem[s], 16)
